import numpy as np
import ml_dtypes


def mxq(x, axis, fmt="e4m3"):
    dtype, down = {"e4m3": (ml_dtypes.float8_e4m3fn, 7), "e5m2": (ml_dtypes.float8_e5m2, 14)}[fmt]
    v = np.moveaxis(np.asarray(x, np.float32).astype(ml_dtypes.bfloat16).astype(np.float64), axis, -1)
    blocks = v.reshape(v.shape[:-1] + (-1, 32))
    amax = np.abs(blocks).max(-1, keepdims=True)
    byte = np.maximum(np.where(amax > 0, np.frexp(amax)[1] - 1 + 127, 0) - down, 1)
    scale = np.exp2(byte - 127.0)
    codes = (blocks / scale).astype(np.float32).astype(dtype).astype(np.float64)
    return np.moveaxis((codes * scale).reshape(v.shape), -1, axis)


WIDE = False


def mx_kscale(k):
    if not WIDE:
        return np.ones(k)
    levels = np.array([10, -10, 5, -5, 0])
    if k % 512:
        return np.exp2(np.random.permutation(np.resize(levels, k // 32))).repeat(32)
    a = np.empty((k // 512, 16))
    for p in range(k // 512):
        a[p, :8] = np.random.permutation(np.resize(levels, 8))
        for g in range(8):
            far = levels[np.abs(levels - a[p, g]) >= 10]
            a[p, g + 8] = far[np.random.randint(len(far))]
    return np.exp2(a.ravel()).repeat(32)


BF16 = ml_dtypes.bfloat16


def bf(x):
    return np.asarray(x, np.float32).astype(BF16)


def f64(x):
    return np.asarray(x).astype(np.float64)


B, D, R, E = 128, 3072, 2048, 2


def softmax(g):
    e = np.exp(g - g.max(axis=-1, keepdims=True))
    return e / e.sum(axis=-1, keepdims=True)


def draw0():
    s, t = mx_kscale(D), mx_kscale(R)
    x0 = bf(np.random.standard_normal((B, D)) * s)
    x = bf(np.random.standard_normal((B, D)) * s)
    v = bf(np.random.standard_normal((E, D, R)) / np.sqrt(D) / s[None, :, None])
    c = bf((1.0 + 0.1 * np.random.standard_normal((E, R))) * t)
    u = bf(1.5 * np.random.standard_normal((E, R, D)) / np.sqrt(R) / t[None, :, None])
    bias = bf(0.3 * np.random.standard_normal(D))
    gate_logits = bf(np.random.standard_normal((B, E)))
    return {"x0": x0, "x": x, "v": v, "c": c, "u": u, "bias": bias, "gate_logits": gate_logits}


def expert_outputs(x, v, c, u):
    a = mxq(x, 1, "e4m3") @ mxq(v, 1, "e4m3")
    h = np.tanh(a) * c[:, None, :]
    return mxq(h, 2, "e4m3") @ mxq(u, 1, "e4m3")


def core(x0, x, v, c, u, bias, gate_logits):
    y = expert_outputs(f64(x), f64(v), f64(c), f64(u))
    p = softmax(f64(gate_logits))
    weights = np.transpose(p)[:, :, None]
    m = np.sum(weights * y, axis=0)
    return f64(x0) * (m + f64(bias)[None, :]) + f64(x)


def e4m3fn_bytes(y):
    return np.clip(np.asarray(y, np.float64), -448.0, 448.0).astype(np.float32).astype(ml_dtypes.float8_e4m3fn).view(np.uint8)


def e4m3fn_values(b):
    return np.asarray(b, np.uint8).view(ml_dtypes.float8_e4m3fn).astype(np.float64)


def setup_inputs():
    d = draw0()
    x0 = np.asarray(d['v']).astype(np.float64)
    s = (np.max(np.abs(x0), axis=(0, 2), keepdims=True) / 448.0).astype(np.float32)
    out = {}
    for k, v in d.items():
        if k == 'v':
            out['v_bytes'] = e4m3fn_bytes(x0 / s.astype(np.float64))
            out['v_scale'] = s
        else:
            out[k] = v
    return out


def reference(x0, x, v_bytes, v_scale, c, u, bias, gate_logits):
    return core(x0, x, e4m3fn_values(v_bytes) * v_scale.astype(np.float64), c, u, bias, gate_logits)

@@ -1,0 +1,307 @@
+from contextlib import ExitStack
+
+import concourse.mybir as mybir
+from concourse.masks import make_identity
+
+B, D, R, E = 128, 3072, 2048, 2
+P = 128
+PACK = 4
+K_PASS = P * PACK
+FLOPS = 2 * 2 * E * B * D * R
+
+F32 = mybir.dt.float32
+BF16 = mybir.dt.bfloat16
+U32 = mybir.dt.uint32
+U8 = mybir.dt.uint8
+FP8 = mybir.dt.float8_e4m3fn
+FP8X4 = mybir.dt.float8_e4m3fn_x4
+ACT = mybir.ActivationFunctionType
+ALU = mybir.AluOpType
+AX = mybir.AxisListType
+
+W = 1024
+NB = 512
+V_PASSES = D // K_PASS
+U_PASSES = R // K_PASS
+RH = R // W
+DB = D // W
+V_WIDEN = 320
+U_VEC = 432
+U_VEC_PE = 352
+U_PE = 256
+
+
+def tile_dcnv2lowrankexpertcross_w_kernel(tc, x0, x, v_bytes, v_scale, c, u, bias, gate_logits, out):
+    nc = tc.nc
+    with ExitStack() as ctx:
+        const = ctx.enter_context(tc.tile_pool(name="const", bufs=1))
+        byte_pool = ctx.enter_context(tc.tile_pool(name="byte_pool", bufs=6))
+        wide_pool = ctx.enter_context(tc.tile_pool(name="wide_pool", bufs=3))
+        raw_pool = ctx.enter_context(tc.tile_pool(name="raw_pool", bufs=8))
+        inter_pool = ctx.enter_context(tc.tile_pool(name="inter_pool", bufs=3))
+        code_pool = ctx.enter_context(tc.tile_pool(name="code_pool", bufs=4))
+        small = ctx.enter_context(tc.tile_pool(name="small", bufs=2))
+        mix = ctx.enter_context(tc.tile_pool(name="mix", bufs=2))
+        acc_pool = ctx.enter_context(tc.psum_pool(name="acc_pool", bufs=4))
+        tr_pool = ctx.enter_context(tc.psum_pool(name="tr_pool", bufs=4))
+
+        ident = const.tile([P, P], F32)
+        ident16 = const.tile([P, P], BF16)
+        scale_sb = const.tile([P, V_PASSES, PACK], F32)
+        x_sb = const.tile([B, D], BF16)
+        x0_sb = const.tile([B, D], BF16)
+        bias_sb = const.tile([B, D], BF16)
+        c_sb = const.tile([B, E, R], BF16)
+        gate_sb = const.tile([B, E], BF16)
+        x_codes = const.tile([P, V_PASSES, B], U32, align_bytes=64)
+        x_scales = const.tile([P, V_PASSES, B], U8, align_bytes=64)
+        h_codes = const.tile([P, E, U_PASSES, B], U32, align_bytes=64)
+        h_scales = const.tile([P, E, U_PASSES, B], U8, align_bytes=64)
+
+        units = [("v", e, hb, g) for e in range(E) for hb in range(RH) for g in range(V_PASSES)]
+        n_v = len(units)
+        units += [("u", e, db, g) for db in range(DB) for e in range(E) for g in range(U_PASSES)]
+        n = len(units)
+        raw = {}
+        wide = {}
+        inter = {}
+        codes = {}
+        accs = {}
+        hid = {}
+        mixed = {}
+        gates = {}
+        pe_out = {}
+
+        def load(i):
+            kind, e, blk, g = units[i]
+            ks = slice(g * K_PASS, (g + 1) * K_PASS)
+            cs = slice(blk * W, (blk + 1) * W)
+            if kind == "v":
+                v_raw = byte_pool.tile([P, PACK, W], U8)
+                nc.sync.dma_start(out=v_raw[:], in_=v_bytes[e, ks, cs].rearrange("(p t) w -> p t w", t=PACK))
+                raw[i] = v_raw
+            else:
+                u_raw = raw_pool.tile([P, PACK, W], BF16)
+                nc.sync.dma_start(out=u_raw[:], in_=u[e, ks, cs].rearrange("(p t) w -> p t w", t=PACK))
+                raw[i] = u_raw
+
+        def widen(i):
+            kind, e, blk, g = units[i]
+            if kind == "u":
+                return
+            v_wide = wide_pool.tile([P, PACK, W], BF16)
+            v_raw = raw.pop(i)
+            ends = {0: (W, W, 0, 0), 1: (W, W, W, 0)}.get(i, (W, W, W, W - V_WIDEN))
+            for t in range(PACK):
+                if ends[t] < W:
+                    nc.vector.tensor_scalar(
+                        out=v_wide[:, t, ends[t]:], in0=v_raw[:, t, ends[t]:].bitcast(FP8),
+                        scalar1=scale_sb[:, g, t:t + 1], scalar2=None, op0=ALU.mult)
+                if ends[t] > 0:
+                    nc.scalar.activation(
+                        out=v_wide[:, t, :ends[t]], in_=v_raw[:, t, :ends[t]].bitcast(FP8),
+                        func=ACT.Copy, scale=scale_sb[:, g, t:t + 1])
+            wide[i] = v_wide
+
+        def interleave(copy, dst, src):
+            copy(out=dst.rearrange("p (c i) t -> p c t i", i=4), in_=src.rearrange("p t (c i) -> p c t i", i=4))
+
+        def arrange(i):
+            kind, e, blk, g = units[i]
+            grouped = inter_pool.tile([P, W, PACK], BF16, align_bytes=64)
+            if kind == "v":
+                interleave(nc.vector.tensor_copy, grouped[:], wide.pop(i)[:])
+            else:
+                u_raw = raw.pop(i)
+                on_pe = pe_out.pop(i, None)
+                a = U_VEC if on_pe is None else U_VEC_PE
+                b = W if on_pe is None else W - U_PE
+                interleave(nc.vector.tensor_copy, grouped[:, :a, :], u_raw[:, :, :a])
+                if on_pe is not None:
+                    nc.scalar.copy(out=grouped[:, b:, :].rearrange("p w t -> p (w t)"), in_=on_pe[:])
+                interleave(nc.scalar.copy, grouped[:, a:b, :], u_raw[:, :, a:b])
+            inter[i] = grouped
+
+        def pe_interleave(i):
+            if units[i][0] == "v" or (i - n_v) % 5 == 0:
+                return
+            slots = tr_pool.tile([P, U_PE * PACK], BF16)
+            for j in range(U_PE // P):
+                cs = slice(W - U_PE + j * P, W - U_PE + (j + 1) * P)
+                nc.tensor.matmul(
+                    out=slots[:, j * NB:(j + 1) * NB], lhsT=ident16[:],
+                    rhs=raw[i][:, :, cs].rearrange("p t w -> p w t"), start=True, stop=True)
+            pe_out[i] = slots
+
+        def quantize(i):
+            w_codes = code_pool.tile([P, W], U32, align_bytes=64)
+            w_scales = code_pool.tile([P, W], U8, align_bytes=64)
+            nc.vector.quantize_mx(
+                out=w_codes[:].bitcast(FP8X4), scales=w_scales[:],
+                in_=inter.pop(i)[:].rearrange("p w t -> p (w t)"))
+            codes[i] = (w_codes, w_scales)
+
+        def multiply(i):
+            kind, e, blk, g = units[i]
+            w_codes, w_scales = codes.pop(i)
+            last = (V_PASSES if kind == "v" else U_PASSES) - 1
+            if g == 0:
+                banks = []
+                for j in range(W // NB):
+                    acc = acc_pool.tile([B, NB], F32)
+                    banks.append(acc)
+                accs[(kind, e, blk)] = banks
+            banks = accs[(kind, e, blk)]
+            for j in range(W // NB):
+                js = slice(j * NB, (j + 1) * NB)
+                lhs = x_codes[:, g, :] if kind == "v" else h_codes[:, e, g, :]
+                lhs_scale = x_scales[:, g, :] if kind == "v" else h_scales[:, e, g, :]
+                nc.tensor.matmul_mx(
+                    out=banks[j][:], lhsT=lhs.bitcast(FP8X4), lhsT_scale=lhs_scale,
+                    rhs=w_codes[:, js].bitcast(FP8X4), rhs_scale=w_scales[:, js],
+                    start=(g == 0), stop=(g == last))
+
+        def turn(src_words, q, slots):
+            for j in range(2):
+                for w in range(2):
+                    first = 256 * (2 * q + j)
+                    nc.tensor.transpose(slots[:, 2 * j + w, :], src_words[:, first + w:first + 256:2], ident[:])
+
+        def group_words(dst, slots):
+            nc.vector.tensor_copy(
+                out=dst.bitcast(F32).rearrange("p (j r w) -> p j r w", j=2, w=2),
+                in_=slots.rearrange("p (j w) r -> p j r w", w=2))
+
+        def hidden_tanh(e, hb):
+            th = small.tile([B, W], F32)
+            for j, acc in enumerate(accs.pop(("v", e, hb))):
+                nc.scalar.activation(out=th[:, j * NB:(j + 1) * NB], in_=acc[:], func=ACT.Tanh)
+            hid[(e, hb)] = th
+
+        def hidden_scale(e, hb):
+            h = small.tile([B, W], BF16)
+            nc.vector.tensor_tensor(out=h[:], in0=hid[(e, hb)][:], in1=c_sb[:, e, hb * W:(hb + 1) * W], op=ALU.mult)
+            slots = tr_pool.tile([P, 4, B], F32)
+            turn(h[:].bitcast(F32), 0, slots)
+            hid[(e, hb)] = slots
+
+        def hidden_group(e, hb):
+            hg = small.tile([P, 2 * B * PACK], BF16, align_bytes=64)
+            group_words(hg[:], hid[(e, hb)][:])
+            hid[(e, hb)] = hg
+
+        def hidden_quantize(e, hb):
+            gs = slice(2 * hb, 2 * hb + 2)
+            nc.vector.quantize_mx(
+                out=h_codes[:, e, gs, :].rearrange("p g b -> p (g b)").bitcast(FP8X4),
+                scales=h_scales[:, e, gs, :].rearrange("p g b -> p (g b)"),
+                in_=hid.pop((e, hb))[:])
+
+        def epilogue(e, db):
+            banks = accs.pop(("u", e, db))
+            for j in range(W // NB):
+                cols = slice(db * W + j * NB, db * W + (j + 1) * NB)
+                if e == 0:
+                    m = mix.tile([B, NB], F32)
+                    nc.vector.scalar_tensor_tensor(
+                        out=m[:], in0=banks[j][:], scalar=gates["p"][:, 0:1], in1=bias_sb[:, cols], op0=ALU.mult, op1=ALU.add)
+                    mixed[(db, j)] = m
+                else:
+                    m2 = mix.tile([B, NB], F32)
+                    nc.vector.scalar_tensor_tensor(
+                        out=m2[:], in0=banks[j][:], scalar=gates["p"][:, 1:2], in1=mixed.pop((db, j))[:], op0=ALU.mult, op1=ALU.add)
+                    mixed[(db, j)] = m2
+            if e == 1:
+                prods = []
+                for j in range(W // NB):
+                    cols = slice(db * W + j * NB, db * W + (j + 1) * NB)
+                    m3 = mix.tile([B, NB], F32)
+                    nc.vector.tensor_tensor(out=m3[:], in0=mixed.pop((db, j))[:], in1=x0_sb[:, cols], op=ALU.mult)
+                    prods.append(m3)
+                for j in range(W // NB):
+                    cols = slice(db * W + j * NB, db * W + (j + 1) * NB)
+                    m4 = mix.tile([B, NB], F32)
+                    nc.vector.tensor_tensor(out=m4[:], in0=prods[j][:], in1=x_sb[:, cols], op=ALU.add)
+                    nc.sync.dma_start(out=out[:, cols], in_=m4[:])
+
+        def softmax_gates():
+            top = small.tile([B, 1], F32)
+            nc.vector.tensor_reduce(out=top[:], in_=gate_sb[:], op=ALU.max, axis=AX.X)
+            shifted = small.tile([B, E], F32)
+            nc.vector.tensor_scalar(out=shifted[:], in0=gate_sb[:], scalar1=top[:], scalar2=None, op0=ALU.subtract)
+            ex = small.tile([B, E], F32)
+            nc.scalar.activation(out=ex[:], in_=shifted[:], func=ACT.Exp)
+            total = small.tile([B, 1], F32)
+            nc.vector.tensor_reduce(out=total[:], in_=ex[:], op=ALU.add, axis=AX.X)
+            inv = small.tile([B, 1], F32)
+            nc.vector.reciprocal(out=inv[:], in_=total[:])
+            p = const.tile([B, E], F32)
+            nc.vector.tensor_scalar(out=p[:], in0=ex[:], scalar1=inv[:], scalar2=None, op0=ALU.mult)
+            gates["p"] = p
+
+        make_identity(nc, ident[:])
+        nc.vector.tensor_copy(out=ident16[:], in_=ident[:])
+        with tc.manual_schedule():
+            nc.sync.dma_start(out=scale_sb[:], in_=v_scale.rearrange("o (g p t) u -> p (o g) (t u)", p=P, t=PACK))
+            load(0)
+            nc.sync.dma_start(out=x_sb[:], in_=x)
+            for i in range(1, 4):
+                load(i)
+            nc.sync.dma_start(out=gate_sb[:], in_=gate_logits)
+            loaded = [4, n_v]
+
+            for i in range(2):
+                widen(i)
+            x_groups = []
+            for q in range(3):
+                slots = tr_pool.tile([P, 4, B], F32)
+                turn(x_sb[:].bitcast(F32), q, slots)
+                xg = const.tile([P, 2 * B * PACK], BF16, align_bytes=64, name="xg%d" % q)
+                group_words(xg[:], slots[:])
+                x_groups.append(xg)
+            for q in range(3):
+                gs = slice(2 * q, 2 * q + 2)
+                nc.vector.quantize_mx(
+                    out=x_codes[:, gs, :].rearrange("p g b -> p (g b)").bitcast(FP8X4),
+                    scales=x_scales[:, gs, :].rearrange("p g b -> p (g b)"),
+                    in_=x_groups[q][:])
+            arrange(0)
+
+            later = {}
+
+            def at(step, fn, *args):
+                later.setdefault(step, []).append((fn, args))
+
+            for s in range(n + 4):
+                if s == 1:
+                    nc.sync.dma_start(out=c_sb[:], in_=c.rearrange("e r -> (e r)").partition_broadcast(P))
+                if s == 4:
+                    nc.sync.dma_start(out=bias_sb[:], in_=bias.partition_broadcast(P))
+                    nc.sync.dma_start(out=x0_sb[:], in_=x0)
+                while loaded[0] < min(n_v, s + 6):
+                    load(loaded[0])
+                    loaded[0] += 1
+                if s >= 6 and loaded[1] < n and (s < n_v - 2 and s % 2 == 0 and loaded[1] < n_v + 8 or loaded[1] < s + 8):
+                    load(loaded[1])
+                    loaded[1] += 1
+                if s + 2 < n:
+                    widen(s + 2)
+                    pe_interleave(s + 2)
+                if s + 1 < n:
+                    arrange(s + 1)
+                if s < n:
+                    quantize(s)
+                if s == 3:
+                    softmax_gates()
+                for fn, args in later.pop(s, []):
+                    fn(*args)
+                if s < n:
+                    multiply(s)
+                    kind, e, blk, g = units[s]
+                    if kind == "v" and g == V_PASSES - 1:
+                        at(s + 1, hidden_tanh, e, blk)
+                        at(s + 2, hidden_scale, e, blk)
+                        at(s + 3, hidden_group, e, blk)
+                        at(s + 4, hidden_quantize, e, blk)
+                    if kind == "u" and g == U_PASSES - 1:
+                        at(s + 1 if s < n - 1 else s + 1, epilogue, e, blk)

@@ -104,7 +104,7 @@ def tile_dcnv2lowrankexpertcross_w_kernel(tc, x0, x, v_bytes, v_scale, c, u, bia
             wide[i] = v_wide
 
         def interleave(copy, dst, src):
-            copy(out=dst.rearrange("p (c i) t -> p c t i", i=4), in_=src.rearrange("p t (c i) -> p c t i", i=4))
+            copy(out=dst.rearrange("p (c i) t -> p c t i", i=2), in_=src.rearrange("p t (c i) -> p c t i", i=2))
 
         def arrange(i):
             kind, e, blk, g = units[i]

@@ -17,7 +17,6 @@ FP8 = mybir.dt.float8_e4m3fn
 FP8X4 = mybir.dt.float8_e4m3fn_x4
 ACT = mybir.ActivationFunctionType
 ALU = mybir.AluOpType
-AX = mybir.AxisListType
 
 W = 1024
 NB = 512
@@ -25,20 +24,24 @@ V_PASSES = D // K_PASS
 U_PASSES = R // K_PASS
 RH = R // W
 DB = D // W
-V_WIDEN = 320
-U_VEC = 432
-U_VEC_PE = 352
+WIDEN_ACT = 0
+V_VEC = 256
+V_VEC0 = 0
+V_VEC_END = 480
+U_VEC = 400
+U_VEC_PE = 320
 U_PE = 256
+U_AHEAD = 6
 
 
 def tile_dcnv2lowrankexpertcross_w_kernel(tc, x0, x, v_bytes, v_scale, c, u, bias, gate_logits, out):
     nc = tc.nc
     with ExitStack() as ctx:
         const = ctx.enter_context(tc.tile_pool(name="const", bufs=1))
-        byte_pool = ctx.enter_context(tc.tile_pool(name="byte_pool", bufs=6))
+        byte_pool = ctx.enter_context(tc.tile_pool(name="byte_pool", bufs=3))
         wide_pool = ctx.enter_context(tc.tile_pool(name="wide_pool", bufs=3))
-        raw_pool = ctx.enter_context(tc.tile_pool(name="raw_pool", bufs=8))
-        inter_pool = ctx.enter_context(tc.tile_pool(name="inter_pool", bufs=3))
+        raw_pool = ctx.enter_context(tc.tile_pool(name="raw_pool", bufs=U_AHEAD))
+        inter_pool = ctx.enter_context(tc.tile_pool(name="inter_pool", bufs=4))
         code_pool = ctx.enter_context(tc.tile_pool(name="code_pool", bufs=4))
         small = ctx.enter_context(tc.tile_pool(name="small", bufs=2))
         mix = ctx.enter_context(tc.tile_pool(name="mix", bufs=2))
@@ -51,79 +54,96 @@ def tile_dcnv2lowrankexpertcross_w_kernel(tc, x0, x, v_bytes, v_scale, c, u, bia
         x_sb = const.tile([B, D], BF16)
         x0_sb = const.tile([B, D], BF16)
         bias_sb = const.tile([B, D], BF16)
-        c_sb = const.tile([B, E, R], BF16)
+        c_sb = const.tile([P, E * U_PASSES, PACK], BF16)
         gate_sb = const.tile([B, E], BF16)
+        share = const.tile([B, E], F32)
+        x_grouped = const.tile([P, V_PASSES * B * PACK], BF16, align_bytes=64)
         x_codes = const.tile([P, V_PASSES, B], U32, align_bytes=64)
         x_scales = const.tile([P, V_PASSES, B], U8, align_bytes=64)
         h_codes = const.tile([P, E, U_PASSES, B], U32, align_bytes=64)
         h_scales = const.tile([P, E, U_PASSES, B], U8, align_bytes=64)
 
-        units = [("v", e, hb, g) for e in range(E) for hb in range(RH) for g in range(V_PASSES)]
+        slabs = [(e, g) for e in range(E) for g in range(V_PASSES)]
+        units = [("v", e, hb, g) for e, g in slabs for hb in range(RH)]
         n_v = len(units)
         units += [("u", e, db, g) for db in range(DB) for e in range(E) for g in range(U_PASSES)]
         n = len(units)
         raw = {}
+        slab_raw = {}
         wide = {}
         inter = {}
         codes = {}
         accs = {}
         hid = {}
         mixed = {}
-        gates = {}
         pe_out = {}
 
-        def load(i):
-            kind, e, blk, g = units[i]
-            ks = slice(g * K_PASS, (g + 1) * K_PASS)
-            cs = slice(blk * W, (blk + 1) * W)
-            if kind == "v":
-                v_raw = byte_pool.tile([P, PACK, W], U8)
-                nc.sync.dma_start(out=v_raw[:], in_=v_bytes[e, ks, cs].rearrange("(p t) w -> p t w", t=PACK))
-                raw[i] = v_raw
-            else:
-                u_raw = raw_pool.tile([P, PACK, W], BF16)
-                nc.sync.dma_start(out=u_raw[:], in_=u[e, ks, cs].rearrange("(p t) w -> p t w", t=PACK))
-                raw[i] = u_raw
+        def load_slab(i, pieces):
+            e, g = slabs[i]
+            if i not in slab_raw:
+                v_raw = byte_pool.tile([P, PACK, R], U8)
+                slab_raw[i] = v_raw
+            rows = v_bytes[e, g * K_PASS:(g + 1) * K_PASS, :].rearrange("(p t) w -> p t w", t=PACK)
+            for ts, cs in pieces:
+                nc.sync.dma_start(out=slab_raw[i][:, ts, cs], in_=rows[:, ts, cs])
 
-        def widen(i):
+        whole = [(slice(0, 2), slice(0, R)), (slice(2, 4), slice(0, R))]
+
+        def load_u(i):
             kind, e, blk, g = units[i]
-            if kind == "u":
+            u_raw = raw_pool.tile([P, PACK, W], BF16)
+            nc.sync.dma_start(
+                out=u_raw[:],
+                in_=u[e, g * K_PASS:(g + 1) * K_PASS, blk * W:(blk + 1) * W].rearrange("(p t) w -> p t w", t=PACK))
+            raw[i] = u_raw
+
+        def widen(i, t, lo, hi, on_act):
+            g = slabs[i][1]
+            if i not in wide:
+                v_wide = wide_pool.tile([P, RH, PACK, W] if i == 0 else [P, PACK, R], BF16)
+                wide[i] = v_wide
+            if lo == hi:
                 return
-            v_wide = wide_pool.tile([P, PACK, W], BF16)
-            v_raw = raw.pop(i)
-            ends = {0: (W, W, 0, 0), 1: (W, W, W, 0)}.get(i, (W, W, W, W - V_WIDEN))
-            for t in range(PACK):
-                if ends[t] < W:
-                    nc.vector.tensor_scalar(
-                        out=v_wide[:, t, ends[t]:], in0=v_raw[:, t, ends[t]:].bitcast(FP8),
-                        scalar1=scale_sb[:, g, t:t + 1], scalar2=None, op0=ALU.mult)
-                if ends[t] > 0:
-                    nc.scalar.activation(
-                        out=v_wide[:, t, :ends[t]], in_=v_raw[:, t, :ends[t]].bitcast(FP8),
-                        func=ACT.Copy, scale=scale_sb[:, g, t:t + 1])
-            wide[i] = v_wide
+            src = slab_raw[i][:, t, lo:hi].bitcast(FP8)
+            dst = wide[i][:, lo // W, t, lo % W:lo % W + hi - lo] if i == 0 else wide[i][:, t, lo:hi]
+            if on_act:
+                nc.scalar.activation(out=dst, in_=src, func=ACT.Copy, scale=scale_sb[:, g, t:t + 1])
+            else:
+                nc.vector.tensor_scalar(out=dst, in0=src, scalar1=scale_sb[:, g, t:t + 1], scalar2=None, op0=ALU.mult)
+
+        def widen_planes(i, planes):
+            for t in planes:
+                cut = min(max(WIDEN_ACT - t * R, 0), R)
+                widen(i, t, 0, cut, True)
+                widen(i, t, cut, R, False)
 
         def interleave(copy, dst, src):
             copy(out=dst.rearrange("p (c i) t -> p c t i", i=2), in_=src.rearrange("p t (c i) -> p c t i", i=2))
 
+        def uses_pe(i):
+            return i >= n_v + 5
+
         def arrange(i):
             kind, e, blk, g = units[i]
             grouped = inter_pool.tile([P, W, PACK], BF16, align_bytes=64)
+            on_pe = pe_out.pop(i, None)
             if kind == "v":
-                interleave(nc.vector.tensor_copy, grouped[:], wide.pop(i)[:])
+                src = wide[0][:, blk, :, :] if i < RH else wide[i // RH][:, :, blk * W:(blk + 1) * W]
+                a = V_VEC_END if i // RH == len(slabs) - 1 else (V_VEC0, V_VEC)[blk]
             else:
-                u_raw = raw.pop(i)
-                on_pe = pe_out.pop(i, None)
+                src = raw.pop(i)[:]
                 a = U_VEC if on_pe is None else U_VEC_PE
-                b = W if on_pe is None else W - U_PE
-                interleave(nc.vector.tensor_copy, grouped[:, :a, :], u_raw[:, :, :a])
-                if on_pe is not None:
-                    nc.scalar.copy(out=grouped[:, b:, :].rearrange("p w t -> p (w t)"), in_=on_pe[:])
-                interleave(nc.scalar.copy, grouped[:, a:b, :], u_raw[:, :, a:b])
+            b = W if on_pe is None else W - U_PE
+            if a > 0:
+                interleave(nc.vector.tensor_copy, grouped[:, :a, :], src[:, :, :a])
+            if on_pe is not None:
+                nc.scalar.copy(out=grouped[:, b:, :].rearrange("p w t -> p (w t)"), in_=on_pe[:])
+            if a < b:
+                interleave(nc.scalar.copy, grouped[:, a:b, :], src[:, :, a:b])
             inter[i] = grouped
 
         def pe_interleave(i):
-            if units[i][0] == "v" or (i - n_v) % 5 == 0:
+            if not uses_pe(i):
                 return
             slots = tr_pool.tile([P, U_PE * PACK], BF16)
             for j in range(U_PE // P):
@@ -161,33 +181,24 @@ def tile_dcnv2lowrankexpertcross_w_kernel(tc, x0, x, v_bytes, v_scale, c, u, bia
                     rhs=w_codes[:, js].bitcast(FP8X4), rhs_scale=w_scales[:, js],
                     start=(g == 0), stop=(g == last))
 
-        def turn(src_words, q, slots):
-            for j in range(2):
-                for w in range(2):
-                    first = 256 * (2 * q + j)
-                    nc.tensor.transpose(slots[:, 2 * j + w, :], src_words[:, first + w:first + 256:2], ident[:])
-
-        def group_words(dst, slots):
-            nc.vector.tensor_copy(
-                out=dst.bitcast(F32).rearrange("p (j r w) -> p j r w", j=2, w=2),
-                in_=slots.rearrange("p (j w) r -> p j r w", w=2))
-
         def hidden_tanh(e, hb):
-            th = small.tile([B, W], F32)
-            for j, acc in enumerate(accs.pop(("v", e, hb))):
-                nc.scalar.activation(out=th[:, j * NB:(j + 1) * NB], in_=acc[:], func=ACT.Tanh)
-            hid[(e, hb)] = th
+            turned = []
+            for acc in accs.pop(("v", e, hb)):
+                th = small.tile([B, PACK, P], F32)
+                nc.scalar.activation(out=th[:], in_=acc[:].rearrange("b (p t) -> b t p", t=PACK), func=ACT.Tanh)
+                slots = tr_pool.tile([P, PACK, B], F32)
+                for t in range(PACK):
+                    nc.tensor.transpose(slots[:, t, :], th[:, t, :], ident[:])
+                turned.append(slots)
+            hid[(e, hb)] = turned
 
         def hidden_scale(e, hb):
-            h = small.tile([B, W], BF16)
-            nc.vector.tensor_tensor(out=h[:], in0=hid[(e, hb)][:], in1=c_sb[:, e, hb * W:(hb + 1) * W], op=ALU.mult)
-            slots = tr_pool.tile([P, 4, B], F32)
-            turn(h[:].bitcast(F32), 0, slots)
-            hid[(e, hb)] = slots
-
-        def hidden_group(e, hb):
-            hg = small.tile([P, 2 * B * PACK], BF16, align_bytes=64)
-            group_words(hg[:], hid[(e, hb)][:])
+            hg = small.tile([P, W // NB, B, PACK], BF16, align_bytes=64)
+            for j, slots in enumerate(hid[(e, hb)]):
+                g = e * U_PASSES + hb * (W // NB) + j
+                nc.vector.tensor_tensor(
+                    out=hg[:, j, :, :], in0=slots[:].rearrange("p t b -> p b t"),
+                    in1=c_sb[:, g:g + 1, :].to_broadcast([P, B, PACK]), op=ALU.mult)
             hid[(e, hb)] = hg
 
         def hidden_quantize(e, hb):
@@ -195,104 +206,96 @@ def tile_dcnv2lowrankexpertcross_w_kernel(tc, x0, x, v_bytes, v_scale, c, u, bia
             nc.vector.quantize_mx(
                 out=h_codes[:, e, gs, :].rearrange("p g b -> p (g b)").bitcast(FP8X4),
                 scales=h_scales[:, e, gs, :].rearrange("p g b -> p (g b)"),
-                in_=hid.pop((e, hb))[:])
+                in_=hid.pop((e, hb))[:].rearrange("p g b t -> p (g b t)"))
 
-        def epilogue(e, db):
-            banks = accs.pop(("u", e, db))
-            for j in range(W // NB):
-                cols = slice(db * W + j * NB, db * W + (j + 1) * NB)
-                if e == 0:
-                    m = mix.tile([B, NB], F32)
-                    nc.vector.scalar_tensor_tensor(
-                        out=m[:], in0=banks[j][:], scalar=gates["p"][:, 0:1], in1=bias_sb[:, cols], op0=ALU.mult, op1=ALU.add)
-                    mixed[(db, j)] = m
-                else:
-                    m2 = mix.tile([B, NB], F32)
-                    nc.vector.scalar_tensor_tensor(
-                        out=m2[:], in0=banks[j][:], scalar=gates["p"][:, 1:2], in1=mixed.pop((db, j))[:], op0=ALU.mult, op1=ALU.add)
-                    mixed[(db, j)] = m2
-            if e == 1:
-                prods = []
-                for j in range(W // NB):
-                    cols = slice(db * W + j * NB, db * W + (j + 1) * NB)
-                    m3 = mix.tile([B, NB], F32)
-                    nc.vector.tensor_tensor(out=m3[:], in0=mixed.pop((db, j))[:], in1=x0_sb[:, cols], op=ALU.mult)
-                    prods.append(m3)
-                for j in range(W // NB):
-                    cols = slice(db * W + j * NB, db * W + (j + 1) * NB)
-                    m4 = mix.tile([B, NB], F32)
-                    nc.vector.tensor_tensor(out=m4[:], in0=prods[j][:], in1=x_sb[:, cols], op=ALU.add)
-                    nc.sync.dma_start(out=out[:, cols], in_=m4[:])
+        def mix_expert(e, db, j):
+            if (db, e) not in mixed:
+                m = mix.tile([B, W], F32)
+                mixed[(db, e)] = m
+            js = slice(j * NB, (j + 1) * NB)
+            other = bias_sb[:, db * W + j * NB:db * W + (j + 1) * NB] if e == 0 else mixed[(db, 0)][:, js]
+            nc.vector.scalar_tensor_tensor(
+                out=mixed[(db, e)][:, js], in0=accs[("u", e, db)][j][:], scalar=share[:, e:e + 1], in1=other,
+                op0=ALU.mult, op1=ALU.add)
 
-        def softmax_gates():
-            top = small.tile([B, 1], F32)
-            nc.vector.tensor_reduce(out=top[:], in_=gate_sb[:], op=ALU.max, axis=AX.X)
-            shifted = small.tile([B, E], F32)
-            nc.vector.tensor_scalar(out=shifted[:], in0=gate_sb[:], scalar1=top[:], scalar2=None, op0=ALU.subtract)
-            ex = small.tile([B, E], F32)
-            nc.scalar.activation(out=ex[:], in_=shifted[:], func=ACT.Exp)
-            total = small.tile([B, 1], F32)
-            nc.vector.tensor_reduce(out=total[:], in_=ex[:], op=ALU.add, axis=AX.X)
-            inv = small.tile([B, 1], F32)
-            nc.vector.reciprocal(out=inv[:], in_=total[:])
-            p = const.tile([B, E], F32)
-            nc.vector.tensor_scalar(out=p[:], in0=ex[:], scalar1=inv[:], scalar2=None, op0=ALU.mult)
-            gates["p"] = p
+        def cross(db, lo, hi):
+            if (db, 2) not in mixed:
+                prod = mix.tile([B, W], F32)
+                mixed[(db, 2)] = prod
+            nc.vector.tensor_tensor(
+                out=mixed[(db, 2)][:, lo:hi], in0=mixed[(db, 1)][:, lo:hi], in1=x0_sb[:, db * W + lo:db * W + hi], op=ALU.mult)
+
+        def finish(db, lo, hi):
+            res = mixed[(db, 2)]
+            nc.vector.tensor_tensor(
+                out=res[:, lo:hi], in0=res[:, lo:hi], in1=x_sb[:, db * W + lo:db * W + hi], op=ALU.add)
+            nc.sync.dma_start(out=out[:, db * W + lo:db * W + hi], in_=res[:, lo:hi])
 
         make_identity(nc, ident[:])
         nc.vector.tensor_copy(out=ident16[:], in_=ident[:])
         with tc.manual_schedule():
-            nc.sync.dma_start(out=scale_sb[:], in_=v_scale.rearrange("o (g p t) u -> p (o g) (t u)", p=P, t=PACK))
-            load(0)
-            nc.sync.dma_start(out=x_sb[:], in_=x)
-            for i in range(1, 4):
-                load(i)
             nc.sync.dma_start(out=gate_sb[:], in_=gate_logits)
-            loaded = [4, n_v]
+            nc.sync.dma_start(out=scale_sb[:], in_=v_scale.rearrange("o (g p t) u -> p (o g) (t u)", p=P, t=PACK))
+            load_slab(0, [(slice(0, 2), slice(0, W)), (slice(2, 4), slice(0, W)), (slice(0, 4), slice(W, R))])
+            load_slab(1, whole)
+            nc.sync.dma_start(out=x_sb[:], in_=x)
+            load_slab(2, whole)
+            nc.sync.dma_start(out=c_sb[:], in_=c.rearrange("e (g p t) -> p (e g) t", p=P, t=PACK))
 
-            for i in range(2):
-                widen(i)
-            x_groups = []
-            for q in range(3):
-                slots = tr_pool.tile([P, 4, B], F32)
-                turn(x_sb[:].bitcast(F32), q, slots)
-                xg = const.tile([P, 2 * B * PACK], BF16, align_bytes=64, name="xg%d" % q)
-                group_words(xg[:], slots[:])
-                x_groups.append(xg)
-            for q in range(3):
-                gs = slice(2 * q, 2 * q + 2)
-                nc.vector.quantize_mx(
-                    out=x_codes[:, gs, :].rearrange("p g b -> p (g b)").bitcast(FP8X4),
-                    scales=x_scales[:, gs, :].rearrange("p g b -> p (g b)"),
-                    in_=x_groups[q][:])
+            for e in range(E):
+                nc.scalar.activation(
+                    out=share[:, e:e + 1], in_=gate_sb[:, 1 - e:2 - e], func=ACT.Sigmoid,
+                    scale=-1.0, bias=gate_sb[:, e:e + 1])
+            widen(0, 0, 0, W, True)
+            for t in range(1, PACK):
+                widen(0, t, 0, W, False)
             arrange(0)
+            for t in range(PACK):
+                widen(0, t, W, R, False)
+            widen_planes(1, range(PACK))
+            x_words = x_sb[:].bitcast(F32)
+            for q in range(V_PASSES // 2):
+                slots = tr_pool.tile([P, 4, B], F32)
+                for j in range(2):
+                    for w in range(2):
+                        first = 256 * (2 * q + j)
+                        nc.tensor.transpose(slots[:, 2 * j + w, :], x_words[:, first + w:first + 256:2], ident[:])
+                nc.scalar.copy(
+                    out=x_grouped[:, q * W:(q + 1) * W].bitcast(F32).rearrange("p (j r w) -> p j r w", j=2, w=2),
+                    in_=slots[:].rearrange("p (j w) r -> p j r w", w=2))
+            arrange(1)
+
+            def quantize_x():
+                for lo, hi in ((0, 4), (4, 6)):
+                    nc.vector.quantize_mx(
+                        out=x_codes[:, lo:hi, :].rearrange("p g b -> p (g b)").bitcast(FP8X4),
+                        scales=x_scales[:, lo:hi, :].rearrange("p g b -> p (g b)"),
+                        in_=x_grouped[:, lo * K_PASS:hi * K_PASS])
 
             later = {}
 
             def at(step, fn, *args):
                 later.setdefault(step, []).append((fn, args))
 
-            for s in range(n + 4):
-                if s == 1:
-                    nc.sync.dma_start(out=c_sb[:], in_=c.rearrange("e r -> (e r)").partition_broadcast(P))
-                if s == 4:
+            at(0, quantize_x)
+            loaded = [n_v]
+            for s in range(n + 1):
+                if s % 2 == 0 and s // 2 + 3 < len(slabs):
+                    load_slab(s // 2 + 3, whole)
+                if s == 5:
                     nc.sync.dma_start(out=bias_sb[:], in_=bias.partition_broadcast(P))
                     nc.sync.dma_start(out=x0_sb[:], in_=x0)
-                while loaded[0] < min(n_v, s + 6):
-                    load(loaded[0])
+                if s >= 7 and loaded[0] < min(n, max(n_v, s + 2) + U_AHEAD) and (s % 2 == 1 or s + 2 >= n_v):
+                    load_u(loaded[0])
                     loaded[0] += 1
-                if s >= 6 and loaded[1] < n and (s < n_v - 2 and s % 2 == 0 and loaded[1] < n_v + 8 or loaded[1] < s + 8):
-                    load(loaded[1])
-                    loaded[1] += 1
+                if s // 2 + 2 < len(slabs):
+                    widen_planes(s // 2 + 2, (2 * (s % 2), 2 * (s % 2) + 1))
+                if s + 3 < n:
+                    pe_interleave(s + 3)
                 if s + 2 < n:
-                    widen(s + 2)
-                    pe_interleave(s + 2)
-                if s + 1 < n:
-                    arrange(s + 1)
+                    arrange(s + 2)
                 if s < n:
                     quantize(s)
-                if s == 3:
-                    softmax_gates()
                 for fn, args in later.pop(s, []):
                     fn(*args)
                 if s < n:
@@ -300,8 +303,17 @@ def tile_dcnv2lowrankexpertcross_w_kernel(tc, x0, x, v_bytes, v_scale, c, u, bia
                     kind, e, blk, g = units[s]
                     if kind == "v" and g == V_PASSES - 1:
                         at(s + 1, hidden_tanh, e, blk)
-                        at(s + 2, hidden_scale, e, blk)
-                        at(s + 3, hidden_group, e, blk)
+                        at(s + 3, hidden_scale, e, blk)
                         at(s + 4, hidden_quantize, e, blk)
-                    if kind == "u" and g == U_PASSES - 1:
-                        at(s + 1 if s < n - 1 else s + 1, epilogue, e, blk)
+                    if kind == "u" and g == U_PASSES - 1 and s < n - 1:
+                        at(s + 1, mix_expert, e, blk, 0)
+                        at(s + 2, mix_expert, e, blk, 1)
+                        if e == 1:
+                            at(s + 3, cross, blk, 0, W)
+                            at(s + 4, finish, blk, 0, W)
+            for j in range(W // NB):
+                mix_expert(1, DB - 1, j)
+            for j in range(W // NB):
+                cross(DB - 1, j * NB, (j + 1) * NB)
+            for j in range(W // NB):
+                finish(DB - 1, j * NB, (j + 1) * NB)

@@ -29,22 +29,34 @@ V_VEC = 256
 V_VEC0 = 0
 V_VEC_END = 480
 U_VEC = 400
-U_VEC_PE = 320
+U_VEC_PE = (352, 280)
+U_VEC_END = (192, 128)
 U_PE = 256
-U_AHEAD = 6
+U_OWN = 4
+U_OVER = 3
+CH = 8
+CW = D // CH
+TL = 128
+TPITCH = 144
+T_BANK = 8
+T_GROUP = 4
+T_FIRST = 15
+V_VEC_T = 376
+V_VEC_PE = 176
 
 
 def tile_dcnv2lowrankexpertcross_w_kernel(tc, x0, x, v_bytes, v_scale, c, u, bias, gate_logits, out):
     nc = tc.nc
     with ExitStack() as ctx:
         const = ctx.enter_context(tc.tile_pool(name="const", bufs=1))
-        byte_pool = ctx.enter_context(tc.tile_pool(name="byte_pool", bufs=3))
+        byte_pool = ctx.enter_context(tc.tile_pool(name="byte_pool", bufs=2))
         wide_pool = ctx.enter_context(tc.tile_pool(name="wide_pool", bufs=3))
-        raw_pool = ctx.enter_context(tc.tile_pool(name="raw_pool", bufs=U_AHEAD))
-        inter_pool = ctx.enter_context(tc.tile_pool(name="inter_pool", bufs=4))
+        raw_pool = ctx.enter_context(tc.tile_pool(name="raw_pool", bufs=U_OWN))
+        inter_pool = ctx.enter_context(tc.tile_pool(name="inter_pool", bufs=5))
         code_pool = ctx.enter_context(tc.tile_pool(name="code_pool", bufs=4))
         small = ctx.enter_context(tc.tile_pool(name="small", bufs=2))
-        mix = ctx.enter_context(tc.tile_pool(name="mix", bufs=2))
+        mix = ctx.enter_context(tc.tile_pool(name="mix", bufs=1))
+        over = ctx.enter_context(tc.tile_pool(name="over", bufs=1))
         acc_pool = ctx.enter_context(tc.psum_pool(name="acc_pool", bufs=4))
         tr_pool = ctx.enter_context(tc.psum_pool(name="tr_pool", bufs=4))
 
@@ -52,12 +64,13 @@ def tile_dcnv2lowrankexpertcross_w_kernel(tc, x0, x, v_bytes, v_scale, c, u, bia
         ident16 = const.tile([P, P], BF16)
         scale_sb = const.tile([P, V_PASSES, PACK], F32)
         x_sb = const.tile([B, D], BF16)
-        x0_sb = const.tile([B, D], BF16)
+        perm16 = const.tile([P, P], BF16)
+        first_mix = const.tile([B, D], F32)
+        u_turn = over.tile([P, P, TPITCH], BF16, offset=0)
         bias_sb = const.tile([B, D], BF16)
         c_sb = const.tile([P, E * U_PASSES, PACK], BF16)
         gate_sb = const.tile([B, E], BF16)
         share = const.tile([B, E], F32)
-        x_grouped = const.tile([P, V_PASSES * B * PACK], BF16, align_bytes=64)
         x_codes = const.tile([P, V_PASSES, B], U32, align_bytes=64)
         x_scales = const.tile([P, V_PASSES, B], U8, align_bytes=64)
         h_codes = const.tile([P, E, U_PASSES, B], U32, align_bytes=64)
@@ -66,7 +79,8 @@ def tile_dcnv2lowrankexpertcross_w_kernel(tc, x0, x, v_bytes, v_scale, c, u, bia
         slabs = [(e, g) for e in range(E) for g in range(V_PASSES)]
         units = [("v", e, hb, g) for e, g in slabs for hb in range(RH)]
         n_v = len(units)
-        units += [("u", e, db, g) for db in range(DB) for e in range(E) for g in range(U_PASSES)]
+        units += [("u", 0, db, g) for db in range(DB - 1) for g in range(U_PASSES)]
+        units += [("u", 1, db, g) for db in range(DB) for g in range(U_PASSES)]
         n = len(units)
         raw = {}
         slab_raw = {}
@@ -77,6 +91,8 @@ def tile_dcnv2lowrankexpertcross_w_kernel(tc, x0, x, v_bytes, v_scale, c, u, bia
         hid = {}
         mixed = {}
         pe_out = {}
+        t_banks = {}
+        late = {}
 
         def load_slab(i, pieces):
             e, g = slabs[i]
@@ -91,11 +107,65 @@ def tile_dcnv2lowrankexpertcross_w_kernel(tc, x0, x, v_bytes, v_scale, c, u, bia
 
         def load_u(i):
             kind, e, blk, g = units[i]
-            u_raw = raw_pool.tile([P, PACK, W], BF16)
-            nc.sync.dma_start(
-                out=u_raw[:],
-                in_=u[e, g * K_PASS:(g + 1) * K_PASS, blk * W:(blk + 1) * W].rearrange("(p t) w -> p t w", t=PACK))
+            slot = (i - n_v) % (U_OWN + U_OVER) - U_OWN
+            if slot < 0:
+                u_raw = raw_pool.tile([P, PACK, W], BF16)
+            else:
+                u_raw = over.tile([P, PACK, W], BF16, offset=slot * PACK * W * 2, name="u_over%d" % slot)
+            rows = u[e, g * K_PASS:(g + 1) * K_PASS, :].rearrange("(p t) w -> p t w", t=PACK)
+            if e == 1:
+                nc.sync.dma_start(out=u_raw[:], in_=rows[:, :, blk * W:(blk + 1) * W])
+            else:
+                for t in range(PACK):
+                    nc.sync.dma_start(
+                        out=u_raw[:, t, :].rearrange("p (c w) -> p c w", c=CH // 2),
+                        in_=rows[:, t, :].rearrange("p (c w) -> p c w", c=CH)[:, 4 * blk:4 * blk + 4, :CW - TL])
             raw[i] = u_raw
+
+        def load_turn(q):
+            g, half = q // 2, q % 2
+            ps = slice(half * P // 2, (half + 1) * P // 2)
+            src = u[0, g * K_PASS:(g + 1) * K_PASS, :].rearrange("(p t) (c w) -> (t c) p w", t=PACK, c=CH)
+            nc.sync.dma_start(out=u_turn[g:P:U_PASSES, ps, :TL], in_=src[:, ps, CW - TL:])
+
+        def turn_bank(b):
+            slots = tr_pool.tile([P, U_PASSES, T_BANK, CH * PACK], BF16)
+            for l in range(T_BANK):
+                nc.tensor.transpose(slots[:, :, l, :], u_turn[:, :, b * T_BANK + l], perm16[:])
+            t_banks[b] = slots
+
+        def empty_bank(b):
+            key = ("t", b // T_GROUP)
+            if key not in inter:
+                grouped = inter_pool.tile([P, W, PACK], BF16, align_bytes=64)
+                inter[key] = grouped
+            dst = inter[key][:].rearrange("p (g q w) t -> p g q (w t)", g=U_PASSES, q=T_GROUP)
+            nc.scalar.copy(
+                out=dst[:, :, b % T_GROUP, :].bitcast(F32),
+                in_=t_banks.pop(b)[:].rearrange("p g l x -> p g (l x)").bitcast(F32))
+
+        def multiply_turned(q):
+            quantize(("t", q))
+            w_codes, w_scales = codes[("t", q)]
+            slots = tr_pool.tile([B, NB], F32)
+            nt = W // U_PASSES
+            for g in range(U_PASSES):
+                nc.tensor.matmul_mx(
+                    out=slots[:, :nt], lhsT=h_codes[:, 0, g, :].bitcast(FP8X4), lhsT_scale=h_scales[:, 0, g, :],
+                    rhs=w_codes[:, g * nt:(g + 1) * nt].bitcast(FP8X4), rhs_scale=w_scales[:, g * nt:(g + 1) * nt],
+                    start=(g == 0), stop=(g == U_PASSES - 1))
+            accs[("t", q)] = slots
+
+        def chunked(ap):
+            return ap.rearrange("b (c w) -> b c w", c=CH)
+
+        def mix_turned(q):
+            nl = T_BANK * T_GROUP
+            ls = slice(CW - TL + q * nl, CW - TL + (q + 1) * nl)
+            nc.vector.scalar_tensor_tensor(
+                out=chunked(first_mix[:])[:, :, ls],
+                in0=accs.pop(("t", q))[:, :nl * CH].rearrange("b (l c) -> b c l", c=CH),
+                scalar=share[:, 0:1], in1=chunked(bias_sb[:])[:, :, ls], op0=ALU.mult, op1=ALU.add)
 
         def widen(i, t, lo, hi, on_act):
             g = slabs[i][1]
@@ -121,7 +191,7 @@ def tile_dcnv2lowrankexpertcross_w_kernel(tc, x0, x, v_bytes, v_scale, c, u, bia
             copy(out=dst.rearrange("p (c i) t -> p c t i", i=2), in_=src.rearrange("p t (c i) -> p c t i", i=2))
 
         def uses_pe(i):
-            return i >= n_v + 5
+            return i >= n_v + 5 or i in (3, 5, 7, 9)
 
         def arrange(i):
             kind, e, blk, g = units[i]
@@ -130,14 +200,23 @@ def tile_dcnv2lowrankexpertcross_w_kernel(tc, x0, x, v_bytes, v_scale, c, u, bia
             if kind == "v":
                 src = wide[0][:, blk, :, :] if i < RH else wide[i // RH][:, :, blk * W:(blk + 1) * W]
                 a = V_VEC_END if i // RH == len(slabs) - 1 else (V_VEC0, V_VEC)[blk]
+                if blk == 1 and on_pe is not None:
+                    a = V_VEC_PE
+                if blk == 1 and T_FIRST + 2 <= i < n_v - 1:
+                    a = V_VEC_T
             else:
                 src = raw.pop(i)[:]
-                a = U_VEC if on_pe is None else U_VEC_PE
+                a = U_VEC if on_pe is None else U_VEC_PE[e]
+                if i >= n - len(U_VEC_END):
+                    a = U_VEC_END[i - n]
             b = W if on_pe is None else W - U_PE
             if a > 0:
                 interleave(nc.vector.tensor_copy, grouped[:, :a, :], src[:, :, :a])
+            if i == n - 1:
+                interleave(nc.scalar.copy, grouped[:, a:NB, :], src[:, :, a:NB])
+                a = NB
             if on_pe is not None:
-                nc.scalar.copy(out=grouped[:, b:, :].rearrange("p w t -> p (w t)"), in_=on_pe[:])
+                nc.scalar.copy(out=grouped[:, b:, :].rearrange("p w t -> p (w t)").bitcast(F32), in_=on_pe[:].bitcast(F32))
             if a < b:
                 interleave(nc.scalar.copy, grouped[:, a:b, :], src[:, :, a:b])
             inter[i] = grouped
@@ -146,24 +225,27 @@ def tile_dcnv2lowrankexpertcross_w_kernel(tc, x0, x, v_bytes, v_scale, c, u, bia
             if not uses_pe(i):
                 return
             slots = tr_pool.tile([P, U_PE * PACK], BF16)
+            src = raw[i][:] if i >= n_v else wide[i // RH][:, :, W:]
             for j in range(U_PE // P):
                 cs = slice(W - U_PE + j * P, W - U_PE + (j + 1) * P)
                 nc.tensor.matmul(
                     out=slots[:, j * NB:(j + 1) * NB], lhsT=ident16[:],
-                    rhs=raw[i][:, :, cs].rearrange("p t w -> p w t"), start=True, stop=True)
+                    rhs=src[:, :, cs].rearrange("p t w -> p w t"), start=True, stop=True)
             pe_out[i] = slots
 
-        def quantize(i):
-            w_codes = code_pool.tile([P, W], U32, align_bytes=64)
-            w_scales = code_pool.tile([P, W], U8, align_bytes=64)
+        def quantize(i, lo=0, hi=W):
+            if i not in codes:
+                w_codes = code_pool.tile([P, W], U32, align_bytes=64)
+                w_scales = code_pool.tile([P, W], U8, align_bytes=64)
+                codes[i] = (w_codes, w_scales)
+            w_codes, w_scales = codes[i]
             nc.vector.quantize_mx(
-                out=w_codes[:].bitcast(FP8X4), scales=w_scales[:],
-                in_=inter.pop(i)[:].rearrange("p w t -> p (w t)"))
-            codes[i] = (w_codes, w_scales)
+                out=w_codes[:, lo:hi].bitcast(FP8X4), scales=w_scales[:, lo:hi],
+                in_=inter[i][:, lo:hi, :].rearrange("p w t -> p (w t)"))
 
-        def multiply(i):
+        def multiply(i, which=range(W // NB)):
             kind, e, blk, g = units[i]
-            w_codes, w_scales = codes.pop(i)
+            w_codes, w_scales = codes[i]
             last = (V_PASSES if kind == "v" else U_PASSES) - 1
             if g == 0:
                 banks = []
@@ -172,7 +254,7 @@ def tile_dcnv2lowrankexpertcross_w_kernel(tc, x0, x, v_bytes, v_scale, c, u, bia
                     banks.append(acc)
                 accs[(kind, e, blk)] = banks
             banks = accs[(kind, e, blk)]
-            for j in range(W // NB):
+            for j in which:
                 js = slice(j * NB, (j + 1) * NB)
                 lhs = x_codes[:, g, :] if kind == "v" else h_codes[:, e, g, :]
                 lhs_scale = x_scales[:, g, :] if kind == "v" else h_scales[:, e, g, :]
@@ -208,52 +290,61 @@ def tile_dcnv2lowrankexpertcross_w_kernel(tc, x0, x, v_bytes, v_scale, c, u, bia
                 scales=h_scales[:, e, gs, :].rearrange("p g b -> p (g b)"),
                 in_=hid.pop((e, hb))[:].rearrange("p g b t -> p (g b t)"))
 
-        def mix_expert(e, db, j):
-            if (db, e) not in mixed:
-                m = mix.tile([B, W], F32)
-                mixed[(db, e)] = m
-            js = slice(j * NB, (j + 1) * NB)
-            other = bias_sb[:, db * W + j * NB:db * W + (j + 1) * NB] if e == 0 else mixed[(db, 0)][:, js]
+        def mix_first(db, j):
+            cs = slice(4 * db + 2 * j, 4 * db + 2 * j + 2)
             nc.vector.scalar_tensor_tensor(
-                out=mixed[(db, e)][:, js], in0=accs[("u", e, db)][j][:], scalar=share[:, e:e + 1], in1=other,
-                op0=ALU.mult, op1=ALU.add)
+                out=chunked(first_mix[:])[:, cs, :CW - TL], in0=accs[("u", 0, db)][j][:].rearrange("b (c w) -> b c w", c=2),
+                scalar=share[:, 0:1], in1=chunked(bias_sb[:])[:, cs, :CW - TL], op0=ALU.mult, op1=ALU.add)
+
+        def mix_second(db, j):
+            if db not in mixed:
+                if db % 2 == 0:
+                    res = mix.tile([B, W], F32)
+                else:
+                    res = over.tile([B, W], F32, offset=U_OVER * PACK * W * 2 + D * 2, name="res_over")
+                mixed[db] = res
+            js = slice(j * NB, (j + 1) * NB)
+            nc.vector.scalar_tensor_tensor(
+                out=mixed[db][:, js], in0=accs[("u", 1, db)][j][:], scalar=share[:, 1:2],
+                in1=first_mix[:, db * W + j * NB:db * W + (j + 1) * NB], op0=ALU.mult, op1=ALU.add)
 
         def cross(db, lo, hi):
-            if (db, 2) not in mixed:
-                prod = mix.tile([B, W], F32)
-                mixed[(db, 2)] = prod
+            res = mixed[db]
             nc.vector.tensor_tensor(
-                out=mixed[(db, 2)][:, lo:hi], in0=mixed[(db, 1)][:, lo:hi], in1=x0_sb[:, db * W + lo:db * W + hi], op=ALU.mult)
+                out=res[:, lo:hi], in0=res[:, lo:hi], in1=late["x0"][:, db * W + lo:db * W + hi], op=ALU.mult)
 
         def finish(db, lo, hi):
-            res = mixed[(db, 2)]
+            res = mixed[db]
             nc.vector.tensor_tensor(
                 out=res[:, lo:hi], in0=res[:, lo:hi], in1=x_sb[:, db * W + lo:db * W + hi], op=ALU.add)
             nc.sync.dma_start(out=out[:, db * W + lo:db * W + hi], in_=res[:, lo:hi])
 
         make_identity(nc, ident[:])
         nc.vector.tensor_copy(out=ident16[:], in_=ident[:])
+        nc.vector.tensor_copy(
+            out=perm16[:].rearrange("q (g c t) -> q g c t", g=U_PASSES, c=CH),
+            in_=ident[:].rearrange("q (t c g) -> q g c t", g=U_PASSES, c=CH))
         with tc.manual_schedule():
-            nc.sync.dma_start(out=gate_sb[:], in_=gate_logits)
-            nc.sync.dma_start(out=scale_sb[:], in_=v_scale.rearrange("o (g p t) u -> p (o g) (t u)", p=P, t=PACK))
-            load_slab(0, [(slice(0, 2), slice(0, W)), (slice(2, 4), slice(0, W)), (slice(0, 4), slice(W, R))])
+            nc.scalar.dma_start(out=scale_sb[:], in_=v_scale.rearrange("o (g p t) u -> p (o g) (t u)", p=P, t=PACK))
+            nc.scalar.dma_start(out=gate_sb[:], in_=gate_logits)
+            load_slab(0, [(slice(t, t + 1), slice(0, W)) for t in range(PACK)] + [(slice(0, 4), slice(W, R))])
             load_slab(1, whole)
             nc.sync.dma_start(out=x_sb[:], in_=x)
-            load_slab(2, whole)
             nc.sync.dma_start(out=c_sb[:], in_=c.rearrange("e (g p t) -> p (e g) t", p=P, t=PACK))
 
             for e in range(E):
                 nc.scalar.activation(
                     out=share[:, e:e + 1], in_=gate_sb[:, 1 - e:2 - e], func=ACT.Sigmoid,
                     scale=-1.0, bias=gate_sb[:, e:e + 1])
-            widen(0, 0, 0, W, True)
-            for t in range(1, PACK):
-                widen(0, t, 0, W, False)
+            for t in range(PACK):
+                widen(0, t, 0, W, t == 1)
             arrange(0)
             for t in range(PACK):
                 widen(0, t, W, R, False)
             widen_planes(1, range(PACK))
+            load_slab(2, whole)
             x_words = x_sb[:].bitcast(F32)
+            x_grouped = inter_pool.tile([P, V_PASSES * B * PACK], BF16, align_bytes=64, tag="grouped")
             for q in range(V_PASSES // 2):
                 slots = tr_pool.tile([P, 4, B], F32)
                 for j in range(2):
@@ -279,40 +370,65 @@ def tile_dcnv2lowrankexpertcross_w_kernel(tc, x0, x, v_bytes, v_scale, c, u, bia
 
             at(0, quantize_x)
             loaded = [n_v]
-            for s in range(n + 1):
+            for q in range(TL // (T_BANK * T_GROUP)):
+                at(T_FIRST + 2 * q + 2, multiply_turned, q)
+                at(T_FIRST + 2 * q + 3, mix_turned, q)
+            t_last = T_FIRST + TL // T_BANK // 2 - 1
+            for s in range(n - 1):
                 if s % 2 == 0 and s // 2 + 3 < len(slabs):
                     load_slab(s // 2 + 3, whole)
-                if s == 5:
+                if 2 <= s < 2 + 2 * U_PASSES:
+                    load_turn(s - 2)
+                if s == 10:
                     nc.sync.dma_start(out=bias_sb[:], in_=bias.partition_broadcast(P))
+                if s <= t_last:
+                    if s >= 11 and s % 2 == 1 and loaded[0] < n_v + U_OWN:
+                        load_u(loaded[0])
+                        loaded[0] += 1
+                else:
+                    while loaded[0] < min(n, s + 2 + U_OWN + U_OVER):
+                        load_u(loaded[0])
+                        loaded[0] += 1
+                if s == n_v + 3:
+                    x0_sb = over.tile([B, D], BF16, offset=U_OVER * PACK * W * 2)
                     nc.sync.dma_start(out=x0_sb[:], in_=x0)
-                if s >= 7 and loaded[0] < min(n, max(n_v, s + 2) + U_AHEAD) and (s % 2 == 1 or s + 2 >= n_v):
-                    load_u(loaded[0])
-                    loaded[0] += 1
+                    late["x0"] = x0_sb
                 if s // 2 + 2 < len(slabs):
                     widen_planes(s // 2 + 2, (2 * (s % 2), 2 * (s % 2) + 1))
+                if T_FIRST <= s <= t_last:
+                    for b in (2 * (s - T_FIRST), 2 * (s - T_FIRST) + 1):
+                        turn_bank(b)
+                if T_FIRST < s <= t_last + 1:
+                    empty_bank(2 * (s - T_FIRST) - 1)
                 if s + 3 < n:
                     pe_interleave(s + 3)
                 if s + 2 < n:
                     arrange(s + 2)
-                if s < n:
-                    quantize(s)
+                if T_FIRST <= s <= t_last:
+                    empty_bank(2 * (s - T_FIRST))
+                quantize(s)
                 for fn, args in later.pop(s, []):
                     fn(*args)
-                if s < n:
-                    multiply(s)
-                    kind, e, blk, g = units[s]
-                    if kind == "v" and g == V_PASSES - 1:
-                        at(s + 1, hidden_tanh, e, blk)
-                        at(s + 3, hidden_scale, e, blk)
-                        at(s + 4, hidden_quantize, e, blk)
-                    if kind == "u" and g == U_PASSES - 1 and s < n - 1:
-                        at(s + 1, mix_expert, e, blk, 0)
-                        at(s + 2, mix_expert, e, blk, 1)
-                        if e == 1:
-                            at(s + 3, cross, blk, 0, W)
-                            at(s + 4, finish, blk, 0, W)
+                multiply(s)
+                kind, e, blk, g = units[s]
+                if kind == "v" and g == V_PASSES - 1:
+                    at(s + 1, hidden_tanh, e, blk)
+                    at(s + 3, hidden_scale, e, blk)
+                    at(s + 4, hidden_quantize, e, blk)
+                if kind == "u" and g == U_PASSES - 1:
+                    mixer = (mix_first, mix_second)[e]
+                    at(s + 1, mixer, blk, 0)
+                    at(s + 2, mixer, blk, 1)
+                    if e == 1:
+                        at(s + 3, cross, blk, 0, W)
+                        at(s + 4, finish, blk, 0, W)
             for j in range(W // NB):
-                mix_expert(1, DB - 1, j)
+                quantize(n - 1, j * NB, (j + 1) * NB)
+                multiply(n - 1, [j])
+            for fn, args in later.pop(n - 1, []):
+                fn(*args)
+            for j in range(W // NB):
+                mix_second(DB - 1, j)
             for j in range(W // NB):
                 cross(DB - 1, j * NB, (j + 1) * NB)
             for j in range(W // NB):

@@ -25,24 +25,26 @@ U_PASSES = R // K_PASS
 RH = R // W
 DB = D // W
 WIDEN_ACT = 0
-V_VEC = 256
+V_VEC = 304
 V_VEC0 = 0
-V_VEC_END = 480
+V_VEC_END = 520
 U_VEC = 400
-U_VEC_PE = (352, 280)
-U_VEC_END = (192, 128)
+U_VEC_PE = (352, 264)
+U_VEC_END = (160, 64)
 U_PE = 256
 U_OWN = 4
-U_OVER = 3
+U_OVER = 4
 CH = 8
 CW = D // CH
 TL = 128
 TPITCH = 144
 T_BANK = 8
 T_GROUP = 4
-T_FIRST = 15
-V_VEC_T = 376
-V_VEC_PE = 176
+T_FIRST = 7
+T_BYTES = P * TPITCH * 2
+UNIT_BYTES = PACK * W * 2
+V_VEC_T = 364
+V_VEC_PE = 224
 
 
 def tile_dcnv2lowrankexpertcross_w_kernel(tc, x0, x, v_bytes, v_scale, c, u, bias, gate_logits, out):
@@ -52,10 +54,9 @@ def tile_dcnv2lowrankexpertcross_w_kernel(tc, x0, x, v_bytes, v_scale, c, u, bia
         byte_pool = ctx.enter_context(tc.tile_pool(name="byte_pool", bufs=2))
         wide_pool = ctx.enter_context(tc.tile_pool(name="wide_pool", bufs=3))
         raw_pool = ctx.enter_context(tc.tile_pool(name="raw_pool", bufs=U_OWN))
-        inter_pool = ctx.enter_context(tc.tile_pool(name="inter_pool", bufs=5))
+        inter_pool = ctx.enter_context(tc.tile_pool(name="inter_pool", bufs=4))
         code_pool = ctx.enter_context(tc.tile_pool(name="code_pool", bufs=4))
         small = ctx.enter_context(tc.tile_pool(name="small", bufs=2))
-        mix = ctx.enter_context(tc.tile_pool(name="mix", bufs=1))
         over = ctx.enter_context(tc.tile_pool(name="over", bufs=1))
         acc_pool = ctx.enter_context(tc.psum_pool(name="acc_pool", bufs=4))
         tr_pool = ctx.enter_context(tc.psum_pool(name="tr_pool", bufs=4))
@@ -111,7 +112,7 @@ def tile_dcnv2lowrankexpertcross_w_kernel(tc, x0, x, v_bytes, v_scale, c, u, bia
             if slot < 0:
                 u_raw = raw_pool.tile([P, PACK, W], BF16)
             else:
-                u_raw = over.tile([P, PACK, W], BF16, offset=slot * PACK * W * 2, name="u_over%d" % slot)
+                u_raw = over.tile([P, PACK, W], BF16, offset=slot * UNIT_BYTES, name="u_over%d" % slot)
             rows = u[e, g * K_PASS:(g + 1) * K_PASS, :].rearrange("(p t) w -> p t w", t=PACK)
             if e == 1:
                 nc.sync.dma_start(out=u_raw[:], in_=rows[:, :, blk * W:(blk + 1) * W])
@@ -137,15 +138,20 @@ def tile_dcnv2lowrankexpertcross_w_kernel(tc, x0, x, v_bytes, v_scale, c, u, bia
         def empty_bank(b):
             key = ("t", b // T_GROUP)
             if key not in inter:
-                grouped = inter_pool.tile([P, W, PACK], BF16, align_bytes=64)
-                inter[key] = grouped
+                t_grouped = over.tile([P, W, PACK], BF16, align_bytes=64, offset=T_BYTES)
+                inter[key] = t_grouped
             dst = inter[key][:].rearrange("p (g q w) t -> p g q (w t)", g=U_PASSES, q=T_GROUP)
             nc.scalar.copy(
                 out=dst[:, :, b % T_GROUP, :].bitcast(F32),
                 in_=t_banks.pop(b)[:].rearrange("p g l x -> p g (l x)").bitcast(F32))
 
-        def multiply_turned(q):
+        def quantize_turned(q):
+            t_codes = over.tile([P, W], U32, align_bytes=64, offset=T_BYTES + UNIT_BYTES)
+            t_scales = over.tile([P, W], U8, align_bytes=64, offset=T_BYTES + UNIT_BYTES + 4 * W)
+            codes[("t", q)] = (t_codes, t_scales)
             quantize(("t", q))
+
+        def multiply_turned(q):
             w_codes, w_scales = codes[("t", q)]
             slots = tr_pool.tile([B, NB], F32)
             nt = W // U_PASSES
@@ -202,7 +208,7 @@ def tile_dcnv2lowrankexpertcross_w_kernel(tc, x0, x, v_bytes, v_scale, c, u, bia
                 a = V_VEC_END if i // RH == len(slabs) - 1 else (V_VEC0, V_VEC)[blk]
                 if blk == 1 and on_pe is not None:
                     a = V_VEC_PE
-                if blk == 1 and T_FIRST + 2 <= i < n_v - 1:
+                elif blk == 1 and T_FIRST + 2 <= i < n_v - 1:
                     a = V_VEC_T
             else:
                 src = raw.pop(i)[:]
@@ -298,11 +304,7 @@ def tile_dcnv2lowrankexpertcross_w_kernel(tc, x0, x, v_bytes, v_scale, c, u, bia
 
         def mix_second(db, j):
             if db not in mixed:
-                if db % 2 == 0:
-                    res = mix.tile([B, W], F32)
-                else:
-                    res = over.tile([B, W], F32, offset=U_OVER * PACK * W * 2 + D * 2, name="res_over")
-                mixed[db] = res
+                mixed[db] = over.tile([B, W], F32, offset=U_OVER * UNIT_BYTES + db % 2 * 4 * W, name="res%d" % (db % 2))
             js = slice(j * NB, (j + 1) * NB)
             nc.vector.scalar_tensor_tensor(
                 out=mixed[db][:, js], in0=accs[("u", 1, db)][j][:], scalar=share[:, 1:2],
@@ -343,6 +345,8 @@ def tile_dcnv2lowrankexpertcross_w_kernel(tc, x0, x, v_bytes, v_scale, c, u, bia
                 widen(0, t, W, R, False)
             widen_planes(1, range(PACK))
             load_slab(2, whole)
+            load_turn(0)
+            load_turn(1)
             x_words = x_sb[:].bitcast(F32)
             x_grouped = inter_pool.tile([P, V_PASSES * B * PACK], BF16, align_bytes=64, tag="grouped")
             for q in range(V_PASSES // 2):
@@ -371,14 +375,15 @@ def tile_dcnv2lowrankexpertcross_w_kernel(tc, x0, x, v_bytes, v_scale, c, u, bia
             at(0, quantize_x)
             loaded = [n_v]
             for q in range(TL // (T_BANK * T_GROUP)):
-                at(T_FIRST + 2 * q + 2, multiply_turned, q)
-                at(T_FIRST + 2 * q + 3, mix_turned, q)
-            t_last = T_FIRST + TL // T_BANK // 2 - 1
+                done = max(T_FIRST + T_GROUP * q + T_GROUP + 1, n_v // 2 + 3)
+                at(done, multiply_turned, q)
+                at(done + 1, mix_turned, q)
+            t_last = T_FIRST + TL // T_BANK - 1
             for s in range(n - 1):
                 if s % 2 == 0 and s // 2 + 3 < len(slabs):
                     load_slab(s // 2 + 3, whole)
-                if 2 <= s < 2 + 2 * U_PASSES:
-                    load_turn(s - 2)
+                if s + 2 < 2 * U_PASSES:
+                    load_turn(s + 2)
                 if s == 10:
                     nc.sync.dma_start(out=bias_sb[:], in_=bias.partition_broadcast(P))
                 if s <= t_last:
@@ -390,22 +395,21 @@ def tile_dcnv2lowrankexpertcross_w_kernel(tc, x0, x, v_bytes, v_scale, c, u, bia
                         load_u(loaded[0])
                         loaded[0] += 1
                 if s == n_v + 3:
-                    x0_sb = over.tile([B, D], BF16, offset=U_OVER * PACK * W * 2)
+                    x0_sb = over.tile([B, D], BF16, offset=U_OVER * UNIT_BYTES + 2 * 4 * W)
                     nc.sync.dma_start(out=x0_sb[:], in_=x0)
                     late["x0"] = x0_sb
+                if s > T_FIRST + 1 and (s - T_FIRST - 1) % T_GROUP == 0 and s <= t_last + 2:
+                    quantize_turned((s - T_FIRST - 1) // T_GROUP - 1)
                 if s // 2 + 2 < len(slabs):
                     widen_planes(s // 2 + 2, (2 * (s % 2), 2 * (s % 2) + 1))
                 if T_FIRST <= s <= t_last:
-                    for b in (2 * (s - T_FIRST), 2 * (s - T_FIRST) + 1):
-                        turn_bank(b)
-                if T_FIRST < s <= t_last + 1:
-                    empty_bank(2 * (s - T_FIRST) - 1)
+                    turn_bank(s - T_FIRST)
                 if s + 3 < n:
                     pe_interleave(s + 3)
                 if s + 2 < n:
                     arrange(s + 2)
-                if T_FIRST <= s <= t_last:
-                    empty_bank(2 * (s - T_FIRST))
+                if T_FIRST < s <= t_last + 1:
+                    empty_bank(s - T_FIRST - 1)
                 quantize(s)
                 for fn, args in later.pop(s, []):
                     fn(*args)
@@ -413,15 +417,18 @@ def tile_dcnv2lowrankexpertcross_w_kernel(tc, x0, x, v_bytes, v_scale, c, u, bia
                 kind, e, blk, g = units[s]
                 if kind == "v" and g == V_PASSES - 1:
                     at(s + 1, hidden_tanh, e, blk)
-                    at(s + 3, hidden_scale, e, blk)
-                    at(s + 4, hidden_quantize, e, blk)
+                    at(s + 2, hidden_scale, e, blk)
+                    at(s + 3, hidden_quantize, e, blk)
                 if kind == "u" and g == U_PASSES - 1:
                     mixer = (mix_first, mix_second)[e]
                     at(s + 1, mixer, blk, 0)
+                    if e == 1:
+                        at(s + 2, cross, blk, 0, NB)
                     at(s + 2, mixer, blk, 1)
                     if e == 1:
-                        at(s + 3, cross, blk, 0, W)
-                        at(s + 4, finish, blk, 0, W)
+                        at(s + 3, finish, blk, 0, NB)
+                        at(s + 3, cross, blk, NB, W)
+                        at(s + 4, finish, blk, NB, W)
             for j in range(W // NB):
                 quantize(n - 1, j * NB, (j + 1) * NB)
                 multiply(n - 1, [j])

@@ -32,7 +32,7 @@ U_VEC = 400
 U_VEC_PE = (352, 264)
 U_VEC_END = (160, 64)
 U_PE = 256
-U_OWN = 4
+STAGE = 6
 U_OVER = 4
 CH = 8
 CW = D // CH
@@ -41,6 +41,7 @@ TPITCH = 144
 T_BANK = 8
 T_GROUP = 4
 T_FIRST = 7
+T_LOADS = {3: (0, 1, 2, 3), 4: (4, 5), 5: (6, 7)}
 T_BYTES = P * TPITCH * 2
 UNIT_BYTES = PACK * W * 2
 V_VEC_T = 364
@@ -51,9 +52,8 @@ def tile_dcnv2lowrankexpertcross_w_kernel(tc, x0, x, v_bytes, v_scale, c, u, bia
     nc = tc.nc
     with ExitStack() as ctx:
         const = ctx.enter_context(tc.tile_pool(name="const", bufs=1))
-        byte_pool = ctx.enter_context(tc.tile_pool(name="byte_pool", bufs=2))
         wide_pool = ctx.enter_context(tc.tile_pool(name="wide_pool", bufs=3))
-        raw_pool = ctx.enter_context(tc.tile_pool(name="raw_pool", bufs=U_OWN))
+        raw_pool = ctx.enter_context(tc.tile_pool(name="raw_pool", bufs=STAGE))
         inter_pool = ctx.enter_context(tc.tile_pool(name="inter_pool", bufs=4))
         code_pool = ctx.enter_context(tc.tile_pool(name="code_pool", bufs=4))
         small = ctx.enter_context(tc.tile_pool(name="small", bufs=2))
@@ -98,7 +98,7 @@ def tile_dcnv2lowrankexpertcross_w_kernel(tc, x0, x, v_bytes, v_scale, c, u, bia
         def load_slab(i, pieces):
             e, g = slabs[i]
             if i not in slab_raw:
-                v_raw = byte_pool.tile([P, PACK, R], U8)
+                v_raw = raw_pool.tile([P, PACK, R], U8, tag="stage")
                 slab_raw[i] = v_raw
             rows = v_bytes[e, g * K_PASS:(g + 1) * K_PASS, :].rearrange("(p t) w -> p t w", t=PACK)
             for ts, cs in pieces:
@@ -108,9 +108,9 @@ def tile_dcnv2lowrankexpertcross_w_kernel(tc, x0, x, v_bytes, v_scale, c, u, bia
 
         def load_u(i):
             kind, e, blk, g = units[i]
-            slot = (i - n_v) % (U_OWN + U_OVER) - U_OWN
+            slot = (i - n_v) % (STAGE + U_OVER) - STAGE
             if slot < 0:
-                u_raw = raw_pool.tile([P, PACK, W], BF16)
+                u_raw = raw_pool.tile([P, PACK, W], BF16, tag="stage")
             else:
                 u_raw = over.tile([P, PACK, W], BF16, offset=slot * UNIT_BYTES, name="u_over%d" % slot)
             rows = u[e, g * K_PASS:(g + 1) * K_PASS, :].rearrange("(p t) w -> p t w", t=PACK)
@@ -270,10 +270,15 @@ def tile_dcnv2lowrankexpertcross_w_kernel(tc, x0, x, v_bytes, v_scale, c, u, bia
                     start=(g == 0), stop=(g == last))
 
         def hidden_tanh(e, hb):
-            turned = []
+            hid[(e, hb)] = []
             for acc in accs.pop(("v", e, hb)):
                 th = small.tile([B, PACK, P], F32)
                 nc.scalar.activation(out=th[:], in_=acc[:].rearrange("b (p t) -> b t p", t=PACK), func=ACT.Tanh)
+                hid[(e, hb)].append(th)
+
+        def hidden_turn(e, hb):
+            turned = []
+            for th in hid[(e, hb)]:
                 slots = tr_pool.tile([P, PACK, B], F32)
                 for t in range(PACK):
                     nc.tensor.transpose(slots[:, t, :], th[:, t, :], ident[:])
@@ -332,6 +337,10 @@ def tile_dcnv2lowrankexpertcross_w_kernel(tc, x0, x, v_bytes, v_scale, c, u, bia
             load_slab(0, [(slice(t, t + 1), slice(0, W)) for t in range(PACK)] + [(slice(0, 4), slice(W, R))])
             load_slab(1, whole)
             nc.sync.dma_start(out=x_sb[:], in_=x)
+            for i in range(2, STAGE):
+                load_slab(i, whole)
+                for q in T_LOADS.get(i, ()):
+                    load_turn(q)
             nc.sync.dma_start(out=c_sb[:], in_=c.rearrange("e (g p t) -> p (e g) t", p=P, t=PACK))
 
             for e in range(E):
@@ -344,9 +353,6 @@ def tile_dcnv2lowrankexpertcross_w_kernel(tc, x0, x, v_bytes, v_scale, c, u, bia
             for t in range(PACK):
                 widen(0, t, W, R, False)
             widen_planes(1, range(PACK))
-            load_slab(2, whole)
-            load_turn(0)
-            load_turn(1)
             x_words = x_sb[:].bitcast(F32)
             x_grouped = inter_pool.tile([P, V_PASSES * B * PACK], BF16, align_bytes=64, tag="grouped")
             for q in range(V_PASSES // 2):
@@ -368,6 +374,7 @@ def tile_dcnv2lowrankexpertcross_w_kernel(tc, x0, x, v_bytes, v_scale, c, u, bia
                         in_=x_grouped[:, lo * K_PASS:hi * K_PASS])
 
             later = {}
+            early = {}
 
             def at(step, fn, *args):
                 later.setdefault(step, []).append((fn, args))
@@ -380,18 +387,16 @@ def tile_dcnv2lowrankexpertcross_w_kernel(tc, x0, x, v_bytes, v_scale, c, u, bia
                 at(done + 1, mix_turned, q)
             t_last = T_FIRST + TL // T_BANK - 1
             for s in range(n - 1):
-                if s % 2 == 0 and s // 2 + 3 < len(slabs):
-                    load_slab(s // 2 + 3, whole)
-                if s + 2 < 2 * U_PASSES:
-                    load_turn(s + 2)
+                if s % 2 == 0 and STAGE <= s // 2 + 4 < len(slabs):
+                    load_slab(s // 2 + 4, whole)
                 if s == 10:
                     nc.sync.dma_start(out=bias_sb[:], in_=bias.partition_broadcast(P))
                 if s <= t_last:
-                    if s >= 11 and s % 2 == 1 and loaded[0] < n_v + U_OWN:
+                    if s >= n_v - 9 and loaded[0] < n_v + STAGE and (s % 2 == 1 or s > n_v - 9 + 2):
                         load_u(loaded[0])
                         loaded[0] += 1
                 else:
-                    while loaded[0] < min(n, s + 2 + U_OWN + U_OVER):
+                    while loaded[0] < min(n, s + 2 + STAGE + U_OVER):
                         load_u(loaded[0])
                         loaded[0] += 1
                 if s == n_v + 3:
@@ -404,6 +409,8 @@ def tile_dcnv2lowrankexpertcross_w_kernel(tc, x0, x, v_bytes, v_scale, c, u, bia
                     widen_planes(s // 2 + 2, (2 * (s % 2), 2 * (s % 2) + 1))
                 if T_FIRST <= s <= t_last:
                     turn_bank(s - T_FIRST)
+                for fn, args in early.pop(s, []):
+                    fn(*args)
                 if s + 3 < n:
                     pe_interleave(s + 3)
                 if s + 2 < n:
@@ -417,6 +424,7 @@ def tile_dcnv2lowrankexpertcross_w_kernel(tc, x0, x, v_bytes, v_scale, c, u, bia
                 kind, e, blk, g = units[s]
                 if kind == "v" and g == V_PASSES - 1:
                     at(s + 1, hidden_tanh, e, blk)
+                    early[s + 2] = [(hidden_turn, (e, blk))]
                     at(s + 2, hidden_scale, e, blk)
                     at(s + 3, hidden_quantize, e, blk)
                 if kind == "u" and g == U_PASSES - 1:

@@ -40,8 +40,8 @@ TL = 128
 TPITCH = 144
 T_BANK = 8
 T_GROUP = 4
-T_FIRST = 7
-T_LOADS = {3: (0, 1, 2, 3), 4: (4, 5), 5: (6, 7)}
+T_FIRST = 9
+T_LOADS = {3: (0, 1), 4: (2, 3, 4), 5: (5,), 6: (6, 7)}
 T_BYTES = P * TPITCH * 2
 UNIT_BYTES = PACK * W * 2
 V_VEC_T = 364
@@ -106,9 +106,26 @@ def tile_dcnv2lowrankexpertcross_w_kernel(tc, x0, x, v_bytes, v_scale, c, u, bia
 
         whole = [(slice(0, 2), slice(0, R)), (slice(2, 4), slice(0, R))]
 
+        t_last = T_FIRST + TL // T_BANK - 1
+        first_over = t_last + 2 + STAGE + 1
+
+        def over_slot(i):
+            slot = (i - first_over) % (STAGE + U_OVER)
+            return slot if i >= first_over and slot < U_OVER else -1
+
+        staged = [i for i in range(n_v, n) if over_slot(i) < 0]
+
+        def free_from(i):
+            if over_slot(i) >= 0:
+                return max(t_last + 1, i - STAGE - U_OVER - 1)
+            place = staged.index(i)
+            if place >= STAGE:
+                return staged[place - STAGE] - 1
+            return 2 * (len(slabs) - STAGE + place) - 2
+
         def load_u(i):
             kind, e, blk, g = units[i]
-            slot = (i - n_v) % (STAGE + U_OVER) - STAGE
+            slot = over_slot(i)
             if slot < 0:
                 u_raw = raw_pool.tile([P, PACK, W], BF16, tag="stage")
             else:
@@ -341,7 +358,6 @@ def tile_dcnv2lowrankexpertcross_w_kernel(tc, x0, x, v_bytes, v_scale, c, u, bia
                 load_slab(i, whole)
                 for q in T_LOADS.get(i, ()):
                     load_turn(q)
-            nc.sync.dma_start(out=c_sb[:], in_=c.rearrange("e (g p t) -> p (e g) t", p=P, t=PACK))
 
             for e in range(E):
                 nc.scalar.activation(
@@ -353,6 +369,10 @@ def tile_dcnv2lowrankexpertcross_w_kernel(tc, x0, x, v_bytes, v_scale, c, u, bia
             for t in range(PACK):
                 widen(0, t, W, R, False)
             widen_planes(1, range(PACK))
+            load_slab(STAGE, whole)
+            for q in T_LOADS[STAGE]:
+                load_turn(q)
+            nc.sync.dma_start(out=c_sb[:], in_=c.rearrange("e (g p t) -> p (e g) t", p=P, t=PACK))
             x_words = x_sb[:].bitcast(F32)
             x_grouped = inter_pool.tile([P, V_PASSES * B * PACK], BF16, align_bytes=64, tag="grouped")
             for q in range(V_PASSES // 2):
@@ -385,20 +405,14 @@ def tile_dcnv2lowrankexpertcross_w_kernel(tc, x0, x, v_bytes, v_scale, c, u, bia
                 done = max(T_FIRST + T_GROUP * q + T_GROUP + 1, n_v // 2 + 3)
                 at(done, multiply_turned, q)
                 at(done + 1, mix_turned, q)
-            t_last = T_FIRST + TL // T_BANK - 1
             for s in range(n - 1):
-                if s % 2 == 0 and STAGE <= s // 2 + 4 < len(slabs):
+                if s % 2 == 0 and STAGE < s // 2 + 4 < len(slabs):
                     load_slab(s // 2 + 4, whole)
                 if s == 10:
                     nc.sync.dma_start(out=bias_sb[:], in_=bias.partition_broadcast(P))
-                if s <= t_last:
-                    if s >= n_v - 9 and loaded[0] < n_v + STAGE and (s % 2 == 1 or s > n_v - 9 + 2):
-                        load_u(loaded[0])
-                        loaded[0] += 1
-                else:
-                    while loaded[0] < min(n, s + 2 + STAGE + U_OVER):
-                        load_u(loaded[0])
-                        loaded[0] += 1
+                while s >= 2 * (len(slabs) - 5) and loaded[0] < n and free_from(loaded[0]) <= s:
+                    load_u(loaded[0])
+                    loaded[0] += 1
                 if s == n_v + 3:
                     x0_sb = over.tile([B, D], BF16, offset=U_OVER * UNIT_BYTES + 2 * 4 * W)
                     nc.sync.dma_start(out=x0_sb[:], in_=x0)

@@ -25,27 +25,27 @@ U_PASSES = R // K_PASS
 RH = R // W
 DB = D // W
 WIDEN_ACT = 0
-V_VEC = 304
+V_VEC = 276
 V_VEC0 = 0
-V_VEC_END = 520
+V_VEC_END = 420
 U_VEC = 400
-U_VEC_PE = (352, 264)
-U_VEC_END = (160, 64)
+U_VEC_PE = (320, 256)
+U_VEC_END = (176, 96)
 U_PE = 256
 STAGE = 6
-U_OVER = 4
 CH = 8
 CW = D // CH
 TL = 128
 TPITCH = 144
 T_BANK = 8
 T_GROUP = 4
-T_FIRST = 9
-T_LOADS = {3: (0, 1), 4: (2, 3, 4), 5: (5,), 6: (6, 7)}
+T_FIRST = 8
+T_LOADS = {3: (0, 1, 2), 4: (3, 4), 5: (5, 6, 7)}
 T_BYTES = P * TPITCH * 2
 UNIT_BYTES = PACK * W * 2
-V_VEC_T = 364
-V_VEC_PE = 224
+V_MORE_T = 60
+V_MORE_HEAD = 80
+V_LESS_PE = 76
 
 
 def tile_dcnv2lowrankexpertcross_w_kernel(tc, x0, x, v_bytes, v_scale, c, u, bias, gate_logits, out):
@@ -106,30 +106,21 @@ def tile_dcnv2lowrankexpertcross_w_kernel(tc, x0, x, v_bytes, v_scale, c, u, bia
 
         whole = [(slice(0, 2), slice(0, R)), (slice(2, 4), slice(0, R))]
 
-        t_last = T_FIRST + TL // T_BANK - 1
-        first_over = t_last + 2 + STAGE + 1
-
-        def over_slot(i):
-            slot = (i - first_over) % (STAGE + U_OVER)
-            return slot if i >= first_over and slot < U_OVER else -1
-
-        staged = [i for i in range(n_v, n) if over_slot(i) < 0]
+        long_steps = 2 * (len(slabs) - 2)
+        t_steps = list(range(T_FIRST, long_steps))
+        t_steps += [long_steps + 1 + 2 * j for j in range(TL // T_BANK - len(t_steps))]
+        t_last = t_steps[-1]
+        t_ready = [t_steps[T_GROUP * q + T_GROUP - 1] + 2 for q in range(len(t_steps) // T_GROUP)]
 
         def free_from(i):
-            if over_slot(i) >= 0:
-                return max(t_last + 1, i - STAGE - U_OVER - 1)
-            place = staged.index(i)
+            place = i - n_v
             if place >= STAGE:
-                return staged[place - STAGE] - 1
+                return i - STAGE - 1
             return 2 * (len(slabs) - STAGE + place) - 2
 
         def load_u(i):
             kind, e, blk, g = units[i]
-            slot = over_slot(i)
-            if slot < 0:
-                u_raw = raw_pool.tile([P, PACK, W], BF16, tag="stage")
-            else:
-                u_raw = over.tile([P, PACK, W], BF16, offset=slot * UNIT_BYTES, name="u_over%d" % slot)
+            u_raw = raw_pool.tile([P, PACK, W], BF16, tag="stage")
             rows = u[e, g * K_PASS:(g + 1) * K_PASS, :].rearrange("(p t) w -> p t w", t=PACK)
             if e == 1:
                 nc.sync.dma_start(out=u_raw[:], in_=rows[:, :, blk * W:(blk + 1) * W])
@@ -214,7 +205,7 @@ def tile_dcnv2lowrankexpertcross_w_kernel(tc, x0, x, v_bytes, v_scale, c, u, bia
             copy(out=dst.rearrange("p (c i) t -> p c t i", i=2), in_=src.rearrange("p t (c i) -> p c t i", i=2))
 
         def uses_pe(i):
-            return i >= n_v + 5 or i in (3, 5, 7, 9)
+            return i >= t_last + 4 or i in (3, 4, 5, 6, 7, 9)
 
         def arrange(i):
             kind, e, blk, g = units[i]
@@ -223,10 +214,12 @@ def tile_dcnv2lowrankexpertcross_w_kernel(tc, x0, x, v_bytes, v_scale, c, u, bia
             if kind == "v":
                 src = wide[0][:, blk, :, :] if i < RH else wide[i // RH][:, :, blk * W:(blk + 1) * W]
                 a = V_VEC_END if i // RH == len(slabs) - 1 else (V_VEC0, V_VEC)[blk]
-                if blk == 1 and on_pe is not None:
-                    a = V_VEC_PE
-                elif blk == 1 and T_FIRST + 2 <= i < n_v - 1:
-                    a = V_VEC_T
+                if blk == 1:
+                    a -= V_LESS_PE * (uses_pe(i) + uses_pe(i - 1))
+                if blk == 1 and T_FIRST + 3 <= i < n_v - 1:
+                    a += V_MORE_T
+                if blk == 1 and i <= T_FIRST + T_GROUP + 1:
+                    a += V_MORE_HEAD
             else:
                 src = raw.pop(i)[:]
                 a = U_VEC if on_pe is None else U_VEC_PE[e]
@@ -248,7 +241,7 @@ def tile_dcnv2lowrankexpertcross_w_kernel(tc, x0, x, v_bytes, v_scale, c, u, bia
             if not uses_pe(i):
                 return
             slots = tr_pool.tile([P, U_PE * PACK], BF16)
-            src = raw[i][:] if i >= n_v else wide[i // RH][:, :, W:]
+            src = raw[i][:] if i >= n_v else wide[i // RH][:, :, i % RH * W:(i % RH + 1) * W]
             for j in range(U_PE // P):
                 cs = slice(W - U_PE + j * P, W - U_PE + (j + 1) * P)
                 nc.tensor.matmul(
@@ -326,7 +319,7 @@ def tile_dcnv2lowrankexpertcross_w_kernel(tc, x0, x, v_bytes, v_scale, c, u, bia
 
         def mix_second(db, j):
             if db not in mixed:
-                mixed[db] = over.tile([B, W], F32, offset=U_OVER * UNIT_BYTES + db % 2 * 4 * W, name="res%d" % (db % 2))
+                mixed[db] = over.tile([B, W], F32, offset=db % 2 * 4 * W, name="res%d" % (db % 2))
             js = slice(j * NB, (j + 1) * NB)
             nc.vector.scalar_tensor_tensor(
                 out=mixed[db][:, js], in0=accs[("u", 1, db)][j][:], scalar=share[:, 1:2],
@@ -370,8 +363,6 @@ def tile_dcnv2lowrankexpertcross_w_kernel(tc, x0, x, v_bytes, v_scale, c, u, bia
                 widen(0, t, W, R, False)
             widen_planes(1, range(PACK))
             load_slab(STAGE, whole)
-            for q in T_LOADS[STAGE]:
-                load_turn(q)
             nc.sync.dma_start(out=c_sb[:], in_=c.rearrange("e (g p t) -> p (e g) t", p=P, t=PACK))
             x_words = x_sb[:].bitcast(F32)
             x_grouped = inter_pool.tile([P, V_PASSES * B * PACK], BF16, align_bytes=64, tag="grouped")
@@ -402,7 +393,8 @@ def tile_dcnv2lowrankexpertcross_w_kernel(tc, x0, x, v_bytes, v_scale, c, u, bia
             at(0, quantize_x)
             loaded = [n_v]
             for q in range(TL // (T_BANK * T_GROUP)):
-                done = max(T_FIRST + T_GROUP * q + T_GROUP + 1, n_v // 2 + 3)
+                at(t_ready[q], quantize_turned, q)
+                done = max(t_ready[q] + 1, n_v // 2 + 3)
                 at(done, multiply_turned, q)
                 at(done + 1, mix_turned, q)
             for s in range(n - 1):
@@ -413,24 +405,23 @@ def tile_dcnv2lowrankexpertcross_w_kernel(tc, x0, x, v_bytes, v_scale, c, u, bia
                 while s >= 2 * (len(slabs) - 5) and loaded[0] < n and free_from(loaded[0]) <= s:
                     load_u(loaded[0])
                     loaded[0] += 1
-                if s == n_v + 3:
-                    x0_sb = over.tile([B, D], BF16, offset=U_OVER * UNIT_BYTES + 2 * 4 * W)
+                if s == t_last + 1:
+                    x0_sb = over.tile([B, D], BF16, offset=2 * 4 * W)
                     nc.sync.dma_start(out=x0_sb[:], in_=x0)
                     late["x0"] = x0_sb
-                if s > T_FIRST + 1 and (s - T_FIRST - 1) % T_GROUP == 0 and s <= t_last + 2:
-                    quantize_turned((s - T_FIRST - 1) // T_GROUP - 1)
                 if s // 2 + 2 < len(slabs):
                     widen_planes(s // 2 + 2, (2 * (s % 2), 2 * (s % 2) + 1))
-                if T_FIRST <= s <= t_last:
-                    turn_bank(s - T_FIRST)
+                if s in t_steps:
+                    turn_bank(t_steps.index(s))
                 for fn, args in early.pop(s, []):
                     fn(*args)
                 if s + 3 < n:
                     pe_interleave(s + 3)
                 if s + 2 < n:
                     arrange(s + 2)
-                if T_FIRST < s <= t_last + 1:
-                    empty_bank(s - T_FIRST - 1)
+                for b, step in enumerate(t_steps):
+                    if s == step + (2 if b % T_GROUP == 0 else 1):
+                        empty_bank(b)
                 quantize(s)
                 for fn, args in later.pop(s, []):
                     fn(*args)

@@ -24,28 +24,29 @@ V_PASSES = D // K_PASS
 U_PASSES = R // K_PASS
 RH = R // W
 DB = D // W
-WIDEN_ACT = 0
-V_VEC = 276
-V_VEC0 = 0
-V_VEC_END = 420
-U_VEC = 400
-U_VEC_PE = (320, 256)
-U_VEC_END = (176, 96)
-U_PE = 256
-STAGE = 6
 CH = 8
 CW = D // CH
-TL = 128
-TPITCH = 144
 T_BANK = 8
 T_GROUP = 4
-T_FIRST = 8
-T_LOADS = {3: (0, 1, 2), 4: (3, 4), 5: (5, 6, 7)}
-T_BYTES = P * TPITCH * 2
+
+T_TILES = 1
+T_COLS = 128
+T_PITCH = 144
+TL = T_TILES * T_COLS
+PLAIN = CW - TL
+U_PE = 256
+STAGE = 6
+T_FIRST = 7
+T_LONG = 8
+T_SHORT = 4
+PE_HEAD = 7
+SHARE_HEAD = 280
+SHARE_TURN = 340
+SHARE_U = 420
+SHARE_PE = 300
+SHARE_END = 120
+T_BYTES = P * T_PITCH * 2
 UNIT_BYTES = PACK * W * 2
-V_MORE_T = 60
-V_MORE_HEAD = 80
-V_LESS_PE = 76
 
 
 def tile_dcnv2lowrankexpertcross_w_kernel(tc, x0, x, v_bytes, v_scale, c, u, bias, gate_logits, out):
@@ -54,8 +55,8 @@ def tile_dcnv2lowrankexpertcross_w_kernel(tc, x0, x, v_bytes, v_scale, c, u, bia
         const = ctx.enter_context(tc.tile_pool(name="const", bufs=1))
         wide_pool = ctx.enter_context(tc.tile_pool(name="wide_pool", bufs=3))
         raw_pool = ctx.enter_context(tc.tile_pool(name="raw_pool", bufs=STAGE))
-        inter_pool = ctx.enter_context(tc.tile_pool(name="inter_pool", bufs=4))
-        code_pool = ctx.enter_context(tc.tile_pool(name="code_pool", bufs=4))
+        inter_pool = ctx.enter_context(tc.tile_pool(name="inter_pool", bufs=5))
+        code_pool = ctx.enter_context(tc.tile_pool(name="code_pool", bufs=5))
         small = ctx.enter_context(tc.tile_pool(name="small", bufs=2))
         over = ctx.enter_context(tc.tile_pool(name="over", bufs=1))
         acc_pool = ctx.enter_context(tc.psum_pool(name="acc_pool", bufs=4))
@@ -63,11 +64,10 @@ def tile_dcnv2lowrankexpertcross_w_kernel(tc, x0, x, v_bytes, v_scale, c, u, bia
 
         ident = const.tile([P, P], F32)
         ident16 = const.tile([P, P], BF16)
-        scale_sb = const.tile([P, V_PASSES, PACK], F32)
-        x_sb = const.tile([B, D], BF16)
         perm16 = const.tile([P, P], BF16)
-        first_mix = const.tile([B, D], F32)
-        u_turn = over.tile([P, P, TPITCH], BF16, offset=0)
+        scale_first = const.tile([P, 1, PACK], F32)
+        scale_rest = const.tile([P, V_PASSES - 1, PACK], F32)
+        mix = const.tile([B, D], F32)
         bias_sb = const.tile([B, D], BF16)
         c_sb = const.tile([P, E * U_PASSES, PACK], BF16)
         gate_sb = const.tile([B, E], BF16)
@@ -76,51 +76,34 @@ def tile_dcnv2lowrankexpertcross_w_kernel(tc, x0, x, v_bytes, v_scale, c, u, bia
         x_scales = const.tile([P, V_PASSES, B], U8, align_bytes=64)
         h_codes = const.tile([P, E, U_PASSES, B], U32, align_bytes=64)
         h_scales = const.tile([P, E, U_PASSES, B], U8, align_bytes=64)
+        u_turn = [over.tile([P, P, T_PITCH], BF16, offset=j * T_BYTES, name="u_turn%d" % j) for j in range(T_TILES)]
 
         slabs = [(e, g) for e in range(E) for g in range(V_PASSES)]
         units = [("v", e, hb, g) for e, g in slabs for hb in range(RH)]
         n_v = len(units)
-        units += [("u", 0, db, g) for db in range(DB - 1) for g in range(U_PASSES)]
+        units += [("u", 0, db, g) for db in range(2) for g in range(U_PASSES)]
+        n_0 = len(units)
         units += [("u", 1, db, g) for db in range(DB) for g in range(U_PASSES)]
         n = len(units)
-        raw = {}
-        slab_raw = {}
-        wide = {}
-        inter = {}
-        codes = {}
-        accs = {}
-        hid = {}
-        mixed = {}
-        pe_out = {}
-        t_banks = {}
-        late = {}
+        raw, slab_raw, wide, inter, codes, accs, hid, pe_out, t_banks, late = {}, {}, {}, {}, {}, {}, {}, {}, {}, {}
+
+        def width(i):
+            return PLAIN * CH // 2 if i in range(n_v, n_0) else W
 
         def load_slab(i, pieces):
             e, g = slabs[i]
-            if i not in slab_raw:
-                v_raw = raw_pool.tile([P, PACK, R], U8, tag="stage")
-                slab_raw[i] = v_raw
+            v_raw = raw_pool.tile([P, PACK, R], U8, tag="stage")
+            slab_raw[i] = v_raw
             rows = v_bytes[e, g * K_PASS:(g + 1) * K_PASS, :].rearrange("(p t) w -> p t w", t=PACK)
             for ts, cs in pieces:
-                nc.sync.dma_start(out=slab_raw[i][:, ts, cs], in_=rows[:, ts, cs])
+                nc.sync.dma_start(out=v_raw[:, ts, cs], in_=rows[:, ts, cs])
 
         whole = [(slice(0, 2), slice(0, R)), (slice(2, 4), slice(0, R))]
-
         long_steps = 2 * (len(slabs) - 2)
-        t_steps = list(range(T_FIRST, long_steps))
-        t_steps += [long_steps + 1 + 2 * j for j in range(TL // T_BANK - len(t_steps))]
-        t_last = t_steps[-1]
-        t_ready = [t_steps[T_GROUP * q + T_GROUP - 1] + 2 for q in range(len(t_steps) // T_GROUP)]
-
-        def free_from(i):
-            place = i - n_v
-            if place >= STAGE:
-                return i - STAGE - 1
-            return 2 * (len(slabs) - STAGE + place) - 2
 
         def load_u(i):
             kind, e, blk, g = units[i]
-            u_raw = raw_pool.tile([P, PACK, W], BF16, tag="stage")
+            u_raw = raw_pool.tile([P, PACK, width(i)], BF16, tag="stage")
             rows = u[e, g * K_PASS:(g + 1) * K_PASS, :].rearrange("(p t) w -> p t w", t=PACK)
             if e == 1:
                 nc.sync.dma_start(out=u_raw[:], in_=rows[:, :, blk * W:(blk + 1) * W])
@@ -128,36 +111,30 @@ def tile_dcnv2lowrankexpertcross_w_kernel(tc, x0, x, v_bytes, v_scale, c, u, bia
                 for t in range(PACK):
                     nc.sync.dma_start(
                         out=u_raw[:, t, :].rearrange("p (c w) -> p c w", c=CH // 2),
-                        in_=rows[:, t, :].rearrange("p (c w) -> p c w", c=CH)[:, 4 * blk:4 * blk + 4, :CW - TL])
+                        in_=rows[:, t, :].rearrange("p (c w) -> p c w", c=CH)[:, 4 * blk:4 * blk + 4, :PLAIN])
             raw[i] = u_raw
 
-        def load_turn(q):
-            g, half = q // 2, q % 2
-            ps = slice(half * P // 2, (half + 1) * P // 2)
+        def load_turn(j, g):
             src = u[0, g * K_PASS:(g + 1) * K_PASS, :].rearrange("(p t) (c w) -> (t c) p w", t=PACK, c=CH)
-            nc.sync.dma_start(out=u_turn[g:P:U_PASSES, ps, :TL], in_=src[:, ps, CW - TL:])
+            first = PLAIN + j * T_COLS
+            nc.sync.dma_start(out=u_turn[j][g:P:U_PASSES, :, :T_COLS], in_=src[:, :, first:first + T_COLS])
 
-        def turn_bank(b):
-            slots = tr_pool.tile([P, U_PASSES, T_BANK, CH * PACK], BF16)
-            for l in range(T_BANK):
-                nc.tensor.transpose(slots[:, :, l, :], u_turn[:, :, b * T_BANK + l], perm16[:])
-            t_banks[b] = slots
+        def turn(l):
+            b = l // T_BANK
+            if b not in t_banks:
+                slots = tr_pool.tile([P, U_PASSES, T_BANK, CH * PACK], BF16)
+                t_banks[b] = slots
+            nc.tensor.transpose(t_banks[b][:, :, l % T_BANK, :], u_turn[l // T_COLS][:, :, l % T_COLS], perm16[:])
 
         def empty_bank(b):
             key = ("t", b // T_GROUP)
             if key not in inter:
-                t_grouped = over.tile([P, W, PACK], BF16, align_bytes=64, offset=T_BYTES)
+                t_grouped = inter_pool.tile([P, W, PACK], BF16, align_bytes=64, tag="grouped")
                 inter[key] = t_grouped
             dst = inter[key][:].rearrange("p (g q w) t -> p g q (w t)", g=U_PASSES, q=T_GROUP)
             nc.scalar.copy(
                 out=dst[:, :, b % T_GROUP, :].bitcast(F32),
                 in_=t_banks.pop(b)[:].rearrange("p g l x -> p g (l x)").bitcast(F32))
-
-        def quantize_turned(q):
-            t_codes = over.tile([P, W], U32, align_bytes=64, offset=T_BYTES + UNIT_BYTES)
-            t_scales = over.tile([P, W], U8, align_bytes=64, offset=T_BYTES + UNIT_BYTES + 4 * W)
-            codes[("t", q)] = (t_codes, t_scales)
-            quantize(("t", q))
 
         def multiply_turned(q):
             w_codes, w_scales = codes[("t", q)]
@@ -175,57 +152,51 @@ def tile_dcnv2lowrankexpertcross_w_kernel(tc, x0, x, v_bytes, v_scale, c, u, bia
 
         def mix_turned(q):
             nl = T_BANK * T_GROUP
-            ls = slice(CW - TL + q * nl, CW - TL + (q + 1) * nl)
+            ls = slice(PLAIN + q * nl, PLAIN + (q + 1) * nl)
             nc.vector.scalar_tensor_tensor(
-                out=chunked(first_mix[:])[:, :, ls],
+                out=chunked(mix[:])[:, :, ls],
                 in0=accs.pop(("t", q))[:, :nl * CH].rearrange("b (l c) -> b c l", c=CH),
                 scalar=share[:, 0:1], in1=chunked(bias_sb[:])[:, :, ls], op0=ALU.mult, op1=ALU.add)
 
-        def widen(i, t, lo, hi, on_act):
+        def widen(i, t, lo, hi, on_act=False):
             g = slabs[i][1]
             if i not in wide:
                 v_wide = wide_pool.tile([P, RH, PACK, W] if i == 0 else [P, PACK, R], BF16)
                 wide[i] = v_wide
-            if lo == hi:
-                return
             src = slab_raw[i][:, t, lo:hi].bitcast(FP8)
-            dst = wide[i][:, lo // W, t, lo % W:lo % W + hi - lo] if i == 0 else wide[i][:, t, lo:hi]
+            dst = wide[i][:, lo // W, t, :] if i == 0 else wide[i][:, t, lo:hi]
+            scale = scale_first[:, 0, t:t + 1] if g == 0 else scale_rest[:, g - 1, t:t + 1]
             if on_act:
-                nc.scalar.activation(out=dst, in_=src, func=ACT.Copy, scale=scale_sb[:, g, t:t + 1])
+                nc.scalar.activation(out=dst, in_=src, func=ACT.Copy, scale=scale)
             else:
-                nc.vector.tensor_scalar(out=dst, in0=src, scalar1=scale_sb[:, g, t:t + 1], scalar2=None, op0=ALU.mult)
-
-        def widen_planes(i, planes):
-            for t in planes:
-                cut = min(max(WIDEN_ACT - t * R, 0), R)
-                widen(i, t, 0, cut, True)
-                widen(i, t, cut, R, False)
+                nc.vector.tensor_scalar(out=dst, in0=src, scalar1=scale, scalar2=None, op0=ALU.mult)
 
         def interleave(copy, dst, src):
             copy(out=dst.rearrange("p (c i) t -> p c t i", i=2), in_=src.rearrange("p t (c i) -> p c t i", i=2))
 
         def uses_pe(i):
-            return i >= t_last + 4 or i in (3, 4, 5, 6, 7, 9)
+            return i >= n_0 or i in range(3, 3 + PE_HEAD)
+
+        def vector_share(i):
+            if i >= n - 2:
+                return SHARE_END
+            if i >= n_0:
+                return SHARE_PE
+            if i >= long_steps + 2:
+                return SHARE_U
+            if i % RH == 0:
+                return 0
+            return SHARE_HEAD if i < 3 + PE_HEAD else SHARE_TURN
 
         def arrange(i):
-            kind, e, blk, g = units[i]
-            grouped = inter_pool.tile([P, W, PACK], BF16, align_bytes=64)
+            grouped = inter_pool.tile([P, width(i), PACK], BF16, align_bytes=64)
             on_pe = pe_out.pop(i, None)
-            if kind == "v":
-                src = wide[0][:, blk, :, :] if i < RH else wide[i // RH][:, :, blk * W:(blk + 1) * W]
-                a = V_VEC_END if i // RH == len(slabs) - 1 else (V_VEC0, V_VEC)[blk]
-                if blk == 1:
-                    a -= V_LESS_PE * (uses_pe(i) + uses_pe(i - 1))
-                if blk == 1 and T_FIRST + 3 <= i < n_v - 1:
-                    a += V_MORE_T
-                if blk == 1 and i <= T_FIRST + T_GROUP + 1:
-                    a += V_MORE_HEAD
+            if i < n_v:
+                src = wide[0][:, i, :, :] if i < RH else wide[i // RH][:, :, i % RH * W:(i % RH + 1) * W]
             else:
                 src = raw.pop(i)[:]
-                a = U_VEC if on_pe is None else U_VEC_PE[e]
-                if i >= n - len(U_VEC_END):
-                    a = U_VEC_END[i - n]
-            b = W if on_pe is None else W - U_PE
+            a = vector_share(i)
+            b = width(i) if on_pe is None else W - U_PE
             if a > 0:
                 interleave(nc.vector.tensor_copy, grouped[:, :a, :], src[:, :, :a])
             if i == n - 1:
@@ -233,8 +204,7 @@ def tile_dcnv2lowrankexpertcross_w_kernel(tc, x0, x, v_bytes, v_scale, c, u, bia
                 a = NB
             if on_pe is not None:
                 nc.scalar.copy(out=grouped[:, b:, :].rearrange("p w t -> p (w t)").bitcast(F32), in_=on_pe[:].bitcast(F32))
-            if a < b:
-                interleave(nc.scalar.copy, grouped[:, a:b, :], src[:, :, a:b])
+            interleave(nc.scalar.copy, grouped[:, a:b, :], src[:, :, a:b])
             inter[i] = grouped
 
         def pe_interleave(i):
@@ -249,7 +219,7 @@ def tile_dcnv2lowrankexpertcross_w_kernel(tc, x0, x, v_bytes, v_scale, c, u, bia
                     rhs=src[:, :, cs].rearrange("p t w -> p w t"), start=True, stop=True)
             pe_out[i] = slots
 
-        def quantize(i, lo=0, hi=W):
+        def quantize(i, lo, hi):
             if i not in codes:
                 w_codes = code_pool.tile([P, W], U32, align_bytes=64)
                 w_scales = code_pool.tile([P, W], U8, align_bytes=64)
@@ -259,30 +229,33 @@ def tile_dcnv2lowrankexpertcross_w_kernel(tc, x0, x, v_bytes, v_scale, c, u, bia
                 out=w_codes[:, lo:hi].bitcast(FP8X4), scales=w_scales[:, lo:hi],
                 in_=inter[i][:, lo:hi, :].rearrange("p w t -> p (w t)"))
 
+        def quantize_unit(i):
+            if width(i) == W:
+                quantize(i, 0, W)
+            else:
+                quantize(i, 0, NB)
+                quantize(i, NB, width(i))
+
         def multiply(i, which=range(W // NB)):
             kind, e, blk, g = units[i]
             w_codes, w_scales = codes[i]
             last = (V_PASSES if kind == "v" else U_PASSES) - 1
             if g == 0:
-                banks = []
-                for j in range(W // NB):
-                    acc = acc_pool.tile([B, NB], F32)
-                    banks.append(acc)
-                accs[(kind, e, blk)] = banks
+                accs[(kind, e, blk)] = [acc_pool.tile([B, NB], F32, name="acc") for j in range(W // NB)]
             banks = accs[(kind, e, blk)]
             for j in which:
-                js = slice(j * NB, (j + 1) * NB)
+                js = slice(j * NB, min((j + 1) * NB, width(i)))
                 lhs = x_codes[:, g, :] if kind == "v" else h_codes[:, e, g, :]
                 lhs_scale = x_scales[:, g, :] if kind == "v" else h_scales[:, e, g, :]
                 nc.tensor.matmul_mx(
-                    out=banks[j][:], lhsT=lhs.bitcast(FP8X4), lhsT_scale=lhs_scale,
+                    out=banks[j][:, :js.stop - js.start], lhsT=lhs.bitcast(FP8X4), lhsT_scale=lhs_scale,
                     rhs=w_codes[:, js].bitcast(FP8X4), rhs_scale=w_scales[:, js],
                     start=(g == 0), stop=(g == last))
 
         def hidden_tanh(e, hb):
             hid[(e, hb)] = []
             for acc in accs.pop(("v", e, hb)):
-                th = small.tile([B, PACK, P], F32)
+                th = small.tile([B, PACK, P], F32, bufs=4)
                 nc.scalar.activation(out=th[:], in_=acc[:].rearrange("b (p t) -> b t p", t=PACK), func=ACT.Tanh)
                 hid[(e, hb)].append(th)
 
@@ -313,28 +286,24 @@ def tile_dcnv2lowrankexpertcross_w_kernel(tc, x0, x, v_bytes, v_scale, c, u, bia
 
         def mix_first(db, j):
             cs = slice(4 * db + 2 * j, 4 * db + 2 * j + 2)
+            ws = slice(0, PLAIN)
             nc.vector.scalar_tensor_tensor(
-                out=chunked(first_mix[:])[:, cs, :CW - TL], in0=accs[("u", 0, db)][j][:].rearrange("b (c w) -> b c w", c=2),
-                scalar=share[:, 0:1], in1=chunked(bias_sb[:])[:, cs, :CW - TL], op0=ALU.mult, op1=ALU.add)
+                out=chunked(mix[:])[:, cs, ws],
+                in0=accs[("u", 0, db)][j][:].rearrange("b (c w) -> b c w", c=2),
+                scalar=share[:, 0:1], in1=chunked(bias_sb[:])[:, cs, ws], op0=ALU.mult, op1=ALU.add)
 
         def mix_second(db, j):
-            if db not in mixed:
-                mixed[db] = over.tile([B, W], F32, offset=db % 2 * 4 * W, name="res%d" % (db % 2))
-            js = slice(j * NB, (j + 1) * NB)
+            cs = slice(db * W + j * NB, db * W + (j + 1) * NB)
             nc.vector.scalar_tensor_tensor(
-                out=mixed[db][:, js], in0=accs[("u", 1, db)][j][:], scalar=share[:, 1:2],
-                in1=first_mix[:, db * W + j * NB:db * W + (j + 1) * NB], op0=ALU.mult, op1=ALU.add)
+                out=mix[:, cs], in0=accs[("u", 1, db)][j][:], scalar=share[:, 1:2], in1=mix[:, cs],
+                op0=ALU.mult, op1=ALU.add)
 
-        def cross(db, lo, hi):
-            res = mixed[db]
-            nc.vector.tensor_tensor(
-                out=res[:, lo:hi], in0=res[:, lo:hi], in1=late["x0"][:, db * W + lo:db * W + hi], op=ALU.mult)
+        def cross(lo, hi):
+            nc.vector.tensor_tensor(out=mix[:, lo:hi], in0=mix[:, lo:hi], in1=late["x0"][:, lo:hi], op=ALU.mult)
 
-        def finish(db, lo, hi):
-            res = mixed[db]
-            nc.vector.tensor_tensor(
-                out=res[:, lo:hi], in0=res[:, lo:hi], in1=x_sb[:, db * W + lo:db * W + hi], op=ALU.add)
-            nc.sync.dma_start(out=out[:, db * W + lo:db * W + hi], in_=res[:, lo:hi])
+        def finish(lo, hi):
+            nc.vector.tensor_tensor(out=mix[:, lo:hi], in0=mix[:, lo:hi], in1=late["x"][:, lo:hi], op=ALU.add)
+            nc.sync.dma_start(out=out[:, lo:hi], in_=mix[:, lo:hi])
 
         make_identity(nc, ident[:])
         nc.vector.tensor_copy(out=ident16[:], in_=ident[:])
@@ -342,29 +311,35 @@ def tile_dcnv2lowrankexpertcross_w_kernel(tc, x0, x, v_bytes, v_scale, c, u, bia
             out=perm16[:].rearrange("q (g c t) -> q g c t", g=U_PASSES, c=CH),
             in_=ident[:].rearrange("q (t c g) -> q g c t", g=U_PASSES, c=CH))
         with tc.manual_schedule():
-            nc.scalar.dma_start(out=scale_sb[:], in_=v_scale.rearrange("o (g p t) u -> p (o g) (t u)", p=P, t=PACK))
+            scales = v_scale.rearrange("o (g p t) u -> p (o g) (t u)", p=P, t=PACK)
+            nc.scalar.dma_start(out=scale_first[:], in_=scales[:, :1, :])
             nc.scalar.dma_start(out=gate_sb[:], in_=gate_logits)
-            load_slab(0, [(slice(t, t + 1), slice(0, W)) for t in range(PACK)] + [(slice(0, 4), slice(W, R))])
+            load_slab(0, [(ts, slice(hb * W, (hb + 1) * W)) for hb in range(RH) for ts, cs in whole])
+            nc.sync.dma_start(out=scale_rest[:], in_=scales[:, 1:, :])
             load_slab(1, whole)
-            nc.sync.dma_start(out=x_sb[:], in_=x)
-            for i in range(2, STAGE):
-                load_slab(i, whole)
-                for q in T_LOADS.get(i, ()):
-                    load_turn(q)
+            x_early = raw_pool.tile([B, D], BF16, tag="stage")
+            nc.sync.dma_start(out=x_early[:], in_=x)
+            for g in range(2):
+                load_slab(2 + g, whole)
+                load_turn(0, g)
 
             for e in range(E):
                 nc.scalar.activation(
                     out=share[:, e:e + 1], in_=gate_sb[:, 1 - e:2 - e], func=ACT.Sigmoid,
                     scale=-1.0, bias=gate_sb[:, e:e + 1])
             for t in range(PACK):
-                widen(0, t, 0, W, t == 1)
+                widen(0, t, 0, W, t % 2 == 1)
             arrange(0)
             for t in range(PACK):
-                widen(0, t, W, R, False)
-            widen_planes(1, range(PACK))
-            load_slab(STAGE, whole)
+                widen(0, t, W, R)
+            for t in range(PACK):
+                widen(1, t, 0, R)
+            for g in range(2, U_PASSES):
+                load_slab(2 + g, whole)
+                load_turn(0, g)
+            load_slab(6, whole)
             nc.sync.dma_start(out=c_sb[:], in_=c.rearrange("e (g p t) -> p (e g) t", p=P, t=PACK))
-            x_words = x_sb[:].bitcast(F32)
+            x_words = x_early[:].bitcast(F32)
             x_grouped = inter_pool.tile([P, V_PASSES * B * PACK], BF16, align_bytes=64, tag="grouped")
             for q in range(V_PASSES // 2):
                 slots = tr_pool.tile([P, 4, B], F32)
@@ -391,65 +366,85 @@ def tile_dcnv2lowrankexpertcross_w_kernel(tc, x0, x, v_bytes, v_scale, c, u, bia
                 later.setdefault(step, []).append((fn, args))
 
             at(0, quantize_x)
-            loaded = [n_v]
-            for q in range(TL // (T_BANK * T_GROUP)):
-                at(t_ready[q], quantize_turned, q)
-                done = max(t_ready[q] + 1, n_v // 2 + 3)
-                at(done, multiply_turned, q)
-                at(done + 1, mix_turned, q)
+            stream = [(load_slab, (i, whole), 2 * i - 3) for i in range(7, len(slabs))]
+            stream += [(load_u, (i,), i - 2) for i in range(n_v, n)]
+            frees = [-1, 1, 3, 5, 7, 9] + [f for fn, args, f in stream]
+            issued = [0]
+            turned = [0]
+            full = []
+            hidden_steps = [i + 3 for i in range(n_v) if units[i][3] == V_PASSES - 1]
             for s in range(n - 1):
-                if s % 2 == 0 and STAGE < s // 2 + 4 < len(slabs):
-                    load_slab(s // 2 + 4, whole)
-                if s == 10:
+                while issued[0] < len(stream) and frees[issued[0]] < s:
+                    fn, args, f = stream[issued[0]]
+                    fn(*args)
+                    if issued[0] < U_PASSES * (T_TILES - 1):
+                        load_turn(1 + issued[0] // U_PASSES, issued[0] % U_PASSES)
+                    issued[0] += 1
+                if s == T_FIRST:
                     nc.sync.dma_start(out=bias_sb[:], in_=bias.partition_broadcast(P))
-                while s >= 2 * (len(slabs) - 5) and loaded[0] < n and free_from(loaded[0]) <= s:
-                    load_u(loaded[0])
-                    loaded[0] += 1
-                if s == t_last + 1:
-                    x0_sb = over.tile([B, D], BF16, offset=2 * 4 * W)
+                if s == n_0:
+                    x0_sb = over.tile([B, D], BF16, offset=0)
                     nc.sync.dma_start(out=x0_sb[:], in_=x0)
-                    late["x0"] = x0_sb
-                if s // 2 + 2 < len(slabs):
-                    widen_planes(s // 2 + 2, (2 * (s % 2), 2 * (s % 2) + 1))
-                if s in t_steps:
-                    turn_bank(t_steps.index(s))
+                    x_sb = over.tile([B, D], BF16, offset=2 * D)
+                    nc.sync.dma_start(out=x_sb[:], in_=x)
+                    late["x0"], late["x"] = x0_sb, x_sb
+                if s < long_steps:
+                    for t in (2 * (s % 2), 2 * (s % 2) + 1):
+                        widen(s // 2 + 2, t, 0, R)
+                ready = full[:]
+                full.clear()
                 for fn, args in early.pop(s, []):
                     fn(*args)
-                if s + 3 < n:
-                    pe_interleave(s + 3)
+                if s >= T_FIRST:
+                    for l in range(turned[0], min(TL, turned[0] + (T_LONG if s < long_steps else T_SHORT))):
+                        turn(l)
+                        turned[0] += 1
+                        if l % T_BANK == T_BANK - 1:
+                            full.append(l // T_BANK)
                 if s + 2 < n:
                     arrange(s + 2)
-                for b, step in enumerate(t_steps):
-                    if s == step + (2 if b % T_GROUP == 0 else 1):
-                        empty_bank(b)
-                quantize(s)
+                for b in ready:
+                    empty_bank(b)
+                    if b % T_GROUP == T_GROUP - 1:
+                        q = b // T_GROUP
+                        done = max(s + 2, n_v // 2 + 4 + 2 * q)
+                        while done + 1 in hidden_steps:
+                            done += 1
+                        at(s + 1, quantize, ("t", q), 0, W)
+                        at(done, multiply_turned, q)
+                        at(done + 1, mix_turned, q)
+                if s + 3 < n:
+                    pe_interleave(s + 3)
+                if s < n - 2:
+                    quantize_unit(s)
                 for fn, args in later.pop(s, []):
                     fn(*args)
+                if s == n - 2:
+                    quantize_unit(s)
                 multiply(s)
                 kind, e, blk, g = units[s]
                 if kind == "v" and g == V_PASSES - 1:
                     at(s + 1, hidden_tanh, e, blk)
-                    early[s + 2] = [(hidden_turn, (e, blk))]
-                    at(s + 2, hidden_scale, e, blk)
-                    at(s + 3, hidden_quantize, e, blk)
+                    early[s + 3] = [(hidden_turn, (e, blk))]
+                    at(s + 3, hidden_scale, e, blk)
+                    at(s + 4, hidden_quantize, e, blk)
                 if kind == "u" and g == U_PASSES - 1:
                     mixer = (mix_first, mix_second)[e]
                     at(s + 1, mixer, blk, 0)
-                    if e == 1:
-                        at(s + 2, cross, blk, 0, NB)
                     at(s + 2, mixer, blk, 1)
                     if e == 1:
-                        at(s + 3, finish, blk, 0, NB)
-                        at(s + 3, cross, blk, NB, W)
-                        at(s + 4, finish, blk, NB, W)
-            for j in range(W // NB):
-                quantize(n - 1, j * NB, (j + 1) * NB)
-                multiply(n - 1, [j])
-            for fn, args in later.pop(n - 1, []):
+                        at(s + 3, cross, blk * W, (blk + 1) * W)
+                        at(s + 4, finish, blk * W, (blk + 1) * W)
+            first, second = [((DB - 1) * W + j * NB, (DB - 1) * W + (j + 1) * NB) for j in range(W // NB)]
+            quantize(n - 1, 0, NB)
+            multiply(n - 1, [0])
+            for fn, args in later.pop(n - 1):
                 fn(*args)
-            for j in range(W // NB):
-                mix_second(DB - 1, j)
-            for j in range(W // NB):
-                cross(DB - 1, j * NB, (j + 1) * NB)
-            for j in range(W // NB):
-                finish(DB - 1, j * NB, (j + 1) * NB)
+            mix_second(DB - 1, 0)
+            quantize(n - 1, NB, W)
+            multiply(n - 1, [1])
+            cross(*first)
+            finish(*first)
+            mix_second(DB - 1, 1)
+            cross(*second)
+            finish(*second)

@@ -35,15 +35,17 @@ T_PITCH = 144
 TL = T_TILES * T_COLS
 PLAIN = CW - TL
 U_PE = 256
+INTER = 5
+POOL_COLS = 104
 STAGE = 6
 T_FIRST = 7
 T_LONG = 8
 T_SHORT = 4
 PE_HEAD = 7
 SHARE_HEAD = 280
-SHARE_TURN = 340
-SHARE_U = 420
-SHARE_PE = 300
+SHARE_TURN = 328
+SHARE_U = 400
+SHARE_PE = 288
 SHARE_END = 120
 T_BYTES = P * T_PITCH * 2
 UNIT_BYTES = PACK * W * 2
@@ -55,7 +57,7 @@ def tile_dcnv2lowrankexpertcross_w_kernel(tc, x0, x, v_bytes, v_scale, c, u, bia
         const = ctx.enter_context(tc.tile_pool(name="const", bufs=1))
         wide_pool = ctx.enter_context(tc.tile_pool(name="wide_pool", bufs=3))
         raw_pool = ctx.enter_context(tc.tile_pool(name="raw_pool", bufs=STAGE))
-        inter_pool = ctx.enter_context(tc.tile_pool(name="inter_pool", bufs=5))
+        inter_pool = ctx.enter_context(tc.tile_pool(name="inter_pool", bufs=1))
         code_pool = ctx.enter_context(tc.tile_pool(name="code_pool", bufs=5))
         small = ctx.enter_context(tc.tile_pool(name="small", bufs=2))
         over = ctx.enter_context(tc.tile_pool(name="over", bufs=1))
@@ -86,6 +88,14 @@ def tile_dcnv2lowrankexpertcross_w_kernel(tc, x0, x, v_bytes, v_scale, c, u, bia
         units += [("u", 1, db, g) for db in range(DB) for g in range(U_PASSES)]
         n = len(units)
         raw, slab_raw, wide, inter, codes, accs, hid, pe_out, t_banks, late = {}, {}, {}, {}, {}, {}, {}, {}, {}, {}
+
+        free_slots = list(range(INTER))
+        slot_of = {}
+
+        def take_grouped(key, shape, newest=False):
+            slot_of[key] = free_slots.pop(-1 if newest else 0)
+            inter[key] = inter_pool.tile(shape, BF16, align_bytes=64, name="grouped%d" % slot_of[key])
+            return inter[key]
 
         def width(i):
             return PLAIN * CH // 2 if i in range(n_v, n_0) else W
@@ -129,8 +139,7 @@ def tile_dcnv2lowrankexpertcross_w_kernel(tc, x0, x, v_bytes, v_scale, c, u, bia
         def empty_bank(b):
             key = ("t", b // T_GROUP)
             if key not in inter:
-                t_grouped = inter_pool.tile([P, W, PACK], BF16, align_bytes=64, tag="grouped")
-                inter[key] = t_grouped
+                take_grouped(key, [P, W, PACK])
             dst = inter[key][:].rearrange("p (g q w) t -> p g q (w t)", g=U_PASSES, q=T_GROUP)
             nc.scalar.copy(
                 out=dst[:, :, b % T_GROUP, :].bitcast(F32),
@@ -174,6 +183,11 @@ def tile_dcnv2lowrankexpertcross_w_kernel(tc, x0, x, v_bytes, v_scale, c, u, bia
         def interleave(copy, dst, src):
             copy(out=dst.rearrange("p (c i) t -> p c t i", i=2), in_=src.rearrange("p t (c i) -> p c t i", i=2))
 
+        def planes(i):
+            if i >= n_v:
+                return raw[i][:]
+            return wide[0][:, i, :, :] if i < RH else wide[i // RH][:, :, i % RH * W:(i % RH + 1) * W]
+
         def uses_pe(i):
             return i >= n_0 or i in range(3, 3 + PE_HEAD)
 
@@ -189,29 +203,35 @@ def tile_dcnv2lowrankexpertcross_w_kernel(tc, x0, x, v_bytes, v_scale, c, u, bia
             return SHARE_HEAD if i < 3 + PE_HEAD else SHARE_TURN
 
         def arrange(i):
-            grouped = inter_pool.tile([P, width(i), PACK], BF16, align_bytes=64)
+            helped = i in inter
+            grouped = inter[i] if helped else take_grouped(i, [P, W, PACK])
             on_pe = pe_out.pop(i, None)
-            if i < n_v:
-                src = wide[0][:, i, :, :] if i < RH else wide[i // RH][:, :, i % RH * W:(i % RH + 1) * W]
-            else:
-                src = raw.pop(i)[:]
+            src = planes(i)
             a = vector_share(i)
-            b = width(i) if on_pe is None else W - U_PE
+            b = (W if on_pe is None else W - U_PE) - (POOL_COLS if helped else 0)
+            b_pe = W - U_PE
             if a > 0:
                 interleave(nc.vector.tensor_copy, grouped[:, :a, :], src[:, :, :a])
             if i == n - 1:
                 interleave(nc.scalar.copy, grouped[:, a:NB, :], src[:, :, a:NB])
                 a = NB
             if on_pe is not None:
-                nc.scalar.copy(out=grouped[:, b:, :].rearrange("p w t -> p (w t)").bitcast(F32), in_=on_pe[:].bitcast(F32))
+                nc.scalar.copy(out=grouped[:, b_pe:, :].rearrange("p w t -> p (w t)").bitcast(F32), in_=on_pe[:].bitcast(F32))
             interleave(nc.scalar.copy, grouped[:, a:b, :], src[:, :, a:b])
-            inter[i] = grouped
+
+        def pool_copy(out, in_):
+            nc.gpsimd.tensor_scalar(out=out, in0=in_, scalar1=1.0, scalar2=0.0, op0=ALU.mult, op1=ALU.add)
+
+        def pool_interleave(i):
+            grouped = take_grouped(i, [P, W, PACK], newest=True)
+            hi = W - U_PE if uses_pe(i) else W
+            interleave(pool_copy, grouped[:, hi - POOL_COLS:hi, :], planes(i)[:, :, hi - POOL_COLS:hi])
 
         def pe_interleave(i):
             if not uses_pe(i):
                 return
             slots = tr_pool.tile([P, U_PE * PACK], BF16)
-            src = raw[i][:] if i >= n_v else wide[i // RH][:, :, i % RH * W:(i % RH + 1) * W]
+            src = planes(i)
             for j in range(U_PE // P):
                 cs = slice(W - U_PE + j * P, W - U_PE + (j + 1) * P)
                 nc.tensor.matmul(
@@ -228,13 +248,8 @@ def tile_dcnv2lowrankexpertcross_w_kernel(tc, x0, x, v_bytes, v_scale, c, u, bia
             nc.vector.quantize_mx(
                 out=w_codes[:, lo:hi].bitcast(FP8X4), scales=w_scales[:, lo:hi],
                 in_=inter[i][:, lo:hi, :].rearrange("p w t -> p (w t)"))
-
-        def quantize_unit(i):
-            if width(i) == W:
-                quantize(i, 0, W)
-            else:
-                quantize(i, 0, NB)
-                quantize(i, NB, width(i))
+            if hi == W:
+                free_slots.append(slot_of.pop(i))
 
         def multiply(i, which=range(W // NB)):
             kind, e, blk, g = units[i]
@@ -292,10 +307,10 @@ def tile_dcnv2lowrankexpertcross_w_kernel(tc, x0, x, v_bytes, v_scale, c, u, bia
                 in0=accs[("u", 0, db)][j][:].rearrange("b (c w) -> b c w", c=2),
                 scalar=share[:, 0:1], in1=chunked(bias_sb[:])[:, cs, ws], op0=ALU.mult, op1=ALU.add)
 
-        def mix_second(db, j):
-            cs = slice(db * W + j * NB, db * W + (j + 1) * NB)
+        def mix_second(db, j, lo=0, hi=NB):
+            cs = slice(db * W + j * NB + lo, db * W + j * NB + hi)
             nc.vector.scalar_tensor_tensor(
-                out=mix[:, cs], in0=accs[("u", 1, db)][j][:], scalar=share[:, 1:2], in1=mix[:, cs],
+                out=mix[:, cs], in0=accs[("u", 1, db)][j][:, lo:hi], scalar=share[:, 1:2], in1=mix[:, cs],
                 op0=ALU.mult, op1=ALU.add)
 
         def cross(lo, hi):
@@ -340,7 +355,7 @@ def tile_dcnv2lowrankexpertcross_w_kernel(tc, x0, x, v_bytes, v_scale, c, u, bia
             load_slab(6, whole)
             nc.sync.dma_start(out=c_sb[:], in_=c.rearrange("e (g p t) -> p (e g) t", p=P, t=PACK))
             x_words = x_early[:].bitcast(F32)
-            x_grouped = inter_pool.tile([P, V_PASSES * B * PACK], BF16, align_bytes=64, tag="grouped")
+            x_grouped = take_grouped("x", [P, V_PASSES * B * PACK])
             for q in range(V_PASSES // 2):
                 slots = tr_pool.tile([P, 4, B], F32)
                 for j in range(2):
@@ -358,9 +373,11 @@ def tile_dcnv2lowrankexpertcross_w_kernel(tc, x0, x, v_bytes, v_scale, c, u, bia
                         out=x_codes[:, lo:hi, :].rearrange("p g b -> p (g b)").bitcast(FP8X4),
                         scales=x_scales[:, lo:hi, :].rearrange("p g b -> p (g b)"),
                         in_=x_grouped[:, lo * K_PASS:hi * K_PASS])
+                free_slots.append(slot_of.pop("x"))
 
             later = {}
             early = {}
+            from_psum = {}
 
             def at(step, fn, *args):
                 later.setdefault(step, []).append((fn, args))
@@ -415,23 +432,28 @@ def tile_dcnv2lowrankexpertcross_w_kernel(tc, x0, x, v_bytes, v_scale, c, u, bia
                         at(done + 1, mix_turned, q)
                 if s + 3 < n:
                     pe_interleave(s + 3)
-                if s < n - 2:
-                    quantize_unit(s)
+                last_of_step = s == n - 2 or s in from_psum
+                if not last_of_step:
+                    quantize(s, 0, W)
                 for fn, args in later.pop(s, []):
                     fn(*args)
-                if s == n - 2:
-                    quantize_unit(s)
+                if last_of_step:
+                    quantize(s, 0, W)
+                if s in from_psum:
+                    if s + 3 < n:
+                        pool_interleave(s + 3)
+                    for fn, args in from_psum.pop(s):
+                        fn(*args)
                 multiply(s)
                 kind, e, blk, g = units[s]
                 if kind == "v" and g == V_PASSES - 1:
                     at(s + 1, hidden_tanh, e, blk)
                     early[s + 3] = [(hidden_turn, (e, blk))]
-                    at(s + 3, hidden_scale, e, blk)
+                    from_psum[s + 3] = [(hidden_scale, (e, blk))]
                     at(s + 4, hidden_quantize, e, blk)
                 if kind == "u" and g == U_PASSES - 1:
                     mixer = (mix_first, mix_second)[e]
-                    at(s + 1, mixer, blk, 0)
-                    at(s + 2, mixer, blk, 1)
+                    from_psum[s + 2] = [(mixer, (blk, j)) for j in range(W // NB)]
                     if e == 1:
                         at(s + 3, cross, blk * W, (blk + 1) * W)
                         at(s + 4, finish, blk * W, (blk + 1) * W)
@@ -445,6 +467,10 @@ def tile_dcnv2lowrankexpertcross_w_kernel(tc, x0, x, v_bytes, v_scale, c, u, bia
             multiply(n - 1, [1])
             cross(*first)
             finish(*first)
-            mix_second(DB - 1, 1)
-            cross(*second)
-            finish(*second)
+            quarters = [(0, NB // 2), (NB // 2, NB)]
+            for lo, hi in quarters:
+                mix_second(DB - 1, 1, lo, hi)
+            for lo, hi in quarters:
+                cross(second[0] + lo, second[0] + hi)
+            for lo, hi in quarters:
+                finish(second[0] + lo, second[0] + hi)

@@ -23,54 +23,61 @@ NB = 512
 V_PASSES = D // K_PASS
 U_PASSES = R // K_PASS
 RH = R // W
-DB = D // W
-CH = 8
-CW = D // CH
+CHUNKS = 4
+CW = D // CHUNKS
+PLAIN = NB
+REST = CW - PLAIN
+HALVES = 2
+RUNS = CHUNKS * HALVES
 T_BANK = 8
-T_GROUP = 4
-
-T_TILES = 1
-T_COLS = 128
+T_GROUP = 32
 T_PITCH = 144
-TL = T_TILES * T_COLS
-PLAIN = CW - TL
-U_PE = 256
-INTER = 5
-POOL_COLS = 104
-STAGE = 6
+GROUP_COLS = RUNS * T_GROUP
+T_GROUPS = (4, 2)
+SIDE = REST - HALVES * T_GROUPS[1] * T_GROUP
+
+EYE_UNITS = range(1, 10)
+EYE_COLS = 512
+EYE_END = 256
 T_FIRST = 7
-T_LONG = 8
-T_SHORT = 4
-PE_HEAD = 7
-SHARE_HEAD = 280
-SHARE_TURN = 328
-SHARE_U = 400
-SHARE_PE = 288
-SHARE_END = 120
+T_LONG = 10
+T_SHORT = 6
+T_HIDDEN = 2
+SHARE_V = 352
+SHARE_BUSY = 288
+SHARE_FREE = 464
+SHARE_END = 128
+POOL_COLS = 104
+
+SLOT = PACK * W * 2
 T_BYTES = P * T_PITCH * 2
-UNIT_BYTES = PACK * W * 2
+WIDE_BYTES = PACK * R * 2
+WIDE_BUFS = 3
+STAGE_SLOTS = 3
+GROUPED_SLOTS = 5
+CODE_SLOTS = 5
+CODE_BYTES = 5 * W
+TANH_BYTES = NB * 4
+AT_TURN = (0, T_BYTES)
+AT_WIDE = 2 * T_BYTES
+AT_STAGE = AT_WIDE + WIDE_BUFS * WIDE_BYTES
+AT_GROUPED = AT_STAGE + STAGE_SLOTS * SLOT
+AT_CODES = AT_GROUPED + GROUPED_SLOTS * SLOT
+AT_TANH = AT_CODES + CODE_SLOTS * CODE_BYTES
 
 
 def tile_dcnv2lowrankexpertcross_w_kernel(tc, x0, x, v_bytes, v_scale, c, u, bias, gate_logits, out):
     nc = tc.nc
     with ExitStack() as ctx:
         const = ctx.enter_context(tc.tile_pool(name="const", bufs=1))
-        wide_pool = ctx.enter_context(tc.tile_pool(name="wide_pool", bufs=3))
-        raw_pool = ctx.enter_context(tc.tile_pool(name="raw_pool", bufs=STAGE))
-        inter_pool = ctx.enter_context(tc.tile_pool(name="inter_pool", bufs=1))
-        code_pool = ctx.enter_context(tc.tile_pool(name="code_pool", bufs=5))
-        small = ctx.enter_context(tc.tile_pool(name="small", bufs=2))
-        over = ctx.enter_context(tc.tile_pool(name="over", bufs=1))
-        acc_pool = ctx.enter_context(tc.psum_pool(name="acc_pool", bufs=4))
-        tr_pool = ctx.enter_context(tc.psum_pool(name="tr_pool", bufs=4))
+        arena = ctx.enter_context(tc.tile_pool(name="arena", bufs=1))
+        psum = ctx.enter_context(tc.psum_pool(name="psum", bufs=1))
 
         ident = const.tile([P, P], F32)
         ident16 = const.tile([P, P], BF16)
         perm16 = const.tile([P, P], BF16)
         scale_first = const.tile([P, 1, PACK], F32)
         scale_rest = const.tile([P, V_PASSES - 1, PACK], F32)
-        mix = const.tile([B, D], F32)
-        bias_sb = const.tile([B, D], BF16)
         c_sb = const.tile([P, E * U_PASSES, PACK], BF16)
         gate_sb = const.tile([B, E], BF16)
         share = const.tile([B, E], F32)
@@ -78,100 +85,177 @@ def tile_dcnv2lowrankexpertcross_w_kernel(tc, x0, x, v_bytes, v_scale, c, u, bia
         x_scales = const.tile([P, V_PASSES, B], U8, align_bytes=64)
         h_codes = const.tile([P, E, U_PASSES, B], U32, align_bytes=64)
         h_scales = const.tile([P, E, U_PASSES, B], U8, align_bytes=64)
-        u_turn = [over.tile([P, P, T_PITCH], BF16, offset=j * T_BYTES, name="u_turn%d" % j) for j in range(T_TILES)]
+        mix_rest = const.tile([B, CHUNKS, REST], F32)
+        bias_rest = const.tile([B, CHUNKS, REST], BF16)
+
+        made = []
+
+        def place(shape, dtype, offset, label):
+            made.append(label)
+            return arena.tile(shape, dtype, offset=offset, align_bytes=64, name="%s%d" % (label, len(made)))
+
+        free_banks = list(range(8))
+        free_stage = [AT_STAGE + j * SLOT for j in range(STAGE_SLOTS)] + [AT_TURN[1] + j * SLOT for j in range(4)]
+        free_grouped = [AT_GROUPED + j * SLOT for j in range(GROUPED_SLOTS)]
+        free_codes = [AT_CODES + j * CODE_BYTES for j in range(CODE_SLOTS)]
+        held = {}
+
+        def take(free, key, newest=False):
+            held[key] = (free, free.pop(-1 if newest else 0))
+            return held[key][1]
+
+        def give(key):
+            free, where = held.pop(key)
+            free.append(where)
+
+        def take_bank(key, shape, dtype):
+            return psum.tile(shape, dtype, name="bank%d" % take(free_banks, ("bank", key)))
 
         slabs = [(e, g) for e in range(E) for g in range(V_PASSES)]
         units = [("v", e, hb, g) for e, g in slabs for hb in range(RH)]
         n_v = len(units)
         units += [("u", 0, db, g) for db in range(2) for g in range(U_PASSES)]
-        n_0 = len(units)
-        units += [("u", 1, db, g) for db in range(DB) for g in range(U_PASSES)]
+        stacks = [(slice(0, CHUNKS), slice(PLAIN, PLAIN + SIDE)), (slice(2, 3), slice(0, PLAIN)),
+                  (slice(3, 4), slice(0, PLAIN // 2)), (slice(3, 4), slice(PLAIN // 2, PLAIN))]
+
+        def stack_width(j):
+            cs, ws = stacks[j]
+            return (cs.stop - cs.start) * (ws.stop - ws.start)
+
+        def stack_units(j):
+            return [("stack", 1, j, g) for g in range(0, U_PASSES, W // stack_width(j))]
+
+        units += stack_units(0) + [("u", 1, 0, g) for g in range(U_PASSES)]
+        units += stack_units(1) + stack_units(2) + stack_units(3)
         n = len(units)
-        raw, slab_raw, wide, inter, codes, accs, hid, pe_out, t_banks, late = {}, {}, {}, {}, {}, {}, {}, {}, {}, {}
+        long_steps = 2 * (len(slabs) - 2)
+        raw, slab_raw, wide, grouped, codes, accs, hid, eye_out, t_banks, turn_sb, late = {}, {}, {}, {}, {}, {}, {}, {}, {}, {}, {}
 
-        free_slots = list(range(INTER))
-        slot_of = {}
-
-        def take_grouped(key, shape, newest=False):
-            slot_of[key] = free_slots.pop(-1 if newest else 0)
-            inter[key] = inter_pool.tile(shape, BF16, align_bytes=64, name="grouped%d" % slot_of[key])
-            return inter[key]
-
-        def width(i):
-            return PLAIN * CH // 2 if i in range(n_v, n_0) else W
+        def chunks(ap):
+            return ap.rearrange("b (c w) -> b c w", c=CHUNKS)
 
         def load_slab(i, pieces):
             e, g = slabs[i]
-            v_raw = raw_pool.tile([P, PACK, R], U8, tag="stage")
-            slab_raw[i] = v_raw
+            slab_raw[i] = place([P, PACK, R], U8, take(free_stage, ("slab", i)), "v_raw")
             rows = v_bytes[e, g * K_PASS:(g + 1) * K_PASS, :].rearrange("(p t) w -> p t w", t=PACK)
             for ts, cs in pieces:
-                nc.sync.dma_start(out=v_raw[:, ts, cs], in_=rows[:, ts, cs])
+                nc.sync.dma_start(out=slab_raw[i][:, ts, cs], in_=rows[:, ts, cs])
 
         whole = [(slice(0, 2), slice(0, R)), (slice(2, 4), slice(0, R))]
-        long_steps = 2 * (len(slabs) - 2)
 
-        def load_u(i):
+        def load_unit(i):
             kind, e, blk, g = units[i]
-            u_raw = raw_pool.tile([P, PACK, width(i)], BF16, tag="stage")
-            rows = u[e, g * K_PASS:(g + 1) * K_PASS, :].rearrange("(p t) w -> p t w", t=PACK)
-            if e == 1:
-                nc.sync.dma_start(out=u_raw[:], in_=rows[:, :, blk * W:(blk + 1) * W])
+            where = take(free_stage, ("raw", i))
+            if kind == "u":
+                raw[i] = place([P, PACK, W], BF16, where, "u_raw")
+                rows = u[e, g * K_PASS:(g + 1) * K_PASS, :].rearrange("(p t) (c w) -> p t c w", t=PACK, c=CHUNKS)
+                for j in range(2):
+                    nc.sync.dma_start(out=raw[i][:, :, j * NB:(j + 1) * NB], in_=rows[:, :, 2 * blk + j, :PLAIN])
             else:
-                for t in range(PACK):
-                    nc.sync.dma_start(
-                        out=u_raw[:, t, :].rearrange("p (c w) -> p c w", c=CH // 2),
-                        in_=rows[:, t, :].rearrange("p (c w) -> p c w", c=CH)[:, 4 * blk:4 * blk + 4, :PLAIN])
-            raw[i] = u_raw
+                cs, ws = stacks[blk]
+                width = stack_width(blk)
+                raw[i] = place([P, W // width, PACK, width], BF16, where, "u_stack")
+                for j in range(W // width):
+                    ks = slice((g + j) * K_PASS, (g + j + 1) * K_PASS)
+                    if cs.stop - cs.start == CHUNKS:
+                        rows = u[e, ks, :].rearrange("(p t) (c w) -> p (t c) w", t=PACK, c=CHUNKS)[:, :, ws]
+                        dst = raw[i][:, j, :, :].rearrange("p t (c w) -> p (t c) w", c=CHUNKS)
+                    else:
+                        rows = u[e, ks, :].rearrange("(p t) (c w) -> p t c w", t=PACK, c=CHUNKS)[:, :, cs.start, ws]
+                        dst = raw[i][:, j, :, :]
+                    nc.sync.dma_start(out=dst, in_=rows)
 
-        def load_turn(j, g):
-            src = u[0, g * K_PASS:(g + 1) * K_PASS, :].rearrange("(p t) (c w) -> (t c) p w", t=PACK, c=CH)
-            first = PLAIN + j * T_COLS
-            nc.sync.dma_start(out=u_turn[j][g:P:U_PASSES, :, :T_COLS], in_=src[:, :, first:first + T_COLS])
+        def load_turn(e, r):
+            g, h = divmod(r, HALVES)
+            run = T_GROUPS[e] * T_GROUP
+            if e not in turn_sb:
+                turn_sb[e] = place([P, P, T_PITCH], BF16, AT_TURN[e], "u_turn")
+            src = u[e, g * K_PASS:(g + 1) * K_PASS, :].rearrange("(p t) (c w) -> (t c) p w", t=PACK, c=CHUNKS)
+            first = CW - (HALVES - h) * run
+            nc.sync.dma_start(out=turn_sb[e][r:P:U_PASSES * HALVES, :, :run], in_=src[:, :, first:first + run])
 
-        def turn(l):
-            b = l // T_BANK
+        turns = [(e, l) for e in range(E) for l in range(T_GROUPS[e] * T_GROUP)]
+
+        def turn(m):
+            e, l = turns[m]
+            b = m // T_BANK
             if b not in t_banks:
-                slots = tr_pool.tile([P, U_PASSES, T_BANK, CH * PACK], BF16)
-                t_banks[b] = slots
-            nc.tensor.transpose(t_banks[b][:, :, l % T_BANK, :], u_turn[l // T_COLS][:, :, l % T_COLS], perm16[:])
+                t_banks[b] = take_bank(("t", b), [P, U_PASSES, T_BANK, RUNS * PACK], BF16)
+            nc.tensor.transpose(t_banks[b][:, :, m % T_BANK, :], turn_sb[e][:, :, l], perm16[:])
 
         def empty_bank(b):
-            key = ("t", b // T_GROUP)
-            if key not in inter:
-                take_grouped(key, [P, W, PACK])
-            dst = inter[key][:].rearrange("p (g q w) t -> p g q (w t)", g=U_PASSES, q=T_GROUP)
+            per = T_GROUP // T_BANK
+            key = ("t", b // per)
+            if key not in grouped:
+                grouped[key] = place([P, W, PACK], BF16, take(free_grouped, ("grouped", key)), "grouped")
+            dst = grouped[key][:].rearrange("p (g q w) t -> p g q (w t)", g=U_PASSES, q=per)
             nc.scalar.copy(
-                out=dst[:, :, b % T_GROUP, :].bitcast(F32),
+                out=dst[:, :, b % per, :].bitcast(F32),
                 in_=t_banks.pop(b)[:].rearrange("p g l x -> p g (l x)").bitcast(F32))
+            give(("bank", ("t", b)))
 
-        def multiply_turned(q):
-            w_codes, w_scales = codes[("t", q)]
-            slots = tr_pool.tile([B, NB], F32)
-            nt = W // U_PASSES
+        def multiply_four(key, e):
+            w_codes, w_scales = codes.pop(key)
+            acc = take_bank(key, [B, NB], F32)
             for g in range(U_PASSES):
+                cs = slice(g * GROUP_COLS, (g + 1) * GROUP_COLS)
                 nc.tensor.matmul_mx(
-                    out=slots[:, :nt], lhsT=h_codes[:, 0, g, :].bitcast(FP8X4), lhsT_scale=h_scales[:, 0, g, :],
-                    rhs=w_codes[:, g * nt:(g + 1) * nt].bitcast(FP8X4), rhs_scale=w_scales[:, g * nt:(g + 1) * nt],
+                    out=acc[:, :GROUP_COLS], lhsT=h_codes[:, e, g, :].bitcast(FP8X4), lhsT_scale=h_scales[:, e, g, :],
+                    rhs=w_codes[:, cs].bitcast(FP8X4), rhs_scale=w_scales[:, cs],
                     start=(g == 0), stop=(g == U_PASSES - 1))
-            accs[("t", q)] = slots
+            accs[key] = acc
+            give(("codes", key))
 
-        def chunked(ap):
-            return ap.rearrange("b (c w) -> b c w", c=CH)
-
-        def mix_turned(q):
-            nl = T_BANK * T_GROUP
-            ls = slice(PLAIN + q * nl, PLAIN + (q + 1) * nl)
+        def mix_into(e, dst, acc, first):
             nc.vector.scalar_tensor_tensor(
-                out=chunked(mix[:])[:, :, ls],
-                in0=accs.pop(("t", q))[:, :nl * CH].rearrange("b (l c) -> b c l", c=CH),
-                scalar=share[:, 0:1], in1=chunked(bias_sb[:])[:, :, ls], op0=ALU.mult, op1=ALU.add)
+                out=dst, in0=acc, scalar=share[:, e:e + 1], in1=first if e == 0 else dst, op0=ALU.mult, op1=ALU.add)
+
+        def mix_group(q):
+            e, l = turns[q * T_GROUP]
+            run = T_GROUPS[e] * T_GROUP
+            acc = accs.pop(("t", q))[:, :GROUP_COLS]
+            if HALVES * run == REST:
+                view = "b c (h w) -> b (c h) w"
+                mix_into(e, mix_rest[:].rearrange(view, h=HALVES)[:, :, l:l + T_GROUP],
+                         acc.rearrange("b (l j) -> b j l", j=RUNS),
+                         bias_rest[:].rearrange(view, h=HALVES)[:, :, l:l + T_GROUP])
+            else:
+                for h in range(HALVES):
+                    first = REST - (HALVES - h) * run + l
+                    mix_into(e, mix_rest[:, :, first:first + T_GROUP],
+                             acc.rearrange("b (l c h) -> b h c l", c=CHUNKS, h=HALVES)[:, h, :, :],
+                             bias_rest[:, :, first:first + T_GROUP])
+            give(("bank", ("t", q)))
+
+        def mix_stack(j, lo, hi):
+            cs, ws = stacks[j]
+            acc = accs[("stack", j)][:, lo:hi]
+            if j == 0:
+                mix_into(1, mix_rest[:, :, :SIDE], chunks(acc), None)
+            else:
+                first = cs.start * PLAIN + ws.start
+                mix_into(1, late["mix"][:, first + lo:first + hi], acc, None)
+            if hi == stack_width(j):
+                give(("bank", ("stack", j)))
+
+        def multiply_stack(i, slots, opens, closes):
+            kind, e, j, first = units[i]
+            width = stack_width(j)
+            w_codes, w_scales = codes[i]
+            if opens:
+                accs[("stack", j)] = take_bank(("stack", j), [B, NB], F32)
+            for m in slots:
+                cs = slice(m * width, (m + 1) * width)
+                nc.tensor.matmul_mx(
+                    out=accs[("stack", j)][:, :width], lhsT=h_codes[:, e, first + m, :].bitcast(FP8X4),
+                    lhsT_scale=h_scales[:, e, first + m, :], rhs=w_codes[:, cs].bitcast(FP8X4),
+                    rhs_scale=w_scales[:, cs], start=(opens and m == slots[0]), stop=(closes and m == slots[-1]))
 
         def widen(i, t, lo, hi, on_act=False):
             g = slabs[i][1]
             if i not in wide:
-                v_wide = wide_pool.tile([P, RH, PACK, W] if i == 0 else [P, PACK, R], BF16)
-                wide[i] = v_wide
+                shape = [P, RH, PACK, W] if i == 0 else [P, PACK, R]
+                wide[i] = place(shape, BF16, AT_WIDE + i % WIDE_BUFS * WIDE_BYTES, "v_wide")
             src = slab_raw[i][:, t, lo:hi].bitcast(FP8)
             dst = wide[i][:, lo // W, t, :] if i == 0 else wide[i][:, t, lo:hi]
             scale = scale_first[:, 0, t:t + 1] if g == 0 else scale_rest[:, g - 1, t:t + 1]
@@ -179,6 +263,8 @@ def tile_dcnv2lowrankexpertcross_w_kernel(tc, x0, x, v_bytes, v_scale, c, u, bia
                 nc.scalar.activation(out=dst, in_=src, func=ACT.Copy, scale=scale)
             else:
                 nc.vector.tensor_scalar(out=dst, in0=src, scalar1=scale, scalar2=None, op0=ALU.mult)
+            if t == PACK - 1 and hi == R:
+                give(("slab", i))
 
         def interleave(copy, dst, src):
             copy(out=dst.rearrange("p (c i) t -> p c t i", i=2), in_=src.rearrange("p t (c i) -> p c t i", i=2))
@@ -188,108 +274,163 @@ def tile_dcnv2lowrankexpertcross_w_kernel(tc, x0, x, v_bytes, v_scale, c, u, bia
                 return raw[i][:]
             return wide[0][:, i, :, :] if i < RH else wide[i // RH][:, :, i % RH * W:(i % RH + 1) * W]
 
-        def uses_pe(i):
-            return i >= n_0 or i in range(3, 3 + PE_HEAD)
+        def tail_planes(i, cols):
+            if units[i][0] == "stack":
+                width = stack_width(units[i][2])
+                return raw[i][:, W // width - 1, :, width - cols:]
+            return planes(i)[:, :, W - cols:]
+
+        def eye_cols(i):
+            return EYE_COLS if i in EYE_UNITS else EYE_END if i == n - 1 else 0
 
         def vector_share(i):
-            if i >= n - 2:
+            if i == n - 2:
                 return SHARE_END
-            if i >= n_0:
-                return SHARE_PE
             if i >= long_steps + 2:
-                return SHARE_U
-            if i % RH == 0:
-                return 0
-            return SHARE_HEAD if i < 3 + PE_HEAD else SHARE_TURN
+                return SHARE_BUSY if i >= n - 2 * U_PASSES else SHARE_FREE
+            if i < RH:
+                return SHARE_BUSY
+            return SHARE_V if i % RH == 1 and i not in EYE_UNITS else 0
 
-        def arrange(i):
-            helped = i in inter
-            grouped = inter[i] if helped else take_grouped(i, [P, W, PACK])
-            on_pe = pe_out.pop(i, None)
+        def take_grouped(i, newest=False):
+            grouped[i] = place([P, W, PACK], BF16, take(free_grouped, ("grouped", i), newest), "grouped")
+            return grouped[i]
+
+        def stack_views(i):
+            depth = W // stack_width(units[i][2])
+            return (grouped[i][:].rearrange("p (g c i) t -> p g c t i", g=depth, i=2),
+                    raw[i][:].rearrange("p g t (c i) -> p g c t i", i=2), depth)
+
+        def arrange_stack(i):
+            helped = i in grouped
+            if not helped:
+                take_grouped(i)
+            dst, src, depth = stack_views(i)
+            a = vector_share(i) // (2 * depth)
+            if a > 0:
+                nc.vector.tensor_copy(out=dst[:, :, :a, :, :], in_=src[:, :, :a, :, :])
+            if helped:
+                b = (W // depth - POOL_COLS) // 2
+                nc.scalar.copy(out=dst[:, :depth - 1, a:, :, :], in_=src[:, :depth - 1, a:, :, :])
+                nc.scalar.copy(out=dst[:, depth - 1, a:b, :, :], in_=src[:, depth - 1, a:b, :, :])
+            else:
+                nc.scalar.copy(out=dst[:, :, a:, :, :], in_=src[:, :, a:, :, :])
+
+        def arrange_last(i):
+            take_grouped(i)
+            dst, src, depth = stack_views(i)
+            empty_eye(i)
+            nc.scalar.copy(out=dst[:, :2, :, :, :], in_=src[:, :2, :, :, :])
+            nc.scalar.copy(out=dst[:, 2, :, :, :], in_=src[:, 2, :, :, :])
+
+        def empty_eye(i):
+            for j, bank in enumerate(eye_out.pop(i, [])):
+                first = W - eye_cols(i) + j * 2 * P
+                nc.scalar.copy(
+                    out=grouped[i][:, first:first + 2 * P, :].rearrange("p w t -> p (w t)").bitcast(F32),
+                    in_=bank[:].bitcast(F32))
+                give(("bank", ("eye", i, j)))
+
+        def arrange_plain(i):
+            helped = i in grouped
+            dst = grouped[i] if helped else take_grouped(i)
             src = planes(i)
             a = vector_share(i)
-            b = (W if on_pe is None else W - U_PE) - (POOL_COLS if helped else 0)
-            b_pe = W - U_PE
-            if a > 0:
-                interleave(nc.vector.tensor_copy, grouped[:, :a, :], src[:, :, :a])
+            b = W - eye_cols(i) - (POOL_COLS if helped else 0)
+            if a > 0 and i > 0:
+                interleave(nc.vector.tensor_copy, dst[:, :a, :], src[:, :, :a])
+            interleave(nc.scalar.copy, dst[:, a:b, :], src[:, :, a:b])
+            empty_eye(i)
+
+        def arrange(i):
             if i == n - 1:
-                interleave(nc.scalar.copy, grouped[:, a:NB, :], src[:, :, a:NB])
-                a = NB
-            if on_pe is not None:
-                nc.scalar.copy(out=grouped[:, b_pe:, :].rearrange("p w t -> p (w t)").bitcast(F32), in_=on_pe[:].bitcast(F32))
-            interleave(nc.scalar.copy, grouped[:, a:b, :], src[:, :, a:b])
+                arrange_last(i)
+            elif units[i][0] == "stack":
+                arrange_stack(i)
+            else:
+                arrange_plain(i)
+            if i >= n_v:
+                give(("raw", i))
+            elif i % RH == RH - 1 and i // RH >= len(slabs) - WIDE_BUFS:
+                at_wide = AT_WIDE + i // RH % WIDE_BUFS * WIDE_BYTES
+                free_stage.extend([at_wide, at_wide + SLOT])
 
         def pool_copy(out, in_):
             nc.gpsimd.tensor_scalar(out=out, in0=in_, scalar1=1.0, scalar2=0.0, op0=ALU.mult, op1=ALU.add)
 
         def pool_interleave(i):
-            grouped = take_grouped(i, [P, W, PACK], newest=True)
-            hi = W - U_PE if uses_pe(i) else W
-            interleave(pool_copy, grouped[:, hi - POOL_COLS:hi, :], planes(i)[:, :, hi - POOL_COLS:hi])
+            dst = take_grouped(i, newest=True)
+            hi = W - eye_cols(i)
+            src = tail_planes(i, W - hi + POOL_COLS)[:, :, :POOL_COLS]
+            interleave(pool_copy, dst[:, hi - POOL_COLS:hi, :], src)
 
-        def pe_interleave(i):
-            if not uses_pe(i):
-                return
-            slots = tr_pool.tile([P, U_PE * PACK], BF16)
-            src = planes(i)
-            for j in range(U_PE // P):
-                cs = slice(W - U_PE + j * P, W - U_PE + (j + 1) * P)
-                nc.tensor.matmul(
-                    out=slots[:, j * NB:(j + 1) * NB], lhsT=ident16[:],
-                    rhs=src[:, :, cs].rearrange("p t w -> p w t"), start=True, stop=True)
-            pe_out[i] = slots
+        def eye_interleave(i):
+            src = tail_planes(i, eye_cols(i))
+            eye_out[i] = []
+            for j in range(eye_cols(i) // (2 * P)):
+                bank = take_bank(("eye", i, j), [P, 2 * NB], BF16)
+                for m in range(2):
+                    first = (2 * j + m) * P
+                    nc.tensor.matmul(
+                        out=bank[:, m * NB:(m + 1) * NB], lhsT=ident16[:],
+                        rhs=src[:, :, first:first + P].rearrange("p t w -> p w t"), start=True, stop=True)
+                eye_out[i].append(bank)
 
-        def quantize(i, lo, hi):
-            if i not in codes:
-                w_codes = code_pool.tile([P, W], U32, align_bytes=64)
-                w_scales = code_pool.tile([P, W], U8, align_bytes=64)
-                codes[i] = (w_codes, w_scales)
-            w_codes, w_scales = codes[i]
+        def quantize(key, lo, hi):
+            if key not in codes:
+                where = take(free_codes, ("codes", key))
+                codes[key] = (place([P, W], U32, where, "w_codes"), place([P, W], U8, where + 4 * W, "w_scales"))
+            w_codes, w_scales = codes[key]
             nc.vector.quantize_mx(
                 out=w_codes[:, lo:hi].bitcast(FP8X4), scales=w_scales[:, lo:hi],
-                in_=inter[i][:, lo:hi, :].rearrange("p w t -> p (w t)"))
+                in_=grouped[key][:, lo:hi, :].rearrange("p w t -> p (w t)"))
             if hi == W:
-                free_slots.append(slot_of.pop(i))
+                give(("grouped", key))
 
         def multiply(i, which=range(W // NB)):
             kind, e, blk, g = units[i]
             w_codes, w_scales = codes[i]
             last = (V_PASSES if kind == "v" else U_PASSES) - 1
-            if g == 0:
-                accs[(kind, e, blk)] = [acc_pool.tile([B, NB], F32, name="acc") for j in range(W // NB)]
-            banks = accs[(kind, e, blk)]
             for j in which:
-                js = slice(j * NB, min((j + 1) * NB, width(i)))
+                key = (kind, e, blk, j)
+                if g == 0:
+                    accs[key] = take_bank(key, [B, NB], F32)
+                js = slice(j * NB, (j + 1) * NB)
                 lhs = x_codes[:, g, :] if kind == "v" else h_codes[:, e, g, :]
                 lhs_scale = x_scales[:, g, :] if kind == "v" else h_scales[:, e, g, :]
                 nc.tensor.matmul_mx(
-                    out=banks[j][:, :js.stop - js.start], lhsT=lhs.bitcast(FP8X4), lhsT_scale=lhs_scale,
+                    out=accs[key][:], lhsT=lhs.bitcast(FP8X4), lhsT_scale=lhs_scale,
                     rhs=w_codes[:, js].bitcast(FP8X4), rhs_scale=w_scales[:, js],
                     start=(g == 0), stop=(g == last))
+                if j == W // NB - 1:
+                    give(("codes", i))
 
         def hidden_tanh(e, hb):
             hid[(e, hb)] = []
-            for acc in accs.pop(("v", e, hb)):
-                th = small.tile([B, PACK, P], F32, bufs=4)
+            for j in range(W // NB):
+                th = place([B, PACK, P], F32, AT_TANH + (2 * hb + j) * TANH_BYTES, "th")
+                acc = accs.pop(("v", e, hb, j))
                 nc.scalar.activation(out=th[:], in_=acc[:].rearrange("b (p t) -> b t p", t=PACK), func=ACT.Tanh)
+                give(("bank", ("v", e, hb, j)))
                 hid[(e, hb)].append(th)
 
         def hidden_turn(e, hb):
             turned = []
-            for th in hid[(e, hb)]:
-                slots = tr_pool.tile([P, PACK, B], F32)
+            for j, th in enumerate(hid[(e, hb)]):
+                bank = take_bank(("h", hb, j), [P, PACK, B], F32)
                 for t in range(PACK):
-                    nc.tensor.transpose(slots[:, t, :], th[:, t, :], ident[:])
-                turned.append(slots)
+                    nc.tensor.transpose(bank[:, t, :], th[:, t, :], ident[:])
+                turned.append(bank)
             hid[(e, hb)] = turned
 
         def hidden_scale(e, hb):
-            hg = small.tile([P, W // NB, B, PACK], BF16, align_bytes=64)
-            for j, slots in enumerate(hid[(e, hb)]):
+            hg = place([P, W // NB, B, PACK], BF16, AT_TANH + (4 + hb) * TANH_BYTES, "hg")
+            for j, bank in enumerate(hid[(e, hb)]):
                 g = e * U_PASSES + hb * (W // NB) + j
                 nc.vector.tensor_tensor(
-                    out=hg[:, j, :, :], in0=slots[:].rearrange("p t b -> p b t"),
+                    out=hg[:, j, :, :], in0=bank[:].rearrange("p t b -> p b t"),
                     in1=c_sb[:, g:g + 1, :].to_broadcast([P, B, PACK]), op=ALU.mult)
+                give(("bank", ("h", hb, j)))
             hid[(e, hb)] = hg
 
         def hidden_quantize(e, hb):
@@ -299,32 +440,46 @@ def tile_dcnv2lowrankexpertcross_w_kernel(tc, x0, x, v_bytes, v_scale, c, u, bia
                 scales=h_scales[:, e, gs, :].rearrange("p g b -> p (g b)"),
                 in_=hid.pop((e, hb))[:].rearrange("p g b t -> p (g b t)"))
 
-        def mix_first(db, j):
-            cs = slice(4 * db + 2 * j, 4 * db + 2 * j + 2)
-            ws = slice(0, PLAIN)
-            nc.vector.scalar_tensor_tensor(
-                out=chunked(mix[:])[:, cs, ws],
-                in0=accs[("u", 0, db)][j][:].rearrange("b (c w) -> b c w", c=2),
-                scalar=share[:, 0:1], in1=chunked(bias_sb[:])[:, cs, ws], op0=ALU.mult, op1=ALU.add)
+        def load_late():
+            at = AT_TURN[0]
+            late["mix"] = place([B, CHUNKS * PLAIN], F32, at, "mix_plain")
+            at += CHUNKS * PLAIN * 4
+            late["bias"] = place([B, CHUNKS, PLAIN], BF16, at, "bias_plain")
+            at += CHUNKS * PLAIN * 2
+            nc.sync.dma_start(
+                out=late["bias"][:], in_=bias.rearrange("(c w) -> c w", c=CHUNKS)[:, :PLAIN].partition_broadcast(P))
+            free_stage.extend(range(at, AT_TURN[0] + T_BYTES, SLOT))
 
-        def mix_second(db, j, lo=0, hi=NB):
-            cs = slice(db * W + j * NB + lo, db * W + j * NB + hi)
-            nc.vector.scalar_tensor_tensor(
-                out=mix[:, cs], in0=accs[("u", 1, db)][j][:, lo:hi], scalar=share[:, 1:2], in1=mix[:, cs],
-                op0=ALU.mult, op1=ALU.add)
+        def load_rows(label, src):
+            late[label] = place([B, D], BF16, take(free_stage, label), label)
+            nc.sync.dma_start(out=late[label][:], in_=src)
 
-        def cross(lo, hi):
-            nc.vector.tensor_tensor(out=mix[:, lo:hi], in0=mix[:, lo:hi], in1=late["x0"][:, lo:hi], op=ALU.mult)
+        def mix_plain(e, db, j, lo=0, hi=NB):
+            ch = 2 * db + j
+            mix_into(e, late["mix"][:, ch * NB + lo:ch * NB + hi], accs[("u", e, db, j)][:, lo:hi],
+                     late["bias"][:, ch, lo:hi])
+            if hi == NB:
+                give(("bank", ("u", e, db, j)))
 
-        def finish(lo, hi):
-            nc.vector.tensor_tensor(out=mix[:, lo:hi], in0=mix[:, lo:hi], in1=late["x"][:, lo:hi], op=ALU.add)
-            nc.sync.dma_start(out=out[:, lo:hi], in_=mix[:, lo:hi])
+        def views(part, cs, ws):
+            mixed = chunks(late["mix"][:]) if part == "plain" else mix_rest[:]
+            shift = 0 if part == "plain" else PLAIN
+            return mixed[:, cs, ws], slice(shift + ws.start, shift + ws.stop)
+
+        def cross(part, cs, ws):
+            mixed, ds = views(part, cs, ws)
+            nc.vector.tensor_tensor(out=mixed, in0=mixed, in1=chunks(late["x0"][:])[:, cs, ds], op=ALU.mult)
+
+        def finish(part, cs, ws):
+            mixed, ds = views(part, cs, ws)
+            nc.vector.tensor_tensor(out=mixed, in0=mixed, in1=chunks(late["x"][:])[:, cs, ds], op=ALU.add)
+            nc.sync.dma_start(out=chunks(out)[:, cs, ds], in_=mixed)
 
         make_identity(nc, ident[:])
         nc.vector.tensor_copy(out=ident16[:], in_=ident[:])
         nc.vector.tensor_copy(
-            out=perm16[:].rearrange("q (g c t) -> q g c t", g=U_PASSES, c=CH),
-            in_=ident[:].rearrange("q (t c g) -> q g c t", g=U_PASSES, c=CH))
+            out=perm16[:].rearrange("q (g c h t) -> q g c h t", g=U_PASSES, c=CHUNKS, h=HALVES),
+            in_=ident[:].rearrange("q (t c g h) -> q g c h t", g=U_PASSES, c=CHUNKS, h=HALVES))
         with tc.manual_schedule():
             scales = v_scale.rearrange("o (g p t) u -> p (o g) (t u)", p=P, t=PACK)
             nc.scalar.dma_start(out=scale_first[:], in_=scales[:, :1, :])
@@ -332,11 +487,12 @@ def tile_dcnv2lowrankexpertcross_w_kernel(tc, x0, x, v_bytes, v_scale, c, u, bia
             load_slab(0, [(ts, slice(hb * W, (hb + 1) * W)) for hb in range(RH) for ts, cs in whole])
             nc.sync.dma_start(out=scale_rest[:], in_=scales[:, 1:, :])
             load_slab(1, whole)
-            x_early = raw_pool.tile([B, D], BF16, tag="stage")
+            x_early = place([B, D], BF16, take(free_stage, "x"), "x_early")
             nc.sync.dma_start(out=x_early[:], in_=x)
-            for g in range(2):
+            for g in range(U_PASSES):
                 load_slab(2 + g, whole)
-                load_turn(0, g)
+                for h in range(HALVES):
+                    load_turn(0, HALVES * g + h)
 
             for e in range(E):
                 nc.scalar.activation(
@@ -347,25 +503,25 @@ def tile_dcnv2lowrankexpertcross_w_kernel(tc, x0, x, v_bytes, v_scale, c, u, bia
             arrange(0)
             for t in range(PACK):
                 widen(0, t, W, R)
+            interleave(nc.vector.tensor_copy, grouped[0][:, :vector_share(0), :], planes(0)[:, :, :vector_share(0)])
+            eye_interleave(1)
+            arrange(1)
             for t in range(PACK):
                 widen(1, t, 0, R)
-            for g in range(2, U_PASSES):
-                load_slab(2 + g, whole)
-                load_turn(0, g)
-            load_slab(6, whole)
-            nc.sync.dma_start(out=c_sb[:], in_=c.rearrange("e (g p t) -> p (e g) t", p=P, t=PACK))
             x_words = x_early[:].bitcast(F32)
-            x_grouped = take_grouped("x", [P, V_PASSES * B * PACK])
+            x_grouped = place([P, V_PASSES * B * PACK], BF16, take(free_grouped, "x_grouped"), "x_grouped")
             for q in range(V_PASSES // 2):
-                slots = tr_pool.tile([P, 4, B], F32)
+                bank = take_bank(("x", q), [P, 4, B], F32)
                 for j in range(2):
                     for w in range(2):
                         first = 256 * (2 * q + j)
-                        nc.tensor.transpose(slots[:, 2 * j + w, :], x_words[:, first + w:first + 256:2], ident[:])
+                        nc.tensor.transpose(bank[:, 2 * j + w, :], x_words[:, first + w:first + 256:2], ident[:])
                 nc.scalar.copy(
                     out=x_grouped[:, q * W:(q + 1) * W].bitcast(F32).rearrange("p (j r w) -> p j r w", j=2, w=2),
-                    in_=slots[:].rearrange("p (j w) r -> p j r w", w=2))
-            arrange(1)
+                    in_=bank[:].rearrange("p (j w) r -> p j r w", w=2))
+                give(("bank", ("x", q)))
+            give("x")
+            eye_interleave(2)
 
             def quantize_x():
                 for lo, hi in ((0, 4), (4, 6)):
@@ -373,104 +529,135 @@ def tile_dcnv2lowrankexpertcross_w_kernel(tc, x0, x, v_bytes, v_scale, c, u, bia
                         out=x_codes[:, lo:hi, :].rearrange("p g b -> p (g b)").bitcast(FP8X4),
                         scales=x_scales[:, lo:hi, :].rearrange("p g b -> p (g b)"),
                         in_=x_grouped[:, lo * K_PASS:hi * K_PASS])
-                free_slots.append(slot_of.pop("x"))
+                give("x_grouped")
 
-            later = {}
-            early = {}
-            from_psum = {}
+            later, early, from_psum, before_mx = {}, {}, {}, {}
 
-            def at(step, fn, *args):
-                later.setdefault(step, []).append((fn, args))
+            def at(table, step, fn, *args):
+                table.setdefault(step, []).append((fn, args))
 
-            at(0, quantize_x)
-            stream = [(load_slab, (i, whole), 2 * i - 3) for i in range(7, len(slabs))]
-            stream += [(load_u, (i,), i - 2) for i in range(n_v, n)]
-            frees = [-1, 1, 3, 5, 7, 9] + [f for fn, args, f in stream]
-            issued = [0]
-            turned = [0]
-            full = []
-            hidden_steps = [i + 3 for i in range(n_v) if units[i][3] == V_PASSES - 1]
-            for s in range(n - 1):
-                while issued[0] < len(stream) and frees[issued[0]] < s:
-                    fn, args, f = stream[issued[0]]
+            def run(table, step):
+                for fn, args in table.pop(step, []):
                     fn(*args)
-                    if issued[0] < U_PASSES * (T_TILES - 1):
-                        load_turn(1 + issued[0] // U_PASSES, issued[0] % U_PASSES)
-                    issued[0] += 1
-                if s == T_FIRST:
-                    nc.sync.dma_start(out=bias_sb[:], in_=bias.partition_broadcast(P))
-                if s == n_0:
-                    x0_sb = over.tile([B, D], BF16, offset=0)
-                    nc.sync.dma_start(out=x0_sb[:], in_=x0)
-                    x_sb = over.tile([B, D], BF16, offset=2 * D)
-                    nc.sync.dma_start(out=x_sb[:], in_=x)
-                    late["x0"], late["x"] = x0_sb, x_sb
+
+            at(later, 0, quantize_x)
+            borrowed = range(AT_TURN[1], AT_TURN[1] + T_BYTES)
+            stream = [(load_slab, (i, whole)) for i in range(6, len(slabs))] + [(load_unit, (i,)) for i in range(n_v, n)]
+            stream[-2:-2] = [(load_rows, ("x0", x0))]
+            stream.append((load_rows, ("x", x)))
+            h_ready = [i + 5 for i in range(n_v) if units[i][3] == V_PASSES - 1 and units[i][2] == RH - 1]
+            hidden_steps = [i + 3 for i in range(n_v) if units[i][3] == V_PASSES - 1]
+            second_from = 2 * (2 + U_PASSES) - 4
+            turned, full, waiting = [0], [], []
+            rest_last = [0]
+            rest_left = [T_GROUPS[1] + 1]
+
+            def rest_done(step):
+                rest_left[0] -= 1
+                rest_last[0] = step = max(step, rest_last[0])
+                if rest_left[0] == 0:
+                    at(later, step + 1, cross, "rest", slice(0, CHUNKS), slice(0, REST))
+                    at(later, step + 2, finish, "rest", slice(0, CHUNKS), slice(0, REST))
+
+            for s in range(n - 1):
+                for where in [w for w in free_stage if w in borrowed]:
+                    free_stage.remove(where)
+                while stream and free_stage:
+                    fn, args = stream.pop(0)
+                    fn(*args)
+                if s == 0:
+                    nc.sync.dma_start(out=c_sb[:], in_=c.rearrange("e (g p t) -> p (e g) t", p=P, t=PACK))
+                    nc.sync.dma_start(
+                        out=bias_rest[:],
+                        in_=bias.rearrange("(c w) -> c w", c=CHUNKS)[:, PLAIN:].partition_broadcast(P))
+                if s in range(second_from, second_from + U_PASSES * HALVES):
+                    load_turn(1, s - second_from)
+                if "mix" not in late and turned[0] >= T_GROUPS[0] * T_GROUP:
+                    load_late()
                 if s < long_steps:
                     for t in (2 * (s % 2), 2 * (s % 2) + 1):
                         widen(s // 2 + 2, t, 0, R)
                 ready = full[:]
                 full.clear()
-                for fn, args in early.pop(s, []):
-                    fn(*args)
+                run(early, s)
+                opens = 0 if units[s][3] > 0 else 1 if units[s][0] == "stack" else 2
                 if s >= T_FIRST:
-                    for l in range(turned[0], min(TL, turned[0] + (T_LONG if s < long_steps else T_SHORT))):
-                        turn(l)
+                    quota = (T_LONG if s < long_steps else T_SHORT) - (T_HIDDEN if s in hidden_steps else 0)
+                    needed = opens + (2 if s + 1 in hidden_steps else 0)
+                    for m in range(turned[0], min(len(turns), turned[0] + quota)):
+                        if m % T_BANK == 0 and min(len(free_banks), len(free_banks) + len(ready) - needed) < 1:
+                            break
+                        turn(m)
                         turned[0] += 1
-                        if l % T_BANK == T_BANK - 1:
-                            full.append(l // T_BANK)
+                        if m % T_BANK == T_BANK - 1:
+                            full.append(m // T_BANK)
                 if s + 2 < n:
                     arrange(s + 2)
                 for b in ready:
                     empty_bank(b)
-                    if b % T_GROUP == T_GROUP - 1:
-                        q = b // T_GROUP
-                        done = max(s + 2, n_v // 2 + 4 + 2 * q)
-                        while done + 1 in hidden_steps:
-                            done += 1
-                        at(s + 1, quantize, ("t", q), 0, W)
-                        at(done, multiply_turned, q)
-                        at(done + 1, mix_turned, q)
+                    if b % (T_GROUP // T_BANK) == T_GROUP // T_BANK - 1:
+                        q = b // (T_GROUP // T_BANK)
+                        at(later, s + 1, quantize, ("t", q), 0, W)
+                        waiting.append((s + 2, ("t", q), turns[q * T_GROUP][0]))
                 if s + 3 < n:
-                    pe_interleave(s + 3)
-                last_of_step = s == n - 2 or s in from_psum
+                    eye_interleave(s + 3)
+                last_of_step = s in from_psum
                 if not last_of_step:
                     quantize(s, 0, W)
-                for fn, args in later.pop(s, []):
-                    fn(*args)
+                run(later, s)
                 if last_of_step:
                     quantize(s, 0, W)
                 if s in from_psum:
                     if s + 3 < n:
                         pool_interleave(s + 3)
-                    for fn, args in from_psum.pop(s):
-                        fn(*args)
-                multiply(s)
+                    run(from_psum, s)
+                while waiting and waiting[0][0] <= s and h_ready[waiting[0][2]] <= s and s + 1 not in hidden_steps and len(free_banks) > opens:
+                    step, key, owner = waiting.pop(0)
+                    multiply_four(key, owner)
+                    mixed = s + (1 if turned[0] == len(turns) else 2)
+                    at(later, mixed, mix_group, key[1])
+                    if owner == 1:
+                        rest_done(mixed)
                 kind, e, blk, g = units[s]
+                if kind == "stack":
+                    depth = W // stack_width(blk)
+                    multiply_stack(s, range(depth), g == 0, g + depth == U_PASSES)
+                    give(("codes", s))
+                    if g + depth == U_PASSES and blk == 0:
+                        at(later, s + 2, mix_stack, blk, 0, stack_width(blk))
+                        rest_done(s + 2)
+                    elif g + depth == U_PASSES:
+                        at(later, s + 1, mix_stack, blk, 0, stack_width(blk))
+                        at(later, s + 2, cross, "plain", *stacks[blk])
+                        at(later, s + 3, finish, "plain", *stacks[blk])
+                else:
+                    multiply(s)
                 if kind == "v" and g == V_PASSES - 1:
-                    at(s + 1, hidden_tanh, e, blk)
-                    early[s + 3] = [(hidden_turn, (e, blk))]
-                    from_psum[s + 3] = [(hidden_scale, (e, blk))]
-                    at(s + 4, hidden_quantize, e, blk)
+                    at(later, s + 1, hidden_tanh, e, blk)
+                    at(early, s + 3, hidden_turn, e, blk)
+                    at(from_psum, s + 3, hidden_scale, e, blk)
+                    at(later, s + 4, hidden_quantize, e, blk)
                 if kind == "u" and g == U_PASSES - 1:
-                    mixer = (mix_first, mix_second)[e]
-                    from_psum[s + 2] = [(mixer, (blk, j)) for j in range(W // NB)]
+                    for j in range(W // NB):
+                        at(from_psum, s + 3 - 2 * e, mix_plain, e, blk, j)
                     if e == 1:
-                        at(s + 3, cross, blk * W, (blk + 1) * W)
-                        at(s + 4, finish, blk * W, (blk + 1) * W)
-            first, second = [((DB - 1) * W + j * NB, (DB - 1) * W + (j + 1) * NB) for j in range(W // NB)]
+                        at(later, s + 2, cross, "plain", slice(0, 2), slice(0, PLAIN))
+                        at(later, s + 3, finish, "plain", slice(0, 2), slice(0, PLAIN))
+            assert not waiting and turned[0] == len(turns) and not full
             quantize(n - 1, 0, NB)
-            multiply(n - 1, [0])
-            for fn, args in later.pop(n - 1):
-                fn(*args)
-            mix_second(DB - 1, 0)
-            quantize(n - 1, NB, W)
-            multiply(n - 1, [1])
-            cross(*first)
-            finish(*first)
-            quarters = [(0, NB // 2), (NB // 2, NB)]
-            for lo, hi in quarters:
-                mix_second(DB - 1, 1, lo, hi)
-            for lo, hi in quarters:
-                cross(second[0] + lo, second[0] + hi)
-            for lo, hi in quarters:
-                finish(second[0] + lo, second[0] + hi)
+            quantize(n - 1, W - EYE_END, W)
+            multiply_stack(n - 1, [0, 1, 3], True, False)
+            run(later, n - 1)
+            quantize(n - 1, NB, W - EYE_END)
+            multiply_stack(n - 1, [2], False, True)
+            run(later, n)
+            run(later, n + 1)
+            last = len(stacks) - 1
+            halves = [(0, P), (P, 2 * P)]
+            for lo, hi in halves:
+                mix_stack(last, lo, hi)
+            for lo, hi in halves:
+                cross("plain", stacks[last][0], slice(stacks[last][1].start + lo, stacks[last][1].start + hi))
+            for lo, hi in halves:
+                finish("plain", stacks[last][0], slice(stacks[last][1].start + lo, stacks[last][1].start + hi))
+            assert not later and not early and not from_psum

@@ -23,30 +23,31 @@ NB = 512
 V_PASSES = D // K_PASS
 U_PASSES = R // K_PASS
 RH = R // W
-CHUNKS = 4
+CHUNKS = 8
 CW = D // CHUNKS
-PLAIN = NB
+PLAIN = 256
 REST = CW - PLAIN
-HALVES = 2
-RUNS = CHUNKS * HALVES
 T_BANK = 8
 T_GROUP = 32
 T_PITCH = 144
-GROUP_COLS = RUNS * T_GROUP
-T_GROUPS = (4, 2)
-SIDE = REST - HALVES * T_GROUPS[1] * T_GROUP
+GROUP_COLS = CHUNKS * T_GROUP
+T_GROUPS = (4, 4)
+SIDE = REST - T_GROUPS[1] * T_GROUP
+MX_BATCH = 4
 
 EYE_UNITS = range(1, 10)
 EYE_COLS = 512
 EYE_END = 256
 T_FIRST = 7
-T_LONG = 10
-T_SHORT = 6
+T_LONG = 16
+T_SHORT = 11
 T_HIDDEN = 2
-SHARE_V = 352
-SHARE_BUSY = 288
+T_AFTER = 0
+LAG = 1
+SHARE_V = 416
+SHARE_HEAD = 192
 SHARE_FREE = 464
-SHARE_END = 128
+SHARE_END = 0
 POOL_COLS = 104
 
 SLOT = PACK * W * 2
@@ -55,7 +56,7 @@ WIDE_BYTES = PACK * R * 2
 WIDE_BUFS = 3
 STAGE_SLOTS = 3
 GROUPED_SLOTS = 5
-CODE_SLOTS = 5
+CODE_SLOTS = 7
 CODE_BYTES = 5 * W
 TANH_BYTES = NB * 4
 AT_TURN = (0, T_BYTES)
@@ -85,8 +86,6 @@ def tile_dcnv2lowrankexpertcross_w_kernel(tc, x0, x, v_bytes, v_scale, c, u, bia
         x_scales = const.tile([P, V_PASSES, B], U8, align_bytes=64)
         h_codes = const.tile([P, E, U_PASSES, B], U32, align_bytes=64)
         h_scales = const.tile([P, E, U_PASSES, B], U8, align_bytes=64)
-        mix_rest = const.tile([B, CHUNKS, REST], F32)
-        bias_rest = const.tile([B, CHUNKS, REST], BF16)
 
         made = []
 
@@ -115,8 +114,8 @@ def tile_dcnv2lowrankexpertcross_w_kernel(tc, x0, x, v_bytes, v_scale, c, u, bia
         units = [("v", e, hb, g) for e, g in slabs for hb in range(RH)]
         n_v = len(units)
         units += [("u", 0, db, g) for db in range(2) for g in range(U_PASSES)]
-        stacks = [(slice(0, CHUNKS), slice(PLAIN, PLAIN + SIDE)), (slice(2, 3), slice(0, PLAIN)),
-                  (slice(3, 4), slice(0, PLAIN // 2)), (slice(3, 4), slice(PLAIN // 2, PLAIN))]
+        stacks = [(slice(0, CHUNKS), slice(PLAIN, PLAIN + SIDE)), (slice(4, 6), slice(0, PLAIN)),
+                  (slice(6, 7), slice(0, PLAIN)), (slice(7, 8), slice(0, PLAIN))]
 
         def stack_width(j):
             cs, ws = stacks[j]
@@ -125,7 +124,7 @@ def tile_dcnv2lowrankexpertcross_w_kernel(tc, x0, x, v_bytes, v_scale, c, u, bia
         def stack_units(j):
             return [("stack", 1, j, g) for g in range(0, U_PASSES, W // stack_width(j))]
 
-        units += stack_units(0) + [("u", 1, 0, g) for g in range(U_PASSES)]
+        units += (stack_units(0) if SIDE else []) + [("u", 1, 0, g) for g in range(U_PASSES)]
         units += stack_units(1) + stack_units(2) + stack_units(3)
         n = len(units)
         long_steps = 2 * (len(slabs) - 2)
@@ -149,8 +148,9 @@ def tile_dcnv2lowrankexpertcross_w_kernel(tc, x0, x, v_bytes, v_scale, c, u, bia
             if kind == "u":
                 raw[i] = place([P, PACK, W], BF16, where, "u_raw")
                 rows = u[e, g * K_PASS:(g + 1) * K_PASS, :].rearrange("(p t) (c w) -> p t c w", t=PACK, c=CHUNKS)
-                for j in range(2):
-                    nc.sync.dma_start(out=raw[i][:, :, j * NB:(j + 1) * NB], in_=rows[:, :, 2 * blk + j, :PLAIN])
+                for j in range(W // PLAIN):
+                    nc.sync.dma_start(
+                        out=raw[i][:, :, j * PLAIN:(j + 1) * PLAIN], in_=rows[:, :, W // PLAIN * blk + j, :PLAIN])
             else:
                 cs, ws = stacks[blk]
                 width = stack_width(blk)
@@ -159,20 +159,22 @@ def tile_dcnv2lowrankexpertcross_w_kernel(tc, x0, x, v_bytes, v_scale, c, u, bia
                     ks = slice((g + j) * K_PASS, (g + j + 1) * K_PASS)
                     if cs.stop - cs.start == CHUNKS:
                         rows = u[e, ks, :].rearrange("(p t) (c w) -> p (t c) w", t=PACK, c=CHUNKS)[:, :, ws]
-                        dst = raw[i][:, j, :, :].rearrange("p t (c w) -> p (t c) w", c=CHUNKS)
+                        nc.sync.dma_start(
+                            out=raw[i][:, j, :, :].rearrange("p t (c w) -> p (t c) w", c=CHUNKS), in_=rows)
                     else:
-                        rows = u[e, ks, :].rearrange("(p t) (c w) -> p t c w", t=PACK, c=CHUNKS)[:, :, cs.start, ws]
-                        dst = raw[i][:, j, :, :]
-                    nc.sync.dma_start(out=dst, in_=rows)
+                        rows = u[e, ks, :].rearrange("(p t) (c w) -> p t c w", t=PACK, c=CHUNKS)
+                        for ch in range(cs.start, cs.stop):
+                            first = (ch - cs.start) * PLAIN
+                            nc.sync.dma_start(out=raw[i][:, j, :, first:first + PLAIN], in_=rows[:, :, ch, ws])
 
         def load_turn(e, r):
-            g, h = divmod(r, HALVES)
+            g, h = divmod(r, 2)
             run = T_GROUPS[e] * T_GROUP
             if e not in turn_sb:
                 turn_sb[e] = place([P, P, T_PITCH], BF16, AT_TURN[e], "u_turn")
             src = u[e, g * K_PASS:(g + 1) * K_PASS, :].rearrange("(p t) (c w) -> (t c) p w", t=PACK, c=CHUNKS)
-            first = CW - (HALVES - h) * run
-            nc.sync.dma_start(out=turn_sb[e][r:P:U_PASSES * HALVES, :, :run], in_=src[:, :, first:first + run])
+            ps = slice(h * P // 2, (h + 1) * P // 2)
+            nc.sync.dma_start(out=turn_sb[e][g:P:U_PASSES, ps, :run], in_=src[:, ps, CW - run:])
 
         turns = [(e, l) for e in range(E) for l in range(T_GROUPS[e] * T_GROUP)]
 
@@ -180,7 +182,7 @@ def tile_dcnv2lowrankexpertcross_w_kernel(tc, x0, x, v_bytes, v_scale, c, u, bia
             e, l = turns[m]
             b = m // T_BANK
             if b not in t_banks:
-                t_banks[b] = take_bank(("t", b), [P, U_PASSES, T_BANK, RUNS * PACK], BF16)
+                t_banks[b] = take_bank(("t", b), [P, U_PASSES, T_BANK, CHUNKS * PACK], BF16)
             nc.tensor.transpose(t_banks[b][:, :, m % T_BANK, :], turn_sb[e][:, :, l], perm16[:])
 
         def empty_bank(b):
@@ -194,47 +196,37 @@ def tile_dcnv2lowrankexpertcross_w_kernel(tc, x0, x, v_bytes, v_scale, c, u, bia
                 in_=t_banks.pop(b)[:].rearrange("p g l x -> p g (l x)").bitcast(F32))
             give(("bank", ("t", b)))
 
-        def multiply_four(key, e):
-            w_codes, w_scales = codes.pop(key)
-            acc = take_bank(key, [B, NB], F32)
-            for g in range(U_PASSES):
-                cs = slice(g * GROUP_COLS, (g + 1) * GROUP_COLS)
-                nc.tensor.matmul_mx(
-                    out=acc[:, :GROUP_COLS], lhsT=h_codes[:, e, g, :].bitcast(FP8X4), lhsT_scale=h_scales[:, e, g, :],
-                    rhs=w_codes[:, cs].bitcast(FP8X4), rhs_scale=w_scales[:, cs],
-                    start=(g == 0), stop=(g == U_PASSES - 1))
-            accs[key] = acc
-            give(("codes", key))
+        def multiply_pair(q):
+            e = turns[q * T_GROUP][0]
+            acc = take_bank(("pair", q), [B, NB], F32)
+            for j in range(2):
+                w_codes, w_scales = codes.pop(("t", q + j))
+                for g in range(U_PASSES):
+                    cs = slice(g * GROUP_COLS, (g + 1) * GROUP_COLS)
+                    nc.tensor.matmul_mx(
+                        out=acc[:, j * GROUP_COLS:(j + 1) * GROUP_COLS], lhsT=h_codes[:, e, g, :].bitcast(FP8X4),
+                        lhsT_scale=h_scales[:, e, g, :], rhs=w_codes[:, cs].bitcast(FP8X4), rhs_scale=w_scales[:, cs],
+                        start=(g == 0), stop=(g == U_PASSES - 1))
+                give(("codes", ("t", q + j)))
+            accs[("pair", q)] = acc
 
-        def mix_into(e, dst, acc, first):
+        def mix_into(e, cs, ws, acc):
+            dst = chunks(late["mix"][:])[:, cs, ws]
             nc.vector.scalar_tensor_tensor(
-                out=dst, in0=acc, scalar=share[:, e:e + 1], in1=first if e == 0 else dst, op0=ALU.mult, op1=ALU.add)
+                out=dst, in0=acc, scalar=share[:, e:e + 1], in1=chunks(late["bias"][:])[:, cs, ws] if e == 0 else dst,
+                op0=ALU.mult, op1=ALU.add)
 
-        def mix_group(q):
+        def mix_pair(q):
             e, l = turns[q * T_GROUP]
-            run = T_GROUPS[e] * T_GROUP
-            acc = accs.pop(("t", q))[:, :GROUP_COLS]
-            if HALVES * run == REST:
-                view = "b c (h w) -> b (c h) w"
-                mix_into(e, mix_rest[:].rearrange(view, h=HALVES)[:, :, l:l + T_GROUP],
-                         acc.rearrange("b (l j) -> b j l", j=RUNS),
-                         bias_rest[:].rearrange(view, h=HALVES)[:, :, l:l + T_GROUP])
-            else:
-                for h in range(HALVES):
-                    first = REST - (HALVES - h) * run + l
-                    mix_into(e, mix_rest[:, :, first:first + T_GROUP],
-                             acc.rearrange("b (l c h) -> b h c l", c=CHUNKS, h=HALVES)[:, h, :, :],
-                             bias_rest[:, :, first:first + T_GROUP])
-            give(("bank", ("t", q)))
+            ws = slice(PLAIN + l, PLAIN + l + 2 * T_GROUP)
+            mix_into(e, slice(0, CHUNKS), ws, accs.pop(("pair", q))[:].rearrange("b (l c) -> b c l", c=CHUNKS))
+            give(("bank", ("pair", q)))
 
         def mix_stack(j, lo, hi):
             cs, ws = stacks[j]
-            acc = accs[("stack", j)][:, lo:hi]
-            if j == 0:
-                mix_into(1, mix_rest[:, :, :SIDE], chunks(acc), None)
-            else:
-                first = cs.start * PLAIN + ws.start
-                mix_into(1, late["mix"][:, first + lo:first + hi], acc, None)
+            count = cs.stop - cs.start
+            mix_into(1, cs, slice(lo // count, hi // count),
+                     accs[("stack", j)][:, lo:hi].rearrange("b (c w) -> b c w", c=count))
             if hi == stack_width(j):
                 give(("bank", ("stack", j)))
 
@@ -284,12 +276,12 @@ def tile_dcnv2lowrankexpertcross_w_kernel(tc, x0, x, v_bytes, v_scale, c, u, bia
             return EYE_COLS if i in EYE_UNITS else EYE_END if i == n - 1 else 0
 
         def vector_share(i):
-            if i == n - 2:
+            if i >= n - U_PASSES:
                 return SHARE_END
             if i >= long_steps + 2:
-                return SHARE_BUSY if i >= n - 2 * U_PASSES else SHARE_FREE
+                return SHARE_FREE
             if i < RH:
-                return SHARE_BUSY
+                return SHARE_HEAD
             return SHARE_V if i % RH == 1 and i not in EYE_UNITS else 0
 
         def take_grouped(i, newest=False):
@@ -424,7 +416,7 @@ def tile_dcnv2lowrankexpertcross_w_kernel(tc, x0, x, v_bytes, v_scale, c, u, bia
             hid[(e, hb)] = turned
 
         def hidden_scale(e, hb):
-            hg = place([P, W // NB, B, PACK], BF16, AT_TANH + (4 + hb) * TANH_BYTES, "hg")
+            hg = place([P, W // NB, B, PACK], BF16, AT_TANH + 2 * hb * TANH_BYTES, "hg")
             for j, bank in enumerate(hid[(e, hb)]):
                 g = e * U_PASSES + hb * (W // NB) + j
                 nc.vector.tensor_tensor(
@@ -441,45 +433,37 @@ def tile_dcnv2lowrankexpertcross_w_kernel(tc, x0, x, v_bytes, v_scale, c, u, bia
                 in_=hid.pop((e, hb))[:].rearrange("p g b t -> p (g b t)"))
 
         def load_late():
-            at = AT_TURN[0]
-            late["mix"] = place([B, CHUNKS * PLAIN], F32, at, "mix_plain")
-            at += CHUNKS * PLAIN * 4
-            late["bias"] = place([B, CHUNKS, PLAIN], BF16, at, "bias_plain")
-            at += CHUNKS * PLAIN * 2
-            nc.sync.dma_start(
-                out=late["bias"][:], in_=bias.rearrange("(c w) -> c w", c=CHUNKS)[:, :PLAIN].partition_broadcast(P))
-            free_stage.extend(range(at, AT_TURN[0] + T_BYTES, SLOT))
+            late["mix"] = place([B, D], F32, AT_TURN[0], "mix")
+            late["bias"] = place([B, D], BF16, AT_TURN[0] + 4 * D, "bias_sb")
+            nc.sync.dma_start(out=late["bias"][:], in_=bias.partition_broadcast(P))
+            at = AT_TURN[0] + 6 * D
+            free_stage.append(at)
+            free_codes.extend([at + SLOT, at + SLOT + CODE_BYTES])
 
         def load_rows(label, src):
             late[label] = place([B, D], BF16, take(free_stage, label), label)
             nc.sync.dma_start(out=late[label][:], in_=src)
 
-        def mix_plain(e, db, j, lo=0, hi=NB):
-            ch = 2 * db + j
-            mix_into(e, late["mix"][:, ch * NB + lo:ch * NB + hi], accs[("u", e, db, j)][:, lo:hi],
-                     late["bias"][:, ch, lo:hi])
-            if hi == NB:
-                give(("bank", ("u", e, db, j)))
+        def mix_plain(e, db, j):
+            first = 4 * db + 2 * j
+            mix_into(e, slice(first, first + 2), slice(0, PLAIN),
+                     accs[("u", e, db, j)][:].rearrange("b (c w) -> b c w", c=2))
+            give(("bank", ("u", e, db, j)))
 
-        def views(part, cs, ws):
-            mixed = chunks(late["mix"][:]) if part == "plain" else mix_rest[:]
-            shift = 0 if part == "plain" else PLAIN
-            return mixed[:, cs, ws], slice(shift + ws.start, shift + ws.stop)
+        def cross(cs, ws):
+            mixed = chunks(late["mix"][:])[:, cs, ws]
+            nc.vector.tensor_tensor(out=mixed, in0=mixed, in1=chunks(late["x0"][:])[:, cs, ws], op=ALU.mult)
 
-        def cross(part, cs, ws):
-            mixed, ds = views(part, cs, ws)
-            nc.vector.tensor_tensor(out=mixed, in0=mixed, in1=chunks(late["x0"][:])[:, cs, ds], op=ALU.mult)
-
-        def finish(part, cs, ws):
-            mixed, ds = views(part, cs, ws)
-            nc.vector.tensor_tensor(out=mixed, in0=mixed, in1=chunks(late["x"][:])[:, cs, ds], op=ALU.add)
-            nc.sync.dma_start(out=chunks(out)[:, cs, ds], in_=mixed)
+        def finish(cs, ws):
+            mixed = chunks(late["mix"][:])[:, cs, ws]
+            nc.vector.tensor_tensor(out=mixed, in0=mixed, in1=chunks(late["x"][:])[:, cs, ws], op=ALU.add)
+            nc.sync.dma_start(out=chunks(out)[:, cs, ws], in_=mixed)
 
         make_identity(nc, ident[:])
         nc.vector.tensor_copy(out=ident16[:], in_=ident[:])
         nc.vector.tensor_copy(
-            out=perm16[:].rearrange("q (g c h t) -> q g c h t", g=U_PASSES, c=CHUNKS, h=HALVES),
-            in_=ident[:].rearrange("q (t c g h) -> q g c h t", g=U_PASSES, c=CHUNKS, h=HALVES))
+            out=perm16[:].rearrange("q (g c t) -> q g c t", g=U_PASSES, c=CHUNKS),
+            in_=ident[:].rearrange("q (t c g) -> q g c t", g=U_PASSES, c=CHUNKS))
         with tc.manual_schedule():
             scales = v_scale.rearrange("o (g p t) u -> p (o g) (t u)", p=P, t=PACK)
             nc.scalar.dma_start(out=scale_first[:], in_=scales[:, :1, :])
@@ -491,8 +475,8 @@ def tile_dcnv2lowrankexpertcross_w_kernel(tc, x0, x, v_bytes, v_scale, c, u, bia
             nc.sync.dma_start(out=x_early[:], in_=x)
             for g in range(U_PASSES):
                 load_slab(2 + g, whole)
-                for h in range(HALVES):
-                    load_turn(0, HALVES * g + h)
+                load_turn(0, 2 * g)
+                load_turn(0, 2 * g + 1)
 
             for e in range(E):
                 nc.scalar.activation(
@@ -543,21 +527,27 @@ def tile_dcnv2lowrankexpertcross_w_kernel(tc, x0, x, v_bytes, v_scale, c, u, bia
             at(later, 0, quantize_x)
             borrowed = range(AT_TURN[1], AT_TURN[1] + T_BYTES)
             stream = [(load_slab, (i, whole)) for i in range(6, len(slabs))] + [(load_unit, (i,)) for i in range(n_v, n)]
-            stream[-2:-2] = [(load_rows, ("x0", x0))]
-            stream.append((load_rows, ("x", x)))
-            h_ready = [i + 5 for i in range(n_v) if units[i][3] == V_PASSES - 1 and units[i][2] == RH - 1]
-            hidden_steps = [i + 3 for i in range(n_v) if units[i][3] == V_PASSES - 1]
+            stream[-2:-2] = [(load_rows, ("x0", x0)), (load_rows, ("x", x))]
+            h_ready = [(e + 1) * n_v // E + 4 for e in range(E)]
+            hidden_steps = [(e + 1) * n_v // E + 2 + hb for e in range(E) for hb in range(RH)]
             second_from = 2 * (2 + U_PASSES) - 4
-            turned, full, waiting = [0], [], []
+            turned, full, waiting, quantized = [0], [], [], []
+
+            def batched(s):
+                return s > T_FIRST and turned[0] < len(turns)
+
+            def batch_end(s):
+                return s - s % MX_BATCH + MX_BATCH - 1 if batched(s) else s
+
             rest_last = [0]
-            rest_left = [T_GROUPS[1] + 1]
+            rest_left = [T_GROUPS[1] // 2]
 
             def rest_done(step):
                 rest_left[0] -= 1
                 rest_last[0] = step = max(step, rest_last[0])
                 if rest_left[0] == 0:
-                    at(later, step + 1, cross, "rest", slice(0, CHUNKS), slice(0, REST))
-                    at(later, step + 2, finish, "rest", slice(0, CHUNKS), slice(0, REST))
+                    at(later, step + 1, cross, slice(0, CHUNKS), slice(PLAIN, CW))
+                    at(later, step + 2, finish, slice(0, CHUNKS), slice(PLAIN, CW))
 
             for s in range(n - 1):
                 for where in [w for w in free_stage if w in borrowed]:
@@ -567,10 +557,7 @@ def tile_dcnv2lowrankexpertcross_w_kernel(tc, x0, x, v_bytes, v_scale, c, u, bia
                     fn(*args)
                 if s == 0:
                     nc.sync.dma_start(out=c_sb[:], in_=c.rearrange("e (g p t) -> p (e g) t", p=P, t=PACK))
-                    nc.sync.dma_start(
-                        out=bias_rest[:],
-                        in_=bias.rearrange("(c w) -> c w", c=CHUNKS)[:, PLAIN:].partition_broadcast(P))
-                if s in range(second_from, second_from + U_PASSES * HALVES):
+                if s in range(second_from, second_from + 2 * U_PASSES):
                     load_turn(1, s - second_from)
                 if "mix" not in late and turned[0] >= T_GROUPS[0] * T_GROUP:
                     load_late()
@@ -580,9 +567,12 @@ def tile_dcnv2lowrankexpertcross_w_kernel(tc, x0, x, v_bytes, v_scale, c, u, bia
                 ready = full[:]
                 full.clear()
                 run(early, s)
-                opens = 0 if units[s][3] > 0 else 1 if units[s][0] == "stack" else 2
+                batch = quantized + [s] if batch_end(s) == s else []
+                opens = sum(0 if units[i][3] > 0 else 1 if units[i][0] == "stack" else 2 for i in batch)
                 if s >= T_FIRST:
                     quota = (T_LONG if s < long_steps else T_SHORT) - (T_HIDDEN if s in hidden_steps else 0)
+                    if MX_BATCH > 1 and s % MX_BATCH == 0 and s > T_FIRST + 1:
+                        quota = T_AFTER
                     needed = opens + (2 if s + 1 in hidden_steps else 0)
                     for m in range(turned[0], min(len(turns), turned[0] + quota)):
                         if m % T_BANK == 0 and min(len(free_banks), len(free_banks) + len(ready) - needed) < 1:
@@ -598,7 +588,8 @@ def tile_dcnv2lowrankexpertcross_w_kernel(tc, x0, x, v_bytes, v_scale, c, u, bia
                     if b % (T_GROUP // T_BANK) == T_GROUP // T_BANK - 1:
                         q = b // (T_GROUP // T_BANK)
                         at(later, s + 1, quantize, ("t", q), 0, W)
-                        waiting.append((s + 2, ("t", q), turns[q * T_GROUP][0]))
+                        if q % 2 == 1:
+                            waiting.append((s + 1, q - 1, turns[q * T_GROUP][0]))
                 if s + 3 < n:
                     eye_interleave(s + 3)
                 last_of_step = s in from_psum
@@ -611,38 +602,41 @@ def tile_dcnv2lowrankexpertcross_w_kernel(tc, x0, x, v_bytes, v_scale, c, u, bia
                     if s + 3 < n:
                         pool_interleave(s + 3)
                     run(from_psum, s)
-                while waiting and waiting[0][0] <= s and h_ready[waiting[0][2]] <= s and s + 1 not in hidden_steps and len(free_banks) > opens:
-                    step, key, owner = waiting.pop(0)
-                    multiply_four(key, owner)
-                    mixed = s + (1 if turned[0] == len(turns) else 2)
-                    at(later, mixed, mix_group, key[1])
+                quantized.append(s)
+                for i in batch:
+                    quantized.remove(i)
+                    kind, e, blk, g = units[i]
+                    if kind == "stack":
+                        depth = W // stack_width(blk)
+                        multiply_stack(i, range(depth), g == 0, g + depth == U_PASSES)
+                        give(("codes", i))
+                        if g + depth == U_PASSES and blk == 0:
+                            at(later, s + 2, mix_stack, blk, 0, stack_width(blk))
+                            rest_done(s + 2)
+                        elif g + depth == U_PASSES:
+                            at(later, s + 1, mix_stack, blk, 0, stack_width(blk))
+                            at(later, s + 2, cross, *stacks[blk])
+                            at(later, s + 3, finish, *stacks[blk])
+                    else:
+                        multiply(i)
+                    if kind == "v" and g == V_PASSES - 1:
+                        at(later, s + 2, hidden_tanh, e, blk)
+                        at(early, s + 3 + blk, hidden_turn, e, blk)
+                        at(from_psum, s + 3 + blk, hidden_scale, e, blk)
+                        at(later, s + 4 + blk, hidden_quantize, e, blk)
+                    if kind == "u" and g == U_PASSES - 1:
+                        for j in range(W // NB):
+                            at(from_psum, s + (1 if e else 2 + LAG), mix_plain, e, blk, j)
+                        if e == 1:
+                            at(later, s + 2, cross, slice(0, CHUNKS // 2), slice(0, PLAIN))
+                            at(later, s + 3, finish, slice(0, CHUNKS // 2), slice(0, PLAIN))
+                while batch and waiting and waiting[0][0] <= s and h_ready[waiting[0][2]] <= s and free_banks:
+                    step, q, owner = waiting.pop(0)
+                    multiply_pair(q)
+                    mixed = s + (2 + LAG if len(batch) > 1 else 2)
+                    at(later, mixed, mix_pair, q)
                     if owner == 1:
                         rest_done(mixed)
-                kind, e, blk, g = units[s]
-                if kind == "stack":
-                    depth = W // stack_width(blk)
-                    multiply_stack(s, range(depth), g == 0, g + depth == U_PASSES)
-                    give(("codes", s))
-                    if g + depth == U_PASSES and blk == 0:
-                        at(later, s + 2, mix_stack, blk, 0, stack_width(blk))
-                        rest_done(s + 2)
-                    elif g + depth == U_PASSES:
-                        at(later, s + 1, mix_stack, blk, 0, stack_width(blk))
-                        at(later, s + 2, cross, "plain", *stacks[blk])
-                        at(later, s + 3, finish, "plain", *stacks[blk])
-                else:
-                    multiply(s)
-                if kind == "v" and g == V_PASSES - 1:
-                    at(later, s + 1, hidden_tanh, e, blk)
-                    at(early, s + 3, hidden_turn, e, blk)
-                    at(from_psum, s + 3, hidden_scale, e, blk)
-                    at(later, s + 4, hidden_quantize, e, blk)
-                if kind == "u" and g == U_PASSES - 1:
-                    for j in range(W // NB):
-                        at(from_psum, s + 3 - 2 * e, mix_plain, e, blk, j)
-                    if e == 1:
-                        at(later, s + 2, cross, "plain", slice(0, 2), slice(0, PLAIN))
-                        at(later, s + 3, finish, "plain", slice(0, 2), slice(0, PLAIN))
             assert not waiting and turned[0] == len(turns) and not full
             quantize(n - 1, 0, NB)
             quantize(n - 1, W - EYE_END, W)
@@ -657,7 +651,7 @@ def tile_dcnv2lowrankexpertcross_w_kernel(tc, x0, x, v_bytes, v_scale, c, u, bia
             for lo, hi in halves:
                 mix_stack(last, lo, hi)
             for lo, hi in halves:
-                cross("plain", stacks[last][0], slice(stacks[last][1].start + lo, stacks[last][1].start + hi))
+                cross(stacks[last][0], slice(lo, hi))
             for lo, hi in halves:
-                finish("plain", stacks[last][0], slice(stacks[last][1].start + lo, stacks[last][1].start + hi))
+                finish(stacks[last][0], slice(lo, hi))
             assert not later and not early and not from_psum

@@ -25,46 +25,50 @@ U_PASSES = R // K_PASS
 RH = R // W
 CHUNKS = 8
 CW = D // CHUNKS
-PLAIN = 256
-REST = CW - PLAIN
+MAIN = W // CHUNKS
 T_BANK = 8
 T_GROUP = 32
-T_PITCH = 144
 GROUP_COLS = CHUNKS * T_GROUP
-T_GROUPS = (4, 4)
-SIDE = REST - T_GROUPS[1] * T_GROUP
+T_GROUPS = (4, 2)
+T_RUN = [T_GROUP * groups for groups in T_GROUPS]
+T_PITCH = [run + 16 for run in T_RUN]
+PLAIN = CW - sum(T_RUN)
+EXTRA = PLAIN - MAIN
+T_START = (PLAIN, PLAIN + T_RUN[0])
 MX_BATCH = 4
 
 EYE_UNITS = range(1, 10)
 EYE_COLS = 512
 EYE_END = 256
 T_FIRST = 7
-T_LONG = 16
-T_SHORT = 11
-T_HIDDEN = 2
+T_LONG = 14
+T_SHORT = 9
+T_HIDDEN = 8
 T_AFTER = 0
+MX_FIRST = 8
 LAG = 1
-SHARE_V = 416
+SHARE_V = 384
 SHARE_HEAD = 192
-SHARE_FREE = 464
+SHARE_FREE = 448
 SHARE_END = 0
 POOL_COLS = 104
+POOL_LONG = 256
 
 SLOT = PACK * W * 2
-T_BYTES = P * T_PITCH * 2
+T_BYTES = [P * pitch * 2 for pitch in T_PITCH]
+PASS_BYTES = PACK * CHUNKS * PLAIN * 2
 WIDE_BYTES = PACK * R * 2
 WIDE_BUFS = 3
-STAGE_SLOTS = 3
+STAGE_SLOTS = 4
 GROUPED_SLOTS = 5
 CODE_SLOTS = 7
 CODE_BYTES = 5 * W
-TANH_BYTES = NB * 4
-AT_TURN = (0, T_BYTES)
-AT_WIDE = 2 * T_BYTES
+AT_TURN = (0, T_BYTES[0])
+AT_SPARE = sum(T_BYTES)
+AT_WIDE = AT_SPARE + PASS_BYTES
 AT_STAGE = AT_WIDE + WIDE_BUFS * WIDE_BYTES
 AT_GROUPED = AT_STAGE + STAGE_SLOTS * SLOT
 AT_CODES = AT_GROUPED + GROUPED_SLOTS * SLOT
-AT_TANH = AT_CODES + CODE_SLOTS * CODE_BYTES
 
 
 def tile_dcnv2lowrankexpertcross_w_kernel(tc, x0, x, v_bytes, v_scale, c, u, bias, gate_logits, out):
@@ -97,6 +101,8 @@ def tile_dcnv2lowrankexpertcross_w_kernel(tc, x0, x, v_bytes, v_scale, c, u, bia
         free_stage = [AT_STAGE + j * SLOT for j in range(STAGE_SLOTS)] + [AT_TURN[1] + j * SLOT for j in range(4)]
         free_grouped = [AT_GROUPED + j * SLOT for j in range(GROUPED_SLOTS)]
         free_codes = [AT_CODES + j * CODE_BYTES for j in range(CODE_SLOTS)]
+        free_pass = []
+        pass_at = {}
         held = {}
 
         def take(free, key, newest=False):
@@ -113,22 +119,23 @@ def tile_dcnv2lowrankexpertcross_w_kernel(tc, x0, x, v_bytes, v_scale, c, u, bia
         slabs = [(e, g) for e in range(E) for g in range(V_PASSES)]
         units = [("v", e, hb, g) for e, g in slabs for hb in range(RH)]
         n_v = len(units)
-        units += [("u", 0, db, g) for db in range(2) for g in range(U_PASSES)]
-        stacks = [(slice(0, CHUNKS), slice(PLAIN, PLAIN + SIDE)), (slice(4, 6), slice(0, PLAIN)),
-                  (slice(6, 7), slice(0, PLAIN)), (slice(7, 8), slice(0, PLAIN))]
+        units += [("main", 0, 0, g) for g in range(U_PASSES)]
+        last_block = D - W
+        stacks = [(0, CHUNKS * EXTRA), (last_block, NB), (last_block + NB, NB // 2), (D - NB // 2, NB // 2)]
 
         def stack_width(j):
-            cs, ws = stacks[j]
-            return (cs.stop - cs.start) * (ws.stop - ws.start)
+            return stacks[j][1]
 
         def stack_units(j):
-            return [("stack", 1, j, g) for g in range(0, U_PASSES, W // stack_width(j))]
+            return [("stack", min(j, 1), j, g) for g in range(0, U_PASSES, W // stack_width(j))]
 
-        units += (stack_units(0) if SIDE else []) + [("u", 1, 0, g) for g in range(U_PASSES)]
+        units += stack_units(0) + [("u", 1, db, g) for db in range(2) for g in range(U_PASSES)]
         units += stack_units(1) + stack_units(2) + stack_units(3)
         n = len(units)
         long_steps = 2 * (len(slabs) - 2)
         raw, slab_raw, wide, grouped, codes, accs, hid, eye_out, t_banks, turn_sb, late = {}, {}, {}, {}, {}, {}, {}, {}, {}, {}, {}
+
+        pooled = {}
 
         def chunks(ap):
             return ap.rearrange("b (c w) -> b c w", c=CHUNKS)
@@ -142,48 +149,42 @@ def tile_dcnv2lowrankexpertcross_w_kernel(tc, x0, x, v_bytes, v_scale, c, u, bia
 
         whole = [(slice(0, 2), slice(0, R)), (slice(2, 4), slice(0, R))]
 
+        def pass_rows(e, g):
+            return u[e, g * K_PASS:(g + 1) * K_PASS, :]
+
+        def load_pass(g, where):
+            pass_at[g] = where
+            raw[n_v + g] = place([P, PACK, CHUNKS, PLAIN], BF16, where, "u_pass")
+            nc.sync.dma_start(
+                out=raw[n_v + g][:].rearrange("p t c w -> p (t c) w"),
+                in_=pass_rows(0, g).rearrange("(p t) (c w) -> p (t c) w", t=PACK, c=CHUNKS)[:, :, :PLAIN])
+
         def load_unit(i):
             kind, e, blk, g = units[i]
-            where = take(free_stage, ("raw", i))
-            if kind == "u":
-                raw[i] = place([P, PACK, W], BF16, where, "u_raw")
-                rows = u[e, g * K_PASS:(g + 1) * K_PASS, :].rearrange("(p t) (c w) -> p t c w", t=PACK, c=CHUNKS)
-                for j in range(W // PLAIN):
-                    nc.sync.dma_start(
-                        out=raw[i][:, :, j * PLAIN:(j + 1) * PLAIN], in_=rows[:, :, W // PLAIN * blk + j, :PLAIN])
-            else:
-                cs, ws = stacks[blk]
-                width = stack_width(blk)
-                raw[i] = place([P, W // width, PACK, width], BF16, where, "u_stack")
-                for j in range(W // width):
-                    ks = slice((g + j) * K_PASS, (g + j + 1) * K_PASS)
-                    if cs.stop - cs.start == CHUNKS:
-                        rows = u[e, ks, :].rearrange("(p t) (c w) -> p (t c) w", t=PACK, c=CHUNKS)[:, :, ws]
-                        nc.sync.dma_start(
-                            out=raw[i][:, j, :, :].rearrange("p t (c w) -> p (t c) w", c=CHUNKS), in_=rows)
-                    else:
-                        rows = u[e, ks, :].rearrange("(p t) (c w) -> p t c w", t=PACK, c=CHUNKS)
-                        for ch in range(cs.start, cs.stop):
-                            first = (ch - cs.start) * PLAIN
-                            nc.sync.dma_start(out=raw[i][:, j, :, first:first + PLAIN], in_=rows[:, :, ch, ws])
+            first, width = (blk * W, W) if kind == "u" else stacks[blk]
+            raw[i] = place([P, W // width, PACK, width], BF16, take(free_stage, ("raw", i)), "u_raw")
+            for j in range(W // width):
+                rows = pass_rows(e, g + j).rearrange("(p t) w -> p t w", t=PACK)
+                nc.sync.dma_start(out=raw[i][:, j, :, :], in_=rows[:, :, first:first + width])
 
-        def load_turn(e, r):
+        def load_turn(k, r):
             g, h = divmod(r, 2)
-            run = T_GROUPS[e] * T_GROUP
-            if e not in turn_sb:
-                turn_sb[e] = place([P, P, T_PITCH], BF16, AT_TURN[e], "u_turn")
-            src = u[e, g * K_PASS:(g + 1) * K_PASS, :].rearrange("(p t) (c w) -> (t c) p w", t=PACK, c=CHUNKS)
+            if k not in turn_sb:
+                turn_sb[k] = place([P, P, T_PITCH[k]], BF16, AT_TURN[k], "u_turn")
+            src = pass_rows(0, g).rearrange("(p t) (c w) -> (t c) p w", t=PACK, c=CHUNKS)
             ps = slice(h * P // 2, (h + 1) * P // 2)
-            nc.sync.dma_start(out=turn_sb[e][g:P:U_PASSES, ps, :run], in_=src[:, ps, CW - run:])
+            nc.sync.dma_start(
+                out=turn_sb[k][g:P:U_PASSES, ps, :T_RUN[k]], in_=src[:, ps, T_START[k]:T_START[k] + T_RUN[k]])
 
-        turns = [(e, l) for e in range(E) for l in range(T_GROUPS[e] * T_GROUP)]
+        turns = [(k, l) for k in range(2) for l in range(T_RUN[k])]
+        n_groups = sum(T_GROUPS)
 
         def turn(m):
-            e, l = turns[m]
+            k, l = turns[m]
             b = m // T_BANK
             if b not in t_banks:
                 t_banks[b] = take_bank(("t", b), [P, U_PASSES, T_BANK, CHUNKS * PACK], BF16)
-            nc.tensor.transpose(t_banks[b][:, :, m % T_BANK, :], turn_sb[e][:, :, l], perm16[:])
+            nc.tensor.transpose(t_banks[b][:, :, m % T_BANK, :], turn_sb[k][:, :, l], perm16[:])
 
         def empty_bank(b):
             per = T_GROUP // T_BANK
@@ -197,36 +198,41 @@ def tile_dcnv2lowrankexpertcross_w_kernel(tc, x0, x, v_bytes, v_scale, c, u, bia
             give(("bank", ("t", b)))
 
         def multiply_pair(q):
-            e = turns[q * T_GROUP][0]
             acc = take_bank(("pair", q), [B, NB], F32)
-            for j in range(2):
+            for j in range(min(2, n_groups - q)):
                 w_codes, w_scales = codes.pop(("t", q + j))
                 for g in range(U_PASSES):
                     cs = slice(g * GROUP_COLS, (g + 1) * GROUP_COLS)
                     nc.tensor.matmul_mx(
-                        out=acc[:, j * GROUP_COLS:(j + 1) * GROUP_COLS], lhsT=h_codes[:, e, g, :].bitcast(FP8X4),
-                        lhsT_scale=h_scales[:, e, g, :], rhs=w_codes[:, cs].bitcast(FP8X4), rhs_scale=w_scales[:, cs],
+                        out=acc[:, j * GROUP_COLS:(j + 1) * GROUP_COLS], lhsT=h_codes[:, 0, g, :].bitcast(FP8X4),
+                        lhsT_scale=h_scales[:, 0, g, :], rhs=w_codes[:, cs].bitcast(FP8X4), rhs_scale=w_scales[:, cs],
                         start=(g == 0), stop=(g == U_PASSES - 1))
                 give(("codes", ("t", q + j)))
             accs[("pair", q)] = acc
 
-        def mix_into(e, cs, ws, acc):
-            dst = chunks(late["mix"][:])[:, cs, ws]
+        def mix_first(ws, acc, cs=slice(0, CHUNKS)):
             nc.vector.scalar_tensor_tensor(
-                out=dst, in0=acc, scalar=share[:, e:e + 1], in1=chunks(late["bias"][:])[:, cs, ws] if e == 0 else dst,
+                out=chunks(late["mix"][:])[:, cs, ws], in0=acc, scalar=share[:, 0:1],
+                in1=chunks(late["bias"][:])[:, cs, ws], op0=ALU.mult, op1=ALU.add)
+
+        def mix_second(ds, acc):
+            nc.vector.scalar_tensor_tensor(
+                out=late["mix"][:, ds], in0=acc, scalar=share[:, 1:2], in1=late["mix"][:, ds],
                 op0=ALU.mult, op1=ALU.add)
 
         def mix_pair(q):
-            e, l = turns[q * T_GROUP]
-            ws = slice(PLAIN + l, PLAIN + l + 2 * T_GROUP)
-            mix_into(e, slice(0, CHUNKS), ws, accs.pop(("pair", q))[:].rearrange("b (l c) -> b c l", c=CHUNKS))
+            count = min(2, n_groups - q) * T_GROUP
+            first = PLAIN + q * T_GROUP
+            acc = accs.pop(("pair", q))[:, :count * CHUNKS]
+            mix_first(slice(first, first + count), acc.rearrange("b (l c) -> b c l", c=CHUNKS))
             give(("bank", ("pair", q)))
 
         def mix_stack(j, lo, hi):
-            cs, ws = stacks[j]
-            count = cs.stop - cs.start
-            mix_into(1, cs, slice(lo // count, hi // count),
-                     accs[("stack", j)][:, lo:hi].rearrange("b (c w) -> b c w", c=count))
+            acc = accs[("stack", j)][:, lo:hi]
+            if j == 0:
+                mix_first(slice(MAIN, PLAIN), chunks(acc))
+            else:
+                mix_second(slice(stacks[j][0] + lo, stacks[j][0] + hi), acc)
             if hi == stack_width(j):
                 give(("bank", ("stack", j)))
 
@@ -263,7 +269,7 @@ def tile_dcnv2lowrankexpertcross_w_kernel(tc, x0, x, v_bytes, v_scale, c, u, bia
 
         def planes(i):
             if i >= n_v:
-                return raw[i][:]
+                return raw[i][:, 0, :, :]
             return wide[0][:, i, :, :] if i < RH else wide[i // RH][:, :, i % RH * W:(i % RH + 1) * W]
 
         def tail_planes(i, cols):
@@ -302,18 +308,38 @@ def tile_dcnv2lowrankexpertcross_w_kernel(tc, x0, x, v_bytes, v_scale, c, u, bia
             if a > 0:
                 nc.vector.tensor_copy(out=dst[:, :, :a, :, :], in_=src[:, :, :a, :, :])
             if helped:
-                b = (W // depth - POOL_COLS) // 2
+                b = (W // depth - pooled[i]) // 2
                 nc.scalar.copy(out=dst[:, :depth - 1, a:, :, :], in_=src[:, :depth - 1, a:, :, :])
                 nc.scalar.copy(out=dst[:, depth - 1, a:b, :, :], in_=src[:, depth - 1, a:b, :, :])
             else:
                 nc.scalar.copy(out=dst[:, :, a:, :, :], in_=src[:, :, a:, :, :])
 
+        def arrange_main(i):
+            dst = take_grouped(i)[:].rearrange("p (c w i) t -> p c w t i", c=CHUNKS, i=2)
+            src = raw[i][:, :, :, :MAIN].rearrange("p t c (w i) -> p c w t i", i=2)
+            a = vector_share(i) // (2 * CHUNKS)
+            nc.vector.tensor_copy(out=dst[:, :, :a, :, :], in_=src[:, :, :a, :, :])
+            nc.scalar.copy(out=dst[:, :, a:, :, :], in_=src[:, :, a:, :, :])
+
+        def arrange_extra(i):
+            depth = W // stack_width(0)
+            dst = take_grouped(i)[:].rearrange("p (g c w i) t -> p g c w t i", g=depth, c=CHUNKS, i=2)
+            for j in range(depth):
+                src = raw[n_v + units[i][3] + j][:, :, :, MAIN:].rearrange("p t c (w i) -> p c w t i", i=2)
+                copy = nc.vector.tensor_copy if j < depth // 2 else nc.scalar.copy
+                copy(out=dst[:, j, :, :, :, :], in_=src)
+                where = pass_at[units[i][3] + j]
+                free_stage.extend([where] if where < AT_WIDE else [where, where + SLOT])
+
         def arrange_last(i):
-            take_grouped(i)
+            if i not in grouped:
+                take_grouped(i)
             dst, src, depth = stack_views(i)
-            empty_eye(i)
+            eye_interleave(i)
             nc.scalar.copy(out=dst[:, :2, :, :, :], in_=src[:, :2, :, :, :])
-            nc.scalar.copy(out=dst[:, 2, :, :, :], in_=src[:, 2, :, :, :])
+            empty_eye(i)
+            b = (W // depth - pooled.get(i, 0)) // 2
+            nc.scalar.copy(out=dst[:, 2, :b, :, :], in_=src[:, 2, :b, :, :])
 
         def empty_eye(i):
             for j, bank in enumerate(eye_out.pop(i, [])):
@@ -328,7 +354,7 @@ def tile_dcnv2lowrankexpertcross_w_kernel(tc, x0, x, v_bytes, v_scale, c, u, bia
             dst = grouped[i] if helped else take_grouped(i)
             src = planes(i)
             a = vector_share(i)
-            b = W - eye_cols(i) - (POOL_COLS if helped else 0)
+            b = W - eye_cols(i) - pooled.get(i, 0)
             if a > 0 and i > 0:
                 interleave(nc.vector.tensor_copy, dst[:, :a, :], src[:, :, :a])
             interleave(nc.scalar.copy, dst[:, a:b, :], src[:, :, a:b])
@@ -337,24 +363,31 @@ def tile_dcnv2lowrankexpertcross_w_kernel(tc, x0, x, v_bytes, v_scale, c, u, bia
         def arrange(i):
             if i == n - 1:
                 arrange_last(i)
+            elif units[i][0] == "main":
+                arrange_main(i)
+            elif units[i][:2] == ("stack", 0):
+                arrange_extra(i)
             elif units[i][0] == "stack":
                 arrange_stack(i)
             else:
                 arrange_plain(i)
-            if i >= n_v:
+            if ("raw", i) in held:
                 give(("raw", i))
-            elif i % RH == RH - 1 and i // RH >= len(slabs) - WIDE_BUFS:
-                at_wide = AT_WIDE + i // RH % WIDE_BUFS * WIDE_BYTES
-                free_stage.extend([at_wide, at_wide + SLOT])
+            elif i < n_v and i % RH == RH - 1 and i // RH >= len(slabs) - WIDE_BUFS:
+                free_pass.append(AT_WIDE + i // RH % WIDE_BUFS * WIDE_BYTES)
 
         def pool_copy(out, in_):
             nc.gpsimd.tensor_scalar(out=out, in0=in_, scalar1=1.0, scalar2=0.0, op0=ALU.mult, op1=ALU.add)
 
-        def pool_interleave(i):
+        def pool_interleave(i, cols):
             dst = take_grouped(i, newest=True)
+            pooled[i] = cols
             hi = W - eye_cols(i)
-            src = tail_planes(i, W - hi + POOL_COLS)[:, :, :POOL_COLS]
-            interleave(pool_copy, dst[:, hi - POOL_COLS:hi, :], src)
+            if i == n - 1:
+                src = raw[i][:, 2, :, EYE_END - cols:]
+            else:
+                src = tail_planes(i, W - hi + cols)[:, :, :cols]
+            interleave(pool_copy, dst[:, hi - cols:hi, :], src)
 
         def eye_interleave(i):
             src = tail_planes(i, eye_cols(i))
@@ -397,67 +430,69 @@ def tile_dcnv2lowrankexpertcross_w_kernel(tc, x0, x, v_bytes, v_scale, c, u, bia
                 if j == W // NB - 1:
                     give(("codes", i))
 
-        def hidden_tanh(e, hb):
-            hid[(e, hb)] = []
-            for j in range(W // NB):
-                th = place([B, PACK, P], F32, AT_TANH + (2 * hb + j) * TANH_BYTES, "th")
-                acc = accs.pop(("v", e, hb, j))
-                nc.scalar.activation(out=th[:], in_=acc[:].rearrange("b (p t) -> b t p", t=PACK), func=ACT.Tanh)
-                give(("bank", ("v", e, hb, j)))
-                hid[(e, hb)].append(th)
+        def hidden_tanh(e):
+            hid[e] = place([B, U_PASSES, PACK, P], F32, take(free_stage, "th"), "th")
+            for g in range(U_PASSES):
+                key = ("v", e, g // 2, g % 2)
+                nc.scalar.activation(
+                    out=hid[e][:, g, :, :], in_=accs.pop(key)[:].rearrange("b (p t) -> b t p", t=PACK), func=ACT.Tanh)
+                give(("bank", key))
 
-        def hidden_turn(e, hb):
-            turned = []
-            for j, th in enumerate(hid[(e, hb)]):
-                bank = take_bank(("h", hb, j), [P, PACK, B], F32)
+        def hidden_turn(e):
+            turned_h = []
+            for g in range(U_PASSES):
+                bank = take_bank(("h", g), [P, PACK, B], F32)
                 for t in range(PACK):
-                    nc.tensor.transpose(bank[:, t, :], th[:, t, :], ident[:])
-                turned.append(bank)
-            hid[(e, hb)] = turned
+                    nc.tensor.transpose(bank[:, t, :], hid[e][:, g, t, :], ident[:])
+                turned_h.append(bank)
+            hid[e] = turned_h
 
-        def hidden_scale(e, hb):
-            hg = place([P, W // NB, B, PACK], BF16, AT_TANH + 2 * hb * TANH_BYTES, "hg")
-            for j, bank in enumerate(hid[(e, hb)]):
-                g = e * U_PASSES + hb * (W // NB) + j
+        def hidden_scale(e):
+            hg = place([P, U_PASSES, B, PACK], BF16, held["th"][1], "hg")
+            for g, bank in enumerate(hid[e]):
+                at_c = e * U_PASSES + g
                 nc.vector.tensor_tensor(
-                    out=hg[:, j, :, :], in0=bank[:].rearrange("p t b -> p b t"),
-                    in1=c_sb[:, g:g + 1, :].to_broadcast([P, B, PACK]), op=ALU.mult)
-                give(("bank", ("h", hb, j)))
-            hid[(e, hb)] = hg
+                    out=hg[:, g, :, :], in0=bank[:].rearrange("p t b -> p b t"),
+                    in1=c_sb[:, at_c:at_c + 1, :].to_broadcast([P, B, PACK]), op=ALU.mult)
+                give(("bank", ("h", g)))
+            hid[e] = hg
 
-        def hidden_quantize(e, hb):
-            gs = slice(2 * hb, 2 * hb + 2)
+        def hidden_quantize(e):
             nc.vector.quantize_mx(
-                out=h_codes[:, e, gs, :].rearrange("p g b -> p (g b)").bitcast(FP8X4),
-                scales=h_scales[:, e, gs, :].rearrange("p g b -> p (g b)"),
-                in_=hid.pop((e, hb))[:].rearrange("p g b t -> p (g b t)"))
+                out=h_codes[:, e, :, :].rearrange("p g b -> p (g b)").bitcast(FP8X4),
+                scales=h_scales[:, e, :, :].rearrange("p g b -> p (g b)"),
+                in_=hid.pop(e)[:].rearrange("p g b t -> p (g b t)"))
+            give("th")
 
         def load_late():
             late["mix"] = place([B, D], F32, AT_TURN[0], "mix")
             late["bias"] = place([B, D], BF16, AT_TURN[0] + 4 * D, "bias_sb")
             nc.sync.dma_start(out=late["bias"][:], in_=bias.partition_broadcast(P))
             at = AT_TURN[0] + 6 * D
-            free_stage.append(at)
-            free_codes.extend([at + SLOT, at + SLOT + CODE_BYTES])
+            free_pass.append(at)
+            free_codes.append(at + PASS_BYTES)
 
         def load_rows(label, src):
             late[label] = place([B, D], BF16, take(free_stage, label), label)
             nc.sync.dma_start(out=late[label][:], in_=src)
 
-        def mix_plain(e, db, j):
-            first = 4 * db + 2 * j
-            mix_into(e, slice(first, first + 2), slice(0, PLAIN),
-                     accs[("u", e, db, j)][:].rearrange("b (c w) -> b c w", c=2))
-            give(("bank", ("u", e, db, j)))
+        def mix_plain(kind, e, blk, j):
+            acc = accs.pop((kind, e, blk, j))
+            if e == 0:
+                half = CHUNKS // 2
+                mix_first(slice(0, MAIN), acc[:].rearrange("b (c w) -> b c w", c=half), slice(j * half, (j + 1) * half))
+            else:
+                mix_second(slice(blk * W + j * NB, blk * W + (j + 1) * NB), acc[:])
+            give(("bank", (kind, e, blk, j)))
 
-        def cross(cs, ws):
-            mixed = chunks(late["mix"][:])[:, cs, ws]
-            nc.vector.tensor_tensor(out=mixed, in0=mixed, in1=chunks(late["x0"][:])[:, cs, ws], op=ALU.mult)
+        def cross(first, width):
+            ds = slice(first, first + width)
+            nc.vector.tensor_tensor(out=late["mix"][:, ds], in0=late["mix"][:, ds], in1=late["x0"][:, ds], op=ALU.mult)
 
-        def finish(cs, ws):
-            mixed = chunks(late["mix"][:])[:, cs, ws]
-            nc.vector.tensor_tensor(out=mixed, in0=mixed, in1=chunks(late["x"][:])[:, cs, ws], op=ALU.add)
-            nc.sync.dma_start(out=chunks(out)[:, cs, ws], in_=mixed)
+        def finish(first, width):
+            ds = slice(first, first + width)
+            nc.vector.tensor_tensor(out=late["mix"][:, ds], in0=late["mix"][:, ds], in1=late["x"][:, ds], op=ALU.add)
+            nc.sync.dma_start(out=out[:, ds], in_=late["mix"][:, ds])
 
         make_identity(nc, ident[:])
         nc.vector.tensor_copy(out=ident16[:], in_=ident[:])
@@ -525,41 +560,41 @@ def tile_dcnv2lowrankexpertcross_w_kernel(tc, x0, x, v_bytes, v_scale, c, u, bia
                     fn(*args)
 
             at(later, 0, quantize_x)
-            borrowed = range(AT_TURN[1], AT_TURN[1] + T_BYTES)
-            stream = [(load_slab, (i, whole)) for i in range(6, len(slabs))] + [(load_unit, (i,)) for i in range(n_v, n)]
-            stream[-2:-2] = [(load_rows, ("x0", x0)), (load_rows, ("x", x))]
+            borrowed = range(AT_TURN[1], AT_WIDE)
+            stream = [(load_slab, (i, whole)) for i in range(6, len(slabs))] + [(load_unit, (i,)) for i in range(n_v, n) if units[i][1] == 1]
+            stream[-6:-6] = [(load_rows, ("x0", x0)), (load_rows, ("x", x))]
+            passes = list(range(U_PASSES))
             h_ready = [(e + 1) * n_v // E + 4 for e in range(E)]
-            hidden_steps = [(e + 1) * n_v // E + 2 + hb for e in range(E) for hb in range(RH)]
+            hidden_steps = [(e + 1) * n_v // E + 2 for e in range(E)]
+            lent = range(hidden_steps[0] + 2, hidden_steps[1] - 4)
             second_from = 2 * (2 + U_PASSES) - 4
-            turned, full, waiting, quantized = [0], [], [], []
+            turned, full, waiting, quantized, first_done = [0], [], [], [], [n]
 
             def batched(s):
-                return s > T_FIRST and turned[0] < len(turns)
+                return s >= MX_FIRST and turned[0] < len(turns)
 
             def batch_end(s):
                 return s - s % MX_BATCH + MX_BATCH - 1 if batched(s) else s
 
-            rest_last = [0]
-            rest_left = [T_GROUPS[1] // 2]
-
-            def rest_done(step):
-                rest_left[0] -= 1
-                rest_last[0] = step = max(step, rest_last[0])
-                if rest_left[0] == 0:
-                    at(later, step + 1, cross, slice(0, CHUNKS), slice(PLAIN, CW))
-                    at(later, step + 2, finish, slice(0, CHUNKS), slice(PLAIN, CW))
 
             for s in range(n - 1):
                 for where in [w for w in free_stage if w in borrowed]:
                     free_stage.remove(where)
-                while stream and free_stage:
+                while stream and (s < long_steps - 4 or not passes) and len(free_stage) > (1 if s < hidden_steps[1] and "th" not in held and s not in lent else 0):
                     fn, args = stream.pop(0)
                     fn(*args)
                 if s == 0:
                     nc.sync.dma_start(out=c_sb[:], in_=c.rearrange("e (g p t) -> p (e g) t", p=P, t=PACK))
                 if s in range(second_from, second_from + 2 * U_PASSES):
                     load_turn(1, s - second_from)
-                if "mix" not in late and turned[0] >= T_GROUPS[0] * T_GROUP:
+                if s == second_from + 2 * U_PASSES:
+                    free_pass.append(AT_SPARE)
+                while free_pass and passes:
+                    load_pass(passes.pop(0), free_pass.pop(0))
+                for where in free_pass:
+                    free_stage.extend([where, where + SLOT])
+                free_pass.clear()
+                if "mix" not in late and turned[0] >= T_RUN[0]:
                     load_late()
                 if s < long_steps:
                     for t in (2 * (s % 2), 2 * (s % 2) + 1):
@@ -569,11 +604,12 @@ def tile_dcnv2lowrankexpertcross_w_kernel(tc, x0, x, v_bytes, v_scale, c, u, bia
                 run(early, s)
                 batch = quantized + [s] if batch_end(s) == s else []
                 opens = sum(0 if units[i][3] > 0 else 1 if units[i][0] == "stack" else 2 for i in batch)
+                freed = U_PASSES if s + 1 in hidden_steps or s - 1 in hidden_steps else 0
                 if s >= T_FIRST:
                     quota = (T_LONG if s < long_steps else T_SHORT) - (T_HIDDEN if s in hidden_steps else 0)
-                    if MX_BATCH > 1 and s % MX_BATCH == 0 and s > T_FIRST + 1:
+                    if MX_BATCH > 1 and s % MX_BATCH == 0 and s > MX_FIRST:
                         quota = T_AFTER
-                    needed = opens + (2 if s + 1 in hidden_steps else 0)
+                    needed = opens + (U_PASSES if s + 1 in hidden_steps else 0) - freed
                     for m in range(turned[0], min(len(turns), turned[0] + quota)):
                         if m % T_BANK == 0 and min(len(free_banks), len(free_banks) + len(ready) - needed) < 1:
                             break
@@ -588,9 +624,9 @@ def tile_dcnv2lowrankexpertcross_w_kernel(tc, x0, x, v_bytes, v_scale, c, u, bia
                     if b % (T_GROUP // T_BANK) == T_GROUP // T_BANK - 1:
                         q = b // (T_GROUP // T_BANK)
                         at(later, s + 1, quantize, ("t", q), 0, W)
-                        if q % 2 == 1:
-                            waiting.append((s + 1, q - 1, turns[q * T_GROUP][0]))
-                if s + 3 < n:
+                        if q % 2 == 1 or q == n_groups - 1:
+                            waiting.append((s + 1, q - q % 2))
+                if s + 3 in EYE_UNITS:
                     eye_interleave(s + 3)
                 last_of_step = s in from_psum
                 if not last_of_step:
@@ -600,7 +636,7 @@ def tile_dcnv2lowrankexpertcross_w_kernel(tc, x0, x, v_bytes, v_scale, c, u, bia
                     quantize(s, 0, W)
                 if s in from_psum:
                     if s + 3 < n:
-                        pool_interleave(s + 3)
+                        pool_interleave(s + 3, POOL_LONG if s - 1 in hidden_steps else POOL_COLS)
                     run(from_psum, s)
                 quantized.append(s)
                 for i in batch:
@@ -611,47 +647,54 @@ def tile_dcnv2lowrankexpertcross_w_kernel(tc, x0, x, v_bytes, v_scale, c, u, bia
                         multiply_stack(i, range(depth), g == 0, g + depth == U_PASSES)
                         give(("codes", i))
                         if g + depth == U_PASSES and blk == 0:
-                            at(later, s + 2, mix_stack, blk, 0, stack_width(blk))
-                            rest_done(s + 2)
+                            at(later, s + 2 + LAG, mix_stack, blk, 0, stack_width(blk))
                         elif g + depth == U_PASSES:
-                            at(later, s + 1, mix_stack, blk, 0, stack_width(blk))
-                            at(later, s + 2, cross, *stacks[blk])
-                            at(later, s + 3, finish, *stacks[blk])
+                            mix_stack(blk, 0, stack_width(blk))
+                            at(later, s + 1, cross, *stacks[blk])
+                            at(later, s + 2, finish, *stacks[blk])
                     else:
                         multiply(i)
-                    if kind == "v" and g == V_PASSES - 1:
-                        at(later, s + 2, hidden_tanh, e, blk)
-                        at(early, s + 3 + blk, hidden_turn, e, blk)
-                        at(from_psum, s + 3 + blk, hidden_scale, e, blk)
-                        at(later, s + 4 + blk, hidden_quantize, e, blk)
-                    if kind == "u" and g == U_PASSES - 1:
+                    if kind == "v" and g == V_PASSES - 1 and blk == RH - 1:
+                        at(later, s + 2, hidden_tanh, e)
+                        at(early, s + 3, hidden_turn, e)
+                        at(from_psum, s + 4, hidden_scale, e)
+                        at(later, s + 5, hidden_quantize, e)
+                    if kind == "main" and g == U_PASSES - 1:
                         for j in range(W // NB):
-                            at(from_psum, s + (1 if e else 2 + LAG), mix_plain, e, blk, j)
-                        if e == 1:
-                            at(later, s + 2, cross, slice(0, CHUNKS // 2), slice(0, PLAIN))
-                            at(later, s + 3, finish, slice(0, CHUNKS // 2), slice(0, PLAIN))
-                while batch and waiting and waiting[0][0] <= s and h_ready[waiting[0][2]] <= s and free_banks:
-                    step, q, owner = waiting.pop(0)
+                            at(from_psum, s + 2 + LAG, mix_plain, kind, e, blk, j)
+                    if kind == "u" and g == U_PASSES - 1:
+                        assert blk == 0 or not waiting
+                        mixed = s if blk == 1 else max(s + (2 + LAG if len(batch) > 1 else 2), first_done[0])
+                        if blk == 1:
+                            pool_interleave(s + 3, POOL_COLS)
+                        for j in range(W // NB):
+                            if blk == 1:
+                                mix_plain(kind, e, blk, j)
+                            else:
+                                at(from_psum, mixed, mix_plain, kind, e, blk, j)
+                        at(later, mixed + 1, cross, blk * W, W)
+                        at(later, mixed + 2, finish, blk * W, W)
+                while batch and waiting and waiting[0][0] <= s and h_ready[0] <= s and "mix" in late and free_banks:
+                    step, q = waiting.pop(0)
                     multiply_pair(q)
                     mixed = s + (2 + LAG if len(batch) > 1 else 2)
                     at(later, mixed, mix_pair, q)
-                    if owner == 1:
-                        rest_done(mixed)
+                    if q + 2 >= n_groups:
+                        first_done[0] = mixed
             assert not waiting and turned[0] == len(turns) and not full
             quantize(n - 1, 0, NB)
+            run(later, n - 1)
             quantize(n - 1, W - EYE_END, W)
             multiply_stack(n - 1, [0, 1, 3], True, False)
-            run(later, n - 1)
             quantize(n - 1, NB, W - EYE_END)
             multiply_stack(n - 1, [2], False, True)
             run(later, n)
-            run(later, n + 1)
             last = len(stacks) - 1
             halves = [(0, P), (P, 2 * P)]
             for lo, hi in halves:
                 mix_stack(last, lo, hi)
             for lo, hi in halves:
-                cross(stacks[last][0], slice(lo, hi))
+                cross(stacks[last][0] + lo, P)
             for lo, hi in halves:
-                finish(stacks[last][0], slice(lo, hi))
+                finish(stacks[last][0] + lo, P)
             assert not later and not early and not from_psum

@@ -34,25 +34,22 @@ T_RUN = [T_GROUP * groups for groups in T_GROUPS]
 T_PITCH = [run + 16 for run in T_RUN]
 PLAIN = CW - sum(T_RUN)
 EXTRA = PLAIN - MAIN
-T_START = (PLAIN, PLAIN + T_RUN[0])
+T_START = (0, T_RUN[0] + PLAIN)
+PLAIN_START = T_RUN[0]
 MX_BATCH = 4
 
 EYE_UNITS = range(1, 10)
 EYE_COLS = 512
 EYE_END = 256
-T_FIRST = 7
-T_LONG = 14
-T_SHORT = 9
-T_HIDDEN = 8
-T_AFTER = 0
-MX_FIRST = 8
-LAG = 1
-SHARE_V = 384
+T_FIRST = 8
+T_DENSE = 99
+Q_LAG = 2
+SHARE_V = 400
 SHARE_HEAD = 192
-SHARE_FREE = 448
+SHARE_FREE = 432
 SHARE_END = 0
-POOL_COLS = 104
-POOL_LONG = 256
+POOL_COLS = 72
+POOL_LESS = 40
 
 SLOT = PACK * W * 2
 T_BYTES = [P * pitch * 2 for pitch in T_PITCH]
@@ -98,10 +95,9 @@ def tile_dcnv2lowrankexpertcross_w_kernel(tc, x0, x, v_bytes, v_scale, c, u, bia
             return arena.tile(shape, dtype, offset=offset, align_bytes=64, name="%s%d" % (label, len(made)))
 
         free_banks = list(range(8))
-        free_stage = [AT_STAGE + j * SLOT for j in range(STAGE_SLOTS)] + [AT_TURN[1] + j * SLOT for j in range(4)]
+        free_stage = []
         free_grouped = [AT_GROUPED + j * SLOT for j in range(GROUPED_SLOTS)]
         free_codes = [AT_CODES + j * CODE_BYTES for j in range(CODE_SLOTS)]
-        free_pass = []
         pass_at = {}
         held = {}
 
@@ -140,9 +136,9 @@ def tile_dcnv2lowrankexpertcross_w_kernel(tc, x0, x, v_bytes, v_scale, c, u, bia
         def chunks(ap):
             return ap.rearrange("b (c w) -> b c w", c=CHUNKS)
 
-        def load_slab(i, pieces):
+        def load_slab(i, pieces, where):
             e, g = slabs[i]
-            slab_raw[i] = place([P, PACK, R], U8, take(free_stage, ("slab", i)), "v_raw")
+            slab_raw[i] = place([P, PACK, R], U8, where, "v_raw")
             rows = v_bytes[e, g * K_PASS:(g + 1) * K_PASS, :].rearrange("(p t) w -> p t w", t=PACK)
             for ts, cs in pieces:
                 nc.sync.dma_start(out=slab_raw[i][:, ts, cs], in_=rows[:, ts, cs])
@@ -152,12 +148,15 @@ def tile_dcnv2lowrankexpertcross_w_kernel(tc, x0, x, v_bytes, v_scale, c, u, bia
         def pass_rows(e, g):
             return u[e, g * K_PASS:(g + 1) * K_PASS, :]
 
-        def load_pass(g, where):
-            pass_at[g] = where
+        def load_c():
+            nc.sync.dma_start(out=c_sb[:], in_=c.rearrange("e (g p t) -> p (e g) t", p=P, t=PACK))
+
+        def load_pass(g, where, slots):
+            pass_at[g] = [where + j * SLOT for j in range(slots)]
             raw[n_v + g] = place([P, PACK, CHUNKS, PLAIN], BF16, where, "u_pass")
             nc.sync.dma_start(
                 out=raw[n_v + g][:].rearrange("p t c w -> p (t c) w"),
-                in_=pass_rows(0, g).rearrange("(p t) (c w) -> p (t c) w", t=PACK, c=CHUNKS)[:, :, :PLAIN])
+                in_=pass_rows(0, g).rearrange("(p t) (c w) -> p (t c) w", t=PACK, c=CHUNKS)[:, :, PLAIN_START:PLAIN_START + PLAIN])
 
         def load_unit(i):
             kind, e, blk, g = units[i]
@@ -222,7 +221,8 @@ def tile_dcnv2lowrankexpertcross_w_kernel(tc, x0, x, v_bytes, v_scale, c, u, bia
 
         def mix_pair(q):
             count = min(2, n_groups - q) * T_GROUP
-            first = PLAIN + q * T_GROUP
+            k, l = turns[q * T_GROUP]
+            first = T_START[k] + l
             acc = accs.pop(("pair", q))[:, :count * CHUNKS]
             mix_first(slice(first, first + count), acc.rearrange("b (l c) -> b c l", c=CHUNKS))
             give(("bank", ("pair", q)))
@@ -230,7 +230,7 @@ def tile_dcnv2lowrankexpertcross_w_kernel(tc, x0, x, v_bytes, v_scale, c, u, bia
         def mix_stack(j, lo, hi):
             acc = accs[("stack", j)][:, lo:hi]
             if j == 0:
-                mix_first(slice(MAIN, PLAIN), chunks(acc))
+                mix_first(slice(PLAIN_START + MAIN, PLAIN_START + PLAIN), chunks(acc))
             else:
                 mix_second(slice(stacks[j][0] + lo, stacks[j][0] + hi), acc)
             if hi == stack_width(j):
@@ -261,8 +261,6 @@ def tile_dcnv2lowrankexpertcross_w_kernel(tc, x0, x, v_bytes, v_scale, c, u, bia
                 nc.scalar.activation(out=dst, in_=src, func=ACT.Copy, scale=scale)
             else:
                 nc.vector.tensor_scalar(out=dst, in0=src, scalar1=scale, scalar2=None, op0=ALU.mult)
-            if t == PACK - 1 and hi == R:
-                give(("slab", i))
 
         def interleave(copy, dst, src):
             copy(out=dst.rearrange("p (c i) t -> p c t i", i=2), in_=src.rearrange("p t (c i) -> p c t i", i=2))
@@ -328,8 +326,7 @@ def tile_dcnv2lowrankexpertcross_w_kernel(tc, x0, x, v_bytes, v_scale, c, u, bia
                 src = raw[n_v + units[i][3] + j][:, :, :, MAIN:].rearrange("p t c (w i) -> p c w t i", i=2)
                 copy = nc.vector.tensor_copy if j < depth // 2 else nc.scalar.copy
                 copy(out=dst[:, j, :, :, :, :], in_=src)
-                where = pass_at[units[i][3] + j]
-                free_stage.extend([where] if where < AT_WIDE else [where, where + SLOT])
+                free_stage.extend(pass_at[units[i][3] + j])
 
         def arrange_last(i):
             if i not in grouped:
@@ -373,8 +370,6 @@ def tile_dcnv2lowrankexpertcross_w_kernel(tc, x0, x, v_bytes, v_scale, c, u, bia
                 arrange_plain(i)
             if ("raw", i) in held:
                 give(("raw", i))
-            elif i < n_v and i % RH == RH - 1 and i // RH >= len(slabs) - WIDE_BUFS:
-                free_pass.append(AT_WIDE + i // RH % WIDE_BUFS * WIDE_BYTES)
 
         def pool_copy(out, in_):
             nc.gpsimd.tensor_scalar(out=out, in0=in_, scalar1=1.0, scalar2=0.0, op0=ALU.mult, op1=ALU.add)
@@ -430,8 +425,8 @@ def tile_dcnv2lowrankexpertcross_w_kernel(tc, x0, x, v_bytes, v_scale, c, u, bia
                 if j == W // NB - 1:
                     give(("codes", i))
 
-        def hidden_tanh(e):
-            hid[e] = place([B, U_PASSES, PACK, P], F32, take(free_stage, "th"), "th")
+        def hidden_tanh(e, where):
+            hid[e] = place([B, U_PASSES, PACK, P], F32, where, "th")
             for g in range(U_PASSES):
                 key = ("v", e, g // 2, g % 2)
                 nc.scalar.activation(
@@ -447,30 +442,28 @@ def tile_dcnv2lowrankexpertcross_w_kernel(tc, x0, x, v_bytes, v_scale, c, u, bia
                 turned_h.append(bank)
             hid[e] = turned_h
 
-        def hidden_scale(e):
-            hg = place([P, U_PASSES, B, PACK], BF16, held["th"][1], "hg")
-            for g, bank in enumerate(hid[e]):
-                at_c = e * U_PASSES + g
-                nc.vector.tensor_tensor(
-                    out=hg[:, g, :, :], in0=bank[:].rearrange("p t b -> p b t"),
-                    in1=c_sb[:, at_c:at_c + 1, :].to_broadcast([P, B, PACK]), op=ALU.mult)
-                give(("bank", ("h", g)))
-            hid[e] = hg
+        def hidden_scale(e, g, where):
+            if g == 0:
+                hid["grouped"] = place([P, U_PASSES, B, PACK], BF16, where, "hg")
+            at_c = e * U_PASSES + g
+            nc.vector.tensor_tensor(
+                out=hid["grouped"][:, g, :, :], in0=hid[e][g][:].rearrange("p t b -> p b t"),
+                in1=c_sb[:, at_c:at_c + 1, :].to_broadcast([P, B, PACK]), op=ALU.mult)
+            give(("bank", ("h", g)))
 
         def hidden_quantize(e):
             nc.vector.quantize_mx(
                 out=h_codes[:, e, :, :].rearrange("p g b -> p (g b)").bitcast(FP8X4),
                 scales=h_scales[:, e, :, :].rearrange("p g b -> p (g b)"),
-                in_=hid.pop(e)[:].rearrange("p g b t -> p (g b t)"))
-            give("th")
+                in_=hid.pop("grouped")[:].rearrange("p g b t -> p (g b t)"))
 
         def load_late():
             late["mix"] = place([B, D], F32, AT_TURN[0], "mix")
             late["bias"] = place([B, D], BF16, AT_TURN[0] + 4 * D, "bias_sb")
             nc.sync.dma_start(out=late["bias"][:], in_=bias.partition_broadcast(P))
             at = AT_TURN[0] + 6 * D
-            free_pass.append(at)
-            free_codes.append(at + PASS_BYTES)
+            free_stage.append(at)
+            free_codes.extend([at + SLOT, at + SLOT + CODE_BYTES])
 
         def load_rows(label, src):
             late[label] = place([B, D], BF16, take(free_stage, label), label)
@@ -480,7 +473,7 @@ def tile_dcnv2lowrankexpertcross_w_kernel(tc, x0, x, v_bytes, v_scale, c, u, bia
             acc = accs.pop((kind, e, blk, j))
             if e == 0:
                 half = CHUNKS // 2
-                mix_first(slice(0, MAIN), acc[:].rearrange("b (c w) -> b c w", c=half), slice(j * half, (j + 1) * half))
+                mix_first(slice(PLAIN_START, PLAIN_START + MAIN), acc[:].rearrange("b (c w) -> b c w", c=half), slice(j * half, (j + 1) * half))
             else:
                 mix_second(slice(blk * W + j * NB, blk * W + (j + 1) * NB), acc[:])
             give(("bank", (kind, e, blk, j)))
@@ -503,15 +496,15 @@ def tile_dcnv2lowrankexpertcross_w_kernel(tc, x0, x, v_bytes, v_scale, c, u, bia
             scales = v_scale.rearrange("o (g p t) u -> p (o g) (t u)", p=P, t=PACK)
             nc.scalar.dma_start(out=scale_first[:], in_=scales[:, :1, :])
             nc.scalar.dma_start(out=gate_sb[:], in_=gate_logits)
-            load_slab(0, [(ts, slice(hb * W, (hb + 1) * W)) for hb in range(RH) for ts, cs in whole])
+            load_slab(0, [(ts, slice(hb * W, (hb + 1) * W)) for hb in range(RH) for ts, cs in whole], AT_STAGE)
             nc.sync.dma_start(out=scale_rest[:], in_=scales[:, 1:, :])
-            load_slab(1, whole)
-            x_early = place([B, D], BF16, take(free_stage, "x"), "x_early")
+            load_slab(1, whole, AT_STAGE + SLOT)
+            x_early = place([B, D], BF16, AT_STAGE + 2 * SLOT, "x_early")
             nc.sync.dma_start(out=x_early[:], in_=x)
-            for g in range(U_PASSES):
-                load_slab(2 + g, whole)
-                load_turn(0, 2 * g)
-                load_turn(0, 2 * g + 1)
+            for g, pieces in enumerate(((0, 1), (2, 3), (4,), (5, 6), (7,))):
+                load_slab(2 + g, whole, AT_STAGE + 3 * SLOT if g == 0 else AT_TURN[1] + (g - 1) * SLOT)
+                for r in pieces:
+                    load_turn(0, r)
 
             for e in range(E):
                 nc.scalar.activation(
@@ -539,7 +532,6 @@ def tile_dcnv2lowrankexpertcross_w_kernel(tc, x0, x, v_bytes, v_scale, c, u, bia
                     out=x_grouped[:, q * W:(q + 1) * W].bitcast(F32).rearrange("p (j r w) -> p j r w", j=2, w=2),
                     in_=bank[:].rearrange("p (j w) r -> p j r w", w=2))
                 give(("bank", ("x", q)))
-            give("x")
             eye_interleave(2)
 
             def quantize_x():
@@ -560,85 +552,77 @@ def tile_dcnv2lowrankexpertcross_w_kernel(tc, x0, x, v_bytes, v_scale, c, u, bia
                     fn(*args)
 
             at(later, 0, quantize_x)
-            borrowed = range(AT_TURN[1], AT_WIDE)
-            stream = [(load_slab, (i, whole)) for i in range(6, len(slabs))] + [(load_unit, (i,)) for i in range(n_v, n) if units[i][1] == 1]
+            stage = [AT_STAGE + j * SLOT for j in range(STAGE_SLOTS)]
+            wide_at = [AT_WIDE + i % WIDE_BUFS * WIDE_BYTES for i in range(len(slabs))]
+            expert_end = [(e + 1) * n_v // E - 1 for e in range(E)]
+            turn_steps = [end + 3 for end in expert_end]
+            loads = {}
+            at(loads, 0, load_slab, 7, whole, stage[0])
+            at(loads, 0, load_slab, 8, whole, stage[1])
+            at(loads, 0, load_c)
+            at(loads, 2, load_slab, 9, whole, stage[2])
+            at(loads, 12, load_slab, 10, whole, stage[0])
+            at(loads, 14, load_slab, 11, whole, stage[1])
+            for r in range(2 * U_PASSES):
+                at(loads, 10 + r // 2, load_turn, 1, r)
+            at(loads, 14, load_pass, 0, AT_SPARE, 1)
+            at(loads, 17, load_pass, 1, stage[2], 2)
+            at(loads, 18, load_pass, 2, wide_at[9], 2)
+            at(loads, 19, load_late)
+            at(loads, 20, load_pass, 3, wide_at[10], 2)
+            at(loads, 20, free_stage.extend, stage[:2])
+            at(loads, 22, free_stage.append, wide_at[11])
+            tanh_at = (stage[3], wide_at[11] + SLOT)
+            stream = [(load_unit, (i,)) for i in range(n_v, n) if units[i][1] == 1]
             stream[-6:-6] = [(load_rows, ("x0", x0)), (load_rows, ("x", x))]
-            passes = list(range(U_PASSES))
-            h_ready = [(e + 1) * n_v // E + 4 for e in range(E)]
-            hidden_steps = [(e + 1) * n_v // E + 2 for e in range(E)]
-            lent = range(hidden_steps[0] + 2, hidden_steps[1] - 4)
-            second_from = 2 * (2 + U_PASSES) - 4
-            turned, full, waiting, quantized, first_done = [0], [], [], [], [n]
+            banks_done, full, pairs, quantized = [0], [], [], []
+            n_banks = len(turns) // T_BANK
+            per_group = T_GROUP // T_BANK
 
-            def batched(s):
-                return s >= MX_FIRST and turned[0] < len(turns)
-
-            def batch_end(s):
-                return s - s % MX_BATCH + MX_BATCH - 1 if batched(s) else s
-
+            def banks_of(s):
+                if s < T_FIRST or (s > T_FIRST and s % MX_BATCH == 0 and s < T_DENSE):
+                    return 0
+                return (2 if T_FIRST < s < long_steps else 1) - (1 if s in turn_steps else 0)
 
             for s in range(n - 1):
-                for where in [w for w in free_stage if w in borrowed]:
-                    free_stage.remove(where)
-                while stream and (s < long_steps - 4 or not passes) and len(free_stage) > (1 if s < hidden_steps[1] and "th" not in held and s not in lent else 0):
+                run(loads, s)
+                while s >= 20 and stream and free_stage:
                     fn, args = stream.pop(0)
                     fn(*args)
-                if s == 0:
-                    nc.sync.dma_start(out=c_sb[:], in_=c.rearrange("e (g p t) -> p (e g) t", p=P, t=PACK))
-                if s in range(second_from, second_from + 2 * U_PASSES):
-                    load_turn(1, s - second_from)
-                if s == second_from + 2 * U_PASSES:
-                    free_pass.append(AT_SPARE)
-                while free_pass and passes:
-                    load_pass(passes.pop(0), free_pass.pop(0))
-                for where in free_pass:
-                    free_stage.extend([where, where + SLOT])
-                free_pass.clear()
-                if "mix" not in late and turned[0] >= T_RUN[0]:
-                    load_late()
                 if s < long_steps:
                     for t in (2 * (s % 2), 2 * (s % 2) + 1):
                         widen(s // 2 + 2, t, 0, R)
                 ready = full[:]
                 full.clear()
                 run(early, s)
-                batch = quantized + [s] if batch_end(s) == s else []
-                opens = sum(0 if units[i][3] > 0 else 1 if units[i][0] == "stack" else 2 for i in batch)
-                freed = U_PASSES if s + 1 in hidden_steps or s - 1 in hidden_steps else 0
-                if s >= T_FIRST:
-                    quota = (T_LONG if s < long_steps else T_SHORT) - (T_HIDDEN if s in hidden_steps else 0)
-                    if MX_BATCH > 1 and s % MX_BATCH == 0 and s > MX_FIRST:
-                        quota = T_AFTER
-                    needed = opens + (U_PASSES if s + 1 in hidden_steps else 0) - freed
-                    for m in range(turned[0], min(len(turns), turned[0] + quota)):
-                        if m % T_BANK == 0 and min(len(free_banks), len(free_banks) + len(ready) - needed) < 1:
-                            break
+                turning = banks_done[0] < n_banks
+                for b in range(banks_done[0], min(n_banks, banks_done[0] + banks_of(s))):
+                    for m in range(b * T_BANK, (b + 1) * T_BANK):
                         turn(m)
-                        turned[0] += 1
-                        if m % T_BANK == T_BANK - 1:
-                            full.append(m // T_BANK)
+                    full.append(b)
+                    banks_done[0] += 1
                 if s + 2 < n:
                     arrange(s + 2)
                 for b in ready:
                     empty_bank(b)
-                    if b % (T_GROUP // T_BANK) == T_GROUP // T_BANK - 1:
-                        q = b // (T_GROUP // T_BANK)
-                        at(later, s + 1, quantize, ("t", q), 0, W)
+                    if b % per_group == per_group - 1:
+                        q = b // per_group
+                        at(later, s + Q_LAG, quantize, ("t", q), 0, W)
                         if q % 2 == 1 or q == n_groups - 1:
-                            waiting.append((s + 1, q - q % 2))
+                            pairs.append((s + Q_LAG, q - q % 2))
                 if s + 3 in EYE_UNITS:
                     eye_interleave(s + 3)
-                last_of_step = s in from_psum
-                if not last_of_step:
+                if s not in from_psum:
                     quantize(s, 0, W)
                 run(later, s)
-                if last_of_step:
-                    quantize(s, 0, W)
                 if s in from_psum:
-                    if s + 3 < n:
-                        pool_interleave(s + 3, POOL_LONG if s - 1 in hidden_steps else POOL_COLS)
+                    quantize(s, 0, W)
+                    pool_interleave(s + 3, POOL_COLS * len(from_psum[s]) - POOL_LESS)
                     run(from_psum, s)
                 quantized.append(s)
+                waits = turning and s >= T_FIRST and s % MX_BATCH < MX_BATCH - 1
+                batch = [] if waits else quantized[:]
+                lag = 3 if len(batch) > 1 else 2
                 for i in batch:
                     quantized.remove(i)
                     kind, e, blk, g = units[i]
@@ -646,49 +630,51 @@ def tile_dcnv2lowrankexpertcross_w_kernel(tc, x0, x, v_bytes, v_scale, c, u, bia
                         depth = W // stack_width(blk)
                         multiply_stack(i, range(depth), g == 0, g + depth == U_PASSES)
                         give(("codes", i))
-                        if g + depth == U_PASSES and blk == 0:
-                            at(later, s + 2 + LAG, mix_stack, blk, 0, stack_width(blk))
-                        elif g + depth == U_PASSES:
+                        if g + depth == U_PASSES and blk == 1:
                             mix_stack(blk, 0, stack_width(blk))
                             at(later, s + 1, cross, *stacks[blk])
-                            at(later, s + 2, finish, *stacks[blk])
                     else:
                         multiply(i)
-                    if kind == "v" and g == V_PASSES - 1 and blk == RH - 1:
-                        at(later, s + 2, hidden_tanh, e)
+                    if i in expert_end:
+                        at(later, s + 2, hidden_tanh, e, tanh_at[e])
                         at(early, s + 3, hidden_turn, e)
-                        at(from_psum, s + 4, hidden_scale, e)
+                        for g4 in range(U_PASSES):
+                            at(from_psum, s + 4, hidden_scale, e, g4, tanh_at[e])
                         at(later, s + 5, hidden_quantize, e)
                     if kind == "main" and g == U_PASSES - 1:
                         for j in range(W // NB):
-                            at(from_psum, s + 2 + LAG, mix_plain, kind, e, blk, j)
-                    if kind == "u" and g == U_PASSES - 1:
-                        assert blk == 0 or not waiting
-                        mixed = s if blk == 1 else max(s + (2 + LAG if len(batch) > 1 else 2), first_done[0])
-                        if blk == 1:
-                            pool_interleave(s + 3, POOL_COLS)
+                            at(from_psum, s + lag, mix_plain, kind, e, blk, j)
+                    if kind == "u" and g == U_PASSES - 1 and blk == 1:
+                        pool_interleave(s + 3, 2 * POOL_COLS - POOL_LESS)
                         for j in range(W // NB):
-                            if blk == 1:
-                                mix_plain(kind, e, blk, j)
-                            else:
-                                at(from_psum, mixed, mix_plain, kind, e, blk, j)
-                        at(later, mixed + 1, cross, blk * W, W)
-                        at(later, mixed + 2, finish, blk * W, W)
-                while batch and waiting and waiting[0][0] <= s and h_ready[0] <= s and "mix" in late and free_banks:
-                    step, q = waiting.pop(0)
+                            mix_plain(kind, e, blk, j)
+                        at(later, s + 1, cross, W, W)
+                        at(later, s + 2, finish, W, W)
+                while batch and pairs and pairs[0][0] <= s and s > expert_end[0] + 5:
+                    step, q = pairs.pop(0)
                     multiply_pair(q)
-                    mixed = s + (2 + LAG if len(batch) > 1 else 2)
-                    at(later, mixed, mix_pair, q)
-                    if q + 2 >= n_groups:
-                        first_done[0] = mixed
-            assert not waiting and turned[0] == len(turns) and not full
+                    if q + 2 < n_groups and q < T_GROUPS[0]:
+                        at(from_psum, expert_end[1] + 4, mix_pair, q)
+                    elif q + 2 < n_groups:
+                        at(later, s + lag, mix_pair, q)
+                    else:
+                        at(from_psum, s + 2, mix_pair, q)
+                        at(from_psum, s + 2, mix_stack, 0, 0, stack_width(0))
+                        mixed = max(s + 3, n - 2 * U_PASSES + 1)
+                        for j in range(W // NB):
+                            at(from_psum, mixed, mix_plain, "u", 1, 0, j)
+                        at(later, mixed + 1, cross, 0, W)
+                        at(later, mixed + 2, finish, 0, W)
+            assert not pairs and banks_done[0] == n_banks and not full and not stream
             quantize(n - 1, 0, NB)
-            run(later, n - 1)
+            mix_stack(2, 0, stack_width(2))
+            finish(*stacks[1])
             quantize(n - 1, W - EYE_END, W)
             multiply_stack(n - 1, [0, 1, 3], True, False)
+            cross(*stacks[2])
             quantize(n - 1, NB, W - EYE_END)
             multiply_stack(n - 1, [2], False, True)
-            run(later, n)
+            finish(*stacks[2])
             last = len(stacks) - 1
             halves = [(0, P), (P, 2 * P)]
             for lo, hi in halves:

@@ -25,7 +25,6 @@ U_PASSES = R // K_PASS
 RH = R // W
 CHUNKS = 8
 CW = D // CHUNKS
-MAIN = W // CHUNKS
 T_BANK = 8
 T_GROUP = 32
 GROUP_COLS = CHUNKS * T_GROUP
@@ -33,7 +32,7 @@ T_GROUPS = (4, 2)
 T_RUN = [T_GROUP * groups for groups in T_GROUPS]
 T_PITCH = [run + 16 for run in T_RUN]
 PLAIN = CW - sum(T_RUN)
-EXTRA = PLAIN - MAIN
+EXTRA = CHUNKS * PLAIN - W
 T_START = (0, T_RUN[0] + PLAIN)
 PLAIN_START = T_RUN[0]
 MX_BATCH = 4
@@ -117,7 +116,7 @@ def tile_dcnv2lowrankexpertcross_w_kernel(tc, x0, x, v_bytes, v_scale, c, u, bia
         n_v = len(units)
         units += [("main", 0, 0, g) for g in range(U_PASSES)]
         last_block = D - W
-        stacks = [(0, CHUNKS * EXTRA), (last_block, NB), (last_block + NB, NB // 2), (D - NB // 2, NB // 2)]
+        stacks = [(W, EXTRA), (last_block, NB), (last_block + NB, NB // 2), (D - NB // 2, NB // 2)]
 
         def stack_width(j):
             return stacks[j][1]
@@ -153,18 +152,18 @@ def tile_dcnv2lowrankexpertcross_w_kernel(tc, x0, x, v_bytes, v_scale, c, u, bia
 
         def load_pass(g, where, slots):
             pass_at[g] = [where + j * SLOT for j in range(slots)]
-            raw[n_v + g] = place([P, PACK, CHUNKS, PLAIN], BF16, where, "u_pass")
+            raw[n_v + g] = place([P, PACK, CHUNKS * PLAIN], BF16, where, "u_pass")
             nc.sync.dma_start(
-                out=raw[n_v + g][:].rearrange("p t c w -> p (t c) w"),
+                out=raw[n_v + g][:].rearrange("p t (c w) -> p (t c) w", c=CHUNKS),
                 in_=pass_rows(0, g).rearrange("(p t) (c w) -> p (t c) w", t=PACK, c=CHUNKS)[:, :, PLAIN_START:PLAIN_START + PLAIN])
 
         def load_unit(i):
             kind, e, blk, g = units[i]
             first, width = (blk * W, W) if kind == "u" else stacks[blk]
-            raw[i] = place([P, W // width, PACK, width], BF16, take(free_stage, ("raw", i)), "u_raw")
+            raw[i] = place([P, PACK, W], BF16, take(free_stage, ("raw", i)), "u_raw")
             for j in range(W // width):
                 rows = pass_rows(e, g + j).rearrange("(p t) w -> p t w", t=PACK)
-                nc.sync.dma_start(out=raw[i][:, j, :, :], in_=rows[:, :, first:first + width])
+                nc.sync.dma_start(out=raw[i][:, :, j * width:(j + 1) * width], in_=rows[:, :, first:first + width])
 
         def load_turn(k, r):
             g, h = divmod(r, 2)
@@ -214,6 +213,18 @@ def tile_dcnv2lowrankexpertcross_w_kernel(tc, x0, x, v_bytes, v_scale, c, u, bia
                 out=chunks(late["mix"][:])[:, cs, ws], in0=acc, scalar=share[:, 0:1],
                 in1=chunks(late["bias"][:])[:, cs, ws], op0=ALU.mult, op1=ALU.add)
 
+        def mix_plain_first(lo, acc):
+            for ch in range(CHUNKS):
+                a, b = max(lo, ch * PLAIN), min(lo + NB, (ch + 1) * PLAIN)
+                whole_next = b + PLAIN <= lo + NB and a == ch * PLAIN
+                whole_before = a - PLAIN >= lo and b == (ch + 1) * PLAIN
+                if a >= b or whole_before:
+                    continue
+                count = (lo + NB - a) // PLAIN if whole_next else 1
+                ws = slice(PLAIN_START + a - ch * PLAIN, PLAIN_START + b - ch * PLAIN)
+                part = acc[:, a - lo:a - lo + count * (b - a)].rearrange("b (c w) -> b c w", c=count)
+                mix_first(ws, part, slice(ch, ch + count))
+
         def mix_second(ds, acc):
             nc.vector.scalar_tensor_tensor(
                 out=late["mix"][:, ds], in0=acc, scalar=share[:, 1:2], in1=late["mix"][:, ds],
@@ -230,7 +241,7 @@ def tile_dcnv2lowrankexpertcross_w_kernel(tc, x0, x, v_bytes, v_scale, c, u, bia
         def mix_stack(j, lo, hi):
             acc = accs[("stack", j)][:, lo:hi]
             if j == 0:
-                mix_first(slice(PLAIN_START + MAIN, PLAIN_START + PLAIN), chunks(acc))
+                mix_plain_first(W, acc)
             else:
                 mix_second(slice(stacks[j][0] + lo, stacks[j][0] + hi), acc)
             if hi == stack_width(j):
@@ -267,14 +278,8 @@ def tile_dcnv2lowrankexpertcross_w_kernel(tc, x0, x, v_bytes, v_scale, c, u, bia
 
         def planes(i):
             if i >= n_v:
-                return raw[i][:, 0, :, :]
+                return raw[i][:, :, :W]
             return wide[0][:, i, :, :] if i < RH else wide[i // RH][:, :, i % RH * W:(i % RH + 1) * W]
-
-        def tail_planes(i, cols):
-            if units[i][0] == "stack":
-                width = stack_width(units[i][2])
-                return raw[i][:, W // width - 1, :, width - cols:]
-            return planes(i)[:, :, W - cols:]
 
         def eye_cols(i):
             return EYE_COLS if i in EYE_UNITS else EYE_END if i == n - 1 else 0
@@ -292,51 +297,20 @@ def tile_dcnv2lowrankexpertcross_w_kernel(tc, x0, x, v_bytes, v_scale, c, u, bia
             grouped[i] = place([P, W, PACK], BF16, take(free_grouped, ("grouped", i), newest), "grouped")
             return grouped[i]
 
-        def stack_views(i):
-            depth = W // stack_width(units[i][2])
-            return (grouped[i][:].rearrange("p (g c i) t -> p g c t i", g=depth, i=2),
-                    raw[i][:].rearrange("p g t (c i) -> p g c t i", i=2), depth)
-
-        def arrange_stack(i):
-            helped = i in grouped
-            if not helped:
-                take_grouped(i)
-            dst, src, depth = stack_views(i)
-            a = vector_share(i) // (2 * depth)
-            if a > 0:
-                nc.vector.tensor_copy(out=dst[:, :, :a, :, :], in_=src[:, :, :a, :, :])
-            if helped:
-                b = (W // depth - pooled[i]) // 2
-                nc.scalar.copy(out=dst[:, :depth - 1, a:, :, :], in_=src[:, :depth - 1, a:, :, :])
-                nc.scalar.copy(out=dst[:, depth - 1, a:b, :, :], in_=src[:, depth - 1, a:b, :, :])
-            else:
-                nc.scalar.copy(out=dst[:, :, a:, :, :], in_=src[:, :, a:, :, :])
-
-        def arrange_main(i):
-            dst = take_grouped(i)[:].rearrange("p (c w i) t -> p c w t i", c=CHUNKS, i=2)
-            src = raw[i][:, :, :, :MAIN].rearrange("p t c (w i) -> p c w t i", i=2)
-            a = vector_share(i) // (2 * CHUNKS)
-            nc.vector.tensor_copy(out=dst[:, :, :a, :, :], in_=src[:, :, :a, :, :])
-            nc.scalar.copy(out=dst[:, :, a:, :, :], in_=src[:, :, a:, :, :])
-
         def arrange_extra(i):
-            depth = W // stack_width(0)
-            dst = take_grouped(i)[:].rearrange("p (g c w i) t -> p g c w t i", g=depth, c=CHUNKS, i=2)
+            depth = W // EXTRA
+            dst = take_grouped(i)
             for j in range(depth):
-                src = raw[n_v + units[i][3] + j][:, :, :, MAIN:].rearrange("p t c (w i) -> p c w t i", i=2)
                 copy = nc.vector.tensor_copy if j < depth // 2 else nc.scalar.copy
-                copy(out=dst[:, j, :, :, :, :], in_=src)
+                interleave(copy, dst[:, j * EXTRA:(j + 1) * EXTRA, :], raw[n_v + units[i][3] + j][:, :, W:])
                 free_stage.extend(pass_at[units[i][3] + j])
 
         def arrange_last(i):
-            if i not in grouped:
-                take_grouped(i)
-            dst, src, depth = stack_views(i)
+            dst = take_grouped(i)
             eye_interleave(i)
-            nc.scalar.copy(out=dst[:, :2, :, :, :], in_=src[:, :2, :, :, :])
+            interleave(nc.scalar.copy, dst[:, :NB, :], planes(i)[:, :, :NB])
             empty_eye(i)
-            b = (W // depth - pooled.get(i, 0)) // 2
-            nc.scalar.copy(out=dst[:, 2, :b, :, :], in_=src[:, 2, :b, :, :])
+            interleave(nc.scalar.copy, dst[:, NB:W - EYE_END, :], planes(i)[:, :, NB:W - EYE_END])
 
         def empty_eye(i):
             for j, bank in enumerate(eye_out.pop(i, [])):
@@ -360,12 +334,8 @@ def tile_dcnv2lowrankexpertcross_w_kernel(tc, x0, x, v_bytes, v_scale, c, u, bia
         def arrange(i):
             if i == n - 1:
                 arrange_last(i)
-            elif units[i][0] == "main":
-                arrange_main(i)
             elif units[i][:2] == ("stack", 0):
                 arrange_extra(i)
-            elif units[i][0] == "stack":
-                arrange_stack(i)
             else:
                 arrange_plain(i)
             if ("raw", i) in held:
@@ -378,14 +348,10 @@ def tile_dcnv2lowrankexpertcross_w_kernel(tc, x0, x, v_bytes, v_scale, c, u, bia
             dst = take_grouped(i, newest=True)
             pooled[i] = cols
             hi = W - eye_cols(i)
-            if i == n - 1:
-                src = raw[i][:, 2, :, EYE_END - cols:]
-            else:
-                src = tail_planes(i, W - hi + cols)[:, :, :cols]
-            interleave(pool_copy, dst[:, hi - cols:hi, :], src)
+            interleave(pool_copy, dst[:, hi - cols:hi, :], planes(i)[:, :, hi - cols:hi])
 
         def eye_interleave(i):
-            src = tail_planes(i, eye_cols(i))
+            src = planes(i)[:, :, W - eye_cols(i):]
             eye_out[i] = []
             for j in range(eye_cols(i) // (2 * P)):
                 bank = take_bank(("eye", i, j), [P, 2 * NB], BF16)
@@ -472,8 +438,7 @@ def tile_dcnv2lowrankexpertcross_w_kernel(tc, x0, x, v_bytes, v_scale, c, u, bia
         def mix_plain(kind, e, blk, j):
             acc = accs.pop((kind, e, blk, j))
             if e == 0:
-                half = CHUNKS // 2
-                mix_first(slice(PLAIN_START, PLAIN_START + MAIN), acc[:].rearrange("b (c w) -> b c w", c=half), slice(j * half, (j + 1) * half))
+                mix_plain_first(j * NB, acc[:])
             else:
                 mix_second(slice(blk * W + j * NB, blk * W + (j + 1) * NB), acc[:])
             give(("bank", (kind, e, blk, j)))

@@ -45,7 +45,7 @@ T_DENSE = 99
 Q_LAG = 2
 SHARE_V = 400
 SHARE_HEAD = 192
-SHARE_FREE = 432
+SHARE_FREE = 416
 SHARE_END = 0
 POOL_COLS = 72
 POOL_LESS = 40
@@ -114,7 +114,6 @@ def tile_dcnv2lowrankexpertcross_w_kernel(tc, x0, x, v_bytes, v_scale, c, u, bia
         slabs = [(e, g) for e in range(E) for g in range(V_PASSES)]
         units = [("v", e, hb, g) for e, g in slabs for hb in range(RH)]
         n_v = len(units)
-        units += [("main", 0, 0, g) for g in range(U_PASSES)]
         last_block = D - W
         stacks = [(W, EXTRA), (last_block, NB), (last_block + NB, NB // 2), (D - NB // 2, NB // 2)]
 
@@ -124,7 +123,9 @@ def tile_dcnv2lowrankexpertcross_w_kernel(tc, x0, x, v_bytes, v_scale, c, u, bia
         def stack_units(j):
             return [("stack", min(j, 1), j, g) for g in range(0, U_PASSES, W // stack_width(j))]
 
-        units += stack_units(0) + [("u", 1, db, g) for db in range(2) for g in range(U_PASSES)]
+        for extra in stack_units(0):
+            units += [("main", 0, 0, g) for g in range(extra[3], extra[3] + W // EXTRA)] + [extra]
+        units += [("u", 1, db, g) for db in range(2) for g in range(U_PASSES)]
         units += stack_units(1) + stack_units(2) + stack_units(3)
         n = len(units)
         long_steps = 2 * (len(slabs) - 2)
@@ -152,9 +153,10 @@ def tile_dcnv2lowrankexpertcross_w_kernel(tc, x0, x, v_bytes, v_scale, c, u, bia
 
         def load_pass(g, where, slots):
             pass_at[g] = [where + j * SLOT for j in range(slots)]
-            raw[n_v + g] = place([P, PACK, CHUNKS * PLAIN], BF16, where, "u_pass")
+            i = units.index(("main", 0, 0, g))
+            raw[i] = place([P, PACK, CHUNKS * PLAIN], BF16, where, "u_pass")
             nc.sync.dma_start(
-                out=raw[n_v + g][:].rearrange("p t (c w) -> p (t c) w", c=CHUNKS),
+                out=raw[i][:].rearrange("p t (c w) -> p (t c) w", c=CHUNKS),
                 in_=pass_rows(0, g).rearrange("(p t) (c w) -> p (t c) w", t=PACK, c=CHUNKS)[:, :, PLAIN_START:PLAIN_START + PLAIN])
 
         def load_unit(i):
@@ -302,7 +304,7 @@ def tile_dcnv2lowrankexpertcross_w_kernel(tc, x0, x, v_bytes, v_scale, c, u, bia
             dst = take_grouped(i)
             for j in range(depth):
                 copy = nc.vector.tensor_copy if j < depth // 2 else nc.scalar.copy
-                interleave(copy, dst[:, j * EXTRA:(j + 1) * EXTRA, :], raw[n_v + units[i][3] + j][:, :, W:])
+                interleave(copy, dst[:, j * EXTRA:(j + 1) * EXTRA, :], raw[i - depth + j][:, :, W:])
                 free_stage.extend(pass_at[units[i][3] + j])
 
         def arrange_last(i):
@@ -426,10 +428,12 @@ def tile_dcnv2lowrankexpertcross_w_kernel(tc, x0, x, v_bytes, v_scale, c, u, bia
         def load_late():
             late["mix"] = place([B, D], F32, AT_TURN[0], "mix")
             late["bias"] = place([B, D], BF16, AT_TURN[0] + 4 * D, "bias_sb")
-            nc.sync.dma_start(out=late["bias"][:], in_=bias.partition_broadcast(P))
             at = AT_TURN[0] + 6 * D
             free_stage.append(at)
             free_codes.extend([at + SLOT, at + SLOT + CODE_BYTES])
+
+        def load_bias():
+            nc.sync.dma_start(out=late["bias"][:], in_=bias.partition_broadcast(P))
 
         def load_rows(label, src):
             late[label] = place([B, D], BF16, take(free_stage, label), label)
@@ -529,12 +533,13 @@ def tile_dcnv2lowrankexpertcross_w_kernel(tc, x0, x, v_bytes, v_scale, c, u, bia
             at(loads, 12, load_slab, 10, whole, stage[0])
             at(loads, 14, load_slab, 11, whole, stage[1])
             for r in range(2 * U_PASSES):
-                at(loads, 10 + r // 2, load_turn, 1, r)
-            at(loads, 14, load_pass, 0, AT_SPARE, 1)
+                at(loads, 8 + r // 2, load_turn, 1, r)
+            at(loads, 12, load_pass, 0, AT_SPARE, 1)
             at(loads, 17, load_pass, 1, stage[2], 2)
             at(loads, 18, load_pass, 2, wide_at[9], 2)
             at(loads, 19, load_late)
             at(loads, 20, load_pass, 3, wide_at[10], 2)
+            at(loads, 20, load_bias)
             at(loads, 20, free_stage.extend, stage[:2])
             at(loads, 22, free_stage.append, wide_at[11])
             tanh_at = (stage[3], wide_at[11] + SLOT)

@@ -30,7 +30,7 @@ T_GROUP = 32
 GROUP_COLS = CHUNKS * T_GROUP
 T_GROUPS = (4, 2)
 T_RUN = [T_GROUP * groups for groups in T_GROUPS]
-T_PITCH = [run + 16 for run in T_RUN]
+T_PITCH = [144, 144]
 PLAIN = CW - sum(T_RUN)
 EXTRA = CHUNKS * PLAIN - W
 T_START = (0, T_RUN[0] + PLAIN)
@@ -60,8 +60,7 @@ GROUPED_SLOTS = 5
 CODE_SLOTS = 7
 CODE_BYTES = 5 * W
 AT_TURN = (0, T_BYTES[0])
-AT_SPARE = sum(T_BYTES)
-AT_WIDE = AT_SPARE + PASS_BYTES
+AT_WIDE = sum(T_BYTES)
 AT_STAGE = AT_WIDE + WIDE_BUFS * WIDE_BYTES
 AT_GROUPED = AT_STAGE + STAGE_SLOTS * SLOT
 AT_CODES = AT_GROUPED + GROUPED_SLOTS * SLOT
@@ -410,9 +409,9 @@ def tile_dcnv2lowrankexpertcross_w_kernel(tc, x0, x, v_bytes, v_scale, c, u, bia
                 turned_h.append(bank)
             hid[e] = turned_h
 
-        def hidden_scale(e, g, where):
+        def hidden_scale(e, g):
             if g == 0:
-                hid["grouped"] = place([P, U_PASSES, B, PACK], BF16, where, "hg")
+                hid["grouped"] = place([P, U_PASSES, B, PACK], BF16, take(free_codes, "hg"), "hg")
             at_c = e * U_PASSES + g
             nc.vector.tensor_tensor(
                 out=hid["grouped"][:, g, :, :], in0=hid[e][g][:].rearrange("p t b -> p b t"),
@@ -424,13 +423,12 @@ def tile_dcnv2lowrankexpertcross_w_kernel(tc, x0, x, v_bytes, v_scale, c, u, bia
                 out=h_codes[:, e, :, :].rearrange("p g b -> p (g b)").bitcast(FP8X4),
                 scales=h_scales[:, e, :, :].rearrange("p g b -> p (g b)"),
                 in_=hid.pop("grouped")[:].rearrange("p g b t -> p (g b t)"))
+            give("hg")
 
         def load_late():
             late["mix"] = place([B, D], F32, AT_TURN[0], "mix")
             late["bias"] = place([B, D], BF16, AT_TURN[0] + 4 * D, "bias_sb")
-            at = AT_TURN[0] + 6 * D
-            free_stage.append(at)
-            free_codes.extend([at + SLOT, at + SLOT + CODE_BYTES])
+            free_codes.append(AT_TURN[0] + 6 * D + PASS_BYTES)
 
         def load_bias():
             nc.sync.dma_start(out=late["bias"][:], in_=bias.partition_broadcast(P))
@@ -533,11 +531,11 @@ def tile_dcnv2lowrankexpertcross_w_kernel(tc, x0, x, v_bytes, v_scale, c, u, bia
             at(loads, 12, load_slab, 10, whole, stage[0])
             at(loads, 14, load_slab, 11, whole, stage[1])
             for r in range(2 * U_PASSES):
-                at(loads, 8 + r // 2, load_turn, 1, r)
-            at(loads, 12, load_pass, 0, AT_SPARE, 1)
-            at(loads, 17, load_pass, 1, stage[2], 2)
-            at(loads, 18, load_pass, 2, wide_at[9], 2)
+                at(loads, 10 + r // 2, load_turn, 1, r)
+            at(loads, 16, load_pass, 0, stage[2], 2)
+            at(loads, 18, load_pass, 1, wide_at[9], 2)
             at(loads, 19, load_late)
+            at(loads, 19, load_pass, 2, AT_TURN[0] + 6 * D, 1)
             at(loads, 20, load_pass, 3, wide_at[10], 2)
             at(loads, 20, load_bias)
             at(loads, 20, free_stage.extend, stage[:2])
@@ -609,7 +607,7 @@ def tile_dcnv2lowrankexpertcross_w_kernel(tc, x0, x, v_bytes, v_scale, c, u, bia
                         at(later, s + 2, hidden_tanh, e, tanh_at[e])
                         at(early, s + 3, hidden_turn, e)
                         for g4 in range(U_PASSES):
-                            at(from_psum, s + 4, hidden_scale, e, g4, tanh_at[e])
+                            at(from_psum, s + 4, hidden_scale, e, g4)
                         at(later, s + 5, hidden_quantize, e)
                     if kind == "main" and g == U_PASSES - 1:
                         for j in range(W // NB):

@@ -20,50 +20,55 @@ ALU = mybir.AluOpType
 
 W = 1024
 NB = 512
+BANKS = 8
 V_PASSES = D // K_PASS
 U_PASSES = R // K_PASS
 RH = R // W
+
 CHUNKS = 8
 CW = D // CHUNKS
+T_RUN = (128, 64)
+T_PITCH = 144
+PLAIN = CW - sum(T_RUN)
+PLAIN_START = T_RUN[0]
+T_START = (0, PLAIN_START + PLAIN)
+EXTRA = CHUNKS * PLAIN - W
 T_BANK = 8
 T_GROUP = 32
 GROUP_COLS = CHUNKS * T_GROUP
-T_GROUPS = (4, 2)
-T_RUN = [T_GROUP * groups for groups in T_GROUPS]
-T_PITCH = [144, 144]
-PLAIN = CW - sum(T_RUN)
-EXTRA = CHUNKS * PLAIN - W
-T_START = (0, T_RUN[0] + PLAIN)
-PLAIN_START = T_RUN[0]
-MX_BATCH = 4
+T_PIECES = 2 * U_PASSES
 
 EYE_UNITS = range(1, 10)
 EYE_COLS = 512
 EYE_END = 256
 T_FIRST = 8
-T_DENSE = 99
-Q_LAG = 2
-SHARE_V = 400
+MX_BATCH = 4
+AFTER_BATCH = 3
+GROUP_LAG = 2
+
 SHARE_HEAD = 192
-SHARE_FREE = 416
-SHARE_END = 0
+SHARE_V = 400
+SHARE_U = 416
 POOL_COLS = 72
 POOL_LESS = 40
 
 SLOT = PACK * W * 2
-T_BYTES = [P * pitch * 2 for pitch in T_PITCH]
+T_BYTES = P * T_PITCH * 2
 PASS_BYTES = PACK * CHUNKS * PLAIN * 2
 WIDE_BYTES = PACK * R * 2
+CODE_BYTES = 5 * W
 WIDE_BUFS = 3
 STAGE_SLOTS = 4
 GROUPED_SLOTS = 5
 CODE_SLOTS = 7
-CODE_BYTES = 5 * W
-AT_TURN = (0, T_BYTES[0])
-AT_WIDE = sum(T_BYTES)
+AT_TURN = (0, T_BYTES)
+AT_WIDE = 2 * T_BYTES
 AT_STAGE = AT_WIDE + WIDE_BUFS * WIDE_BYTES
 AT_GROUPED = AT_STAGE + STAGE_SLOTS * SLOT
 AT_CODES = AT_GROUPED + GROUPED_SLOTS * SLOT
+AT_MIX = AT_TURN[0]
+AT_BIAS = AT_MIX + 4 * D
+AT_PASS = AT_BIAS + 2 * D
 
 
 def tile_dcnv2lowrankexpertcross_w_kernel(tc, x0, x, v_bytes, v_scale, c, u, bias, gate_logits, out):
@@ -80,7 +85,7 @@ def tile_dcnv2lowrankexpertcross_w_kernel(tc, x0, x, v_bytes, v_scale, c, u, bia
         scale_rest = const.tile([P, V_PASSES - 1, PACK], F32)
         c_sb = const.tile([P, E * U_PASSES, PACK], BF16)
         gate_sb = const.tile([B, E], BF16)
-        share = const.tile([B, E], F32)
+        prob = const.tile([B, E], F32)
         x_codes = const.tile([P, V_PASSES, B], U32, align_bytes=64)
         x_scales = const.tile([P, V_PASSES, B], U8, align_bytes=64)
         h_codes = const.tile([P, E, U_PASSES, B], U32, align_bytes=64)
@@ -92,11 +97,10 @@ def tile_dcnv2lowrankexpertcross_w_kernel(tc, x0, x, v_bytes, v_scale, c, u, bia
             made.append(label)
             return arena.tile(shape, dtype, offset=offset, align_bytes=64, name="%s%d" % (label, len(made)))
 
-        free_banks = list(range(8))
+        free_banks = list(range(BANKS))
         free_stage = []
         free_grouped = [AT_GROUPED + j * SLOT for j in range(GROUPED_SLOTS)]
         free_codes = [AT_CODES + j * CODE_BYTES for j in range(CODE_SLOTS)]
-        pass_at = {}
         held = {}
 
         def take(free, key, newest=False):
@@ -113,50 +117,58 @@ def tile_dcnv2lowrankexpertcross_w_kernel(tc, x0, x, v_bytes, v_scale, c, u, bia
         slabs = [(e, g) for e in range(E) for g in range(V_PASSES)]
         units = [("v", e, hb, g) for e, g in slabs for hb in range(RH)]
         n_v = len(units)
-        last_block = D - W
-        stacks = [(W, EXTRA), (last_block, NB), (last_block + NB, NB // 2), (D - NB // 2, NB // 2)]
+        stacks = [(W, EXTRA), (D - W, NB), (D - NB, NB // 2), (D - NB // 2, NB // 2)]
 
-        def stack_width(j):
-            return stacks[j][1]
+        def stack_depth(j):
+            return W // stacks[j][1]
 
         def stack_units(j):
-            return [("stack", min(j, 1), j, g) for g in range(0, U_PASSES, W // stack_width(j))]
+            return [("stack", min(j, 1), j, g) for g in range(0, U_PASSES, stack_depth(j))]
 
         for extra in stack_units(0):
-            units += [("main", 0, 0, g) for g in range(extra[3], extra[3] + W // EXTRA)] + [extra]
-        units += [("u", 1, db, g) for db in range(2) for g in range(U_PASSES)]
+            units += [("main", 0, 0, g) for g in range(extra[3], extra[3] + stack_depth(0))] + [extra]
+        units += [("u", 1, db, g) for db in range(D // W - 1) for g in range(U_PASSES)]
         units += stack_units(1) + stack_units(2) + stack_units(3)
         n = len(units)
-        long_steps = 2 * (len(slabs) - 2)
-        raw, slab_raw, wide, grouped, codes, accs, hid, eye_out, t_banks, turn_sb, late = {}, {}, {}, {}, {}, {}, {}, {}, {}, {}, {}
-
-        pooled = {}
+        long_steps = RH * (len(slabs) - 2)
+        turns = [(k, l) for k in range(len(T_RUN)) for l in range(T_RUN[k])]
+        n_banks = len(turns) // T_BANK
+        per_group = T_GROUP // T_BANK
+        raw, slab_raw, wide, grouped, codes, accs, hid = {}, {}, {}, {}, {}, {}, {}
+        eye_out, t_banks, turn_sb, late, pooled, pass_slots = {}, {}, {}, {}, {}, {}
 
         def chunks(ap):
             return ap.rearrange("b (c w) -> b c w", c=CHUNKS)
 
-        def load_slab(i, pieces, where):
+        whole = [(slice(0, 2), slice(0, R)), (slice(2, 4), slice(0, R))]
+
+        def load_slab(i, where, pieces=whole):
             e, g = slabs[i]
             slab_raw[i] = place([P, PACK, R], U8, where, "v_raw")
             rows = v_bytes[e, g * K_PASS:(g + 1) * K_PASS, :].rearrange("(p t) w -> p t w", t=PACK)
             for ts, cs in pieces:
                 nc.sync.dma_start(out=slab_raw[i][:, ts, cs], in_=rows[:, ts, cs])
 
-        whole = [(slice(0, 2), slice(0, R)), (slice(2, 4), slice(0, R))]
-
         def pass_rows(e, g):
             return u[e, g * K_PASS:(g + 1) * K_PASS, :]
 
-        def load_c():
-            nc.sync.dma_start(out=c_sb[:], in_=c.rearrange("e (g p t) -> p (e g) t", p=P, t=PACK))
+        def load_turn(k, r):
+            g, half = divmod(r, 2)
+            if k not in turn_sb:
+                turn_sb[k] = place([P, P, T_PITCH], BF16, AT_TURN[k], "u_turn")
+            src = pass_rows(0, g).rearrange("(p t) (c w) -> (t c) p w", t=PACK, c=CHUNKS)
+            ps = slice(half * P // 2, (half + 1) * P // 2)
+            nc.sync.dma_start(
+                out=turn_sb[k][g:P:U_PASSES, ps, :T_RUN[k]], in_=src[:, ps, T_START[k]:T_START[k] + T_RUN[k]])
 
         def load_pass(g, where, slots):
-            pass_at[g] = [where + j * SLOT for j in range(slots)]
+            pass_slots[g] = [where + j * SLOT for j in range(slots)]
             i = units.index(("main", 0, 0, g))
             raw[i] = place([P, PACK, CHUNKS * PLAIN], BF16, where, "u_pass")
+            src = pass_rows(0, g).rearrange("(p t) (c w) -> p (t c) w", t=PACK, c=CHUNKS)
             nc.sync.dma_start(
                 out=raw[i][:].rearrange("p t (c w) -> p (t c) w", c=CHUNKS),
-                in_=pass_rows(0, g).rearrange("(p t) (c w) -> p (t c) w", t=PACK, c=CHUNKS)[:, :, PLAIN_START:PLAIN_START + PLAIN])
+                in_=src[:, :, PLAIN_START:PLAIN_START + PLAIN])
 
         def load_unit(i):
             kind, e, blk, g = units[i]
@@ -166,102 +178,23 @@ def tile_dcnv2lowrankexpertcross_w_kernel(tc, x0, x, v_bytes, v_scale, c, u, bia
                 rows = pass_rows(e, g + j).rearrange("(p t) w -> p t w", t=PACK)
                 nc.sync.dma_start(out=raw[i][:, :, j * width:(j + 1) * width], in_=rows[:, :, first:first + width])
 
-        def load_turn(k, r):
-            g, h = divmod(r, 2)
-            if k not in turn_sb:
-                turn_sb[k] = place([P, P, T_PITCH[k]], BF16, AT_TURN[k], "u_turn")
-            src = pass_rows(0, g).rearrange("(p t) (c w) -> (t c) p w", t=PACK, c=CHUNKS)
-            ps = slice(h * P // 2, (h + 1) * P // 2)
-            nc.sync.dma_start(
-                out=turn_sb[k][g:P:U_PASSES, ps, :T_RUN[k]], in_=src[:, ps, T_START[k]:T_START[k] + T_RUN[k]])
+        def load_c():
+            nc.sync.dma_start(out=c_sb[:], in_=c.rearrange("e (g p t) -> p (e g) t", p=P, t=PACK))
 
-        turns = [(k, l) for k in range(2) for l in range(T_RUN[k])]
-        n_groups = sum(T_GROUPS)
+        def load_bias():
+            nc.sync.dma_start(out=late["bias"][:], in_=bias.partition_broadcast(P))
 
-        def turn(m):
-            k, l = turns[m]
-            b = m // T_BANK
-            if b not in t_banks:
-                t_banks[b] = take_bank(("t", b), [P, U_PASSES, T_BANK, CHUNKS * PACK], BF16)
-            nc.tensor.transpose(t_banks[b][:, :, m % T_BANK, :], turn_sb[k][:, :, l], perm16[:])
+        def load_rows(label, src):
+            late[label] = place([B, D], BF16, take(free_stage, label), label)
+            nc.sync.dma_start(out=late[label][:], in_=src)
 
-        def empty_bank(b):
-            per = T_GROUP // T_BANK
-            key = ("t", b // per)
-            if key not in grouped:
-                grouped[key] = place([P, W, PACK], BF16, take(free_grouped, ("grouped", key)), "grouped")
-            dst = grouped[key][:].rearrange("p (g q w) t -> p g q (w t)", g=U_PASSES, q=per)
-            nc.scalar.copy(
-                out=dst[:, :, b % per, :].bitcast(F32),
-                in_=t_banks.pop(b)[:].rearrange("p g l x -> p g (l x)").bitcast(F32))
-            give(("bank", ("t", b)))
+        def reuse_first_turned():
+            late["mix"] = place([B, D], F32, AT_MIX, "mix")
+            late["bias"] = place([B, D], BF16, AT_BIAS, "bias_sb")
+            free_codes.append(AT_PASS + PASS_BYTES)
+            load_pass(2, AT_PASS, 1)
 
-        def multiply_pair(q):
-            acc = take_bank(("pair", q), [B, NB], F32)
-            for j in range(min(2, n_groups - q)):
-                w_codes, w_scales = codes.pop(("t", q + j))
-                for g in range(U_PASSES):
-                    cs = slice(g * GROUP_COLS, (g + 1) * GROUP_COLS)
-                    nc.tensor.matmul_mx(
-                        out=acc[:, j * GROUP_COLS:(j + 1) * GROUP_COLS], lhsT=h_codes[:, 0, g, :].bitcast(FP8X4),
-                        lhsT_scale=h_scales[:, 0, g, :], rhs=w_codes[:, cs].bitcast(FP8X4), rhs_scale=w_scales[:, cs],
-                        start=(g == 0), stop=(g == U_PASSES - 1))
-                give(("codes", ("t", q + j)))
-            accs[("pair", q)] = acc
-
-        def mix_first(ws, acc, cs=slice(0, CHUNKS)):
-            nc.vector.scalar_tensor_tensor(
-                out=chunks(late["mix"][:])[:, cs, ws], in0=acc, scalar=share[:, 0:1],
-                in1=chunks(late["bias"][:])[:, cs, ws], op0=ALU.mult, op1=ALU.add)
-
-        def mix_plain_first(lo, acc):
-            for ch in range(CHUNKS):
-                a, b = max(lo, ch * PLAIN), min(lo + NB, (ch + 1) * PLAIN)
-                whole_next = b + PLAIN <= lo + NB and a == ch * PLAIN
-                whole_before = a - PLAIN >= lo and b == (ch + 1) * PLAIN
-                if a >= b or whole_before:
-                    continue
-                count = (lo + NB - a) // PLAIN if whole_next else 1
-                ws = slice(PLAIN_START + a - ch * PLAIN, PLAIN_START + b - ch * PLAIN)
-                part = acc[:, a - lo:a - lo + count * (b - a)].rearrange("b (c w) -> b c w", c=count)
-                mix_first(ws, part, slice(ch, ch + count))
-
-        def mix_second(ds, acc):
-            nc.vector.scalar_tensor_tensor(
-                out=late["mix"][:, ds], in0=acc, scalar=share[:, 1:2], in1=late["mix"][:, ds],
-                op0=ALU.mult, op1=ALU.add)
-
-        def mix_pair(q):
-            count = min(2, n_groups - q) * T_GROUP
-            k, l = turns[q * T_GROUP]
-            first = T_START[k] + l
-            acc = accs.pop(("pair", q))[:, :count * CHUNKS]
-            mix_first(slice(first, first + count), acc.rearrange("b (l c) -> b c l", c=CHUNKS))
-            give(("bank", ("pair", q)))
-
-        def mix_stack(j, lo, hi):
-            acc = accs[("stack", j)][:, lo:hi]
-            if j == 0:
-                mix_plain_first(W, acc)
-            else:
-                mix_second(slice(stacks[j][0] + lo, stacks[j][0] + hi), acc)
-            if hi == stack_width(j):
-                give(("bank", ("stack", j)))
-
-        def multiply_stack(i, slots, opens, closes):
-            kind, e, j, first = units[i]
-            width = stack_width(j)
-            w_codes, w_scales = codes[i]
-            if opens:
-                accs[("stack", j)] = take_bank(("stack", j), [B, NB], F32)
-            for m in slots:
-                cs = slice(m * width, (m + 1) * width)
-                nc.tensor.matmul_mx(
-                    out=accs[("stack", j)][:, :width], lhsT=h_codes[:, e, first + m, :].bitcast(FP8X4),
-                    lhsT_scale=h_scales[:, e, first + m, :], rhs=w_codes[:, cs].bitcast(FP8X4),
-                    rhs_scale=w_scales[:, cs], start=(opens and m == slots[0]), stop=(closes and m == slots[-1]))
-
-        def widen(i, t, lo, hi, on_act=False):
+        def widen(i, t, lo, hi, on_scalar=False):
             g = slabs[i][1]
             if i not in wide:
                 shape = [P, RH, PACK, W] if i == 0 else [P, PACK, R]
@@ -269,87 +202,47 @@ def tile_dcnv2lowrankexpertcross_w_kernel(tc, x0, x, v_bytes, v_scale, c, u, bia
             src = slab_raw[i][:, t, lo:hi].bitcast(FP8)
             dst = wide[i][:, lo // W, t, :] if i == 0 else wide[i][:, t, lo:hi]
             scale = scale_first[:, 0, t:t + 1] if g == 0 else scale_rest[:, g - 1, t:t + 1]
-            if on_act:
+            if on_scalar:
                 nc.scalar.activation(out=dst, in_=src, func=ACT.Copy, scale=scale)
             else:
                 nc.vector.tensor_scalar(out=dst, in0=src, scalar1=scale, scalar2=None, op0=ALU.mult)
-
-        def interleave(copy, dst, src):
-            copy(out=dst.rearrange("p (c i) t -> p c t i", i=2), in_=src.rearrange("p t (c i) -> p c t i", i=2))
 
         def planes(i):
             if i >= n_v:
                 return raw[i][:, :, :W]
             return wide[0][:, i, :, :] if i < RH else wide[i // RH][:, :, i % RH * W:(i % RH + 1) * W]
 
+        def interleave(copy, dst, src):
+            copy(out=dst.rearrange("p (c i) t -> p c t i", i=2), in_=src.rearrange("p t (c i) -> p c t i", i=2))
+
+        def interleave_vector(dst, src):
+            nc.vector.tensor_copy(
+                out=dst.rearrange("p (c h i) t -> p h c t i", h=2, i=2),
+                in_=src.rearrange("p t (c h i) -> p h c t i", h=2, i=2))
+
+        def pool_copy(out, in_):
+            nc.gpsimd.tensor_scalar(out=out, in0=in_, scalar1=1.0, scalar2=0.0, op0=ALU.mult, op1=ALU.add)
+
         def eye_cols(i):
             return EYE_COLS if i in EYE_UNITS else EYE_END if i == n - 1 else 0
 
         def vector_share(i):
             if i >= n - U_PASSES:
-                return SHARE_END
+                return 0
             if i >= long_steps + 2:
-                return SHARE_FREE
+                return SHARE_U
             if i < RH:
                 return SHARE_HEAD
             return SHARE_V if i % RH == 1 and i not in EYE_UNITS else 0
 
-        def take_grouped(i, newest=False):
-            grouped[i] = place([P, W, PACK], BF16, take(free_grouped, ("grouped", i), newest), "grouped")
-            return grouped[i]
+        def take_grouped(key, newest=False):
+            grouped[key] = place([P, W, PACK], BF16, take(free_grouped, ("grouped", key), newest), "grouped")
+            return grouped[key]
 
-        def arrange_extra(i):
-            depth = W // EXTRA
-            dst = take_grouped(i)
-            for j in range(depth):
-                copy = nc.vector.tensor_copy if j < depth // 2 else nc.scalar.copy
-                interleave(copy, dst[:, j * EXTRA:(j + 1) * EXTRA, :], raw[i - depth + j][:, :, W:])
-                free_stage.extend(pass_at[units[i][3] + j])
-
-        def arrange_last(i):
-            dst = take_grouped(i)
-            eye_interleave(i)
-            interleave(nc.scalar.copy, dst[:, :NB, :], planes(i)[:, :, :NB])
-            empty_eye(i)
-            interleave(nc.scalar.copy, dst[:, NB:W - EYE_END, :], planes(i)[:, :, NB:W - EYE_END])
-
-        def empty_eye(i):
-            for j, bank in enumerate(eye_out.pop(i, [])):
-                first = W - eye_cols(i) + j * 2 * P
-                nc.scalar.copy(
-                    out=grouped[i][:, first:first + 2 * P, :].rearrange("p w t -> p (w t)").bitcast(F32),
-                    in_=bank[:].bitcast(F32))
-                give(("bank", ("eye", i, j)))
-
-        def arrange_plain(i):
-            helped = i in grouped
-            dst = grouped[i] if helped else take_grouped(i)
-            src = planes(i)
-            a = vector_share(i)
-            b = W - eye_cols(i) - pooled.get(i, 0)
-            if a > 0 and i > 0:
-                interleave(nc.vector.tensor_copy, dst[:, :a, :], src[:, :, :a])
-            interleave(nc.scalar.copy, dst[:, a:b, :], src[:, :, a:b])
-            empty_eye(i)
-
-        def arrange(i):
-            if i == n - 1:
-                arrange_last(i)
-            elif units[i][:2] == ("stack", 0):
-                arrange_extra(i)
-            else:
-                arrange_plain(i)
-            if ("raw", i) in held:
-                give(("raw", i))
-
-        def pool_copy(out, in_):
-            nc.gpsimd.tensor_scalar(out=out, in0=in_, scalar1=1.0, scalar2=0.0, op0=ALU.mult, op1=ALU.add)
-
-        def pool_interleave(i, cols):
-            dst = take_grouped(i, newest=True)
-            pooled[i] = cols
-            hi = W - eye_cols(i)
-            interleave(pool_copy, dst[:, hi - cols:hi, :], planes(i)[:, :, hi - cols:hi])
+        def pool_interleave(i, reads):
+            pooled[i] = POOL_COLS * reads - POOL_LESS
+            cs = slice(W - pooled[i], W)
+            interleave(pool_copy, take_grouped(i, newest=True)[:, cs, :], planes(i)[:, :, cs])
 
         def eye_interleave(i):
             src = planes(i)[:, :, W - eye_cols(i):]
@@ -363,7 +256,67 @@ def tile_dcnv2lowrankexpertcross_w_kernel(tc, x0, x, v_bytes, v_scale, c, u, bia
                         rhs=src[:, :, first:first + P].rearrange("p t w -> p w t"), start=True, stop=True)
                 eye_out[i].append(bank)
 
-        def quantize(key, lo, hi):
+        def empty_eye(i):
+            for j, bank in enumerate(eye_out.pop(i, [])):
+                first = W - eye_cols(i) + j * 2 * P
+                nc.scalar.copy(
+                    out=grouped[i][:, first:first + 2 * P, :].rearrange("p w t -> p (w t)").bitcast(F32),
+                    in_=bank[:].bitcast(F32))
+                give(("bank", ("eye", i, j)))
+
+        def arrange_vector(i):
+            a = vector_share(i)
+            interleave_vector(grouped[i][:, :a, :], planes(i)[:, :, :a])
+
+        def arrange_scalar(i):
+            cs = slice(vector_share(i), W - eye_cols(i) - pooled.get(i, 0))
+            interleave(nc.scalar.copy, grouped[i][:, cs, :], planes(i)[:, :, cs])
+            empty_eye(i)
+
+        def arrange_extra(i):
+            dst = take_grouped(i)
+            interleave_vector(dst[:, :EXTRA, :], raw[i - 2][:, :, W:])
+            interleave(nc.scalar.copy, dst[:, EXTRA:, :], raw[i - 1][:, :, W:])
+            free_stage.extend(pass_slots[units[i][3]] + pass_slots[units[i][3] + 1])
+
+        def arrange_last(i):
+            dst = take_grouped(i)
+            eye_interleave(i)
+            interleave(nc.scalar.copy, dst[:, :NB, :], planes(i)[:, :, :NB])
+            empty_eye(i)
+            interleave(nc.scalar.copy, dst[:, NB:W - EYE_END, :], planes(i)[:, :, NB:W - EYE_END])
+
+        def arrange(i):
+            if i == n - 1:
+                arrange_last(i)
+            elif units[i][:2] == ("stack", 0):
+                arrange_extra(i)
+            else:
+                if i not in grouped:
+                    take_grouped(i)
+                if vector_share(i) > 0:
+                    arrange_vector(i)
+                arrange_scalar(i)
+            if ("raw", i) in held:
+                give(("raw", i))
+
+        def turn_bank(b):
+            t_banks[b] = take_bank(("t", b), [P, U_PASSES, T_BANK, CHUNKS * PACK], BF16)
+            for j in range(T_BANK):
+                k, l = turns[b * T_BANK + j]
+                nc.tensor.transpose(t_banks[b][:, :, j, :], turn_sb[k][:, :, l], perm16[:])
+
+        def empty_bank(b):
+            key = ("t", b // per_group)
+            if key not in grouped:
+                take_grouped(key)
+            dst = grouped[key][:].rearrange("p (g q w) t -> p g q (w t)", g=U_PASSES, q=per_group)
+            nc.scalar.copy(
+                out=dst[:, :, b % per_group, :].bitcast(F32),
+                in_=t_banks.pop(b)[:].rearrange("p g l x -> p g (l x)").bitcast(F32))
+            give(("bank", ("t", b)))
+
+        def quantize(key, lo=0, hi=W):
             if key not in codes:
                 where = take(free_codes, ("codes", key))
                 codes[key] = (place([P, W], U32, where, "w_codes"), place([P, W], U8, where + 4 * W, "w_scales"))
@@ -374,23 +327,41 @@ def tile_dcnv2lowrankexpertcross_w_kernel(tc, x0, x, v_bytes, v_scale, c, u, bia
             if hi == W:
                 give(("grouped", key))
 
-        def multiply(i, which=range(W // NB)):
+        def mx_pass(acc, lhs, lhs_scale, key, cs, start, stop):
+            w_codes, w_scales = codes[key]
+            nc.tensor.matmul_mx(
+                out=acc, lhsT=lhs.bitcast(FP8X4), lhsT_scale=lhs_scale,
+                rhs=w_codes[:, cs].bitcast(FP8X4), rhs_scale=w_scales[:, cs], start=start, stop=stop)
+
+        def multiply(i):
             kind, e, blk, g = units[i]
-            w_codes, w_scales = codes[i]
             last = (V_PASSES if kind == "v" else U_PASSES) - 1
-            for j in which:
+            lhs = x_codes[:, g, :] if kind == "v" else h_codes[:, e, g, :]
+            lhs_scale = x_scales[:, g, :] if kind == "v" else h_scales[:, e, g, :]
+            for j in range(W // NB):
                 key = (kind, e, blk, j)
                 if g == 0:
                     accs[key] = take_bank(key, [B, NB], F32)
-                js = slice(j * NB, (j + 1) * NB)
-                lhs = x_codes[:, g, :] if kind == "v" else h_codes[:, e, g, :]
-                lhs_scale = x_scales[:, g, :] if kind == "v" else h_scales[:, e, g, :]
-                nc.tensor.matmul_mx(
-                    out=accs[key][:], lhsT=lhs.bitcast(FP8X4), lhsT_scale=lhs_scale,
-                    rhs=w_codes[:, js].bitcast(FP8X4), rhs_scale=w_scales[:, js],
-                    start=(g == 0), stop=(g == last))
-                if j == W // NB - 1:
-                    give(("codes", i))
+                mx_pass(accs[key][:], lhs, lhs_scale, i, slice(j * NB, (j + 1) * NB), g == 0, g == last)
+            give(("codes", i))
+
+        def multiply_stack(i, parts, opens, closes):
+            kind, e, j, first = units[i]
+            width = stacks[j][1]
+            if opens:
+                accs[("stack", j)] = take_bank(("stack", j), [B, NB], F32)
+            for m in parts:
+                mx_pass(accs[("stack", j)][:, :width], h_codes[:, e, first + m, :], h_scales[:, e, first + m, :],
+                        i, slice(m * width, (m + 1) * width), opens and m == parts[0], closes and m == parts[-1])
+
+        def multiply_pair(q):
+            accs[("pair", q)] = take_bank(("pair", q), [B, NB], F32)
+            for j in range(2):
+                for g in range(U_PASSES):
+                    mx_pass(accs[("pair", q)][:, j * GROUP_COLS:(j + 1) * GROUP_COLS], h_codes[:, 0, g, :],
+                            h_scales[:, 0, g, :], ("t", q + j), slice(g * GROUP_COLS, (g + 1) * GROUP_COLS),
+                            g == 0, g == U_PASSES - 1)
+                give(("codes", ("t", q + j)))
 
         def hidden_tanh(e, where):
             hid[e] = place([B, U_PASSES, PACK, P], F32, where, "th")
@@ -401,20 +372,17 @@ def tile_dcnv2lowrankexpertcross_w_kernel(tc, x0, x, v_bytes, v_scale, c, u, bia
                 give(("bank", key))
 
         def hidden_turn(e):
-            turned_h = []
             for g in range(U_PASSES):
-                bank = take_bank(("h", g), [P, PACK, B], F32)
+                accs[("h", g)] = take_bank(("h", g), [P, PACK, B], F32)
                 for t in range(PACK):
-                    nc.tensor.transpose(bank[:, t, :], hid[e][:, g, t, :], ident[:])
-                turned_h.append(bank)
-            hid[e] = turned_h
+                    nc.tensor.transpose(accs[("h", g)][:, t, :], hid[e][:, g, t, :], ident[:])
 
         def hidden_scale(e, g):
             if g == 0:
-                hid["grouped"] = place([P, U_PASSES, B, PACK], BF16, take(free_codes, "hg"), "hg")
+                hid[e] = place([P, U_PASSES, B, PACK], BF16, take(free_codes, "hg"), "hg")
             at_c = e * U_PASSES + g
             nc.vector.tensor_tensor(
-                out=hid["grouped"][:, g, :, :], in0=hid[e][g][:].rearrange("p t b -> p b t"),
+                out=hid[e][:, g, :, :], in0=accs.pop(("h", g))[:].rearrange("p t b -> p b t"),
                 in1=c_sb[:, at_c:at_c + 1, :].to_broadcast([P, B, PACK]), op=ALU.mult)
             give(("bank", ("h", g)))
 
@@ -422,28 +390,45 @@ def tile_dcnv2lowrankexpertcross_w_kernel(tc, x0, x, v_bytes, v_scale, c, u, bia
             nc.vector.quantize_mx(
                 out=h_codes[:, e, :, :].rearrange("p g b -> p (g b)").bitcast(FP8X4),
                 scales=h_scales[:, e, :, :].rearrange("p g b -> p (g b)"),
-                in_=hid.pop("grouped")[:].rearrange("p g b t -> p (g b t)"))
+                in_=hid.pop(e)[:].rearrange("p g b t -> p (g b t)"))
             give("hg")
 
-        def load_late():
-            late["mix"] = place([B, D], F32, AT_TURN[0], "mix")
-            late["bias"] = place([B, D], BF16, AT_TURN[0] + 4 * D, "bias_sb")
-            free_codes.append(AT_TURN[0] + 6 * D + PASS_BYTES)
+        def mix_first(cs, ws, acc):
+            nc.vector.scalar_tensor_tensor(
+                out=chunks(late["mix"][:])[:, cs, ws], in0=acc, scalar=prob[:, 0:1],
+                in1=chunks(late["bias"][:])[:, cs, ws], op0=ALU.mult, op1=ALU.add)
 
-        def load_bias():
-            nc.sync.dma_start(out=late["bias"][:], in_=bias.partition_broadcast(P))
+        def mix_first_plain(lo, key):
+            acc = accs.pop(key)
+            first_whole, end_whole = -(-lo // PLAIN), (lo + NB) // PLAIN
+            cuts = [lo, first_whole * PLAIN, end_whole * PLAIN, lo + NB]
+            for a, b in zip(cuts, cuts[1:]):
+                if a < b:
+                    count = max(1, (b - a) // PLAIN)
+                    first = PLAIN_START + a % PLAIN
+                    mix_first(slice(a // PLAIN, a // PLAIN + count), slice(first, first + (b - a) // count),
+                              acc[:, a - lo:b - lo].rearrange("b (c w) -> b c w", c=count))
+            give(("bank", key))
 
-        def load_rows(label, src):
-            late[label] = place([B, D], BF16, take(free_stage, label), label)
-            nc.sync.dma_start(out=late[label][:], in_=src)
+        def mix_pair(q):
+            k, l = turns[q * T_GROUP]
+            first = T_START[k] + l
+            mix_first(slice(0, CHUNKS), slice(first, first + 2 * T_GROUP),
+                      accs.pop(("pair", q))[:].rearrange("b (l c) -> b c l", c=CHUNKS))
+            give(("bank", ("pair", q)))
 
-        def mix_plain(kind, e, blk, j):
-            acc = accs.pop((kind, e, blk, j))
-            if e == 0:
-                mix_plain_first(j * NB, acc[:])
-            else:
-                mix_second(slice(blk * W + j * NB, blk * W + (j + 1) * NB), acc[:])
-            give(("bank", (kind, e, blk, j)))
+        def mix_second(first, key, lo, hi):
+            ds = slice(first + lo, first + hi)
+            nc.vector.scalar_tensor_tensor(
+                out=late["mix"][:, ds], in0=accs[key][:, lo:hi], scalar=prob[:, 1:2], in1=late["mix"][:, ds],
+                op0=ALU.mult, op1=ALU.add)
+
+        def mix_block(blk, j):
+            mix_second(blk * W + j * NB, ("u", 1, blk, j), 0, NB)
+            give(("bank", ("u", 1, blk, j)))
+
+        def mix_stack(j):
+            mix_second(stacks[j][0], ("stack", j), 0, stacks[j][1])
 
         def cross(first, width):
             ds = slice(first, first + width)
@@ -459,42 +444,48 @@ def tile_dcnv2lowrankexpertcross_w_kernel(tc, x0, x, v_bytes, v_scale, c, u, bia
         nc.vector.tensor_copy(
             out=perm16[:].rearrange("q (g c t) -> q g c t", g=U_PASSES, c=CHUNKS),
             in_=ident[:].rearrange("q (t c g) -> q g c t", g=U_PASSES, c=CHUNKS))
+
         with tc.manual_schedule():
+            stage = [AT_STAGE + j * SLOT for j in range(STAGE_SLOTS)]
             scales = v_scale.rearrange("o (g p t) u -> p (o g) (t u)", p=P, t=PACK)
             nc.scalar.dma_start(out=scale_first[:], in_=scales[:, :1, :])
             nc.scalar.dma_start(out=gate_sb[:], in_=gate_logits)
-            load_slab(0, [(ts, slice(hb * W, (hb + 1) * W)) for hb in range(RH) for ts, cs in whole], AT_STAGE)
+            load_slab(0, stage[0], [(ts, slice(hb * W, (hb + 1) * W)) for hb in range(RH) for ts, cs in whole])
             nc.sync.dma_start(out=scale_rest[:], in_=scales[:, 1:, :])
-            load_slab(1, whole, AT_STAGE + SLOT)
-            x_early = place([B, D], BF16, AT_STAGE + 2 * SLOT, "x_early")
+            load_slab(1, stage[1])
+            x_early = place([B, D], BF16, stage[2], "x_early")
             nc.sync.dma_start(out=x_early[:], in_=x)
-            for g, pieces in enumerate(((0, 1), (2, 3), (4,), (5, 6), (7,))):
-                load_slab(2 + g, whole, AT_STAGE + 3 * SLOT if g == 0 else AT_TURN[1] + (g - 1) * SLOT)
-                for r in pieces:
+            early_at = [stage[3]] + [AT_TURN[1] + j * SLOT for j in range(T_BYTES // SLOT)]
+            for j, where in enumerate(early_at):
+                load_slab(2 + j, where)
+                for r in range(-(-T_PIECES * j // len(early_at)), -(-T_PIECES * (j + 1) // len(early_at))):
                     load_turn(0, r)
+            next_slab = 2 + len(early_at)
 
             for e in range(E):
                 nc.scalar.activation(
-                    out=share[:, e:e + 1], in_=gate_sb[:, 1 - e:2 - e], func=ACT.Sigmoid,
+                    out=prob[:, e:e + 1], in_=gate_sb[:, 1 - e:2 - e], func=ACT.Sigmoid,
                     scale=-1.0, bias=gate_sb[:, e:e + 1])
             for t in range(PACK):
-                widen(0, t, 0, W, t % 2 == 1)
-            arrange(0)
+                widen(0, t, 0, W, on_scalar=(t % 2 == 1))
+            take_grouped(0)
+            arrange_scalar(0)
             for t in range(PACK):
                 widen(0, t, W, R)
-            interleave(nc.vector.tensor_copy, grouped[0][:, :vector_share(0), :], planes(0)[:, :, :vector_share(0)])
+            arrange_vector(0)
             eye_interleave(1)
             arrange(1)
             for t in range(PACK):
                 widen(1, t, 0, R)
             x_words = x_early[:].bitcast(F32)
-            x_grouped = place([P, V_PASSES * B * PACK], BF16, take(free_grouped, "x_grouped"), "x_grouped")
+            x_grouped = take_grouped("x")[:].rearrange("p w t -> p (w t)")
             for q in range(V_PASSES // 2):
                 bank = take_bank(("x", q), [P, 4, B], F32)
                 for j in range(2):
                     for w in range(2):
-                        first = 256 * (2 * q + j)
-                        nc.tensor.transpose(bank[:, 2 * j + w, :], x_words[:, first + w:first + 256:2], ident[:])
+                        first = K_PASS // 2 * (2 * q + j)
+                        nc.tensor.transpose(
+                            bank[:, 2 * j + w, :], x_words[:, first + w:first + K_PASS // 2:2], ident[:])
                 nc.scalar.copy(
                     out=x_grouped[:, q * W:(q + 1) * W].bitcast(F32).rearrange("p (j r w) -> p j r w", j=2, w=2),
                     in_=bank[:].rearrange("p (j w) r -> p j r w", w=2))
@@ -502,14 +493,14 @@ def tile_dcnv2lowrankexpertcross_w_kernel(tc, x0, x, v_bytes, v_scale, c, u, bia
             eye_interleave(2)
 
             def quantize_x():
-                for lo, hi in ((0, 4), (4, 6)):
+                for lo, hi in ((0, 4), (4, V_PASSES)):
                     nc.vector.quantize_mx(
                         out=x_codes[:, lo:hi, :].rearrange("p g b -> p (g b)").bitcast(FP8X4),
                         scales=x_scales[:, lo:hi, :].rearrange("p g b -> p (g b)"),
                         in_=x_grouped[:, lo * K_PASS:hi * K_PASS])
-                give("x_grouped")
+                give(("grouped", "x"))
 
-            later, early, from_psum, before_mx = {}, {}, {}, {}
+            loads, early, later, from_psum = {}, {}, {}, {}
 
             def at(table, step, fn, *args):
                 table.setdefault(step, []).append((fn, args))
@@ -518,124 +509,121 @@ def tile_dcnv2lowrankexpertcross_w_kernel(tc, x0, x, v_bytes, v_scale, c, u, bia
                 for fn, args in table.pop(step, []):
                     fn(*args)
 
-            at(later, 0, quantize_x)
-            stage = [AT_STAGE + j * SLOT for j in range(STAGE_SLOTS)]
+            def widened(i):
+                return RH * (i - 1)
+
+            def arranged(i):
+                return RH * (i + 1) - 2
+
+            ring = STAGE_SLOTS - 1
+            last_slab = len(slabs) - 1
             wide_at = [AT_WIDE + i % WIDE_BUFS * WIDE_BYTES for i in range(len(slabs))]
-            expert_end = [(e + 1) * n_v // E - 1 for e in range(E)]
-            turn_steps = [end + 3 for end in expert_end]
-            loads = {}
-            at(loads, 0, load_slab, 7, whole, stage[0])
-            at(loads, 0, load_slab, 8, whole, stage[1])
+            for i in range(next_slab, len(slabs)):
+                at(loads, 0 if i < next_slab + ring else widened(i - ring), load_slab, i, stage[(i - next_slab) % ring])
             at(loads, 0, load_c)
-            at(loads, 2, load_slab, 9, whole, stage[2])
-            at(loads, 12, load_slab, 10, whole, stage[0])
-            at(loads, 14, load_slab, 11, whole, stage[1])
-            for r in range(2 * U_PASSES):
-                at(loads, 10 + r // 2, load_turn, 1, r)
-            at(loads, 16, load_pass, 0, stage[2], 2)
-            at(loads, 18, load_pass, 1, wide_at[9], 2)
-            at(loads, 19, load_late)
-            at(loads, 19, load_pass, 2, AT_TURN[0] + 6 * D, 1)
-            at(loads, 20, load_pass, 3, wide_at[10], 2)
-            at(loads, 20, load_bias)
-            at(loads, 20, free_stage.extend, stage[:2])
-            at(loads, 22, free_stage.append, wide_at[11])
-            tanh_at = (stage[3], wide_at[11] + SLOT)
+            for r in range(T_PIECES):
+                at(loads, widened(next_slab - 1) + r // 2, load_turn, 1, r)
+            at(loads, widened(last_slab - 2), load_pass, 0, stage[2], 2)
+            at(loads, arranged(last_slab - 2), load_pass, 1, wide_at[last_slab - 2], 2)
+            at(loads, arranged(last_slab - 1), load_pass, 3, wide_at[last_slab - 1], 2)
+            at(loads, arranged(last_slab - 1), load_bias)
+            at(loads, widened(last_slab), free_stage.extend, stage[:2])
+            at(loads, arranged(last_slab), free_stage.append, wide_at[last_slab])
+            tanh_at = (stage[3], wide_at[last_slab] + SLOT)
             stream = [(load_unit, (i,)) for i in range(n_v, n) if units[i][1] == 1]
-            stream[-6:-6] = [(load_rows, ("x0", x0)), (load_rows, ("x", x))]
-            banks_done, full, pairs, quantized = [0], [], [], []
-            n_banks = len(turns) // T_BANK
-            per_group = T_GROUP // T_BANK
+            stream[U_PASSES + 2:U_PASSES + 2] = [(load_rows, ("x0", x0)), (load_rows, ("x", x))]
+
+            expert_end = [(e + 1) * n_v // E - 1 for e in range(E)]
+            hidden_turns = [end + 3 for end in expert_end]
+            hidden_scales = [end + 4 for end in expert_end]
+            hidden_done = [end + 5 for end in expert_end]
 
             def banks_of(s):
-                if s < T_FIRST or (s > T_FIRST and s % MX_BATCH == 0 and s < T_DENSE):
+                if s < T_FIRST or (s > T_FIRST and s % MX_BATCH == 0):
                     return 0
-                return (2 if T_FIRST < s < long_steps else 1) - (1 if s in turn_steps else 0)
+                return (2 if T_FIRST < s < long_steps else 1) - (1 if s in hidden_turns else 0)
 
+            at(later, 0, quantize_x)
+            turned, full, pairs, quantized = 0, [], [], []
             for s in range(n - 1):
                 run(loads, s)
-                while s >= 20 and stream and free_stage:
+                while stream and free_stage:
                     fn, args = stream.pop(0)
                     fn(*args)
                 if s < long_steps:
                     for t in (2 * (s % 2), 2 * (s % 2) + 1):
                         widen(s // 2 + 2, t, 0, R)
-                ready = full[:]
-                full.clear()
                 run(early, s)
-                turning = banks_done[0] < n_banks
-                for b in range(banks_done[0], min(n_banks, banks_done[0] + banks_of(s))):
-                    for m in range(b * T_BANK, (b + 1) * T_BANK):
-                        turn(m)
-                    full.append(b)
-                    banks_done[0] += 1
+                turning = T_FIRST <= s and turned < n_banks
+                ready, full = full, list(range(turned, min(n_banks, turned + banks_of(s))))
+                for b in full:
+                    turn_bank(b)
+                    if b + 1 == T_RUN[0] // T_BANK:
+                        at(loads, s + 1, reuse_first_turned)
+                turned += len(full)
                 if s + 2 < n:
                     arrange(s + 2)
                 for b in ready:
                     empty_bank(b)
                     if b % per_group == per_group - 1:
-                        q = b // per_group
-                        at(later, s + Q_LAG, quantize, ("t", q), 0, W)
-                        if q % 2 == 1 or q == n_groups - 1:
-                            pairs.append((s + Q_LAG, q - q % 2))
+                        at(later, s + GROUP_LAG, quantize, ("t", b // per_group))
+                    if b % (2 * per_group) == 2 * per_group - 1:
+                        pairs.append((s + GROUP_LAG, b // per_group - 1))
                 if s + 3 in EYE_UNITS:
                     eye_interleave(s + 3)
-                if s not in from_psum:
-                    quantize(s, 0, W)
-                run(later, s)
                 if s in from_psum:
-                    quantize(s, 0, W)
-                    pool_interleave(s + 3, POOL_COLS * len(from_psum[s]) - POOL_LESS)
+                    run(later, s)
+                    quantize(s)
+                    pool_interleave(s + 3, len(from_psum[s]))
                     run(from_psum, s)
+                else:
+                    quantize(s)
+                    run(later, s)
                 quantized.append(s)
-                waits = turning and s >= T_FIRST and s % MX_BATCH < MX_BATCH - 1
-                batch = [] if waits else quantized[:]
-                lag = 3 if len(batch) > 1 else 2
+                if turning and s % MX_BATCH < MX_BATCH - 1:
+                    continue
+                batch, quantized = quantized, []
                 for i in batch:
-                    quantized.remove(i)
                     kind, e, blk, g = units[i]
                     if kind == "stack":
-                        depth = W // stack_width(blk)
-                        multiply_stack(i, range(depth), g == 0, g + depth == U_PASSES)
+                        closes = g + stack_depth(blk) == U_PASSES
+                        multiply_stack(i, range(stack_depth(blk)), g == 0, closes)
                         give(("codes", i))
-                        if g + depth == U_PASSES and blk == 1:
-                            mix_stack(blk, 0, stack_width(blk))
+                        if closes and blk == 1:
+                            mix_stack(blk)
                             at(later, s + 1, cross, *stacks[blk])
                     else:
                         multiply(i)
                     if i in expert_end:
                         at(later, s + 2, hidden_tanh, e, tanh_at[e])
-                        at(early, s + 3, hidden_turn, e)
-                        for g4 in range(U_PASSES):
-                            at(from_psum, s + 4, hidden_scale, e, g4)
-                        at(later, s + 5, hidden_quantize, e)
+                        at(early, hidden_turns[e], hidden_turn, e)
+                        for bank_g in range(U_PASSES):
+                            at(from_psum, hidden_scales[e], hidden_scale, e, bank_g)
+                        at(later, hidden_done[e], hidden_quantize, e)
                     if kind == "main" and g == U_PASSES - 1:
                         for j in range(W // NB):
-                            at(from_psum, s + lag, mix_plain, kind, e, blk, j)
+                            at(from_psum, s + AFTER_BATCH, mix_first_plain, j * NB, (kind, e, blk, j))
                     if kind == "u" and g == U_PASSES - 1 and blk == 1:
-                        pool_interleave(s + 3, 2 * POOL_COLS - POOL_LESS)
+                        pool_interleave(s + 3, W // NB)
                         for j in range(W // NB):
-                            mix_plain(kind, e, blk, j)
+                            mix_block(blk, j)
                         at(later, s + 1, cross, W, W)
                         at(later, s + 2, finish, W, W)
-                while batch and pairs and pairs[0][0] <= s and s > expert_end[0] + 5:
-                    step, q = pairs.pop(0)
+                while pairs and pairs[0][0] <= s and s > hidden_done[0]:
+                    q = pairs.pop(0)[1]
                     multiply_pair(q)
-                    if q + 2 < n_groups and q < T_GROUPS[0]:
-                        at(from_psum, expert_end[1] + 4, mix_pair, q)
-                    elif q + 2 < n_groups:
-                        at(later, s + lag, mix_pair, q)
+                    if turns[q * T_GROUP][0] == 0:
+                        at(from_psum, hidden_scales[1], mix_pair, q)
                     else:
                         at(from_psum, s + 2, mix_pair, q)
-                        at(from_psum, s + 2, mix_stack, 0, 0, stack_width(0))
-                        mixed = max(s + 3, n - 2 * U_PASSES + 1)
+                        at(from_psum, s + 2, mix_first_plain, stacks[0][0], ("stack", 0))
                         for j in range(W // NB):
-                            at(from_psum, mixed, mix_plain, "u", 1, 0, j)
-                        at(later, mixed + 1, cross, 0, W)
-                        at(later, mixed + 2, finish, 0, W)
-            assert not pairs and banks_done[0] == n_banks and not full and not stream
+                            at(from_psum, s + 3, mix_block, 0, j)
+                        at(later, s + 4, cross, 0, W)
+                        at(later, s + 5, finish, 0, W)
+
             quantize(n - 1, 0, NB)
-            mix_stack(2, 0, stack_width(2))
+            mix_stack(2)
             finish(*stacks[1])
             quantize(n - 1, W - EYE_END, W)
             multiply_stack(n - 1, [0, 1, 3], True, False)
@@ -643,12 +631,9 @@ def tile_dcnv2lowrankexpertcross_w_kernel(tc, x0, x, v_bytes, v_scale, c, u, bia
             quantize(n - 1, NB, W - EYE_END)
             multiply_stack(n - 1, [2], False, True)
             finish(*stacks[2])
-            last = len(stacks) - 1
-            halves = [(0, P), (P, 2 * P)]
-            for lo, hi in halves:
-                mix_stack(last, lo, hi)
-            for lo, hi in halves:
-                cross(stacks[last][0] + lo, P)
-            for lo, hi in halves:
-                finish(stacks[last][0] + lo, P)
-            assert not later and not early and not from_psum
+            for lo in (0, P):
+                mix_second(stacks[3][0], ("stack", 3), lo, lo + P)
+            for lo in (0, P):
+                cross(stacks[3][0] + lo, P)
+            for lo in (0, P):
+                finish(stacks[3][0] + lo, P)

@@ -27,7 +27,7 @@ RH = R // W
 
 CHUNKS = 8
 CW = D // CHUNKS
-T_RUN = (128, 64)
+T_RUN = (128, 96)
 T_PITCH = 144
 PLAIN = CW - sum(T_RUN)
 PLAIN_START = T_RUN[0]
@@ -47,7 +47,7 @@ AFTER_BATCH = 3
 GROUP_LAG = 2
 
 SHARE_HEAD = 192
-SHARE_V = 400
+SHARE_V = 432
 SHARE_U = 416
 POOL_COLS = 72
 POOL_LESS = 40
@@ -215,11 +215,6 @@ def tile_dcnv2lowrankexpertcross_w_kernel(tc, x0, x, v_bytes, v_scale, c, u, bia
         def interleave(copy, dst, src):
             copy(out=dst.rearrange("p (c i) t -> p c t i", i=2), in_=src.rearrange("p t (c i) -> p c t i", i=2))
 
-        def interleave_vector(dst, src):
-            nc.vector.tensor_copy(
-                out=dst.rearrange("p (c h i) t -> p h c t i", h=2, i=2),
-                in_=src.rearrange("p t (c h i) -> p h c t i", h=2, i=2))
-
         def pool_copy(out, in_):
             nc.gpsimd.tensor_scalar(out=out, in0=in_, scalar1=1.0, scalar2=0.0, op0=ALU.mult, op1=ALU.add)
 
@@ -266,7 +261,7 @@ def tile_dcnv2lowrankexpertcross_w_kernel(tc, x0, x, v_bytes, v_scale, c, u, bia
 
         def arrange_vector(i):
             a = vector_share(i)
-            interleave_vector(grouped[i][:, :a, :], planes(i)[:, :, :a])
+            interleave(nc.vector.tensor_copy, grouped[i][:, :a, :], planes(i)[:, :, :a])
 
         def arrange_scalar(i):
             cs = slice(vector_share(i), W - eye_cols(i) - pooled.get(i, 0))
@@ -275,9 +270,10 @@ def tile_dcnv2lowrankexpertcross_w_kernel(tc, x0, x, v_bytes, v_scale, c, u, bia
 
         def arrange_extra(i):
             dst = take_grouped(i)
-            interleave_vector(dst[:, :EXTRA, :], raw[i - 2][:, :, W:])
-            interleave(nc.scalar.copy, dst[:, EXTRA:, :], raw[i - 1][:, :, W:])
-            free_stage.extend(pass_slots[units[i][3]] + pass_slots[units[i][3] + 1])
+            for g in range(U_PASSES):
+                copy = nc.vector.tensor_copy if g < U_PASSES // 2 else nc.scalar.copy
+                interleave(copy, dst[:, g * EXTRA:(g + 1) * EXTRA, :], raw[i - U_PASSES + g][:, :, W:])
+                free_stage.extend(pass_slots[g])
 
         def arrange_last(i):
             dst = take_grouped(i)
@@ -354,9 +350,9 @@ def tile_dcnv2lowrankexpertcross_w_kernel(tc, x0, x, v_bytes, v_scale, c, u, bia
                 mx_pass(accs[("stack", j)][:, :width], h_codes[:, e, first + m, :], h_scales[:, e, first + m, :],
                         i, slice(m * width, (m + 1) * width), opens and m == parts[0], closes and m == parts[-1])
 
-        def multiply_pair(q):
+        def multiply_pair(q, count):
             accs[("pair", q)] = take_bank(("pair", q), [B, NB], F32)
-            for j in range(2):
+            for j in range(count):
                 for g in range(U_PASSES):
                     mx_pass(accs[("pair", q)][:, j * GROUP_COLS:(j + 1) * GROUP_COLS], h_codes[:, 0, g, :],
                             h_scales[:, 0, g, :], ("t", q + j), slice(g * GROUP_COLS, (g + 1) * GROUP_COLS),
@@ -398,10 +394,10 @@ def tile_dcnv2lowrankexpertcross_w_kernel(tc, x0, x, v_bytes, v_scale, c, u, bia
                 out=chunks(late["mix"][:])[:, cs, ws], in0=acc, scalar=prob[:, 0:1],
                 in1=chunks(late["bias"][:])[:, cs, ws], op0=ALU.mult, op1=ALU.add)
 
-        def mix_first_plain(lo, key):
+        def mix_first_plain(lo, key, width):
             acc = accs.pop(key)
-            first_whole, end_whole = -(-lo // PLAIN), (lo + NB) // PLAIN
-            cuts = [lo, first_whole * PLAIN, end_whole * PLAIN, lo + NB]
+            first_whole, end_whole = -(-lo // PLAIN), (lo + width) // PLAIN
+            cuts = [lo, first_whole * PLAIN, end_whole * PLAIN, lo + width]
             for a, b in zip(cuts, cuts[1:]):
                 if a < b:
                     count = max(1, (b - a) // PLAIN)
@@ -410,11 +406,11 @@ def tile_dcnv2lowrankexpertcross_w_kernel(tc, x0, x, v_bytes, v_scale, c, u, bia
                               acc[:, a - lo:b - lo].rearrange("b (c w) -> b c w", c=count))
             give(("bank", key))
 
-        def mix_pair(q):
+        def mix_pair(q, count):
             k, l = turns[q * T_GROUP]
             first = T_START[k] + l
-            mix_first(slice(0, CHUNKS), slice(first, first + 2 * T_GROUP),
-                      accs.pop(("pair", q))[:].rearrange("b (l c) -> b c l", c=CHUNKS))
+            mix_first(slice(0, CHUNKS), slice(first, first + count * T_GROUP),
+                      accs.pop(("pair", q))[:, :count * GROUP_COLS].rearrange("b (l c) -> b c l", c=CHUNKS))
             give(("bank", ("pair", q)))
 
         def mix_second(first, key, lo, hi):
@@ -539,7 +535,7 @@ def tile_dcnv2lowrankexpertcross_w_kernel(tc, x0, x, v_bytes, v_scale, c, u, bia
             hidden_done = [end + 5 for end in expert_end]
 
             def banks_of(s):
-                if s < T_FIRST or (s > T_FIRST and s % MX_BATCH == 0):
+                if s < T_FIRST or (T_FIRST < s < n_v and s % MX_BATCH == 0):
                     return 0
                 return (2 if T_FIRST < s < long_steps else 1) - (1 if s in hidden_turns else 0)
 
@@ -565,10 +561,13 @@ def tile_dcnv2lowrankexpertcross_w_kernel(tc, x0, x, v_bytes, v_scale, c, u, bia
                     arrange(s + 2)
                 for b in ready:
                     empty_bank(b)
+                    lag = 1 if b == n_banks - 1 else GROUP_LAG
                     if b % per_group == per_group - 1:
-                        at(later, s + GROUP_LAG, quantize, ("t", b // per_group))
+                        at(later, s + lag, quantize, ("t", b // per_group))
                     if b % (2 * per_group) == 2 * per_group - 1:
-                        pairs.append((s + GROUP_LAG, b // per_group - 1))
+                        pairs.append((s + lag, b // per_group - 1, 2))
+                    elif b == n_banks - 1:
+                        pairs.append((s + lag, b // per_group, 1))
                 if s + 3 in EYE_UNITS:
                     eye_interleave(s + 3)
                 if s in from_psum:
@@ -602,7 +601,7 @@ def tile_dcnv2lowrankexpertcross_w_kernel(tc, x0, x, v_bytes, v_scale, c, u, bia
                         at(later, hidden_done[e], hidden_quantize, e)
                     if kind == "main" and g == U_PASSES - 1:
                         for j in range(W // NB):
-                            at(from_psum, s + AFTER_BATCH, mix_first_plain, j * NB, (kind, e, blk, j))
+                            at(from_psum, s + AFTER_BATCH, mix_first_plain, j * NB, (kind, e, blk, j), NB)
                     if kind == "u" and g == U_PASSES - 1 and blk == 1:
                         pool_interleave(s + 3, W // NB)
                         for j in range(W // NB):
@@ -610,17 +609,19 @@ def tile_dcnv2lowrankexpertcross_w_kernel(tc, x0, x, v_bytes, v_scale, c, u, bia
                         at(later, s + 1, cross, W, W)
                         at(later, s + 2, finish, W, W)
                 while pairs and pairs[0][0] <= s and s > hidden_done[0]:
-                    q = pairs.pop(0)[1]
-                    multiply_pair(q)
+                    q, count = pairs.pop(0)[1:]
+                    multiply_pair(q, count)
                     if turns[q * T_GROUP][0] == 0:
-                        at(from_psum, hidden_scales[1], mix_pair, q)
+                        at(from_psum, hidden_scales[1], mix_pair, q, count)
+                    elif count == 2:
+                        at(from_psum, s + AFTER_BATCH, mix_pair, q, count)
+                        at(from_psum, s + AFTER_BATCH, mix_first_plain, stacks[0][0], ("stack", 0), EXTRA)
                     else:
-                        at(from_psum, s + 2, mix_pair, q)
-                        at(from_psum, s + 2, mix_first_plain, stacks[0][0], ("stack", 0))
+                        at(from_psum, s + 2, mix_pair, q, count)
                         for j in range(W // NB):
-                            at(from_psum, s + 3, mix_block, 0, j)
-                        at(later, s + 4, cross, 0, W)
-                        at(later, s + 5, finish, 0, W)
+                            at(from_psum, s + 2, mix_block, 0, j)
+                        at(later, s + 3, cross, 0, W)
+                        at(later, s + 4, finish, 0, W)
 
             quantize(n - 1, 0, NB)
             mix_stack(2)

@@ -27,48 +27,46 @@ RH = R // W
 
 CHUNKS = 8
 CW = D // CHUNKS
-T_RUN = (128, 96)
-T_PITCH = 144
-PLAIN = CW - sum(T_RUN)
-PLAIN_START = T_RUN[0]
-T_START = (0, PLAIN_START + PLAIN)
-EXTRA = CHUNKS * PLAIN - W
+T_RUN = 128
+T_PITCH = 128
+PLAIN = CW - T_RUN
 T_BANK = 8
 T_GROUP = 32
-GROUP_COLS = CHUNKS * T_GROUP
+YW = 256
 T_PIECES = 2 * U_PASSES
+PER_GROUP = T_GROUP // T_BANK
+GROUPS = T_RUN // T_GROUP
 
 EYE_UNITS = range(1, 10)
 EYE_COLS = 512
 EYE_END = 256
-T_FIRST = 8
-MX_BATCH = 4
-AFTER_BATCH = 3
-GROUP_LAG = 2
 
 SHARE_HEAD = 192
 SHARE_V = 432
 SHARE_U = 416
-POOL_COLS = 72
+T_FIRST = 7
+MX_BATCH = 4
+T_LAST = 32
+SHARE_END = (320, 128, 0, 0)
+GROUP_LAG = 2
+POOL_COLS = 36
 POOL_LESS = 40
 
 SLOT = PACK * W * 2
 T_BYTES = P * T_PITCH * 2
-PASS_BYTES = PACK * CHUNKS * PLAIN * 2
 WIDE_BYTES = PACK * R * 2
 CODE_BYTES = 5 * W
-WIDE_BUFS = 3
 STAGE_SLOTS = 4
-GROUPED_SLOTS = 5
+GROUPED_SLOTS = 6
 CODE_SLOTS = 7
 AT_TURN = (0, T_BYTES)
 AT_WIDE = 2 * T_BYTES
-AT_STAGE = AT_WIDE + WIDE_BUFS * WIDE_BYTES
+AT_STAGE = AT_WIDE + 3 * WIDE_BYTES
 AT_GROUPED = AT_STAGE + STAGE_SLOTS * SLOT
 AT_CODES = AT_GROUPED + GROUPED_SLOTS * SLOT
 AT_MIX = AT_TURN[0]
 AT_BIAS = AT_MIX + 4 * D
-AT_PASS = AT_BIAS + 2 * D
+AT_LATE = AT_BIAS + 2 * D
 
 
 def tile_dcnv2lowrankexpertcross_w_kernel(tc, x0, x, v_bytes, v_scale, c, u, bias, gate_logits, out):
@@ -115,101 +113,69 @@ def tile_dcnv2lowrankexpertcross_w_kernel(tc, x0, x, v_bytes, v_scale, c, u, bia
             return psum.tile(shape, dtype, name="bank%d" % take(free_banks, ("bank", key)))
 
         slabs = [(e, g) for e in range(E) for g in range(V_PASSES)]
-        units = [("v", e, hb, g) for e, g in slabs for hb in range(RH)]
-        n_v = len(units)
-        stacks = [(W, EXTRA), (D - W, NB), (D - NB, NB // 2), (D - NB // 2, NB // 2)]
-
-        def stack_depth(j):
-            return W // stacks[j][1]
-
-        def stack_units(j):
-            return [("stack", min(j, 1), j, g) for g in range(0, U_PASSES, stack_depth(j))]
-
-        for extra in stack_units(0):
-            units += [("main", 0, 0, g) for g in range(extra[3], extra[3] + stack_depth(0))] + [extra]
-        units += [("u", 1, db, g) for db in range(D // W - 1) for g in range(U_PASSES)]
-        units += stack_units(1) + stack_units(2) + stack_units(3)
-        n = len(units)
-        long_steps = RH * (len(slabs) - 2)
-        turns = [(k, l) for k in range(len(T_RUN)) for l in range(T_RUN[k])]
-        n_banks = len(turns) // T_BANK
-        per_group = T_GROUP // T_BANK
         raw, slab_raw, wide, grouped, codes, accs, hid = {}, {}, {}, {}, {}, {}, {}
-        eye_out, t_banks, turn_sb, late, pooled, pass_slots = {}, {}, {}, {}, {}, {}
+        eye_out, t_banks, turn_sb, late, pooled = {}, {}, {}, {}, {}
+        last = ("y", 1, CHUNKS - 1)
 
         def chunks(ap):
             return ap.rearrange("b (c w) -> b c w", c=CHUNKS)
 
         whole = [(slice(0, 2), slice(0, R)), (slice(2, 4), slice(0, R))]
 
-        def load_slab(i, where, pieces=whole):
+        def load_slab(i, where=None, pieces=whole):
             e, g = slabs[i]
-            slab_raw[i] = place([P, PACK, R], U8, where, "v_raw")
+            if i not in slab_raw:
+                slab_raw[i] = place([P, PACK, R], U8, where, "v_raw")
             rows = v_bytes[e, g * K_PASS:(g + 1) * K_PASS, :].rearrange("(p t) w -> p t w", t=PACK)
             for ts, cs in pieces:
                 nc.sync.dma_start(out=slab_raw[i][:, ts, cs], in_=rows[:, ts, cs])
 
-        def pass_rows(e, g):
-            return u[e, g * K_PASS:(g + 1) * K_PASS, :]
-
-        def load_turn(k, r):
+        def load_turn(e, r):
             g, half = divmod(r, 2)
-            if k not in turn_sb:
-                turn_sb[k] = place([P, P, T_PITCH], BF16, AT_TURN[k], "u_turn")
-            src = pass_rows(0, g).rearrange("(p t) (c w) -> (t c) p w", t=PACK, c=CHUNKS)
+            if e not in turn_sb:
+                turn_sb[e] = place([P, P, T_PITCH], BF16, AT_TURN[e], "u_turn")
+            src = u[e, g * K_PASS:(g + 1) * K_PASS, :].rearrange("(p t) (c w) -> (t c) p w", t=PACK, c=CHUNKS)
             ps = slice(half * P // 2, (half + 1) * P // 2)
-            nc.sync.dma_start(
-                out=turn_sb[k][g:P:U_PASSES, ps, :T_RUN[k]], in_=src[:, ps, T_START[k]:T_START[k] + T_RUN[k]])
+            nc.sync.dma_start(out=turn_sb[e][g:P:U_PASSES, ps, :T_RUN], in_=src[:, ps, :T_RUN])
 
-        def load_pass(g, where, slots):
-            pass_slots[g] = [where + j * SLOT for j in range(slots)]
-            i = units.index(("main", 0, 0, g))
-            raw[i] = place([P, PACK, CHUNKS * PLAIN], BF16, where, "u_pass")
-            src = pass_rows(0, g).rearrange("(p t) (c w) -> p (t c) w", t=PACK, c=CHUNKS)
-            nc.sync.dma_start(
-                out=raw[i][:].rearrange("p t (c w) -> p (t c) w", c=CHUNKS),
-                in_=src[:, :, PLAIN_START:PLAIN_START + PLAIN])
-
-        def load_unit(i):
-            kind, e, blk, g = units[i]
-            first, width = (blk * W, W) if kind == "u" else stacks[blk]
-            raw[i] = place([P, PACK, W], BF16, take(free_stage, ("raw", i)), "u_raw")
-            for j in range(W // width):
-                rows = pass_rows(e, g + j).rearrange("(p t) w -> p t w", t=PACK)
-                nc.sync.dma_start(out=raw[i][:, :, j * width:(j + 1) * width], in_=rows[:, :, first:first + width])
+        def load_y(key):
+            kind, e, ch = key
+            first = ch * CW + T_RUN
+            raw[key] = place([P, PACK, W], BF16, take(free_stage, ("raw", key)), "u_raw")
+            for g in range(U_PASSES):
+                rows = u[e, g * K_PASS:(g + 1) * K_PASS, :].rearrange("(p t) w -> p t w", t=PACK)
+                nc.sync.dma_start(out=raw[key][:, :, g * YW:(g + 1) * YW], in_=rows[:, :, first:first + YW])
 
         def load_c():
             nc.sync.dma_start(out=c_sb[:], in_=c.rearrange("e (g p t) -> p (e g) t", p=P, t=PACK))
 
         def load_bias():
+            late["bias"] = place([B, D], BF16, AT_BIAS, "bias_sb")
             nc.sync.dma_start(out=late["bias"][:], in_=bias.partition_broadcast(P))
 
         def load_rows(label, src):
             late[label] = place([B, D], BF16, take(free_stage, label), label)
             nc.sync.dma_start(out=late[label][:], in_=src)
 
-        def reuse_first_turned():
-            late["mix"] = place([B, D], F32, AT_MIX, "mix")
-            late["bias"] = place([B, D], BF16, AT_BIAS, "bias_sb")
-            free_codes.append(AT_PASS + PASS_BYTES)
-            load_pass(2, AT_PASS, 1)
-
         def widen(i, t, lo, hi, on_scalar=False):
-            g = slabs[i][1]
+            e, g = slabs[i]
             if i not in wide:
-                shape = [P, RH, PACK, W] if i == 0 else [P, PACK, R]
-                wide[i] = place(shape, BF16, AT_WIDE + i % WIDE_BUFS * WIDE_BYTES, "v_wide")
+                if i == 0:
+                    wide[i] = place([P, RH, PACK, W], BF16, AT_WIDE, "v_wide")
+                else:
+                    wide[i] = place([P, PACK, R], BF16, AT_WIDE + i % 3 * WIDE_BYTES, "v_wide")
             src = slab_raw[i][:, t, lo:hi].bitcast(FP8)
-            dst = wide[i][:, lo // W, t, :] if i == 0 else wide[i][:, t, lo:hi]
+            dst = wide[i][:, lo // W, t, :] if i == 0 else wide[i][:, t, :]
             scale = scale_first[:, 0, t:t + 1] if g == 0 else scale_rest[:, g - 1, t:t + 1]
             if on_scalar:
                 nc.scalar.activation(out=dst, in_=src, func=ACT.Copy, scale=scale)
             else:
                 nc.vector.tensor_scalar(out=dst, in0=src, scalar1=scale, scalar2=None, op0=ALU.mult)
 
-        def planes(i):
-            if i >= n_v:
-                return raw[i][:, :, :W]
+        def planes(key):
+            if key[0] == "y":
+                return raw[key][:]
+            i = key[1]
             return wide[0][:, i, :, :] if i < RH else wide[i // RH][:, :, i % RH * W:(i % RH + 1) * W]
 
         def interleave(copy, dst, src):
@@ -218,26 +184,18 @@ def tile_dcnv2lowrankexpertcross_w_kernel(tc, x0, x, v_bytes, v_scale, c, u, bia
         def pool_copy(out, in_):
             nc.gpsimd.tensor_scalar(out=out, in0=in_, scalar1=1.0, scalar2=0.0, op0=ALU.mult, op1=ALU.add)
 
-        def eye_cols(i):
-            return EYE_COLS if i in EYE_UNITS else EYE_END if i == n - 1 else 0
-
-        def vector_share(i):
-            if i >= n - U_PASSES:
-                return 0
-            if i >= long_steps + 2:
-                return SHARE_U
-            if i < RH:
-                return SHARE_HEAD
-            return SHARE_V if i % RH == 1 and i not in EYE_UNITS else 0
+        def eye_cols(key):
+            return EYE_COLS if key[0] == "v" and key[1] in EYE_UNITS else EYE_END if key == last else 0
 
         def take_grouped(key, newest=False):
-            grouped[key] = place([P, W, PACK], BF16, take(free_grouped, ("grouped", key), newest), "grouped")
+            if key not in grouped:
+                grouped[key] = place([P, W, PACK], BF16, take(free_grouped, ("grouped", key), newest), "grouped")
             return grouped[key]
 
-        def pool_interleave(i, reads):
-            pooled[i] = POOL_COLS * reads - POOL_LESS
-            cs = slice(W - pooled[i], W)
-            interleave(pool_copy, take_grouped(i, newest=True)[:, cs, :], planes(i)[:, :, cs])
+        def pool_interleave(key, halves):
+            pooled[key] = POOL_COLS * halves - POOL_LESS
+            cs = slice(W - pooled[key], W)
+            interleave(pool_copy, take_grouped(key, newest=True)[:, cs, :], planes(key)[:, :, cs])
 
         def eye_interleave(i):
             src = planes(i)[:, :, W - eye_cols(i):]
@@ -259,58 +217,40 @@ def tile_dcnv2lowrankexpertcross_w_kernel(tc, x0, x, v_bytes, v_scale, c, u, bia
                     in_=bank[:].bitcast(F32))
                 give(("bank", ("eye", i, j)))
 
-        def arrange_vector(i):
-            a = vector_share(i)
-            interleave(nc.vector.tensor_copy, grouped[i][:, :a, :], planes(i)[:, :, :a])
+        def by_vector(key, lo, hi):
+            interleave(nc.vector.tensor_copy, take_grouped(key)[:, lo:hi, :], planes(key)[:, :, lo:hi])
 
-        def arrange_scalar(i):
-            cs = slice(vector_share(i), W - eye_cols(i) - pooled.get(i, 0))
-            interleave(nc.scalar.copy, grouped[i][:, cs, :], planes(i)[:, :, cs])
-            empty_eye(i)
+        def by_scalar(key, lo, hi):
+            hi = min(hi, W - eye_cols(key) - pooled.get(key, 0))
+            interleave(nc.scalar.copy, take_grouped(key)[:, lo:hi, :], planes(key)[:, :, lo:hi])
 
-        def arrange_extra(i):
-            dst = take_grouped(i)
-            for g in range(U_PASSES):
-                copy = nc.vector.tensor_copy if g < U_PASSES // 2 else nc.scalar.copy
-                interleave(copy, dst[:, g * EXTRA:(g + 1) * EXTRA, :], raw[i - U_PASSES + g][:, :, W:])
-                free_stage.extend(pass_slots[g])
+        def arrange(key, share):
+            if share > 0:
+                by_vector(key, 0, share)
+            by_scalar(key, share, W)
+            empty_eye(key)
 
-        def arrange_last(i):
-            dst = take_grouped(i)
-            eye_interleave(i)
-            interleave(nc.scalar.copy, dst[:, :NB, :], planes(i)[:, :, :NB])
-            empty_eye(i)
-            interleave(nc.scalar.copy, dst[:, NB:W - EYE_END, :], planes(i)[:, :, NB:W - EYE_END])
+        turned, full, groups_full = [], [], []
 
-        def arrange(i):
-            if i == n - 1:
-                arrange_last(i)
-            elif units[i][:2] == ("stack", 0):
-                arrange_extra(i)
-            else:
-                if i not in grouped:
-                    take_grouped(i)
-                if vector_share(i) > 0:
-                    arrange_vector(i)
-                arrange_scalar(i)
-            if ("raw", i) in held:
-                give(("raw", i))
+        def turn(count):
+            for b in range(len(turned), min(len(turned) + count, E * T_RUN // T_BANK)):
+                e, first = divmod(b * T_BANK, T_RUN)
+                t_banks[b] = take_bank(("t", b), [P, U_PASSES, T_BANK, CHUNKS * PACK], BF16)
+                for j in range(T_BANK):
+                    nc.tensor.transpose(t_banks[b][:, :, j, :], turn_sb[e][:, :, first + j], perm16[:])
+                turned.append(b)
+                full.append(b)
 
-        def turn_bank(b):
-            t_banks[b] = take_bank(("t", b), [P, U_PASSES, T_BANK, CHUNKS * PACK], BF16)
-            for j in range(T_BANK):
-                k, l = turns[b * T_BANK + j]
-                nc.tensor.transpose(t_banks[b][:, :, j, :], turn_sb[k][:, :, l], perm16[:])
-
-        def empty_bank(b):
-            key = ("t", b // per_group)
-            if key not in grouped:
-                take_grouped(key)
-            dst = grouped[key][:].rearrange("p (g q w) t -> p g q (w t)", g=U_PASSES, q=per_group)
+        def empty_bank():
+            b = full.pop(0)
+            key = ("t", b // PER_GROUP)
+            dst = take_grouped(key)[:].rearrange("p (g q w) t -> p g q (w t)", g=U_PASSES, q=PER_GROUP)
             nc.scalar.copy(
-                out=dst[:, :, b % per_group, :].bitcast(F32),
+                out=dst[:, :, b % PER_GROUP, :].bitcast(F32),
                 in_=t_banks.pop(b)[:].rearrange("p g l x -> p g (l x)").bitcast(F32))
             give(("bank", ("t", b)))
+            if b % PER_GROUP == PER_GROUP - 1:
+                groups_full.append(key)
 
         def quantize(key, lo=0, hi=W):
             if key not in codes:
@@ -329,35 +269,29 @@ def tile_dcnv2lowrankexpertcross_w_kernel(tc, x0, x, v_bytes, v_scale, c, u, bia
                 out=acc, lhsT=lhs.bitcast(FP8X4), lhsT_scale=lhs_scale,
                 rhs=w_codes[:, cs].bitcast(FP8X4), rhs_scale=w_scales[:, cs], start=start, stop=stop)
 
-        def multiply(i):
-            kind, e, blk, g = units[i]
-            last = (V_PASSES if kind == "v" else U_PASSES) - 1
-            lhs = x_codes[:, g, :] if kind == "v" else h_codes[:, e, g, :]
-            lhs_scale = x_scales[:, g, :] if kind == "v" else h_scales[:, e, g, :]
+        def quantize_groups():
+            while groups_full:
+                quantize(groups_full.pop(0))
+
+        def multiply_v(i):
+            (e, g), hb = slabs[i // RH], i % RH
             for j in range(W // NB):
-                key = (kind, e, blk, j)
+                key = ("v", e, hb, j)
                 if g == 0:
                     accs[key] = take_bank(key, [B, NB], F32)
-                mx_pass(accs[key][:], lhs, lhs_scale, i, slice(j * NB, (j + 1) * NB), g == 0, g == last)
-            give(("codes", i))
+                mx_pass(accs[key][:], x_codes[:, g, :], x_scales[:, g, :], ("v", i), slice(j * NB, (j + 1) * NB),
+                        g == 0, g == V_PASSES - 1)
+            give(("codes", ("v", i)))
 
-        def multiply_stack(i, parts, opens, closes):
-            kind, e, j, first = units[i]
-            width = stacks[j][1]
-            if opens:
-                accs[("stack", j)] = take_bank(("stack", j), [B, NB], F32)
-            for m in parts:
-                mx_pass(accs[("stack", j)][:, :width], h_codes[:, e, first + m, :], h_scales[:, e, first + m, :],
-                        i, slice(m * width, (m + 1) * width), opens and m == parts[0], closes and m == parts[-1])
-
-        def multiply_pair(q, count):
-            accs[("pair", q)] = take_bank(("pair", q), [B, NB], F32)
-            for j in range(count):
-                for g in range(U_PASSES):
-                    mx_pass(accs[("pair", q)][:, j * GROUP_COLS:(j + 1) * GROUP_COLS], h_codes[:, 0, g, :],
-                            h_scales[:, 0, g, :], ("t", q + j), slice(g * GROUP_COLS, (g + 1) * GROUP_COLS),
-                            g == 0, g == U_PASSES - 1)
-                give(("codes", ("t", q + j)))
+        def multiply_y(key, bank, half, passes=range(U_PASSES), opens=True, closes=True):
+            e = key[1] if key[0] == "y" else key[1] // GROUPS
+            if bank not in accs:
+                accs[bank] = take_bank(bank, [B, NB], F32)
+            for g in passes:
+                mx_pass(accs[bank][:, half * YW:(half + 1) * YW], h_codes[:, e, g, :], h_scales[:, e, g, :], key,
+                        slice(g * YW, (g + 1) * YW), opens and g == passes[0], closes and g == passes[-1])
+            if closes:
+                give(("codes", key))
 
         def hidden_tanh(e, where):
             hid[e] = place([B, U_PASSES, PACK, P], F32, where, "th")
@@ -389,51 +323,39 @@ def tile_dcnv2lowrankexpertcross_w_kernel(tc, x0, x, v_bytes, v_scale, c, u, bia
                 in_=hid.pop(e)[:].rearrange("p g b t -> p (g b t)"))
             give("hg")
 
-        def mix_first(cs, ws, acc):
+        def region(key, count):
+            if key[0] == "y":
+                return slice(key[2], key[2] + count), slice(T_RUN, CW)
+            first = key[1] % GROUPS * T_GROUP
+            return slice(0, CHUNKS), slice(first, first + count * T_GROUP)
+
+        def sums(key, bank, half, count):
+            acc = accs[bank][:, half * YW:(half + count) * YW]
+            if key[0] == "y":
+                return acc.rearrange("b (c w) -> b c w", c=count)
+            return acc.rearrange("b (l c) -> b c l", c=CHUNKS)
+
+        def mix(e, cs, ws, acc):
+            if "mix" not in late:
+                late["mix"] = place([B, D], F32, AT_MIX, "mix")
             nc.vector.scalar_tensor_tensor(
-                out=chunks(late["mix"][:])[:, cs, ws], in0=acc, scalar=prob[:, 0:1],
-                in1=chunks(late["bias"][:])[:, cs, ws], op0=ALU.mult, op1=ALU.add)
+                out=chunks(late["mix"][:])[:, cs, ws], in0=acc, scalar=prob[:, e:e + 1],
+                in1=chunks(late["mix" if e else "bias"][:])[:, cs, ws], op0=ALU.mult, op1=ALU.add)
 
-        def mix_first_plain(lo, key, width):
-            acc = accs.pop(key)
-            first_whole, end_whole = -(-lo // PLAIN), (lo + width) // PLAIN
-            cuts = [lo, first_whole * PLAIN, end_whole * PLAIN, lo + width]
-            for a, b in zip(cuts, cuts[1:]):
-                if a < b:
-                    count = max(1, (b - a) // PLAIN)
-                    first = PLAIN_START + a % PLAIN
-                    mix_first(slice(a // PLAIN, a // PLAIN + count), slice(first, first + (b - a) // count),
-                              acc[:, a - lo:b - lo].rearrange("b (c w) -> b c w", c=count))
-            give(("bank", key))
+        def mix_bank(e, bank, parts):
+            for key, half, count in parts:
+                mix(e, *region(key, count), sums(key, bank, half, count))
+            accs.pop(bank)
+            give(("bank", bank))
 
-        def mix_pair(q, count):
-            k, l = turns[q * T_GROUP]
-            first = T_START[k] + l
-            mix_first(slice(0, CHUNKS), slice(first, first + count * T_GROUP),
-                      accs.pop(("pair", q))[:, :count * GROUP_COLS].rearrange("b (l c) -> b c l", c=CHUNKS))
-            give(("bank", ("pair", q)))
+        def cross(cs, ws):
+            part = chunks(late["mix"][:])[:, cs, ws]
+            nc.vector.tensor_tensor(out=part, in0=part, in1=chunks(late["x0"][:])[:, cs, ws], op=ALU.mult)
 
-        def mix_second(first, key, lo, hi):
-            ds = slice(first + lo, first + hi)
-            nc.vector.scalar_tensor_tensor(
-                out=late["mix"][:, ds], in0=accs[key][:, lo:hi], scalar=prob[:, 1:2], in1=late["mix"][:, ds],
-                op0=ALU.mult, op1=ALU.add)
-
-        def mix_block(blk, j):
-            mix_second(blk * W + j * NB, ("u", 1, blk, j), 0, NB)
-            give(("bank", ("u", 1, blk, j)))
-
-        def mix_stack(j):
-            mix_second(stacks[j][0], ("stack", j), 0, stacks[j][1])
-
-        def cross(first, width):
-            ds = slice(first, first + width)
-            nc.vector.tensor_tensor(out=late["mix"][:, ds], in0=late["mix"][:, ds], in1=late["x0"][:, ds], op=ALU.mult)
-
-        def finish(first, width):
-            ds = slice(first, first + width)
-            nc.vector.tensor_tensor(out=late["mix"][:, ds], in0=late["mix"][:, ds], in1=late["x"][:, ds], op=ALU.add)
-            nc.sync.dma_start(out=out[:, ds], in_=late["mix"][:, ds])
+        def finish(cs, ws):
+            part = chunks(late["mix"][:])[:, cs, ws]
+            nc.vector.tensor_tensor(out=part, in0=part, in1=chunks(late["x"][:])[:, cs, ws], op=ALU.add)
+            nc.sync.dma_start(out=chunks(out)[:, cs, ws], in_=part)
 
         make_identity(nc, ident[:])
         nc.vector.tensor_copy(out=ident16[:], in_=ident[:])
@@ -446,16 +368,18 @@ def tile_dcnv2lowrankexpertcross_w_kernel(tc, x0, x, v_bytes, v_scale, c, u, bia
             scales = v_scale.rearrange("o (g p t) u -> p (o g) (t u)", p=P, t=PACK)
             nc.scalar.dma_start(out=scale_first[:], in_=scales[:, :1, :])
             nc.scalar.dma_start(out=gate_sb[:], in_=gate_logits)
-            load_slab(0, stage[0], [(ts, slice(hb * W, (hb + 1) * W)) for hb in range(RH) for ts, cs in whole])
+            load_slab(0, stage[0], [(slice(t, t + 1), slice(0, W)) for t in range(PACK)]
+                      + [(ts, slice(W, R)) for ts, cs in whole])
             nc.sync.dma_start(out=scale_rest[:], in_=scales[:, 1:, :])
             load_slab(1, stage[1])
             x_early = place([B, D], BF16, stage[2], "x_early")
             nc.sync.dma_start(out=x_early[:], in_=x)
             early_at = [stage[3]] + [AT_TURN[1] + j * SLOT for j in range(T_BYTES // SLOT)]
             for j, where in enumerate(early_at):
-                load_slab(2 + j, where)
-                for r in range(-(-T_PIECES * j // len(early_at)), -(-T_PIECES * (j + 1) // len(early_at))):
+                load_slab(2 + j, where, whole if j < 4 else whole[:1])
+                for r in ([2 * j, 2 * j + 1] if j < 3 else [3 + j]):
                     load_turn(0, r)
+            load_slab(6, None, whole[1:])
             next_slab = 2 + len(early_at)
 
             for e in range(E):
@@ -463,14 +387,13 @@ def tile_dcnv2lowrankexpertcross_w_kernel(tc, x0, x, v_bytes, v_scale, c, u, bia
                     out=prob[:, e:e + 1], in_=gate_sb[:, 1 - e:2 - e], func=ACT.Sigmoid,
                     scale=-1.0, bias=gate_sb[:, e:e + 1])
             for t in range(PACK):
-                widen(0, t, 0, W, on_scalar=(t % 2 == 1))
-            take_grouped(0)
-            arrange_scalar(0)
+                widen(0, t, 0, W, on_scalar=(t == 1))
+            by_scalar(("v", 0), SHARE_HEAD, W)
             for t in range(PACK):
                 widen(0, t, W, R)
-            arrange_vector(0)
-            eye_interleave(1)
-            arrange(1)
+            by_vector(("v", 0), 0, SHARE_HEAD)
+            eye_interleave(("v", 1))
+            arrange(("v", 1), SHARE_HEAD)
             for t in range(PACK):
                 widen(1, t, 0, R)
             x_words = x_early[:].bitcast(F32)
@@ -486,7 +409,7 @@ def tile_dcnv2lowrankexpertcross_w_kernel(tc, x0, x, v_bytes, v_scale, c, u, bia
                     out=x_grouped[:, q * W:(q + 1) * W].bitcast(F32).rearrange("p (j r w) -> p j r w", j=2, w=2),
                     in_=bank[:].rearrange("p (j w) r -> p j r w", w=2))
                 give(("bank", ("x", q)))
-            eye_interleave(2)
+            eye_interleave(("v", 2))
 
             def quantize_x():
                 for lo, hi in ((0, 4), (4, V_PASSES)):
@@ -496,6 +419,9 @@ def tile_dcnv2lowrankexpertcross_w_kernel(tc, x0, x, v_bytes, v_scale, c, u, bia
                         in_=x_grouped[:, lo * K_PASS:hi * K_PASS])
                 give(("grouped", "x"))
 
+            units = [("v", i) for i in range(RH * len(slabs))] + [("y", e, ch) for e in range(E) for ch in range(CHUNKS)]
+            n, n_v = len(units), RH * len(slabs)
+            long_steps = n_v - 2 * RH
             loads, early, later, from_psum = {}, {}, {}, {}
 
             def at(table, step, fn, *args):
@@ -511,36 +437,63 @@ def tile_dcnv2lowrankexpertcross_w_kernel(tc, x0, x, v_bytes, v_scale, c, u, bia
             def arranged(i):
                 return RH * (i + 1) - 2
 
+            def share(i):
+                if i >= n - len(SHARE_END):
+                    return SHARE_END[i - n]
+                if i >= long_steps + 2:
+                    return SHARE_U
+                return SHARE_V if i % RH == 1 and i not in EYE_UNITS else 0
+
             ring = STAGE_SLOTS - 1
             last_slab = len(slabs) - 1
-            wide_at = [AT_WIDE + i % WIDE_BUFS * WIDE_BYTES for i in range(len(slabs))]
+            wide_at = [AT_WIDE + i % 3 * WIDE_BYTES for i in range(len(slabs))]
             for i in range(next_slab, len(slabs)):
                 at(loads, 0 if i < next_slab + ring else widened(i - ring), load_slab, i, stage[(i - next_slab) % ring])
             at(loads, 0, load_c)
             for r in range(T_PIECES):
                 at(loads, widened(next_slab - 1) + r // 2, load_turn, 1, r)
-            at(loads, widened(last_slab - 2), load_pass, 0, stage[2], 2)
-            at(loads, arranged(last_slab - 2), load_pass, 1, wide_at[last_slab - 2], 2)
-            at(loads, arranged(last_slab - 1), load_pass, 3, wide_at[last_slab - 1], 2)
-            at(loads, arranged(last_slab - 1), load_bias)
-            at(loads, widened(last_slab), free_stage.extend, stage[:2])
-            at(loads, arranged(last_slab), free_stage.append, wide_at[last_slab])
+            at(loads, widened(last_slab - 2), free_stage.extend, stage[2:])
+            for i in range(last_slab - 2, last_slab + 1):
+                at(loads, arranged(i), free_stage.extend, [wide_at[i]] + ([wide_at[i] + SLOT] if i < last_slab else []))
+            for i in (last_slab - 1, last_slab):
+                at(loads, widened(i), free_stage.append, stage[(i - next_slab) % ring])
             tanh_at = (stage[3], wide_at[last_slab] + SLOT)
-            stream = [(load_unit, (i,)) for i in range(n_v, n) if units[i][1] == 1]
-            stream[U_PASSES + 2:U_PASSES + 2] = [(load_rows, ("x0", x0)), (load_rows, ("x", x))]
+            stream = [(load_y, (key,)) for key in units[n_v:]]
+            stream[CHUNKS + 1:CHUNKS + 1] = [(load_rows, ("x0", x0)), (load_rows, ("x", x))]
 
             expert_end = [(e + 1) * n_v // E - 1 for e in range(E)]
             hidden_turns = [end + 3 for end in expert_end]
             hidden_scales = [end + 4 for end in expert_end]
             hidden_done = [end + 5 for end in expert_end]
+            n_banks = E * T_RUN // T_BANK
+
+            batch_at = list(range(T_FIRST + MX_BATCH, n_v, MX_BATCH)) + [hidden_done[1], T_LAST + 1]
+            short = [s for s in range(long_steps + 1, T_LAST + 1) if s - 1 != hidden_done[1]]
+            left = n_banks - 2 * len([s for s in range(T_FIRST, long_steps) if s - 1 not in batch_at]) + 2
 
             def banks_of(s):
-                if s < T_FIRST or (T_FIRST < s < n_v and s % MX_BATCH == 0):
+                if s < T_FIRST or s > T_LAST or (s - 1 in batch_at and s != n_v):
                     return 0
-                return (2 if T_FIRST < s < long_steps else 1) - (1 if s in hidden_turns else 0)
+                if s < long_steps:
+                    return 1 if s in hidden_turns or s == T_FIRST else 2
+                j = short.index(s)
+                return left * (j + 1) // len(short) - left * j // len(short)
+
+            def reuse_first_turned():
+                load_bias()
+                free_codes.extend([AT_LATE, AT_LATE + CODE_BYTES])
+
+            def after(s):
+                return 3 if s == hidden_done[1] else 1 if s > T_LAST + 1 else 2
+
+            def reads(step, e, bank, key, count):
+                at(from_psum, step, mix_bank, e, bank, [(key, 0, count)])
+                if e == 1:
+                    at(later, step + 1, cross, *region(key, count))
+                    at(later, step + 2, finish, *region(key, count))
 
             at(later, 0, quantize_x)
-            turned, full, pairs, quantized = 0, [], [], []
+            pairs, quantized = [], []
             for s in range(n - 1):
                 run(loads, s)
                 while stream and free_stage:
@@ -550,91 +503,81 @@ def tile_dcnv2lowrankexpertcross_w_kernel(tc, x0, x, v_bytes, v_scale, c, u, bia
                     for t in (2 * (s % 2), 2 * (s % 2) + 1):
                         widen(s // 2 + 2, t, 0, R)
                 run(early, s)
-                turning = T_FIRST <= s and turned < n_banks
-                ready, full = full, list(range(turned, min(n_banks, turned + banks_of(s))))
-                for b in full:
-                    turn_bank(b)
-                    if b + 1 == T_RUN[0] // T_BANK:
-                        at(loads, s + 1, reuse_first_turned)
-                turned += len(full)
-                if s + 2 < n:
-                    arrange(s + 2)
-                for b in ready:
-                    empty_bank(b)
-                    lag = 1 if b == n_banks - 1 else GROUP_LAG
-                    if b % per_group == per_group - 1:
-                        at(later, s + lag, quantize, ("t", b // per_group))
-                    if b % (2 * per_group) == 2 * per_group - 1:
-                        pairs.append((s + lag, b // per_group - 1, 2))
-                    elif b == n_banks - 1:
-                        pairs.append((s + lag, b // per_group, 1))
+                ready = len(full)
+                turn(banks_of(s))
+                if len(turned) - banks_of(s) < T_RUN // T_BANK <= len(turned):
+                    at(loads, s + 1, reuse_first_turned)
+                if s + 2 < n - 1:
+                    arrange(units[s + 2], share(s + 2))
+                elif s + 2 == n - 1:
+                    eye_interleave(last)
+                    by_scalar(last, 0, NB)
+                    empty_eye(last)
+                    by_scalar(last, NB, W)
+                if n_v <= s + 2 < n:
+                    give(("raw", units[s + 2]))
+                for b in range(ready):
+                    empty_bank()
+                while groups_full:
+                    key = groups_full.pop(0)
+                    lag = 1 if key[1] == E * GROUPS - 1 else GROUP_LAG
+                    at(later, s + lag, quantize, key)
+                    if key[1] % 2 == 1:
+                        pairs.append((s + lag, key[1] - 1))
                 if s + 3 in EYE_UNITS:
-                    eye_interleave(s + 3)
+                    eye_interleave(units[s + 3])
                 if s in from_psum:
                     run(later, s)
-                    quantize(s)
-                    pool_interleave(s + 3, len(from_psum[s]))
+                    quantize(units[s])
+                    if s + 3 < n - 1:
+                        pool_interleave(units[s + 3], 2 * len(from_psum[s]))
                     run(from_psum, s)
                 else:
-                    quantize(s)
+                    quantize(units[s])
                     run(later, s)
                 quantized.append(s)
-                if turning and s % MX_BATCH < MX_BATCH - 1:
+                if T_FIRST <= s < batch_at[-1] and s not in batch_at:
                     continue
                 batch, quantized = quantized, []
                 for i in batch:
-                    kind, e, blk, g = units[i]
-                    if kind == "stack":
-                        closes = g + stack_depth(blk) == U_PASSES
-                        multiply_stack(i, range(stack_depth(blk)), g == 0, closes)
-                        give(("codes", i))
-                        if closes and blk == 1:
-                            mix_stack(blk)
-                            at(later, s + 1, cross, *stacks[blk])
+                    key = units[i]
+                    if key[0] == "v":
+                        multiply_v(i)
+                    elif key[1:] < (1, CHUNKS - 2):
+                        bank = ("y", key[1], key[2] // 2)
+                        multiply_y(key, bank, key[2] % 2)
+                        if key[2] % 2 == 1:
+                            reads(s + after(s), key[1], bank, units[i - 1], 2)
                     else:
-                        multiply(i)
+                        multiply_y(key, "next to last", 0)
                     if i in expert_end:
+                        e = expert_end.index(i)
                         at(later, s + 2, hidden_tanh, e, tanh_at[e])
                         at(early, hidden_turns[e], hidden_turn, e)
-                        for bank_g in range(U_PASSES):
-                            at(from_psum, hidden_scales[e], hidden_scale, e, bank_g)
+                        for g in range(U_PASSES):
+                            at(from_psum, hidden_scales[e], hidden_scale, e, g)
                         at(later, hidden_done[e], hidden_quantize, e)
-                    if kind == "main" and g == U_PASSES - 1:
-                        for j in range(W // NB):
-                            at(from_psum, s + AFTER_BATCH, mix_first_plain, j * NB, (kind, e, blk, j), NB)
-                    if kind == "u" and g == U_PASSES - 1 and blk == 1:
-                        pool_interleave(s + 3, W // NB)
-                        for j in range(W // NB):
-                            mix_block(blk, j)
-                        at(later, s + 1, cross, W, W)
-                        at(later, s + 2, finish, W, W)
-                while pairs and pairs[0][0] <= s and s > hidden_done[0]:
-                    q, count = pairs.pop(0)[1:]
-                    multiply_pair(q, count)
-                    if turns[q * T_GROUP][0] == 0:
-                        at(from_psum, hidden_scales[1], mix_pair, q, count)
-                    elif count == 2:
-                        at(from_psum, s + AFTER_BATCH, mix_pair, q, count)
-                        at(from_psum, s + AFTER_BATCH, mix_first_plain, stacks[0][0], ("stack", 0), EXTRA)
-                    else:
-                        at(from_psum, s + 2, mix_pair, q, count)
-                        for j in range(W // NB):
-                            at(from_psum, s + 2, mix_block, 0, j)
-                        at(later, s + 3, cross, 0, W)
-                        at(later, s + 4, finish, 0, W)
+                while pairs and pairs[0][0] <= s and s >= (n_v - 1, hidden_done[1])[pairs[0][1] // GROUPS]:
+                    q = pairs.pop(0)[1]
+                    for half in range(2):
+                        multiply_y(("t", q + half), ("pair", q), half)
+                    e = q // GROUPS
+                    reads(s + after(s), e, ("pair", q), ("t", q), 2)
 
-            quantize(n - 1, 0, NB)
-            mix_stack(2)
-            finish(*stacks[1])
-            quantize(n - 1, W - EYE_END, W)
-            multiply_stack(n - 1, [0, 1, 3], True, False)
-            cross(*stacks[2])
-            quantize(n - 1, NB, W - EYE_END)
-            multiply_stack(n - 1, [2], False, True)
-            finish(*stacks[2])
-            for lo in (0, P):
-                mix_second(stacks[3][0], ("stack", 3), lo, lo + P)
-            for lo in (0, P):
-                cross(stacks[3][0] + lo, P)
-            for lo in (0, P):
-                finish(stacks[3][0] + lo, P)
+            quantize(last, 0, NB)
+            mix_bank(1, "next to last", [(units[n - 2], 0, 1)])
+            run(later, n - 1)
+            quantize(last, W - EYE_END, W)
+            multiply_y(last, "last", 0, [0, 1, 3], True, False)
+            cross(*region(units[n - 2], 1))
+            quantize(last, NB, W - EYE_END)
+            multiply_y(last, "last", 0, [2], False, True)
+            run(later, n)
+            finish(*region(units[n - 2], 1))
+            halves = [(slice(CHUNKS - 1, CHUNKS), slice(T_RUN + lo, T_RUN + lo + P)) for lo in (0, P)]
+            for j, (cs, ws) in enumerate(halves):
+                mix(1, cs, ws, accs["last"][:, j * P:(j + 1) * P].unsqueeze(1))
+            for cs, ws in halves:
+                cross(cs, ws)
+            for cs, ws in halves:
+                finish(cs, ws)

@@ -28,7 +28,7 @@ RH = R // W
 CHUNKS = 8
 CW = D // CHUNKS
 T_RUN = 128
-T_PITCH = 128
+T_PITCH = 144
 PLAIN = CW - T_RUN
 T_BANK = 8
 T_GROUP = 32
@@ -57,7 +57,7 @@ T_BYTES = P * T_PITCH * 2
 WIDE_BYTES = PACK * R * 2
 CODE_BYTES = 5 * W
 STAGE_SLOTS = 4
-GROUPED_SLOTS = 6
+GROUPED_SLOTS = 5
 CODE_SLOTS = 7
 AT_TURN = (0, T_BYTES)
 AT_WIDE = 2 * T_BYTES
@@ -422,7 +422,7 @@ def tile_dcnv2lowrankexpertcross_w_kernel(tc, x0, x, v_bytes, v_scale, c, u, bia
             units = [("v", i) for i in range(RH * len(slabs))] + [("y", e, ch) for e in range(E) for ch in range(CHUNKS)]
             n, n_v = len(units), RH * len(slabs)
             long_steps = n_v - 2 * RH
-            loads, early, later, from_psum = {}, {}, {}, {}
+            loads, early, groups, later, from_psum = {}, {}, {}, {}, {}
 
             def at(table, step, fn, *args):
                 table.setdefault(step, []).append((fn, args))
@@ -452,7 +452,8 @@ def tile_dcnv2lowrankexpertcross_w_kernel(tc, x0, x, v_bytes, v_scale, c, u, bia
             at(loads, 0, load_c)
             for r in range(T_PIECES):
                 at(loads, widened(next_slab - 1) + r // 2, load_turn, 1, r)
-            at(loads, widened(last_slab - 2), free_stage.extend, stage[2:])
+            at(loads, widened(last_slab - 2), free_stage.append, stage[2])
+            at(loads, widened(last_slab - 2), free_grouped.append, stage[3])
             for i in range(last_slab - 2, last_slab + 1):
                 at(loads, arranged(i), free_stage.extend, [wide_at[i]] + ([wide_at[i] + SLOT] if i < last_slab else []))
             for i in (last_slab - 1, last_slab):
@@ -482,6 +483,7 @@ def tile_dcnv2lowrankexpertcross_w_kernel(tc, x0, x, v_bytes, v_scale, c, u, bia
             def reuse_first_turned():
                 load_bias()
                 free_codes.extend([AT_LATE, AT_LATE + CODE_BYTES])
+                free_stage.append(AT_LATE + 2 * CODE_BYTES)
 
             def after(s):
                 return 3 if s == hidden_done[1] else 1 if s > T_LAST + 1 else 2
@@ -516,12 +518,13 @@ def tile_dcnv2lowrankexpertcross_w_kernel(tc, x0, x, v_bytes, v_scale, c, u, bia
                     by_scalar(last, NB, W)
                 if n_v <= s + 2 < n:
                     give(("raw", units[s + 2]))
+                run(groups, s)
                 for b in range(ready):
                     empty_bank()
                 while groups_full:
                     key = groups_full.pop(0)
                     lag = 1 if key[1] == E * GROUPS - 1 else GROUP_LAG
-                    at(later, s + lag, quantize, key)
+                    at(groups if lag == GROUP_LAG else later, s + lag, quantize, key)
                     if key[1] % 2 == 1:
                         pairs.append((s + lag, key[1] - 1))
                 if s + 3 in EYE_UNITS:

@@ -43,11 +43,10 @@ EYE_END = 256
 
 SHARE_HEAD = 192
 SHARE_V = 432
-SHARE_U = 416
+SHARE_U = 424
 T_FIRST = 7
-MX_BATCH = 4
 T_LAST = 32
-SHARE_END = (320, 128, 0, 0)
+SHARE_END = (192, 0, 0, 0)
 GROUP_LAG = 2
 POOL_COLS = 36
 POOL_LESS = 40
@@ -62,8 +61,9 @@ CODE_SLOTS = 7
 AT_TURN = (0, T_BYTES)
 AT_WIDE = 2 * T_BYTES
 AT_STAGE = AT_WIDE + 3 * WIDE_BYTES
-AT_GROUPED = AT_STAGE + STAGE_SLOTS * SLOT
+AT_GROUPED = AT_STAGE + (STAGE_SLOTS - 1) * SLOT
 AT_CODES = AT_GROUPED + GROUPED_SLOTS * SLOT
+AT_SPARE = AT_CODES + CODE_SLOTS * CODE_BYTES
 AT_MIX = AT_TURN[0]
 AT_BIAS = AT_MIX + 4 * D
 AT_LATE = AT_BIAS + 2 * D
@@ -225,8 +225,6 @@ def tile_dcnv2lowrankexpertcross_w_kernel(tc, x0, x, v_bytes, v_scale, c, u, bia
             interleave(nc.scalar.copy, take_grouped(key)[:, lo:hi, :], planes(key)[:, :, lo:hi])
 
         def arrange(key, share):
-            if share > 0:
-                by_vector(key, 0, share)
             by_scalar(key, share, W)
             empty_eye(key)
 
@@ -364,7 +362,7 @@ def tile_dcnv2lowrankexpertcross_w_kernel(tc, x0, x, v_bytes, v_scale, c, u, bia
             in_=ident[:].rearrange("q (t c g) -> q g c t", g=U_PASSES, c=CHUNKS))
 
         with tc.manual_schedule():
-            stage = [AT_STAGE + j * SLOT for j in range(STAGE_SLOTS)]
+            stage = [AT_STAGE + j * SLOT for j in range(STAGE_SLOTS - 1)] + [AT_SPARE]
             scales = v_scale.rearrange("o (g p t) u -> p (o g) (t u)", p=P, t=PACK)
             nc.scalar.dma_start(out=scale_first[:], in_=scales[:, :1, :])
             nc.scalar.dma_start(out=gate_sb[:], in_=gate_logits)
@@ -376,10 +374,9 @@ def tile_dcnv2lowrankexpertcross_w_kernel(tc, x0, x, v_bytes, v_scale, c, u, bia
             nc.sync.dma_start(out=x_early[:], in_=x)
             early_at = [stage[3]] + [AT_TURN[1] + j * SLOT for j in range(T_BYTES // SLOT)]
             for j, where in enumerate(early_at):
-                load_slab(2 + j, where, whole if j < 4 else whole[:1])
-                for r in ([2 * j, 2 * j + 1] if j < 3 else [3 + j]):
+                load_slab(2 + j, where, whole)
+                for r in range(2 * j, min(2 * j + 2, T_PIECES)):
                     load_turn(0, r)
-            load_slab(6, None, whole[1:])
             next_slab = 2 + len(early_at)
 
             for e in range(E):
@@ -394,6 +391,7 @@ def tile_dcnv2lowrankexpertcross_w_kernel(tc, x0, x, v_bytes, v_scale, c, u, bia
             by_vector(("v", 0), 0, SHARE_HEAD)
             eye_interleave(("v", 1))
             arrange(("v", 1), SHARE_HEAD)
+            by_vector(("v", 1), 0, SHARE_HEAD)
             for t in range(PACK):
                 widen(1, t, 0, R)
             x_words = x_early[:].bitcast(F32)
@@ -453,9 +451,11 @@ def tile_dcnv2lowrankexpertcross_w_kernel(tc, x0, x, v_bytes, v_scale, c, u, bia
             for r in range(T_PIECES):
                 at(loads, widened(next_slab - 1) + r // 2, load_turn, 1, r)
             at(loads, widened(last_slab - 2), free_stage.append, stage[2])
-            at(loads, widened(last_slab - 2), free_grouped.append, stage[3])
+            at(loads, 15, free_codes.extend, [AT_SPARE, AT_SPARE + CODE_BYTES])
             for i in range(last_slab - 2, last_slab + 1):
-                at(loads, arranged(i), free_stage.extend, [wide_at[i]] + ([wide_at[i] + SLOT] if i < last_slab else []))
+                at(loads, arranged(i), free_stage.append, wide_at[i])
+            at(loads, arranged(last_slab - 2), free_stage.append, wide_at[last_slab - 2] + SLOT)
+            at(loads, arranged(last_slab - 1), free_codes.append, wide_at[last_slab - 1] + SLOT)
             for i in (last_slab - 1, last_slab):
                 at(loads, widened(i), free_stage.append, stage[(i - next_slab) % ring])
             tanh_at = (stage[3], wide_at[last_slab] + SLOT)
@@ -468,25 +468,22 @@ def tile_dcnv2lowrankexpertcross_w_kernel(tc, x0, x, v_bytes, v_scale, c, u, bia
             hidden_done = [end + 5 for end in expert_end]
             n_banks = E * T_RUN // T_BANK
 
-            batch_at = list(range(T_FIRST + MX_BATCH, n_v, MX_BATCH)) + [hidden_done[1], T_LAST + 1]
-            short = [s for s in range(long_steps + 1, T_LAST + 1) if s - 1 != hidden_done[1]]
-            left = n_banks - 2 * len([s for s in range(T_FIRST, long_steps) if s - 1 not in batch_at]) + 2
+            batch_at = [11, 17, 23] + [hidden_done[1], T_LAST + 1]
 
             def banks_of(s):
-                if s < T_FIRST or s > T_LAST or (s - 1 in batch_at and s != n_v):
+                if s < T_FIRST or s > T_LAST:
                     return 0
-                if s < long_steps:
-                    return 1 if s in hidden_turns or s == T_FIRST else 2
-                j = short.index(s)
-                return left * (j + 1) // len(short) - left * j // len(short)
+                count = 2 if s <= long_steps or s == T_LAST - 1 else 1
+                less = s == T_FIRST or s in hidden_turns or (s in batch_at and s < n_v) or (s - 1 in batch_at and s != n_v)
+                return count - (1 if less else 0)
 
             def reuse_first_turned():
                 load_bias()
-                free_codes.extend([AT_LATE, AT_LATE + CODE_BYTES])
-                free_stage.append(AT_LATE + 2 * CODE_BYTES)
+                free_codes.extend([AT_LATE + j * CODE_BYTES for j in range(2)])
+                free_grouped.append(AT_LATE + 2 * CODE_BYTES)
 
             def after(s):
-                return 3 if s == hidden_done[1] else 1 if s > T_LAST + 1 else 2
+                return 3 if s in (n_v - 1, hidden_done[1]) else 1 if s > T_LAST + 1 else 2
 
             def reads(step, e, bank, key, count):
                 at(from_psum, step, mix_bank, e, bank, [(key, 0, count)])
@@ -516,15 +513,13 @@ def tile_dcnv2lowrankexpertcross_w_kernel(tc, x0, x, v_bytes, v_scale, c, u, bia
                     by_scalar(last, 0, NB)
                     empty_eye(last)
                     by_scalar(last, NB, W)
-                if n_v <= s + 2 < n:
-                    give(("raw", units[s + 2]))
                 run(groups, s)
                 for b in range(ready):
                     empty_bank()
                 while groups_full:
                     key = groups_full.pop(0)
                     lag = 1 if key[1] == E * GROUPS - 1 else GROUP_LAG
-                    at(groups if lag == GROUP_LAG else later, s + lag, quantize, key)
+                    at(groups if s < long_steps - 2 else later, s + lag, quantize, key)
                     if key[1] % 2 == 1:
                         pairs.append((s + lag, key[1] - 1))
                 if s + 3 in EYE_UNITS:
@@ -538,6 +533,10 @@ def tile_dcnv2lowrankexpertcross_w_kernel(tc, x0, x, v_bytes, v_scale, c, u, bia
                 else:
                     quantize(units[s])
                     run(later, s)
+                if s + 2 < n and share(s + 2) > 0:
+                    by_vector(units[s + 2], 0, share(s + 2))
+                if n_v <= s + 2 < n:
+                    give(("raw", units[s + 2]))
                 quantized.append(s)
                 if T_FIRST <= s < batch_at[-1] and s not in batch_at:
                     continue
@@ -555,7 +554,7 @@ def tile_dcnv2lowrankexpertcross_w_kernel(tc, x0, x, v_bytes, v_scale, c, u, bia
                         multiply_y(key, "next to last", 0)
                     if i in expert_end:
                         e = expert_end.index(i)
-                        at(later, s + 2, hidden_tanh, e, tanh_at[e])
+                        at(groups, s + 2, hidden_tanh, e, tanh_at[e])
                         at(early, hidden_turns[e], hidden_turn, e)
                         for g in range(U_PASSES):
                             at(from_psum, hidden_scales[e], hidden_scale, e, g)
@@ -568,13 +567,13 @@ def tile_dcnv2lowrankexpertcross_w_kernel(tc, x0, x, v_bytes, v_scale, c, u, bia
                     reads(s + after(s), e, ("pair", q), ("t", q), 2)
 
             quantize(last, 0, NB)
-            mix_bank(1, "next to last", [(units[n - 2], 0, 1)])
             run(later, n - 1)
             quantize(last, W - EYE_END, W)
             multiply_y(last, "last", 0, [0, 1, 3], True, False)
-            cross(*region(units[n - 2], 1))
+            mix_bank(1, "next to last", [(units[n - 2], 0, 1)])
             quantize(last, NB, W - EYE_END)
             multiply_y(last, "last", 0, [2], False, True)
+            cross(*region(units[n - 2], 1))
             run(later, n)
             finish(*region(units[n - 2], 1))
             halves = [(slice(CHUNKS - 1, CHUNKS), slice(T_RUN + lo, T_RUN + lo + P)) for lo in (0, P)]

@@ -43,13 +43,13 @@ EYE_END = 256
 
 SHARE_HEAD = 192
 SHARE_V = 432
-SHARE_U = 424
+SHARE_U = 416
 T_FIRST = 7
 T_LAST = 32
-SHARE_END = (192, 0, 0, 0)
+SHARE_END = (0, 192, 0, 0)
 GROUP_LAG = 2
-POOL_COLS = 36
-POOL_LESS = 40
+POOL_COLS = 80
+POOL_LESS = 16
 
 SLOT = PACK * W * 2
 T_BYTES = P * T_PITCH * 2
@@ -192,9 +192,9 @@ def tile_dcnv2lowrankexpertcross_w_kernel(tc, x0, x, v_bytes, v_scale, c, u, bia
                 grouped[key] = place([P, W, PACK], BF16, take(free_grouped, ("grouped", key), newest), "grouped")
             return grouped[key]
 
-        def pool_interleave(key, halves):
-            pooled[key] = POOL_COLS * halves - POOL_LESS
-            cs = slice(W - pooled[key], W)
+        def pool_interleave(key, reads):
+            pooled[key] = POOL_COLS * reads - POOL_LESS
+            cs = slice(W - eye_cols(key) - pooled[key], W - eye_cols(key))
             interleave(pool_copy, take_grouped(key, newest=True)[:, cs, :], planes(key)[:, :, cs])
 
         def eye_interleave(i):
@@ -436,6 +436,8 @@ def tile_dcnv2lowrankexpertcross_w_kernel(tc, x0, x, v_bytes, v_scale, c, u, bia
                 return RH * (i + 1) - 2
 
             def share(i):
+                if i >= n:
+                    return 0
                 if i >= n - len(SHARE_END):
                     return SHARE_END[i - n]
                 if i >= long_steps + 2:
@@ -525,16 +527,19 @@ def tile_dcnv2lowrankexpertcross_w_kernel(tc, x0, x, v_bytes, v_scale, c, u, bia
                 if s + 3 in EYE_UNITS:
                     eye_interleave(units[s + 3])
                 if s in from_psum:
+                    kept = later.get(s, [])[-1:] if share(s + 2) == 0 else []
+                    later[s] = later.get(s, [])[:len(later.get(s, [])) - len(kept)]
                     run(later, s)
+                    later[s] = kept
                     quantize(units[s])
-                    if s + 3 < n - 1:
-                        pool_interleave(units[s + 3], 2 * len(from_psum[s]))
-                    run(from_psum, s)
+                    if s + 3 < n:
+                        pool_interleave(units[s + 3], len(from_psum[s]))
                 else:
                     quantize(units[s])
-                    run(later, s)
-                if s + 2 < n and share(s + 2) > 0:
+                run(later, s)
+                if share(s + 2) > 0:
                     by_vector(units[s + 2], 0, share(s + 2))
+                run(from_psum, s)
                 if n_v <= s + 2 < n:
                     give(("raw", units[s + 2]))
                 quantized.append(s)

@@ -43,12 +43,13 @@ EYE_END = 256
 
 SHARE_HEAD = 192
 SHARE_V = 432
-SHARE_U = 416
+SHARE_U = 420
 T_FIRST = 7
 T_LAST = 32
+X_AT = 24
 SHARE_END = (0, 192, 0, 0)
 GROUP_LAG = 2
-POOL_COLS = 80
+POOL_COLS = 84
 POOL_LESS = 16
 
 SLOT = PACK * W * 2
@@ -138,10 +139,10 @@ def tile_dcnv2lowrankexpertcross_w_kernel(tc, x0, x, v_bytes, v_scale, c, u, bia
             ps = slice(half * P // 2, (half + 1) * P // 2)
             nc.sync.dma_start(out=turn_sb[e][g:P:U_PASSES, ps, :T_RUN], in_=src[:, ps, :T_RUN])
 
-        def load_y(key):
+        def load_y(key, free=free_stage):
             kind, e, ch = key
             first = ch * CW + T_RUN
-            raw[key] = place([P, PACK, W], BF16, take(free_stage, ("raw", key)), "u_raw")
+            raw[key] = place([P, PACK, W], BF16, take(free, ("raw", key)), "u_raw")
             for g in range(U_PASSES):
                 rows = u[e, g * K_PASS:(g + 1) * K_PASS, :].rearrange("(p t) w -> p t w", t=PACK)
                 nc.sync.dma_start(out=raw[key][:, :, g * YW:(g + 1) * YW], in_=rows[:, :, first:first + YW])
@@ -154,7 +155,10 @@ def tile_dcnv2lowrankexpertcross_w_kernel(tc, x0, x, v_bytes, v_scale, c, u, bia
             nc.sync.dma_start(out=late["bias"][:], in_=bias.partition_broadcast(P))
 
         def load_rows(label, src):
-            late[label] = place([B, D], BF16, take(free_stage, label), label)
+            where = min(a for a in free_codes if a + CODE_BYTES in free_codes)
+            free_codes.remove(where)
+            free_codes.remove(where + CODE_BYTES)
+            late[label] = place([B, D], BF16, where, label)
             nc.sync.dma_start(out=late[label][:], in_=src)
 
         def widen(i, t, lo, hi, on_scalar=False):
@@ -350,10 +354,10 @@ def tile_dcnv2lowrankexpertcross_w_kernel(tc, x0, x, v_bytes, v_scale, c, u, bia
             part = chunks(late["mix"][:])[:, cs, ws]
             nc.vector.tensor_tensor(out=part, in0=part, in1=chunks(late["x0"][:])[:, cs, ws], op=ALU.mult)
 
-        def finish(cs, ws):
+        def finish(cs, ws, queue=nc.sync):
             part = chunks(late["mix"][:])[:, cs, ws]
             nc.vector.tensor_tensor(out=part, in0=part, in1=chunks(late["x"][:])[:, cs, ws], op=ALU.add)
-            nc.sync.dma_start(out=chunks(out)[:, cs, ws], in_=part)
+            queue.dma_start(out=chunks(out)[:, cs, ws], in_=part)
 
         make_identity(nc, ident[:])
         nc.vector.tensor_copy(out=ident16[:], in_=ident[:])
@@ -384,7 +388,7 @@ def tile_dcnv2lowrankexpertcross_w_kernel(tc, x0, x, v_bytes, v_scale, c, u, bia
                     out=prob[:, e:e + 1], in_=gate_sb[:, 1 - e:2 - e], func=ACT.Sigmoid,
                     scale=-1.0, bias=gate_sb[:, e:e + 1])
             for t in range(PACK):
-                widen(0, t, 0, W, on_scalar=(t == 1))
+                widen(0, t, 0, W, on_scalar=(t == 2))
             by_scalar(("v", 0), SHARE_HEAD, W)
             for t in range(PACK):
                 widen(0, t, W, R)
@@ -461,8 +465,10 @@ def tile_dcnv2lowrankexpertcross_w_kernel(tc, x0, x, v_bytes, v_scale, c, u, bia
             for i in (last_slab - 1, last_slab):
                 at(loads, widened(i), free_stage.append, stage[(i - next_slab) % ring])
             tanh_at = (stage[3], wide_at[last_slab] + SLOT)
+            at(loads, n_v + 3, free_stage.append, tanh_at[1])
             stream = [(load_y, (key,)) for key in units[n_v:]]
-            stream[CHUNKS + 1:CHUNKS + 1] = [(load_rows, ("x0", x0)), (load_rows, ("x", x))]
+            at(loads, n_v, load_rows, "x0", x0)
+            at(loads, X_AT, load_rows, "x", x)
 
             expert_end = [(e + 1) * n_v // E - 1 for e in range(E)]
             hidden_turns = [end + 3 for end in expert_end]
@@ -480,6 +486,8 @@ def tile_dcnv2lowrankexpertcross_w_kernel(tc, x0, x, v_bytes, v_scale, c, u, bia
                 return count - (1 if less else 0)
 
             def reuse_first_turned():
+                fn, args = stream.pop(0)
+                fn(*args, [AT_MIX])
                 load_bias()
                 free_codes.extend([AT_LATE + j * CODE_BYTES for j in range(2)])
                 free_grouped.append(AT_LATE + 2 * CODE_BYTES)
@@ -504,7 +512,7 @@ def tile_dcnv2lowrankexpertcross_w_kernel(tc, x0, x, v_bytes, v_scale, c, u, bia
                     for t in (2 * (s % 2), 2 * (s % 2) + 1):
                         widen(s // 2 + 2, t, 0, R)
                 run(early, s)
-                ready = len(full)
+                ready = 1 if s == T_LAST else len(full)
                 turn(banks_of(s))
                 if len(turned) - banks_of(s) < T_RUN // T_BANK <= len(turned):
                     at(loads, s + 1, reuse_first_turned)
@@ -586,5 +594,5 @@ def tile_dcnv2lowrankexpertcross_w_kernel(tc, x0, x, v_bytes, v_scale, c, u, bia
                 mix(1, cs, ws, accs["last"][:, j * P:(j + 1) * P].unsqueeze(1))
             for cs, ws in halves:
                 cross(cs, ws)
-            for cs, ws in halves:
-                finish(cs, ws)
+            for (cs, ws), queue in zip(halves, (nc.sync, nc.scalar)):
+                finish(cs, ws, queue)

@@ -28,7 +28,7 @@ RH = R // W
 CHUNKS = 8
 CW = D // CHUNKS
 T_RUN = 128
-T_PITCH = 144
+T_PITCH = 136
 PLAIN = CW - T_RUN
 T_BANK = 8
 T_GROUP = 32
@@ -53,7 +53,7 @@ POOL_COLS = 84
 POOL_LESS = 16
 
 SLOT = PACK * W * 2
-T_BYTES = P * T_PITCH * 2
+T_BYTES = 36 * W
 WIDE_BYTES = PACK * R * 2
 CODE_BYTES = 5 * W
 STAGE_SLOTS = 4

@@ -29,7 +29,6 @@ CHUNKS = 8
 CW = D // CHUNKS
 T_RUN = 128
 T_PITCH = 136
-PLAIN = CW - T_RUN
 T_BANK = 8
 T_GROUP = 32
 YW = 256
@@ -43,17 +42,16 @@ EYE_END = 256
 
 SHARE_HEAD = 192
 SHARE_V = 432
-SHARE_U = 420
+SHARE_U = 416
 T_FIRST = 7
 T_LAST = 32
-X_AT = 24
-SHARE_END = (0, 192, 0, 0)
+SHARE_END = 128
 GROUP_LAG = 2
-POOL_COLS = 84
+POOL_COLS = 80
 POOL_LESS = 16
 
 SLOT = PACK * W * 2
-T_BYTES = 36 * W
+T_BYTES = P * T_PITCH * 2
 WIDE_BYTES = PACK * R * 2
 CODE_BYTES = 5 * W
 STAGE_SLOTS = 4
@@ -65,7 +63,10 @@ AT_STAGE = AT_WIDE + 3 * WIDE_BYTES
 AT_GROUPED = AT_STAGE + (STAGE_SLOTS - 1) * SLOT
 AT_CODES = AT_GROUPED + GROUPED_SLOTS * SLOT
 AT_SPARE = AT_CODES + CODE_SLOTS * CODE_BYTES
-AT_MIX = AT_TURN[0]
+AT_X = AT_SPARE + 2 * CODE_BYTES
+AT_LHS = AT_X + 2 * D
+AT_ONCE = AT_TURN[0]
+AT_MIX = AT_ONCE + 3 * W
 AT_BIAS = AT_MIX + 4 * D
 AT_LATE = AT_BIAS + 2 * D
 
@@ -85,16 +86,19 @@ def tile_dcnv2lowrankexpertcross_w_kernel(tc, x0, x, v_bytes, v_scale, c, u, bia
         c_sb = const.tile([P, E * U_PASSES, PACK], BF16)
         gate_sb = const.tile([B, E], BF16)
         prob = const.tile([B, E], F32)
-        x_codes = const.tile([P, V_PASSES, B], U32, align_bytes=64)
-        x_scales = const.tile([P, V_PASSES, B], U8, align_bytes=64)
-        h_codes = const.tile([P, E, U_PASSES, B], U32, align_bytes=64)
-        h_scales = const.tile([P, E, U_PASSES, B], U8, align_bytes=64)
+        h_first = (const.tile([P, U_PASSES, B], U32, align_bytes=64, name="h_codes"),
+                   const.tile([P, U_PASSES, B], U8, align_bytes=64, name="h_scales"))
 
         made = []
 
         def place(shape, dtype, offset, label):
             made.append(label)
             return arena.tile(shape, dtype, offset=offset, align_bytes=64, name="%s%d" % (label, len(made)))
+
+        x_grouped = place([P, V_PASSES * K_PASS], BF16, AT_X, "x_grouped")
+        x_codes = place([P, V_PASSES, B], U32, AT_LHS, "x_codes")
+        x_scales = place([P, V_PASSES, B], U8, AT_LHS + 4 * V_PASSES * B, "x_scales")
+        h_mx = {0: h_first}
 
         free_banks = list(range(BANKS))
         free_stage = []
@@ -115,8 +119,10 @@ def tile_dcnv2lowrankexpertcross_w_kernel(tc, x0, x, v_bytes, v_scale, c, u, bia
 
         slabs = [(e, g) for e in range(E) for g in range(V_PASSES)]
         raw, slab_raw, wide, grouped, codes, accs, hid = {}, {}, {}, {}, {}, {}, {}
-        eye_out, t_banks, turn_sb, late, pooled = {}, {}, {}, {}, {}
+        eye_out, t_banks, turn_sb, late, pooled, crossed, x_banks = {}, {}, {}, {}, {}, {}, {}
         last = ("y", 1, CHUNKS - 1)
+        last_cuts = (0, NB, W - EYE_END, W)
+        last_parts = {}
 
         def chunks(ap):
             return ap.rearrange("b (c w) -> b c w", c=CHUNKS)
@@ -154,12 +160,12 @@ def tile_dcnv2lowrankexpertcross_w_kernel(tc, x0, x, v_bytes, v_scale, c, u, bia
             late["bias"] = place([B, D], BF16, AT_BIAS, "bias_sb")
             nc.sync.dma_start(out=late["bias"][:], in_=bias.partition_broadcast(P))
 
-        def load_rows(label, src):
+        def load_x0():
             where = min(a for a in free_codes if a + CODE_BYTES in free_codes)
             free_codes.remove(where)
             free_codes.remove(where + CODE_BYTES)
-            late[label] = place([B, D], BF16, where, label)
-            nc.sync.dma_start(out=late[label][:], in_=src)
+            late["x0"] = place([B, D], BF16, where, "x0_sb")
+            nc.sync.dma_start(out=late["x0"][:], in_=x0)
 
         def widen(i, t, lo, hi, on_scalar=False):
             e, g = slabs[i]
@@ -196,6 +202,16 @@ def tile_dcnv2lowrankexpertcross_w_kernel(tc, x0, x, v_bytes, v_scale, c, u, bia
                 grouped[key] = place([P, W, PACK], BF16, take(free_grouped, ("grouped", key), newest), "grouped")
             return grouped[key]
 
+        def columns(key, lo, hi):
+            if key != last:
+                return take_grouped(key)[:, lo:hi, :]
+            if not last_parts:
+                where = take(free_grouped, ("grouped", key))
+                for a, b in zip(last_cuts, last_cuts[1:]):
+                    last_parts[a] = (where + a * PACK * 2, place([P, b - a, PACK], BF16, where + a * PACK * 2, "last"))
+            first = max(a for a in last_cuts if a <= lo)
+            return last_parts[first][1][:, lo - first:hi - first, :]
+
         def pool_interleave(key, reads):
             pooled[key] = POOL_COLS * reads - POOL_LESS
             cs = slice(W - eye_cols(key) - pooled[key], W - eye_cols(key))
@@ -217,16 +233,16 @@ def tile_dcnv2lowrankexpertcross_w_kernel(tc, x0, x, v_bytes, v_scale, c, u, bia
             for j, bank in enumerate(eye_out.pop(i, [])):
                 first = W - eye_cols(i) + j * 2 * P
                 nc.scalar.copy(
-                    out=grouped[i][:, first:first + 2 * P, :].rearrange("p w t -> p (w t)").bitcast(F32),
+                    out=columns(i, first, first + 2 * P).rearrange("p w t -> p (w t)").bitcast(F32),
                     in_=bank[:].bitcast(F32))
                 give(("bank", ("eye", i, j)))
 
         def by_vector(key, lo, hi):
-            interleave(nc.vector.tensor_copy, take_grouped(key)[:, lo:hi, :], planes(key)[:, :, lo:hi])
+            interleave(nc.vector.tensor_copy, columns(key, lo, hi), planes(key)[:, :, lo:hi])
 
         def by_scalar(key, lo, hi):
             hi = min(hi, W - eye_cols(key) - pooled.get(key, 0))
-            interleave(nc.scalar.copy, take_grouped(key)[:, lo:hi, :], planes(key)[:, :, lo:hi])
+            interleave(nc.scalar.copy, columns(key, lo, hi), planes(key)[:, :, lo:hi])
 
         def arrange(key, share):
             by_scalar(key, share, W)
@@ -256,13 +272,13 @@ def tile_dcnv2lowrankexpertcross_w_kernel(tc, x0, x, v_bytes, v_scale, c, u, bia
 
         def quantize(key, lo=0, hi=W):
             if key not in codes:
-                where = take(free_codes, ("codes", key))
+                where = take([AT_ONCE] if key == ("v", RH * len(slabs) - 1) else free_codes, ("codes", key))
                 codes[key] = (place([P, W], U32, where, "w_codes"), place([P, W], U8, where + 4 * W, "w_scales"))
             w_codes, w_scales = codes[key]
             nc.vector.quantize_mx(
                 out=w_codes[:, lo:hi].bitcast(FP8X4), scales=w_scales[:, lo:hi],
-                in_=grouped[key][:, lo:hi, :].rearrange("p w t -> p (w t)"))
-            if hi == W:
+                in_=columns(key, lo, hi).rearrange("p w t -> p (w t)"))
+            if key != last:
                 give(("grouped", key))
 
         def mx_pass(acc, lhs, lhs_scale, key, cs, start, stop):
@@ -270,10 +286,6 @@ def tile_dcnv2lowrankexpertcross_w_kernel(tc, x0, x, v_bytes, v_scale, c, u, bia
             nc.tensor.matmul_mx(
                 out=acc, lhsT=lhs.bitcast(FP8X4), lhsT_scale=lhs_scale,
                 rhs=w_codes[:, cs].bitcast(FP8X4), rhs_scale=w_scales[:, cs], start=start, stop=stop)
-
-        def quantize_groups():
-            while groups_full:
-                quantize(groups_full.pop(0))
 
         def multiply_v(i):
             (e, g), hb = slabs[i // RH], i % RH
@@ -290,7 +302,7 @@ def tile_dcnv2lowrankexpertcross_w_kernel(tc, x0, x, v_bytes, v_scale, c, u, bia
             if bank not in accs:
                 accs[bank] = take_bank(bank, [B, NB], F32)
             for g in passes:
-                mx_pass(accs[bank][:, half * YW:(half + 1) * YW], h_codes[:, e, g, :], h_scales[:, e, g, :], key,
+                mx_pass(accs[bank][:, half * YW:(half + 1) * YW], h_mx[e][0][:, g, :], h_mx[e][1][:, g, :], key,
                         slice(g * YW, (g + 1) * YW), opens and g == passes[0], closes and g == passes[-1])
             if closes:
                 give(("codes", key))
@@ -319,9 +331,12 @@ def tile_dcnv2lowrankexpertcross_w_kernel(tc, x0, x, v_bytes, v_scale, c, u, bia
             give(("bank", ("h", g)))
 
         def hidden_quantize(e):
+            if e not in h_mx:
+                h_mx[e] = (place([P, U_PASSES, B], U32, AT_LHS, "h_codes"),
+                           place([P, U_PASSES, B], U8, AT_LHS + 4 * U_PASSES * B, "h_scales"))
             nc.vector.quantize_mx(
-                out=h_codes[:, e, :, :].rearrange("p g b -> p (g b)").bitcast(FP8X4),
-                scales=h_scales[:, e, :, :].rearrange("p g b -> p (g b)"),
+                out=h_mx[e][0][:].rearrange("p g b -> p (g b)").bitcast(FP8X4),
+                scales=h_mx[e][1][:].rearrange("p g b -> p (g b)"),
                 in_=hid.pop(e)[:].rearrange("p g b t -> p (g b t)"))
             give("hg")
 
@@ -350,14 +365,52 @@ def tile_dcnv2lowrankexpertcross_w_kernel(tc, x0, x, v_bytes, v_scale, c, u, bia
             accs.pop(bank)
             give(("bank", bank))
 
-        def cross(cs, ws):
-            part = chunks(late["mix"][:])[:, cs, ws]
-            nc.vector.tensor_tensor(out=part, in0=part, in1=chunks(late["x0"][:])[:, cs, ws], op=ALU.mult)
+        def turn_x_back(j):
+            first = 2 * j * CW // K_PASS
+            bank = take_bank(("x", j), [B, 2, P, 2], F32)
+            words = x_grouped[:].bitcast(F32).rearrange("p (g b w) -> p g b w", g=V_PASSES, w=2)
+            for g in range(2):
+                for w in range(2):
+                    nc.tensor.transpose(bank[:, g, :, w], words[:, first + g, :, w], ident[:])
+            skip = 2 * j * CW - first * K_PASS
+            flat = bank[:].rearrange("b g p w -> b (g p w)").bitcast(BF16)
+            x_banks[j] = flat[:, skip:skip + 2 * CW].rearrange("b (c w) -> b c w", c=2)
 
-        def finish(cs, ws, queue=nc.sync):
-            part = chunks(late["mix"][:])[:, cs, ws]
-            nc.vector.tensor_tensor(out=part, in0=part, in1=chunks(late["x"][:])[:, cs, ws], op=ALU.add)
+        def cross(engine, dst, cs, ws):
+            engine.tensor_tensor(
+                out=dst, in0=chunks(late["mix"][:])[:, cs, ws], in1=chunks(late["x0"][:])[:, cs, ws], op=ALU.mult)
+
+        def finish(part, cs, ws):
+            j = cs.start // 2
+            nc.vector.tensor_tensor(
+                out=part, in0=part, in1=x_banks[j][:, cs.start - 2 * j:cs.stop - 2 * j, ws], op=ALU.add)
+
+        def store(part, cs, ws, queue=nc.sync):
             queue.dma_start(out=chunks(out)[:, cs, ws], in_=part)
+
+        def cross_turned(half):
+            if half == 0:
+                crossed["t"] = place([B, CHUNKS, T_RUN], F32, take(free_grouped, "crossed t", newest=True), "crossed")
+            ws = slice(half * T_RUN // 2, (half + 1) * T_RUN // 2)
+            cross(nc.gpsimd, crossed["t"][:, :, ws], slice(0, CHUNKS), ws)
+
+        def finish_turned(j):
+            cs = slice(2 * j, 2 * j + 2)
+            finish(crossed["t"][:, cs, :], cs, slice(0, T_RUN))
+            if cs.stop == CHUNKS:
+                store(crossed["t"][:], slice(0, CHUNKS), slice(0, T_RUN))
+
+        def cross_plain(j, where=None):
+            if where is None:
+                where = take(free_grouped, ("crossed", j), newest=True)
+            crossed[j] = place([B, 2, YW], F32, where, "crossed")
+            cross(nc.gpsimd, crossed[j][:], slice(2 * j, 2 * j + 2), slice(T_RUN, CW))
+
+        def finish_plain(j):
+            cs, ws = slice(2 * j, 2 * j + 2), slice(T_RUN, CW)
+            finish(crossed[j][:], cs, ws)
+            store(crossed[j][:], cs, ws)
+            give(("bank", ("x", j)))
 
         make_identity(nc, ident[:])
         nc.vector.tensor_copy(out=ident16[:], in_=ident[:])
@@ -399,7 +452,6 @@ def tile_dcnv2lowrankexpertcross_w_kernel(tc, x0, x, v_bytes, v_scale, c, u, bia
             for t in range(PACK):
                 widen(1, t, 0, R)
             x_words = x_early[:].bitcast(F32)
-            x_grouped = take_grouped("x")[:].rearrange("p w t -> p (w t)")
             for q in range(V_PASSES // 2):
                 bank = take_bank(("x", q), [P, 4, B], F32)
                 for j in range(2):
@@ -419,9 +471,10 @@ def tile_dcnv2lowrankexpertcross_w_kernel(tc, x0, x, v_bytes, v_scale, c, u, bia
                         out=x_codes[:, lo:hi, :].rearrange("p g b -> p (g b)").bitcast(FP8X4),
                         scales=x_scales[:, lo:hi, :].rearrange("p g b -> p (g b)"),
                         in_=x_grouped[:, lo * K_PASS:hi * K_PASS])
-                give(("grouped", "x"))
 
-            units = [("v", i) for i in range(RH * len(slabs))] + [("y", e, ch) for e in range(E) for ch in range(CHUNKS)]
+            units = [("v", i) for i in range(RH * len(slabs))]
+            for e, lo, hi in ((0, 0, 6), (1, 0, 4), (0, 6, 8), (1, 4, 8)):
+                units.extend([("y", e, ch) for ch in range(lo, hi)])
             n, n_v = len(units), RH * len(slabs)
             long_steps = n_v - 2 * RH
             loads, early, groups, later, from_psum = {}, {}, {}, {}, {}
@@ -442,8 +495,8 @@ def tile_dcnv2lowrankexpertcross_w_kernel(tc, x0, x, v_bytes, v_scale, c, u, bia
             def share(i):
                 if i >= n:
                     return 0
-                if i >= n - len(SHARE_END):
-                    return SHARE_END[i - n]
+                if i >= n - 2:
+                    return SHARE_END
                 if i >= long_steps + 2:
                     return SHARE_U
                 return SHARE_V if i % RH == 1 and i not in EYE_UNITS else 0
@@ -467,14 +520,12 @@ def tile_dcnv2lowrankexpertcross_w_kernel(tc, x0, x, v_bytes, v_scale, c, u, bia
             tanh_at = (stage[3], wide_at[last_slab] + SLOT)
             at(loads, n_v + 3, free_stage.append, tanh_at[1])
             stream = [(load_y, (key,)) for key in units[n_v:]]
-            at(loads, n_v, load_rows, "x0", x0)
-            at(loads, X_AT, load_rows, "x", x)
+            at(loads, n_v, load_x0)
 
             expert_end = [(e + 1) * n_v // E - 1 for e in range(E)]
             hidden_turns = [end + 3 for end in expert_end]
             hidden_scales = [end + 4 for end in expert_end]
             hidden_done = [end + 5 for end in expert_end]
-            n_banks = E * T_RUN // T_BANK
 
             batch_at = [11, 17, 23] + [hidden_done[1], T_LAST + 1]
 
@@ -487,22 +538,37 @@ def tile_dcnv2lowrankexpertcross_w_kernel(tc, x0, x, v_bytes, v_scale, c, u, bia
 
             def reuse_first_turned():
                 fn, args = stream.pop(0)
-                fn(*args, [AT_MIX])
+                fn(*args, [AT_ONCE + CODE_BYTES])
                 load_bias()
-                free_codes.extend([AT_LATE + j * CODE_BYTES for j in range(2)])
-                free_grouped.append(AT_LATE + 2 * CODE_BYTES)
+                free_codes.append(AT_LATE)
+                free_grouped.append(AT_LATE + CODE_BYTES)
 
             def after(s):
-                return 3 if s in (n_v - 1, hidden_done[1]) else 1 if s > T_LAST + 1 else 2
+                return 3 if s in batch_at else 1
 
             def reads(step, e, bank, key, count):
                 at(from_psum, step, mix_bank, e, bank, [(key, 0, count)])
-                if e == 1:
-                    at(later, step + 1, cross, *region(key, count))
-                    at(later, step + 2, finish, *region(key, count))
+
+            end = batch_at[-1] + 3
+            released = {}
+            at(released, end, cross_turned, 0)
+            at(released, end + 1, cross_plain, 0)
+            at(released, end + 2, cross_plain, 1)
+            closing = {}
+            for j in range(CHUNKS // 2):
+                at(closing, end + 1, finish_turned, j)
+            at(closing, end + 2, finish_plain, 0)
+
+            pairs, quantized = [], []
+
+            def multiply_pairs(s):
+                while pairs and pairs[0][0] <= s and s >= (n_v - 1, hidden_done[1])[pairs[0][1] // GROUPS]:
+                    q = pairs.pop(0)[1]
+                    for half in range(2):
+                        multiply_y(("t", q + half), ("pair", q), half)
+                    reads(s + after(s) if s < batch_at[-1] else end, q // GROUPS, ("pair", q), ("t", q), 2)
 
             at(later, 0, quantize_x)
-            pairs, quantized = [], []
             for s in range(n - 1):
                 run(loads, s)
                 while stream and free_stage:
@@ -520,7 +586,7 @@ def tile_dcnv2lowrankexpertcross_w_kernel(tc, x0, x, v_bytes, v_scale, c, u, bia
                     arrange(units[s + 2], share(s + 2))
                 elif s + 2 == n - 1:
                     eye_interleave(last)
-                    by_scalar(last, 0, NB)
+                    by_scalar(last, share(s + 2), NB)
                     empty_eye(last)
                     by_scalar(last, NB, W)
                 run(groups, s)
@@ -528,32 +594,40 @@ def tile_dcnv2lowrankexpertcross_w_kernel(tc, x0, x, v_bytes, v_scale, c, u, bia
                     empty_bank()
                 while groups_full:
                     key = groups_full.pop(0)
-                    lag = 1 if key[1] == E * GROUPS - 1 else GROUP_LAG
-                    at(groups if s < long_steps - 2 else later, s + lag, quantize, key)
+                    if key[1] == E * GROUPS - 1:
+                        lag, table = 1, closing
+                    else:
+                        lag, table = GROUP_LAG, groups if s < long_steps - 2 else later
+                    at(table, s + lag, quantize, key)
                     if key[1] % 2 == 1:
                         pairs.append((s + lag, key[1] - 1))
                 if s + 3 in EYE_UNITS:
                     eye_interleave(units[s + 3])
                 if s in from_psum:
-                    kept = later.get(s, [])[-1:] if share(s + 2) == 0 else []
-                    later[s] = later.get(s, [])[:len(later.get(s, [])) - len(kept)]
                     run(later, s)
-                    later[s] = kept
-                    quantize(units[s])
-                    if s + 3 < n:
-                        pool_interleave(units[s + 3], len(from_psum[s]))
-                else:
-                    quantize(units[s])
+                quantize(units[s])
+                if s in from_psum and s < end:
+                    pool_interleave(units[s + 3], len(from_psum[s]))
+                run(released, s)
                 run(later, s)
                 if share(s + 2) > 0:
                     by_vector(units[s + 2], 0, share(s + 2))
+                if s == n - 2:
+                    quantize(last, *last_cuts[0:2])
+                if s == end:
+                    for fn, args in (from_psum[s].pop(0), from_psum[s].pop(2)):
+                        fn(*args)
+                    cross_turned(1)
                 run(from_psum, s)
+                run(closing, s)
                 if n_v <= s + 2 < n:
                     give(("raw", units[s + 2]))
                 quantized.append(s)
                 if T_FIRST <= s < batch_at[-1] and s not in batch_at:
                     continue
                 batch, quantized = quantized, []
+                if s > batch_at[-1]:
+                    multiply_pairs(s)
                 for i in batch:
                     key = units[i]
                     if key[0] == "v":
@@ -572,27 +646,23 @@ def tile_dcnv2lowrankexpertcross_w_kernel(tc, x0, x, v_bytes, v_scale, c, u, bia
                         for g in range(U_PASSES):
                             at(from_psum, hidden_scales[e], hidden_scale, e, g)
                         at(later, hidden_done[e], hidden_quantize, e)
-                while pairs and pairs[0][0] <= s and s >= (n_v - 1, hidden_done[1])[pairs[0][1] // GROUPS]:
-                    q = pairs.pop(0)[1]
-                    for half in range(2):
-                        multiply_y(("t", q + half), ("pair", q), half)
-                    e = q // GROUPS
-                    reads(s + after(s), e, ("pair", q), ("t", q), 2)
+                multiply_pairs(s)
+                if end - 1 <= s <= end:
+                    for j in range(2):
+                        turn_x_back(2 * (s - end + 1) + j)
 
-            quantize(last, 0, NB)
-            run(later, n - 1)
-            quantize(last, W - EYE_END, W)
-            multiply_y(last, "last", 0, [0, 1, 3], True, False)
+            multiply_y(last, "last", 0, [0, 1], True, False)
+            quantize(last, *last_cuts[1:3])
+            cross_plain(2, last_parts[last_cuts[1]][0])
+            quantize(last, *last_cuts[2:4])
+            multiply_y(last, "last", 0, [2, 3], False, True)
+            finish_plain(1)
             mix_bank(1, "next to last", [(units[n - 2], 0, 1)])
-            quantize(last, NB, W - EYE_END)
-            multiply_y(last, "last", 0, [2], False, True)
-            cross(*region(units[n - 2], 1))
-            run(later, n)
-            finish(*region(units[n - 2], 1))
-            halves = [(slice(CHUNKS - 1, CHUNKS), slice(T_RUN + lo, T_RUN + lo + P)) for lo in (0, P)]
-            for j, (cs, ws) in enumerate(halves):
-                mix(1, cs, ws, accs["last"][:, j * P:(j + 1) * P].unsqueeze(1))
-            for cs, ws in halves:
-                cross(cs, ws)
-            for (cs, ws), queue in zip(halves, (nc.sync, nc.scalar)):
-                finish(cs, ws, queue)
+            mix_bank(1, "last", [(last, 0, 1)])
+            ends = [region(key, 1) for key in units[n - 2:]]
+            for cs, ws in ends:
+                cross(nc.vector, chunks(late["mix"][:])[:, cs, ws], cs, ws)
+            finish_plain(2)
+            for (cs, ws), queue in zip(ends, (nc.sync, nc.scalar)):
+                finish(chunks(late["mix"][:])[:, cs, ws], cs, ws)
+                store(chunks(late["mix"][:])[:, cs, ws], cs, ws, queue)

@@ -42,11 +42,13 @@ EYE_END = 256
 
 SHARE_HEAD = 192
 SHARE_V = 432
-SHARE_U = 416
+SHARE_U = 432
 T_FIRST = 7
-T_LAST = 32
-SHARE_END = 128
+T_LAST = 31
+SHARE_END = (96, 96, 96)
 GROUP_LAG = 2
+READ_LAG = 2
+REDIR = (31, 32)
 POOL_COLS = 80
 POOL_LESS = 16
 
@@ -121,8 +123,9 @@ def tile_dcnv2lowrankexpertcross_w_kernel(tc, x0, x, v_bytes, v_scale, c, u, bia
         raw, slab_raw, wide, grouped, codes, accs, hid = {}, {}, {}, {}, {}, {}, {}
         eye_out, t_banks, turn_sb, late, pooled, crossed, x_banks = {}, {}, {}, {}, {}, {}, {}
         last = ("y", 1, CHUNKS - 1)
-        last_cuts = (0, NB, W - EYE_END, W)
-        last_parts = {}
+        before_last = ("y", 1, CHUNKS - 2)
+        cuts = {before_last: (0, NB, W), last: (0, NB, W - EYE_END, W)}
+        parts = {}
 
         def chunks(ap):
             return ap.rearrange("b (c w) -> b c w", c=CHUNKS)
@@ -161,10 +164,7 @@ def tile_dcnv2lowrankexpertcross_w_kernel(tc, x0, x, v_bytes, v_scale, c, u, bia
             nc.sync.dma_start(out=late["bias"][:], in_=bias.partition_broadcast(P))
 
         def load_x0():
-            where = min(a for a in free_codes if a + CODE_BYTES in free_codes)
-            free_codes.remove(where)
-            free_codes.remove(where + CODE_BYTES)
-            late["x0"] = place([B, D], BF16, where, "x0_sb")
+            late["x0"] = place([B, D], BF16, take(free_stage, "x0"), "x0_sb")
             nc.sync.dma_start(out=late["x0"][:], in_=x0)
 
         def widen(i, t, lo, hi, on_scalar=False):
@@ -202,20 +202,20 @@ def tile_dcnv2lowrankexpertcross_w_kernel(tc, x0, x, v_bytes, v_scale, c, u, bia
                 grouped[key] = place([P, W, PACK], BF16, take(free_grouped, ("grouped", key), newest), "grouped")
             return grouped[key]
 
-        def columns(key, lo, hi):
-            if key != last:
-                return take_grouped(key)[:, lo:hi, :]
-            if not last_parts:
-                where = take(free_grouped, ("grouped", key))
-                for a, b in zip(last_cuts, last_cuts[1:]):
-                    last_parts[a] = (where + a * PACK * 2, place([P, b - a, PACK], BF16, where + a * PACK * 2, "last"))
-            first = max(a for a in last_cuts if a <= lo)
-            return last_parts[first][1][:, lo - first:hi - first, :]
+        def columns(key, lo, hi, newest=False):
+            if key not in cuts:
+                return take_grouped(key, newest)[:, lo:hi, :]
+            if (key, 0) not in parts:
+                where = take(free_grouped, ("grouped", key), newest)
+                for a, b in zip(cuts[key], cuts[key][1:]):
+                    parts[key, a] = (where + a * PACK * 2, place([P, b - a, PACK], BF16, where + a * PACK * 2, "part"))
+            first = max(a for a in cuts[key] if a <= lo)
+            return parts[key, first][1][:, lo - first:hi - first, :]
 
         def pool_interleave(key, reads):
             pooled[key] = POOL_COLS * reads - POOL_LESS
             cs = slice(W - eye_cols(key) - pooled[key], W - eye_cols(key))
-            interleave(pool_copy, take_grouped(key, newest=True)[:, cs, :], planes(key)[:, :, cs])
+            interleave(pool_copy, columns(key, cs.start, cs.stop, newest=True), planes(key)[:, :, cs])
 
         def eye_interleave(i):
             src = planes(i)[:, :, W - eye_cols(i):]
@@ -278,7 +278,7 @@ def tile_dcnv2lowrankexpertcross_w_kernel(tc, x0, x, v_bytes, v_scale, c, u, bia
             nc.vector.quantize_mx(
                 out=w_codes[:, lo:hi].bitcast(FP8X4), scales=w_scales[:, lo:hi],
                 in_=columns(key, lo, hi).rearrange("p w t -> p (w t)"))
-            if key != last:
+            if key not in cuts:
                 give(("grouped", key))
 
         def mx_pass(acc, lhs, lhs_scale, key, cs, start, stop):
@@ -495,8 +495,8 @@ def tile_dcnv2lowrankexpertcross_w_kernel(tc, x0, x, v_bytes, v_scale, c, u, bia
             def share(i):
                 if i >= n:
                     return 0
-                if i >= n - 2:
-                    return SHARE_END
+                if i >= n - len(SHARE_END):
+                    return SHARE_END[i - n]
                 if i >= long_steps + 2:
                     return SHARE_U
                 return SHARE_V if i % RH == 1 and i not in EYE_UNITS else 0
@@ -518,21 +518,21 @@ def tile_dcnv2lowrankexpertcross_w_kernel(tc, x0, x, v_bytes, v_scale, c, u, bia
             for i in (last_slab - 1, last_slab):
                 at(loads, widened(i), free_stage.append, stage[(i - next_slab) % ring])
             tanh_at = (stage[3], wide_at[last_slab] + SLOT)
-            at(loads, n_v + 3, free_stage.append, tanh_at[1])
+            at(loads, n_v + 3, free_codes.append, tanh_at[1])
             stream = [(load_y, (key,)) for key in units[n_v:]]
-            at(loads, n_v, load_x0)
+            stream.insert(len(stream) - 4, (load_x0, ()))
 
             expert_end = [(e + 1) * n_v // E - 1 for e in range(E)]
             hidden_turns = [end + 3 for end in expert_end]
             hidden_scales = [end + 4 for end in expert_end]
             hidden_done = [end + 5 for end in expert_end]
 
-            batch_at = [11, 17, 23] + [hidden_done[1], T_LAST + 1]
+            batch_at = [11, 17, 23, T_LAST + 1]
 
             def banks_of(s):
                 if s < T_FIRST or s > T_LAST:
                     return 0
-                count = 2 if s <= long_steps or s == T_LAST - 1 else 1
+                count = 2 if s < long_steps or s >= T_LAST - 1 else 1
                 less = s == T_FIRST or s in hidden_turns or (s in batch_at and s < n_v) or (s - 1 in batch_at and s != n_v)
                 return count - (1 if less else 0)
 
@@ -543,17 +543,14 @@ def tile_dcnv2lowrankexpertcross_w_kernel(tc, x0, x, v_bytes, v_scale, c, u, bia
                 free_codes.append(AT_LATE)
                 free_grouped.append(AT_LATE + CODE_BYTES)
 
-            def after(s):
-                return 3 if s in batch_at else 1
-
             def reads(step, e, bank, key, count):
                 at(from_psum, step, mix_bank, e, bank, [(key, 0, count)])
 
-            end = batch_at[-1] + 3
+            end = n - 4
+            first_reads = batch_at[-1] + READ_LAG
             released = {}
             at(released, end, cross_turned, 0)
             at(released, end + 1, cross_plain, 0)
-            at(released, end + 2, cross_plain, 1)
             closing = {}
             for j in range(CHUNKS // 2):
                 at(closing, end + 1, finish_turned, j)
@@ -562,11 +559,11 @@ def tile_dcnv2lowrankexpertcross_w_kernel(tc, x0, x, v_bytes, v_scale, c, u, bia
             pairs, quantized = [], []
 
             def multiply_pairs(s):
-                while pairs and pairs[0][0] <= s and s >= (n_v - 1, hidden_done[1])[pairs[0][1] // GROUPS]:
+                while pairs and pairs[0][0] <= s and s >= (n_v - 1, batch_at[-1])[pairs[0][1] // GROUPS]:
                     q = pairs.pop(0)[1]
                     for half in range(2):
                         multiply_y(("t", q + half), ("pair", q), half)
-                    reads(s + after(s) if s < batch_at[-1] else end, q // GROUPS, ("pair", q), ("t", q), 2)
+                    reads(s + 3 if s < batch_at[-1] else first_reads if s == batch_at[-1] else end, q // GROUPS, ("pair", q), ("t", q), 2)
 
             at(later, 0, quantize_x)
             for s in range(n - 1):
@@ -578,12 +575,15 @@ def tile_dcnv2lowrankexpertcross_w_kernel(tc, x0, x, v_bytes, v_scale, c, u, bia
                     for t in (2 * (s % 2), 2 * (s % 2) + 1):
                         widen(s // 2 + 2, t, 0, R)
                 run(early, s)
-                ready = 1 if s == T_LAST else len(full)
+                ready = len(full) if s <= T_LAST else min(len(full), 1)
                 turn(banks_of(s))
                 if len(turned) - banks_of(s) < T_RUN // T_BANK <= len(turned):
                     at(loads, s + 1, reuse_first_turned)
-                if s + 2 < n - 1:
+                if s + 2 < n - 2:
                     arrange(units[s + 2], share(s + 2))
+                elif s + 2 == n - 2:
+                    by_scalar(before_last, share(s + 2), NB)
+                    by_scalar(before_last, NB, W)
                 elif s + 2 == n - 1:
                     eye_interleave(last)
                     by_scalar(last, share(s + 2), NB)
@@ -594,39 +594,42 @@ def tile_dcnv2lowrankexpertcross_w_kernel(tc, x0, x, v_bytes, v_scale, c, u, bia
                     empty_bank()
                 while groups_full:
                     key = groups_full.pop(0)
-                    if key[1] == E * GROUPS - 1:
-                        lag, table = 1, closing
-                    else:
-                        lag, table = GROUP_LAG, groups if s < long_steps - 2 else later
-                    at(table, s + lag, quantize, key)
+                    at(groups if s < long_steps - 2 else later, s + GROUP_LAG, quantize, key)
                     if key[1] % 2 == 1:
-                        pairs.append((s + lag, key[1] - 1))
+                        pairs.append((s + GROUP_LAG, key[1] - 1))
                 if s + 3 in EYE_UNITS:
                     eye_interleave(units[s + 3])
-                if s in from_psum:
-                    run(later, s)
-                quantize(units[s])
+                if s < n - 2:
+                    quantize(units[s])
+                else:
+                    quantize(before_last, 0, NB)
+                    cross_plain(1, parts[before_last, 0][0])
+                    quantize(before_last, NB, W)
                 if s in from_psum and s < end:
                     pool_interleave(units[s + 3], len(from_psum[s]))
                 run(released, s)
-                run(later, s)
+                if s not in from_psum:
+                    run(later, s)
                 if share(s + 2) > 0:
                     by_vector(units[s + 2], 0, share(s + 2))
-                if s == n - 2:
-                    quantize(last, *last_cuts[0:2])
                 if s == end:
-                    for fn, args in (from_psum[s].pop(0), from_psum[s].pop(2)):
+                    pair = [job for job in from_psum[s] if job[1][1][0] == "pair"]
+                    from_psum[s].remove(pair[0])
+                    for fn, args in [from_psum[s].pop(0)] + pair:
                         fn(*args)
                     cross_turned(1)
                 run(from_psum, s)
                 run(closing, s)
-                if n_v <= s + 2 < n:
+                run(later, s)
+                if s in REDIR:
+                    free_codes.append(held.pop(("raw", units[s + 2]))[1])
+                elif n_v <= s + 2 < n:
                     give(("raw", units[s + 2]))
                 quantized.append(s)
                 if T_FIRST <= s < batch_at[-1] and s not in batch_at:
                     continue
                 batch, quantized = quantized, []
-                if s > batch_at[-1]:
+                if s >= batch_at[-1]:
                     multiply_pairs(s)
                 for i in batch:
                     key = units[i]
@@ -636,7 +639,7 @@ def tile_dcnv2lowrankexpertcross_w_kernel(tc, x0, x, v_bytes, v_scale, c, u, bia
                         bank = ("y", key[1], key[2] // 2)
                         multiply_y(key, bank, key[2] % 2)
                         if key[2] % 2 == 1:
-                            reads(s + after(s), key[1], bank, units[i - 1], 2)
+                            reads(first_reads if i < n_v + 4 else max(end, s + 1), key[1], bank, units[i - 1], 2)
                     else:
                         multiply_y(key, "next to last", 0)
                     if i in expert_end:
@@ -651,10 +654,11 @@ def tile_dcnv2lowrankexpertcross_w_kernel(tc, x0, x, v_bytes, v_scale, c, u, bia
                     for j in range(2):
                         turn_x_back(2 * (s - end + 1) + j)
 
+            quantize(last, 0, NB)
             multiply_y(last, "last", 0, [0, 1], True, False)
-            quantize(last, *last_cuts[1:3])
-            cross_plain(2, last_parts[last_cuts[1]][0])
-            quantize(last, *last_cuts[2:4])
+            quantize(last, NB, W - EYE_END)
+            cross_plain(2, parts[last, NB][0])
+            quantize(last, W - EYE_END, W)
             multiply_y(last, "last", 0, [2, 3], False, True)
             finish_plain(1)
             mix_bank(1, "next to last", [(units[n - 2], 0, 1)])

from contextlib import ExitStack

import concourse.mybir as mybir
from concourse.masks import make_identity

B, D, R, E = 128, 3072, 2048, 2
P = 128
PACK = 4
K_PASS = P * PACK
FLOPS = 2 * 2 * E * B * D * R

F32 = mybir.dt.float32
BF16 = mybir.dt.bfloat16
U32 = mybir.dt.uint32
U8 = mybir.dt.uint8
FP8 = mybir.dt.float8_e4m3fn
FP8X4 = mybir.dt.float8_e4m3fn_x4
ACT = mybir.ActivationFunctionType
ALU = mybir.AluOpType

W = 1024
NB = 512
BANKS = 8
V_PASSES = D // K_PASS
U_PASSES = R // K_PASS
RH = R // W

CHUNKS = 8
CW = D // CHUNKS
T_RUN = 128
T_PITCH = 136
T_BANK = 8
T_GROUP = 32
YW = 256
T_PIECES = 2 * U_PASSES
PER_GROUP = T_GROUP // T_BANK
GROUPS = T_RUN // T_GROUP

EYE_UNITS = range(1, 10)
EYE_COLS = 512
EYE_END = 256

SHARE_HEAD = 192
SHARE_V = 432
SHARE_U = 432
T_FIRST = 7
T_LAST = 31
SHARE_END = (96, 96, 96)
GROUP_LAG = 2
READ_LAG = 2
REDIR = (31, 32)
POOL_COLS = 80
POOL_LESS = 16

SLOT = PACK * W * 2
T_BYTES = P * T_PITCH * 2
WIDE_BYTES = PACK * R * 2
CODE_BYTES = 5 * W
STAGE_SLOTS = 4
GROUPED_SLOTS = 5
CODE_SLOTS = 7
AT_TURN = (0, T_BYTES)
AT_WIDE = 2 * T_BYTES
AT_STAGE = AT_WIDE + 3 * WIDE_BYTES
AT_GROUPED = AT_STAGE + (STAGE_SLOTS - 1) * SLOT
AT_CODES = AT_GROUPED + GROUPED_SLOTS * SLOT
AT_SPARE = AT_CODES + CODE_SLOTS * CODE_BYTES
AT_X = AT_SPARE + 2 * CODE_BYTES
AT_LHS = AT_X + 2 * D
AT_ONCE = AT_TURN[0]
AT_MIX = AT_ONCE + 3 * W
AT_BIAS = AT_MIX + 4 * D
AT_LATE = AT_BIAS + 2 * D


def tile_dcnv2lowrankexpertcross_w_kernel(tc, x0, x, v_bytes, v_scale, c, u, bias, gate_logits, out):
    nc = tc.nc
    with ExitStack() as ctx:
        const = ctx.enter_context(tc.tile_pool(name="const", bufs=1))
        arena = ctx.enter_context(tc.tile_pool(name="arena", bufs=1))
        psum = ctx.enter_context(tc.psum_pool(name="psum", bufs=1))

        ident = const.tile([P, P], F32)
        ident16 = const.tile([P, P], BF16)
        perm16 = const.tile([P, P], BF16)
        scale_first = const.tile([P, 1, PACK], F32)
        scale_rest = const.tile([P, V_PASSES - 1, PACK], F32)
        c_sb = const.tile([P, E * U_PASSES, PACK], BF16)
        gate_sb = const.tile([B, E], BF16)
        prob = const.tile([B, E], F32)
        h_first = (const.tile([P, U_PASSES, B], U32, align_bytes=64, name="h_codes"),
                   const.tile([P, U_PASSES, B], U8, align_bytes=64, name="h_scales"))

        made = []

        def place(shape, dtype, offset, label):
            made.append(label)
            return arena.tile(shape, dtype, offset=offset, align_bytes=64, name="%s%d" % (label, len(made)))

        x_grouped = place([P, V_PASSES * K_PASS], BF16, AT_X, "x_grouped")
        x_codes = place([P, V_PASSES, B], U32, AT_LHS, "x_codes")
        x_scales = place([P, V_PASSES, B], U8, AT_LHS + 4 * V_PASSES * B, "x_scales")
        h_mx = {0: h_first}

        free_banks = list(range(BANKS))
        free_stage = []
        free_grouped = [AT_GROUPED + j * SLOT for j in range(GROUPED_SLOTS)]
        free_codes = [AT_CODES + j * CODE_BYTES for j in range(CODE_SLOTS)]
        held = {}

        def take(free, key, newest=False):
            held[key] = (free, free.pop(-1 if newest else 0))
            return held[key][1]

        def give(key):
            free, where = held.pop(key)
            free.append(where)

        def take_bank(key, shape, dtype):
            return psum.tile(shape, dtype, name="bank%d" % take(free_banks, ("bank", key)))

        slabs = [(e, g) for e in range(E) for g in range(V_PASSES)]
        raw, slab_raw, wide, grouped, codes, accs, hid = {}, {}, {}, {}, {}, {}, {}
        eye_out, t_banks, turn_sb, late, pooled, crossed, x_banks = {}, {}, {}, {}, {}, {}, {}
        last = ("y", 1, CHUNKS - 1)
        before_last = ("y", 1, CHUNKS - 2)
        cuts = {before_last: (0, NB, W), last: (0, NB, W - EYE_END, W)}
        parts = {}

        def chunks(ap):
            return ap.rearrange("b (c w) -> b c w", c=CHUNKS)

        whole = [(slice(0, 2), slice(0, R)), (slice(2, 4), slice(0, R))]

        def load_slab(i, where=None, pieces=whole):
            e, g = slabs[i]
            if i not in slab_raw:
                slab_raw[i] = place([P, PACK, R], U8, where, "v_raw")
            rows = v_bytes[e, g * K_PASS:(g + 1) * K_PASS, :].rearrange("(p t) w -> p t w", t=PACK)
            for ts, cs in pieces:
                nc.sync.dma_start(out=slab_raw[i][:, ts, cs], in_=rows[:, ts, cs])

        def load_turn(e, r):
            g, half = divmod(r, 2)
            if e not in turn_sb:
                turn_sb[e] = place([P, P, T_PITCH], BF16, AT_TURN[e], "u_turn")
            src = u[e, g * K_PASS:(g + 1) * K_PASS, :].rearrange("(p t) (c w) -> (t c) p w", t=PACK, c=CHUNKS)
            ps = slice(half * P // 2, (half + 1) * P // 2)
            nc.sync.dma_start(out=turn_sb[e][g:P:U_PASSES, ps, :T_RUN], in_=src[:, ps, :T_RUN])

        def load_y(key, free=free_stage):
            kind, e, ch = key
            first = ch * CW + T_RUN
            raw[key] = place([P, PACK, W], BF16, take(free, ("raw", key)), "u_raw")
            for g in range(U_PASSES):
                rows = u[e, g * K_PASS:(g + 1) * K_PASS, :].rearrange("(p t) w -> p t w", t=PACK)
                nc.sync.dma_start(out=raw[key][:, :, g * YW:(g + 1) * YW], in_=rows[:, :, first:first + YW])

        def load_c():
            nc.sync.dma_start(out=c_sb[:], in_=c.rearrange("e (g p t) -> p (e g) t", p=P, t=PACK))

        def load_bias():
            late["bias"] = place([B, D], BF16, AT_BIAS, "bias_sb")
            nc.sync.dma_start(out=late["bias"][:], in_=bias.partition_broadcast(P))

        def load_x0():
            late["x0"] = place([B, D], BF16, take(free_stage, "x0"), "x0_sb")
            nc.sync.dma_start(out=late["x0"][:], in_=x0)

        def widen(i, t, lo, hi, on_scalar=False):
            e, g = slabs[i]
            if i not in wide:
                if i == 0:
                    wide[i] = place([P, RH, PACK, W], BF16, AT_WIDE, "v_wide")
                else:
                    wide[i] = place([P, PACK, R], BF16, AT_WIDE + i % 3 * WIDE_BYTES, "v_wide")
            src = slab_raw[i][:, t, lo:hi].bitcast(FP8)
            dst = wide[i][:, lo // W, t, :] if i == 0 else wide[i][:, t, :]
            scale = scale_first[:, 0, t:t + 1] if g == 0 else scale_rest[:, g - 1, t:t + 1]
            if on_scalar:
                nc.scalar.activation(out=dst, in_=src, func=ACT.Copy, scale=scale)
            else:
                nc.vector.tensor_scalar(out=dst, in0=src, scalar1=scale, scalar2=None, op0=ALU.mult)

        def planes(key):
            if key[0] == "y":
                return raw[key][:]
            i = key[1]
            return wide[0][:, i, :, :] if i < RH else wide[i // RH][:, :, i % RH * W:(i % RH + 1) * W]

        def interleave(copy, dst, src):
            copy(out=dst.rearrange("p (c i) t -> p c t i", i=2), in_=src.rearrange("p t (c i) -> p c t i", i=2))

        def pool_copy(out, in_):
            nc.gpsimd.tensor_scalar(out=out, in0=in_, scalar1=1.0, scalar2=0.0, op0=ALU.mult, op1=ALU.add)

        def eye_cols(key):
            return EYE_COLS if key[0] == "v" and key[1] in EYE_UNITS else EYE_END if key == last else 0

        def take_grouped(key, newest=False):
            if key not in grouped:
                grouped[key] = place([P, W, PACK], BF16, take(free_grouped, ("grouped", key), newest), "grouped")
            return grouped[key]

        def columns(key, lo, hi, newest=False):
            if key not in cuts:
                return take_grouped(key, newest)[:, lo:hi, :]
            if (key, 0) not in parts:
                where = take(free_grouped, ("grouped", key), newest)
                for a, b in zip(cuts[key], cuts[key][1:]):
                    parts[key, a] = (where + a * PACK * 2, place([P, b - a, PACK], BF16, where + a * PACK * 2, "part"))
            first = max(a for a in cuts[key] if a <= lo)
            return parts[key, first][1][:, lo - first:hi - first, :]

        def pool_interleave(key, reads):
            pooled[key] = POOL_COLS * reads - POOL_LESS
            cs = slice(W - eye_cols(key) - pooled[key], W - eye_cols(key))
            interleave(pool_copy, columns(key, cs.start, cs.stop, newest=True), planes(key)[:, :, cs])

        def eye_interleave(i):
            src = planes(i)[:, :, W - eye_cols(i):]
            eye_out[i] = []
            for j in range(eye_cols(i) // (2 * P)):
                bank = take_bank(("eye", i, j), [P, 2 * NB], BF16)
                for m in range(2):
                    first = (2 * j + m) * P
                    nc.tensor.matmul(
                        out=bank[:, m * NB:(m + 1) * NB], lhsT=ident16[:],
                        rhs=src[:, :, first:first + P].rearrange("p t w -> p w t"), start=True, stop=True)
                eye_out[i].append(bank)

        def empty_eye(i):
            for j, bank in enumerate(eye_out.pop(i, [])):
                first = W - eye_cols(i) + j * 2 * P
                nc.scalar.copy(
                    out=columns(i, first, first + 2 * P).rearrange("p w t -> p (w t)").bitcast(F32),
                    in_=bank[:].bitcast(F32))
                give(("bank", ("eye", i, j)))

        def by_vector(key, lo, hi):
            interleave(nc.vector.tensor_copy, columns(key, lo, hi), planes(key)[:, :, lo:hi])

        def by_scalar(key, lo, hi):
            hi = min(hi, W - eye_cols(key) - pooled.get(key, 0))
            interleave(nc.scalar.copy, columns(key, lo, hi), planes(key)[:, :, lo:hi])

        def arrange(key, share):
            by_scalar(key, share, W)
            empty_eye(key)

        turned, full, groups_full = [], [], []

        def turn(count):
            for b in range(len(turned), min(len(turned) + count, E * T_RUN // T_BANK)):
                e, first = divmod(b * T_BANK, T_RUN)
                t_banks[b] = take_bank(("t", b), [P, U_PASSES, T_BANK, CHUNKS * PACK], BF16)
                for j in range(T_BANK):
                    nc.tensor.transpose(t_banks[b][:, :, j, :], turn_sb[e][:, :, first + j], perm16[:])
                turned.append(b)
                full.append(b)

        def empty_bank():
            b = full.pop(0)
            key = ("t", b // PER_GROUP)
            dst = take_grouped(key)[:].rearrange("p (g q w) t -> p g q (w t)", g=U_PASSES, q=PER_GROUP)
            nc.scalar.copy(
                out=dst[:, :, b % PER_GROUP, :].bitcast(F32),
                in_=t_banks.pop(b)[:].rearrange("p g l x -> p g (l x)").bitcast(F32))
            give(("bank", ("t", b)))
            if b % PER_GROUP == PER_GROUP - 1:
                groups_full.append(key)

        def quantize(key, lo=0, hi=W):
            if key not in codes:
                where = take([AT_ONCE] if key == ("v", RH * len(slabs) - 1) else free_codes, ("codes", key))
                codes[key] = (place([P, W], U32, where, "w_codes"), place([P, W], U8, where + 4 * W, "w_scales"))
            w_codes, w_scales = codes[key]
            nc.vector.quantize_mx(
                out=w_codes[:, lo:hi].bitcast(FP8X4), scales=w_scales[:, lo:hi],
                in_=columns(key, lo, hi).rearrange("p w t -> p (w t)"))
            if key not in cuts:
                give(("grouped", key))

        def mx_pass(acc, lhs, lhs_scale, key, cs, start, stop):
            w_codes, w_scales = codes[key]
            nc.tensor.matmul_mx(
                out=acc, lhsT=lhs.bitcast(FP8X4), lhsT_scale=lhs_scale,
                rhs=w_codes[:, cs].bitcast(FP8X4), rhs_scale=w_scales[:, cs], start=start, stop=stop)

        def multiply_v(i):
            (e, g), hb = slabs[i // RH], i % RH
            for j in range(W // NB):
                key = ("v", e, hb, j)
                if g == 0:
                    accs[key] = take_bank(key, [B, NB], F32)
                mx_pass(accs[key][:], x_codes[:, g, :], x_scales[:, g, :], ("v", i), slice(j * NB, (j + 1) * NB),
                        g == 0, g == V_PASSES - 1)
            give(("codes", ("v", i)))

        def multiply_y(key, bank, half, passes=range(U_PASSES), opens=True, closes=True):
            e = key[1] if key[0] == "y" else key[1] // GROUPS
            if bank not in accs:
                accs[bank] = take_bank(bank, [B, NB], F32)
            for g in passes:
                mx_pass(accs[bank][:, half * YW:(half + 1) * YW], h_mx[e][0][:, g, :], h_mx[e][1][:, g, :], key,
                        slice(g * YW, (g + 1) * YW), opens and g == passes[0], closes and g == passes[-1])
            if closes:
                give(("codes", key))

        def hidden_tanh(e, where):
            hid[e] = place([B, U_PASSES, PACK, P], F32, where, "th")
            for g in range(U_PASSES):
                key = ("v", e, g // 2, g % 2)
                nc.scalar.activation(
                    out=hid[e][:, g, :, :], in_=accs.pop(key)[:].rearrange("b (p t) -> b t p", t=PACK), func=ACT.Tanh)
                give(("bank", key))

        def hidden_turn(e):
            for g in range(U_PASSES):
                accs[("h", g)] = take_bank(("h", g), [P, PACK, B], F32)
                for t in range(PACK):
                    nc.tensor.transpose(accs[("h", g)][:, t, :], hid[e][:, g, t, :], ident[:])

        def hidden_scale(e, g):
            if g == 0:
                hid[e] = place([P, U_PASSES, B, PACK], BF16, take(free_codes, "hg"), "hg")
            at_c = e * U_PASSES + g
            nc.vector.tensor_tensor(
                out=hid[e][:, g, :, :], in0=accs.pop(("h", g))[:].rearrange("p t b -> p b t"),
                in1=c_sb[:, at_c:at_c + 1, :].to_broadcast([P, B, PACK]), op=ALU.mult)
            give(("bank", ("h", g)))

        def hidden_quantize(e):
            if e not in h_mx:
                h_mx[e] = (place([P, U_PASSES, B], U32, AT_LHS, "h_codes"),
                           place([P, U_PASSES, B], U8, AT_LHS + 4 * U_PASSES * B, "h_scales"))
            nc.vector.quantize_mx(
                out=h_mx[e][0][:].rearrange("p g b -> p (g b)").bitcast(FP8X4),
                scales=h_mx[e][1][:].rearrange("p g b -> p (g b)"),
                in_=hid.pop(e)[:].rearrange("p g b t -> p (g b t)"))
            give("hg")

        def region(key, count):
            if key[0] == "y":
                return slice(key[2], key[2] + count), slice(T_RUN, CW)
            first = key[1] % GROUPS * T_GROUP
            return slice(0, CHUNKS), slice(first, first + count * T_GROUP)

        def sums(key, bank, half, count):
            acc = accs[bank][:, half * YW:(half + count) * YW]
            if key[0] == "y":
                return acc.rearrange("b (c w) -> b c w", c=count)
            return acc.rearrange("b (l c) -> b c l", c=CHUNKS)

        def mix(e, cs, ws, acc):
            if "mix" not in late:
                late["mix"] = place([B, D], F32, AT_MIX, "mix")
            nc.vector.scalar_tensor_tensor(
                out=chunks(late["mix"][:])[:, cs, ws], in0=acc, scalar=prob[:, e:e + 1],
                in1=chunks(late["mix" if e else "bias"][:])[:, cs, ws], op0=ALU.mult, op1=ALU.add)

        def mix_bank(e, bank, parts):
            for key, half, count in parts:
                mix(e, *region(key, count), sums(key, bank, half, count))
            accs.pop(bank)
            give(("bank", bank))

        def turn_x_back(j):
            first = 2 * j * CW // K_PASS
            bank = take_bank(("x", j), [B, 2, P, 2], F32)
            words = x_grouped[:].bitcast(F32).rearrange("p (g b w) -> p g b w", g=V_PASSES, w=2)
            for g in range(2):
                for w in range(2):
                    nc.tensor.transpose(bank[:, g, :, w], words[:, first + g, :, w], ident[:])
            skip = 2 * j * CW - first * K_PASS
            flat = bank[:].rearrange("b g p w -> b (g p w)").bitcast(BF16)
            x_banks[j] = flat[:, skip:skip + 2 * CW].rearrange("b (c w) -> b c w", c=2)

        def cross(engine, dst, cs, ws):
            engine.tensor_tensor(
                out=dst, in0=chunks(late["mix"][:])[:, cs, ws], in1=chunks(late["x0"][:])[:, cs, ws], op=ALU.mult)

        def finish(part, cs, ws):
            j = cs.start // 2
            nc.vector.tensor_tensor(
                out=part, in0=part, in1=x_banks[j][:, cs.start - 2 * j:cs.stop - 2 * j, ws], op=ALU.add)

        def store(part, cs, ws, queue=nc.sync):
            queue.dma_start(out=chunks(out)[:, cs, ws], in_=part)

        def cross_turned(half):
            if half == 0:
                crossed["t"] = place([B, CHUNKS, T_RUN], F32, take(free_grouped, "crossed t", newest=True), "crossed")
            ws = slice(half * T_RUN // 2, (half + 1) * T_RUN // 2)
            cross(nc.gpsimd, crossed["t"][:, :, ws], slice(0, CHUNKS), ws)

        def finish_turned(j):
            cs = slice(2 * j, 2 * j + 2)
            finish(crossed["t"][:, cs, :], cs, slice(0, T_RUN))
            if cs.stop == CHUNKS:
                store(crossed["t"][:], slice(0, CHUNKS), slice(0, T_RUN))

        def cross_plain(j, where=None):
            if where is None:
                where = take(free_grouped, ("crossed", j), newest=True)
            crossed[j] = place([B, 2, YW], F32, where, "crossed")
            cross(nc.gpsimd, crossed[j][:], slice(2 * j, 2 * j + 2), slice(T_RUN, CW))

        def finish_plain(j):
            cs, ws = slice(2 * j, 2 * j + 2), slice(T_RUN, CW)
            finish(crossed[j][:], cs, ws)
            store(crossed[j][:], cs, ws)
            give(("bank", ("x", j)))

        make_identity(nc, ident[:])
        nc.vector.tensor_copy(out=ident16[:], in_=ident[:])
        nc.vector.tensor_copy(
            out=perm16[:].rearrange("q (g c t) -> q g c t", g=U_PASSES, c=CHUNKS),
            in_=ident[:].rearrange("q (t c g) -> q g c t", g=U_PASSES, c=CHUNKS))

        with tc.manual_schedule():
            stage = [AT_STAGE + j * SLOT for j in range(STAGE_SLOTS - 1)] + [AT_SPARE]
            scales = v_scale.rearrange("o (g p t) u -> p (o g) (t u)", p=P, t=PACK)
            nc.scalar.dma_start(out=scale_first[:], in_=scales[:, :1, :])
            nc.scalar.dma_start(out=gate_sb[:], in_=gate_logits)
            load_slab(0, stage[0], [(slice(t, t + 1), slice(0, W)) for t in range(PACK)]
                      + [(ts, slice(W, R)) for ts, cs in whole])
            nc.sync.dma_start(out=scale_rest[:], in_=scales[:, 1:, :])
            load_slab(1, stage[1])
            x_early = place([B, D], BF16, stage[2], "x_early")
            nc.sync.dma_start(out=x_early[:], in_=x)
            early_at = [stage[3]] + [AT_TURN[1] + j * SLOT for j in range(T_BYTES // SLOT)]
            for j, where in enumerate(early_at):
                load_slab(2 + j, where, whole)
                for r in range(2 * j, min(2 * j + 2, T_PIECES)):
                    load_turn(0, r)
            next_slab = 2 + len(early_at)

            for e in range(E):
                nc.scalar.activation(
                    out=prob[:, e:e + 1], in_=gate_sb[:, 1 - e:2 - e], func=ACT.Sigmoid,
                    scale=-1.0, bias=gate_sb[:, e:e + 1])
            for t in range(PACK):
                widen(0, t, 0, W, on_scalar=(t == 2))
            by_scalar(("v", 0), SHARE_HEAD, W)
            for t in range(PACK):
                widen(0, t, W, R)
            by_vector(("v", 0), 0, SHARE_HEAD)
            eye_interleave(("v", 1))
            arrange(("v", 1), SHARE_HEAD)
            by_vector(("v", 1), 0, SHARE_HEAD)
            for t in range(PACK):
                widen(1, t, 0, R)
            x_words = x_early[:].bitcast(F32)
            for q in range(V_PASSES // 2):
                bank = take_bank(("x", q), [P, 4, B], F32)
                for j in range(2):
                    for w in range(2):
                        first = K_PASS // 2 * (2 * q + j)
                        nc.tensor.transpose(
                            bank[:, 2 * j + w, :], x_words[:, first + w:first + K_PASS // 2:2], ident[:])
                nc.scalar.copy(
                    out=x_grouped[:, q * W:(q + 1) * W].bitcast(F32).rearrange("p (j r w) -> p j r w", j=2, w=2),
                    in_=bank[:].rearrange("p (j w) r -> p j r w", w=2))
                give(("bank", ("x", q)))
            eye_interleave(("v", 2))

            def quantize_x():
                for lo, hi in ((0, 4), (4, V_PASSES)):
                    nc.vector.quantize_mx(
                        out=x_codes[:, lo:hi, :].rearrange("p g b -> p (g b)").bitcast(FP8X4),
                        scales=x_scales[:, lo:hi, :].rearrange("p g b -> p (g b)"),
                        in_=x_grouped[:, lo * K_PASS:hi * K_PASS])

            units = [("v", i) for i in range(RH * len(slabs))]
            for e, lo, hi in ((0, 0, 6), (1, 0, 4), (0, 6, 8), (1, 4, 8)):
                units.extend([("y", e, ch) for ch in range(lo, hi)])
            n, n_v = len(units), RH * len(slabs)
            long_steps = n_v - 2 * RH
            loads, early, groups, later, from_psum = {}, {}, {}, {}, {}

            def at(table, step, fn, *args):
                table.setdefault(step, []).append((fn, args))

            def run(table, step):
                for fn, args in table.pop(step, []):
                    fn(*args)

            def widened(i):
                return RH * (i - 1)

            def arranged(i):
                return RH * (i + 1) - 2

            def share(i):
                if i >= n:
                    return 0
                if i >= n - len(SHARE_END):
                    return SHARE_END[i - n]
                if i >= long_steps + 2:
                    return SHARE_U
                return SHARE_V if i % RH == 1 and i not in EYE_UNITS else 0

            ring = STAGE_SLOTS - 1
            last_slab = len(slabs) - 1
            wide_at = [AT_WIDE + i % 3 * WIDE_BYTES for i in range(len(slabs))]
            for i in range(next_slab, len(slabs)):
                at(loads, 0 if i < next_slab + ring else widened(i - ring), load_slab, i, stage[(i - next_slab) % ring])
            at(loads, 0, load_c)
            for r in range(T_PIECES):
                at(loads, widened(next_slab - 1) + r // 2, load_turn, 1, r)
            at(loads, widened(last_slab - 2), free_stage.append, stage[2])
            at(loads, 15, free_codes.extend, [AT_SPARE, AT_SPARE + CODE_BYTES])
            for i in range(last_slab - 2, last_slab + 1):
                at(loads, arranged(i), free_stage.append, wide_at[i])
            at(loads, arranged(last_slab - 2), free_stage.append, wide_at[last_slab - 2] + SLOT)
            at(loads, arranged(last_slab - 1), free_codes.append, wide_at[last_slab - 1] + SLOT)
            for i in (last_slab - 1, last_slab):
                at(loads, widened(i), free_stage.append, stage[(i - next_slab) % ring])
            tanh_at = (stage[3], wide_at[last_slab] + SLOT)
            at(loads, n_v + 3, free_codes.append, tanh_at[1])
            stream = [(load_y, (key,)) for key in units[n_v:]]
            stream.insert(len(stream) - 4, (load_x0, ()))

            expert_end = [(e + 1) * n_v // E - 1 for e in range(E)]
            hidden_turns = [end + 3 for end in expert_end]
            hidden_scales = [end + 4 for end in expert_end]
            hidden_done = [end + 5 for end in expert_end]

            batch_at = [11, 17, 23, T_LAST + 1]

            def banks_of(s):
                if s < T_FIRST or s > T_LAST:
                    return 0
                count = 2 if s < long_steps or s >= T_LAST - 1 else 1
                less = s == T_FIRST or s in hidden_turns or (s in batch_at and s < n_v) or (s - 1 in batch_at and s != n_v)
                return count - (1 if less else 0)

            def reuse_first_turned():
                fn, args = stream.pop(0)
                fn(*args, [AT_ONCE + CODE_BYTES])
                load_bias()
                free_codes.append(AT_LATE)
                free_grouped.append(AT_LATE + CODE_BYTES)

            def reads(step, e, bank, key, count):
                at(from_psum, step, mix_bank, e, bank, [(key, 0, count)])

            end = n - 4
            first_reads = batch_at[-1] + READ_LAG
            released = {}
            at(released, end, cross_turned, 0)
            at(released, end + 1, cross_plain, 0)
            closing = {}
            for j in range(CHUNKS // 2):
                at(closing, end + 1, finish_turned, j)
            at(closing, end + 2, finish_plain, 0)

            pairs, quantized = [], []

            def multiply_pairs(s):
                while pairs and pairs[0][0] <= s and s >= (n_v - 1, batch_at[-1])[pairs[0][1] // GROUPS]:
                    q = pairs.pop(0)[1]
                    for half in range(2):
                        multiply_y(("t", q + half), ("pair", q), half)
                    reads(s + 3 if s < batch_at[-1] else first_reads if s == batch_at[-1] else end, q // GROUPS, ("pair", q), ("t", q), 2)

            at(later, 0, quantize_x)
            for s in range(n - 1):
                run(loads, s)
                while stream and free_stage:
                    fn, args = stream.pop(0)
                    fn(*args)
                if s < long_steps:
                    for t in (2 * (s % 2), 2 * (s % 2) + 1):
                        widen(s // 2 + 2, t, 0, R)
                run(early, s)
                ready = len(full) if s <= T_LAST else min(len(full), 1)
                turn(banks_of(s))
                if len(turned) - banks_of(s) < T_RUN // T_BANK <= len(turned):
                    at(loads, s + 1, reuse_first_turned)
                if s + 2 < n - 2:
                    arrange(units[s + 2], share(s + 2))
                elif s + 2 == n - 2:
                    by_scalar(before_last, share(s + 2), NB)
                    by_scalar(before_last, NB, W)
                elif s + 2 == n - 1:
                    eye_interleave(last)
                    by_scalar(last, share(s + 2), NB)
                    empty_eye(last)
                    by_scalar(last, NB, W)
                run(groups, s)
                for b in range(ready):
                    empty_bank()
                while groups_full:
                    key = groups_full.pop(0)
                    at(groups if s < long_steps - 2 else later, s + GROUP_LAG, quantize, key)
                    if key[1] % 2 == 1:
                        pairs.append((s + GROUP_LAG, key[1] - 1))
                if s + 3 in EYE_UNITS:
                    eye_interleave(units[s + 3])
                if s < n - 2:
                    quantize(units[s])
                else:
                    quantize(before_last, 0, NB)
                    cross_plain(1, parts[before_last, 0][0])
                    quantize(before_last, NB, W)
                if s in from_psum and s < end:
                    pool_interleave(units[s + 3], len(from_psum[s]))
                run(released, s)
                if s not in from_psum:
                    run(later, s)
                if share(s + 2) > 0:
                    by_vector(units[s + 2], 0, share(s + 2))
                if s == end:
                    pair = [job for job in from_psum[s] if job[1][1][0] == "pair"]
                    from_psum[s].remove(pair[0])
                    for fn, args in [from_psum[s].pop(0)] + pair:
                        fn(*args)
                    cross_turned(1)
                run(from_psum, s)
                run(closing, s)
                run(later, s)
                if s in REDIR:
                    free_codes.append(held.pop(("raw", units[s + 2]))[1])
                elif n_v <= s + 2 < n:
                    give(("raw", units[s + 2]))
                quantized.append(s)
                if T_FIRST <= s < batch_at[-1] and s not in batch_at:
                    continue
                batch, quantized = quantized, []
                if s >= batch_at[-1]:
                    multiply_pairs(s)
                for i in batch:
                    key = units[i]
                    if key[0] == "v":
                        multiply_v(i)
                    elif key[1:] < (1, CHUNKS - 2):
                        bank = ("y", key[1], key[2] // 2)
                        multiply_y(key, bank, key[2] % 2)
                        if key[2] % 2 == 1:
                            reads(first_reads if i < n_v + 4 else max(end, s + 1), key[1], bank, units[i - 1], 2)
                    else:
                        multiply_y(key, "next to last", 0)
                    if i in expert_end:
                        e = expert_end.index(i)
                        at(groups, s + 2, hidden_tanh, e, tanh_at[e])
                        at(early, hidden_turns[e], hidden_turn, e)
                        for g in range(U_PASSES):
                            at(from_psum, hidden_scales[e], hidden_scale, e, g)
                        at(later, hidden_done[e], hidden_quantize, e)
                multiply_pairs(s)
                if end - 1 <= s <= end:
                    for j in range(2):
                        turn_x_back(2 * (s - end + 1) + j)

            quantize(last, 0, NB)
            multiply_y(last, "last", 0, [0, 1], True, False)
            quantize(last, NB, W - EYE_END)
            cross_plain(2, parts[last, NB][0])
            quantize(last, W - EYE_END, W)
            multiply_y(last, "last", 0, [2, 3], False, True)
            finish_plain(1)
            mix_bank(1, "next to last", [(units[n - 2], 0, 1)])
            mix_bank(1, "last", [(last, 0, 1)])
            ends = [region(key, 1) for key in units[n - 2:]]
            for cs, ws in ends:
                cross(nc.vector, chunks(late["mix"][:])[:, cs, ws], cs, ws)
            finish_plain(2)
            for (cs, ws), queue in zip(ends, (nc.sync, nc.scalar)):
                finish(chunks(late["mix"][:])[:, cs, ws], cs, ws)
                store(chunks(late["mix"][:])[:, cs, ws], cs, ws, queue)
